import numpy as np, ml_dtypes
CORES = [10,34,74,98]
N = 4
import mx_ref
BF = ml_dtypes.bfloat16
def entries(a):
    return np.ascontiguousarray(a.T).reshape(-1)
def table(e):
    return np.ascontiguousarray(np.reshape(e, (-1, 16)).T).astype(np.int32)
def pick(q, e):
    c = np.concatenate([q[0].reshape(128, -1, 4), np.zeros((128, 1, 4), np.uint8)], axis=1); s = np.concatenate([q[1], np.ones((16, 1), np.uint8)], axis=1)
    return (np.ascontiguousarray(c[:, e].reshape(128, -1)), np.ascontiguousarray(s[:, e]))
def join(*qs):
    return (np.concatenate([q[0] for q in qs], axis=1), np.concatenate([q[1] for q in qs], axis=1))
def put(q, e, v):
    c, s = q[0].reshape(128, -1, 4).copy(), q[1].copy(); c[:, e] = v[0].reshape(128, -1, 4); s[:, e] = v[1]
    return (c.reshape(128, -1), s)
def pk(c, s):
    return (np.ascontiguousarray(c), mx_ref.live(s))
def emit(q):
    return q[0], q[1]
def decode(q):
    o = []
    for b in range(4):
        e = np.zeros((128, 128, 4), np.float32); e[np.arange(128), np.arange(128), b] = 1
        o.append(mx_ref.matmul(mx_ref.quantize(e.reshape(128, 512).astype(BF)), q))
    return np.stack(o, axis=2).reshape(128, -1)
def f(rng, *shape):
    return mx_ref.flush((rng.standard_normal(shape, dtype=np.float32) * np.exp2(rng.integers(-2, 3, shape[:-1] + (1,)))).astype(BF))
def wide(rng, *shape, cols=0):
    v = rng.standard_normal(shape, dtype=np.float32) * np.exp2(rng.integers(-12, 13, shape)).astype(np.float32)
    if cols: v *= np.repeat(np.exp2(rng.integers(-cols, cols + 1, shape[:-2] + (1, shape[-1] // 4))) * (rng.random(shape[:-2] + (1, shape[-1] // 4)) > 0.0625), 4, axis=-1).astype(np.float32)
    return mx_ref.flush(v.astype(BF))
M, K, J, R = 256, 80, 3, 3
def unpack(q):
    c = q[0].reshape(16, 8, -1, 4).astype(int)
    s = np.broadcast_to(q[1].astype(int)[:, None, :, None], c.shape)
    k = np.unique(q[1]).astype(int)
    k = np.concatenate([k, np.ones(4 + k.size % 2, int)])
    here = np.zeros((256, 256), np.uint8)
    here[s, c] = c
    z = np.zeros((128, k.size, 4), np.uint8)
    z[:64] = here[k].reshape(-1, 64, 4).transpose(1, 0, 2)
    v = decode((z.reshape(128, -1), np.repeat(k[None], 16, axis=0).astype(np.uint8)))
    held = np.zeros((256, 256), np.float32)
    held[k] = v.reshape(128, -1, 4)[:64].transpose(1, 0, 2).reshape(-1, 256)
    return held[s, c].reshape(128, -1)
def big(v):
    v = np.array(v)
    v[np.abs(v.astype(np.float32)) < np.float32(2.0 ** -16)] = 0
    return v
def bf(v):
    return np.asarray(v, np.float32).astype(BF)
def parts(t):
    return t.reshape(N, 128, -1, 4)
def store(e):
    return np.stack([table(v.T) for v in e.reshape(N, M, J)])
def setup_inputs(rng):
    return {"x": big(f(rng, N, 128, 4 * M)), "u": np.array(f(rng, N, 128, 512)), "w": np.array(f(rng, N, 128, 512)), "nb": store(rng.integers(0, N * M, (N * M, J)))}
def setup_inputs_chain(rng):
    d, n = setup_inputs(rng), N * M
    at = rng.permutation(n)
    e = at[rng.integers(0, np.arange(1, n + 1)[:, None], (n, J))]
    j = np.arange(n - 1)
    e[j, rng.integers(0, J, n - 1)] = at[j + 1]
    nb, h = np.zeros((n, J), int), np.zeros(n, int)
    nb[at], h[at] = e, np.arange(n)
    x, u = parts(d["x"]), parts(d["u"])
    x[:, :16] = 0
    u[:, :, :R] = 0
    for k in range(12):
        x[:, 4 * (k // 4), :, k % 4] = bf((h >> k & 1).reshape(N, M))
        u[:, 4 * (k // 4), :R, k % 4] = 2.0 ** k
    return {"x": x.reshape(N, 128, -1), "u": u.reshape(N, 128, -1), "w": d["w"], "nb": store(nb)}
def setup_inputs_deep(rng):
    d, n = setup_inputs(rng), N * M
    at = np.sort(rng.permutation(n).reshape(-1, 4), axis=1)
    nb, low = np.zeros((n, J), int), np.zeros(n)
    for k in range(4): nb[at[:, k]] = at[:, [min(k + i, 3) for i in (1, 2, 3)]]
    low[at[1::2]] = 11
    x, u = parts(d["x"]), parts(d["u"])
    u[:, :, :R] = 0
    for t, k in enumerate(rng.permutation(R)):
        v = np.zeros(n)
        v[at] = [(4, 4, 4, 7), (4, 7, 4, 6), (7, 7, 5, 5)][k]
        x[:, 40 * t:40 * t + 40] = bf((v - low).reshape(N, 1, M, 1) * 2.0 ** 27)
        u[:, 40 * t:40 * t + 40, t] = 2.0 ** 30
    return {"x": x.reshape(N, 128, -1), "u": u.reshape(N, 128, -1), "w": d["w"], "nb": store(rng.permuted(nb, axis=1))}
def setup_inputs_peaks(rng):
    d, n = setup_inputs(rng), N * M
    who = rng.permutation(N)
    peaks = [M * who[t] + rng.permutation(M)[:K] for t in range(R)]
    lone = np.zeros(n, bool)
    lone[np.concatenate(peaks)] = True
    lone[M * who[R]:M * who[R] + M] = True
    m = np.flatnonzero(~lone)
    nb = np.repeat(np.arange(n)[:, None], J, axis=1)
    x, u = parts(d["x"]), parts(d["u"])
    u[:, :, :R] = mx_ref.flush(bf(u[:, :, :R].astype(np.float32) * np.float32(2.0 ** -6)))
    for t in range(R):
        nb[m, t] = rng.permutation(np.concatenate([peaks[t], peaks[t], rng.choice(peaks[t], m.size - 2 * K)]))
        level = rng.integers(1, 4, n)
        level[peaks[t]] = 7
        x[:, 32 * t:32 * t + 16] = 0
        u[:, 32 * t:32 * t + 16, :R] = 0
        x[:, 32 * t, :, 0] = bf(level.reshape(N, M))
        u[:, 32 * t, t, 0] = 1024
    return {"x": x.reshape(N, 128, -1), "u": u.reshape(N, 128, -1), "w": d["w"], "nb": store(rng.permuted(nb, axis=1))}
def setup_inputs_spread(rng):
    return {**setup_inputs(rng), "x": big(wide(rng, N, 128, 4 * M, cols=6))}
def setup_inputs_ties(rng):
    d = setup_inputs(rng)
    x, u = parts(d["x"]), parts(d["u"])
    x[:, :16] = 0
    x[:, 0, :, 0] = 4
    u[:, :, :R] = 0
    u[:, 0, :R, 0] = -2.0 ** 30
    for t in range(R):
        p = 32 * t + 32
        x[:, p:p + 16] = 0
        x[:, p, :, 0] = bf(rng.integers(4, 8, (N, M)))
        u[:, p, t, 0] = 1024
    return {"x": x.reshape(N, 128, -1), "u": u.reshape(N, 128, -1), "w": d["w"], "nb": d["nb"]}
def check_inputs(d):
    b = []
    for k in ("x", "u", "w"):
        v = np.abs(d[k].astype(np.float32))
        if not (np.isfinite(v).all() and ((v == 0) | (v >= 2.0 ** -30) & (v <= 2.0 ** 30)).all()): b.append("a value of " + k)
    if d["nb"].min() < 0 or d["nb"].max() >= N * M: b.append("nb")
    return b
def reference(x, u, w, nb):
    node = np.arange(N * M)
    near = np.concatenate([entries(nb[r]).reshape(J, M).T for r in range(N)])
    near = np.sort(np.concatenate([node[:, None], near], axis=1), axis=1)
    state = join(*[mx_ref.quantize(np.ascontiguousarray(x[r])) for r in range(N)])
    own = node.reshape(N, M)
    pieces = [np.concatenate([own[r], np.full(-M % 128, -1)]).reshape(-1, 128) for r in range(N)]
    qu = [mx_ref.quantize(np.ascontiguousarray(u[r][:, :16])) for r in range(N)]
    y, rt = np.zeros((N, 128, M), np.float32), np.zeros((N, 1, R * M), np.float32)
    oc, osc = np.zeros((N, 128, 4 * M), np.uint8), np.zeros((N, 16, M), np.uint8)
    for t in range(R):
        h = np.concatenate([np.concatenate([mx_ref.matmul(pick(state, e), qu[r])[:, t] for e in pieces[r]])[:M] for r in range(N)]) + np.float32(0)
        root = near[node, np.argmax(h[near], axis=1)]
        while (root[root] != root).any(): root = root[root]
        size = np.bincount(root, minlength=N * M)
        chosen = np.argsort(-size, kind="stable")[:K]
        m = np.flatnonzero(np.isin(root, chosen) & (root != node))
        if m.size:
            v = unpack(state).reshape(128, N * M, 4)
            v = (v[:, m] + v[:, root[m]]) * np.float32(0.5)
            v = np.concatenate([v, np.zeros((128, -m.size % 4, 4), np.float32)], axis=1)
            new = mx_ref.quantize(np.ascontiguousarray(v.reshape(128, -1).astype(BF)))
            state = put(state, m, pick(new, np.arange(m.size)))
        rt[:, 0, t * M:t * M + M] = root.reshape(N, M)
    for r in range(N):
        y[r] = mx_ref.matmul(mx_ref.quantize(np.ascontiguousarray(w[r])), pick(state, own[r]))
        oc[r], osc[r] = emit(pick(state, own[r]))
    return {"y": y, "oc": oc, "osc": osc, "rt": rt}

@@ -1,0 +1,687 @@
+import numpy as np
+from concourse.bass import DstId, RemoteDMATransfer
+from concourse.mybir import dt, AluOpType, AxisListType, ActivationFunctionType
+
+ALU = AluOpType
+AF = ActivationFunctionType
+N, M, K, J, R = 4, 256, 80, 3, 3
+NM = N * M
+H = M // 2
+SMAX = NM // K + 1
+NTH = SMAX - 1
+NTS = 8
+BIG = 4.0 * NM
+BIGR = NM + K
+WINV = BIGR + M + K
+RUNS = ((0, 128, 0, 4), (128, 256, 512, 2), (256, 768, 768, 1), (768, 896, 1280, 2), (896, 1024, 1536, 4))
+WS, MID = 2048, 1024.0
+TOP = 1100.0
+UP = float(2 ** 30)
+VPART = ((0, 128), (128, 256), (256, 288))
+SPART = ((288, 768), (768, 896), (896, 1024))
+SCUT = SPART[0][1]
+CUT3 = 512
+C8, U8, F32, B16, I32, U16 = "float8_e4m3fn_x4", "uint8", "float32", "bfloat16", "int32", "uint16"
+
+SCRATCH = {
+    "xt": ("sbuf", [128, 4 * M], B16), "ut": ("sbuf", [128, 512], B16), "wt": ("sbuf", [128, 512], B16),
+    "qu": ("sbuf", [128, 128], C8), "su": ("sbuf", [128, 128], U8),
+    "qw": ("sbuf", [128, 128], C8), "sw": ("sbuf", [128, 128], U8),
+    "qr": ("sbuf", [128, 384], C8), "sr": ("sbuf", [128, 384], U8),
+    "one": ("sbuf", [128, NM], B16), "et": ("sbuf", [128, 2048], B16),
+    "qe": ("sbuf", [128, 512], C8), "se": ("sbuf", [128, 512], U8),
+    "bl": ("psum", [128, 4096], F32),
+    "d0": ("sbuf", [128, 512], B16), "io2": ("sbuf", [128, M], F32),
+    "dg": ("sbuf", [128, NM], B16), "dw": ("sbuf", [128, NM], B16), "wb": ("sbuf", [128, NM + 16], B16),
+    "w0": ("sbuf", [128, WS], B16), "w1": ("sbuf", [128, WS], B16), "w2": ("sbuf", [128, WS], B16), "w3": ("sbuf", [128, WS], B16),
+    "idn": ("sbuf", [128, WS], F32), "rtf": ("sbuf", [128, M], F32),
+    "xe": ("sbuf", [128, NM], F32), "xb": ("sbuf", [128, NM], B16), "fh": ("sbuf", [128, NM], F32), "fs": ("sbuf", [128, WS], B16),
+    "fa": ("sbuf", [128, WS], B16), "fb": ("sbuf", [128, WS], B16), "fc": ("sbuf", [128, WS], B16),
+    "la": ("sbuf", [128, 64], U16), "lb": ("sbuf", [128, 64], U16), "lc": ("sbuf", [128, 64], U16), "l0": ("sbuf", [128, 64], U16),
+    "sc": ("sbuf", [128, NM], B16), "scf": ("sbuf", [128, 128], F32), "ra": ("sbuf", [128, 1536], F32), "rb": ("sbuf", [128, 1536], F32),
+    "trs": ("sbuf", [128, NM], F32), "dvs": ("sbuf", [128, NM], F32), "dvt": ("sbuf", [128, NM - CUT3], F32),
+    "ht": ("sbuf", [128, M], F32), "ho": ("sbuf", [128, M], F32), "rs": ("sbuf", [128, M], B16), "inv": ("sbuf", [128, WINV], F32),
+    "iw": ("sbuf", [128, 64], I32), "iu": ("sbuf", [128, 24], I32), "id16": ("sbuf", [128, 16], I32),
+    "cm": ("sbuf", [128, 32 * NTH], F32),
+    "nbe": ("sbuf", [128, 48], I32), "nbl": ("sbuf", [128, 64], U16), "nbw": ("sbuf", [128, 64], U16), "lnb": ("sbuf", [128, 96], U16),
+    "lnw": ("sbuf", [128, 96], U16),
+    "sz8": ("sbuf", [128, 8], F32), "rot": ("sbuf", [128, 32], F32), "acc": ("sbuf", [128, 8], F32), "ypd": ("sbuf", [128, 32], F32),
+    "szs": ("sbuf", [128, 32], F32), "hb": ("sbuf", [128, 4 * M], B16), "ys": ("sbuf", [128, M], F32),
+}
+SMALL = {
+    "zf": (F32, {"d16": 16, "d17": 16, "cf": 32, "ri": 32, "mlt": 32, "rest": 32, "rest2": 64, "alp": 32, "one32": 32, "cn": 128, "sn": 16, "ki": 16, "s80": 8,
+                 "nn": 128, "nm": 96, "n1": 128, "n2": 128, "n3": 128, "n4": 128,
+                 "m1": 32, "mm": 32, "eq4": 128, "b4": 128, "b2": 64, "b1": 32, "tn": 32, "zz": 64, "zt": 64, "thr": 8, "t2": 8,
+                 "ytr": 32, "col": 8, "a1": 32, "cs": 32, "f2": 32, "g1": 32, "ge": 64, "inc": 64, "hh": 64, "je": 64, "a2": 64, "a2t": 64,
+                 "ug": 32, "ue": 32, "um": 32, "slot": 32, "sx": 32,
+                 "rho": 64, "j2f": 8, "mx": 8, "mx1": 8, "xo": 8, "xm": 8}),
+    "zi": (I32, {"ip": 16, "aci": 4}),
+    "zu": (U16, {"cexp": 64, "crep": 64, "cu": 24, "twice": 4, "rotl": 2, "lro": 16, "sll": 16, "j1": 6, "j2": 6, "pl": 16, "kl": 16}),
+}
+AT = {}
+for _b, (_d, _parts) in SMALL.items():
+    _o = 0
+    for _n, _w in _parts.items():
+        AT[_n] = (_b, _o, _w)
+        _o += -(-_w // 16) * 16
+    SCRATCH[_b] = ("sbuf", [128, _o], _d)
+for _t in range(R):
+    SCRATCH["xh%d" % _t] = ("sbuf", [128, 32], F32)
+    for _n in ("a", "b"):
+        SCRATCH["q%s%d" % (_n, _t)] = ("sbuf", [128, 2 * K], C8)
+        SCRATCH["s%s%d" % (_n, _t)] = ("sbuf", [128, 2 * K], U8)
+    SCRATCH["qp%d" % _t] = ("sbuf", [128, M], C8)
+    SCRATCH["sp%d" % _t] = ("sbuf", [128, M], U8)
+for _t in range(R + 1):
+    SCRATCH["qc%d" % _t] = ("sbuf", [128, 2 * M if _t < R else M], C8)
+    SCRATCH["scp%d" % _t] = ("sbuf", [128, 2 * M if _t < R else M], U8)
+
+SEMAPHORES = (["ev", "es", "et", "eg", "loc", "nbr"] + ["h%d" % t for t in range(R)]
+              + ["%s%d" % (k, t) for t in range(R) for k in ("ac", "as", "bc", "bs")]
+              + ["dx", "du", "dw", "dnb", "dswap", "dnum", "drot", "drt", "dout"])
+
+
+def place(n):
+    for n0, n1, c, s in RUNS:
+        if n0 <= n < n1:
+            return c + s * (n - n0)
+    return WS
+
+
+def rank_program(g, core, T, topo):
+    rank = T.rank_of(core)
+    if rank is None:
+        return
+    queue = {"v": g.vector, "s": g.scalar, "t": g.tensor, "g": g, "y": g.sync}
+    esem = {"v": "ev", "s": "es", "t": "et", "g": "eg"}
+    cnt, known, clock, hist = {}, {k: {} for k in queue}, {}, {}
+
+    def V(name, a=0, b=None, step=1, p0=0, p1=128):
+        buf, off, w = AT[name] if name in AT else (name, 0, SCRATCH[name][1][1])
+        return (buf, off + a, off + (w if b is None else b), step, p0, p1)
+
+    def A(r):
+        return T[r[0]][r[4]:r[5], r[1]:r[2]] if r[3] == 1 else T[r[0]][r[4]:r[5], r[1]:r[2]:r[3]]
+
+    def meets(a, b):
+        if a[1] >= b[2] or b[1] >= a[2] or a[4] >= b[5] or b[4] >= a[5]:
+            return False
+        return not (a[3] == b[3] and a[3] > 1 and (a[1] - b[1]) % a[3])
+
+    def grown(r):
+        return (r[0], r[1] // 512 * 512, -(-r[2] // 512) * 512, 1, 0, 128)
+
+    def split(reads, writes):
+        ps = [r for r in list(reads) + list(writes) if SCRATCH[r[0]][0] == "psum"]
+        return ([r for r in reads if SCRATCH[r[0]][0] != "psum"],
+                [r for r in writes if SCRATCH[r[0]][0] != "psum"] + [grown(r) for r in ps])
+
+    def use(qn, reads, writes):
+        reads, writes = split(reads, writes)
+        need = {}
+        for r, w in [(r, False) for r in reads] + [(r, True) for r in writes]:
+            for e, ew, sem, val in hist.get(r[0], []):
+                if (w or ew) and meets(r, e) and known[qn].get(sem, 0) < val:
+                    need[sem] = max(need.get(sem, 0), val)
+        for sem in sorted(need):
+            if any(o != sem and clock[(o, need[o])].get(sem, 0) >= need[sem] for o in need):
+                continue
+            queue[qn].wait_ge(T.sem[sem], need[sem])
+        for sem in need:
+            for s2, v2 in clock[(sem, need[sem])].items():
+                known[qn][s2] = max(known[qn].get(s2, 0), v2)
+            known[qn][sem] = max(known[qn].get(sem, 0), need[sem])
+
+    def mark(sem, val, reads, writes):
+        reads, writes = split(reads, writes)
+        for r in writes:
+            hist[r[0]] = [h for h in hist.get(r[0], [])
+                          if not ((r[3] == 1 or h[0] == r) and r[1] <= h[0][1] and h[0][2] <= r[2] and r[4] <= h[0][4] and h[0][5] <= r[5])]
+        for r, w in [(r, False) for r in reads] + [(r, True) for r in writes]:
+            hist.setdefault(r[0], []).append((r, w, sem, val))
+
+    def done(qn, inst, sem, n, reads, writes):
+        cnt[sem] = cnt.get(sem, 0) + n
+        inst.then_inc(T.sem[sem], n)
+        clock[(sem, cnt[sem])] = dict(known[qn])
+        mark(sem, cnt[sem], reads, writes)
+
+    def emit(qn, fn, outs, ins):
+        use(qn, ins, outs)
+        if qn == "g" and known["g"].get("eg", 0) < cnt.get("eg", 0):
+            g.wait_ge(T.sem.eg, cnt["eg"])
+            known["g"]["eg"] = cnt["eg"]
+        done(qn, fn(), esem[qn], 1, ins, outs)
+
+    def dmas(sem, items):
+        tot = cnt.get(sem, 0) + 16 * len(items)
+        merged = {}
+        for qn, out, in_, outs, ins in items:
+            use(qn, ins, outs)
+            queue[qn].dma_start(out, in_).then_inc(T.sem[sem], 16)
+            for s, v in known[qn].items():
+                merged[s] = max(merged.get(s, 0), v)
+        cnt[sem] = tot
+        clock[(sem, tot)] = merged
+        for qn, out, in_, outs, ins in items:
+            mark(sem, tot, ins, outs)
+
+    def arrives(sem, n, writes):
+        cnt[sem] = cnt.get(sem, 0) + n
+        clock[(sem, cnt[sem])] = {}
+        mark(sem, cnt[sem], [], writes)
+
+    def ind(win, off):
+        return A(win).indirect(A(off))
+
+    def cp(out, in_, off=None):
+        emit("v", lambda: g.vector.tensor_copy(A(out), A(in_) if off is None else ind(in_, off)), [out], [in_] + ([off] if off else []))
+
+    def ts(out, in0, s1, op0, s2=None, op1=None, off=None):
+        cols = [s for s in (s1, s2) if isinstance(s, tuple)]
+        val = lambda s: A(s) if isinstance(s, tuple) else s
+        src = lambda: A(in0) if off is None else ind(in0, off)
+        if op1 is None:
+            fn = lambda: g.vector.tensor_scalar(A(out), src(), val(s1), None, op0)
+        else:
+            fn = lambda: g.vector.tensor_scalar(A(out), src(), val(s1), val(s2), op0, op1)
+        emit("v", fn, [out], [in0] + cols + ([off] if off else []))
+
+    def tt(out, a, b, op, off=None):
+        emit("v", lambda: g.vector.tensor_tensor(A(out), A(a) if off is None else ind(a, off), A(b), op), [out], [a, b] + ([off] if off else []))
+
+    def red(out, in_, op):
+        emit("v", lambda: g.vector.tensor_reduce(A(out), A(in_), AxisListType.X, op), [out], [in_])
+
+    def scan(out, d0, d1, op0, op1):
+        emit("v", lambda: g.vector.tensor_tensor_scan(A(out), A(d0), A(d1), 0.0, op0, op1), [out], [d0, d1])
+
+    def tr(out, in_):
+        emit("v", lambda: g.vector.transpose(A(out), A(in_)), [out], [in_])
+
+    def fill(out, c):
+        emit("v", lambda: g.vector.memset(A(out), c), [out], [])
+
+    def act(out, in_, func=AF.Copy, off=None, accum=None, scale=None, **kw):
+        src = lambda: A(in_) if off is None else ind(in_, off)
+        cols = [scale] if isinstance(scale, tuple) else []
+        def fn():
+            k2 = dict(kw)
+            if scale is not None:
+                k2["scale"] = A(scale) if cols else scale
+            if accum is not None:
+                k2["accum_out"] = A(accum)
+            return g.scalar.activation(A(out), src(), func, **k2)
+        emit("s", fn, [out] + ([accum] if accum else []), [in_] + cols + ([off] if off else []))
+
+    def iota(out, pattern, base, cm):
+        if SCRATCH[out[0]][2] == I32:
+            fn = lambda: g.iota(A(out), pattern, base, cm)
+        else:
+            fn = lambda: g.iota(A(out), pattern, base, cm, allow_small_or_imprecise_dtypes=True)
+        emit("g", fn, [out], [])
+
+    def select(out, in_, pattern, cmp, fillv, base, cm):
+        emit("g", lambda: g.affine_select(A(out), A(in_), pattern, cmp, fillv, base, cm), [out], [in_])
+
+    def quant(q, s, in_):
+        emit("v", lambda: g.vector.quantize_mx(A(q), A(s), A(in_)), [q, s], [in_])
+
+    def mm(out, lq, ls, rq, rs, start, stop):
+        emit("t", lambda: g.tensor.matmul_mx(A(out), A(lq), A(ls), A(rq), A(rs), start, stop), [out], [lq, ls, rq, rs])
+
+    def pick(qo, so, qi, si, off):
+        emit("v", lambda: g.vector.tensor_copy(A(qo).bitcast(dt.uint32), A(qi).bitcast(dt.uint32).indirect(A(off))), [qo], [qi, off])
+        act(so, si, off=off)
+
+    others = [d for d in range(N) if d != rank]
+    mask3 = 0xFFFF
+    for d in others:
+        mask3 &= topo.mask(core, T.cores[d])
+    groups = bin(mask3).count("1")
+
+    def spread(src, sem):
+        use("g", [src], [])
+        ids = [DstId(rid=topo.addr(T.cores[d])[0], pnc=topo.addr(T.cores[d])[1]) for d in others]
+        g.remote_dma_fused([RemoteDMATransfer(dst_ids=ids, dma_engine_mask=mask3, remote_sem=T.sem[sem], srcs=[A(src)], dsts=[A(src) for d in others])],
+                           local_sem=T.sem.loc)
+        cnt["loc"] = cnt.get("loc", 0) + groups
+
+    near = [d for d in others if topo.same_plane(topo.chip(core), topo.chip(T.cores[d]))][0]
+    pair = sorted([rank, near])
+    pair2 = [d for d in range(N) if d not in pair]
+    far = pair2[pair.index(rank)]
+
+    def swap(q, s, d, semc, sems):
+        dst = T.cores[d]
+        rid, pid = topo.addr(dst)[:2]
+        mask, n = topo.mask(core, dst), len(topo.engines(core, dst))
+        use("g", [V(q, 0, K)], [])
+        g.remote_dma(A(V(q, K, 2 * K)).bitcast(dt.uint8), A(V(q, 0, K)).bitcast(dt.uint8), T.sem[semc], T.sem.loc, pid, rid, mask)
+        use("g", [V(s, 0, K)], [])
+        g.remote_dma(A(V(s, K, 2 * K)), A(V(s, 0, K)), T.sem[sems], T.sem.loc, pid, rid, mask)
+        cnt["loc"] = cnt.get("loc", 0) + 2 * n
+        arrives(semc, n, [V(q, K, 2 * K)])
+        arrives(sems, n, [V(s, K, 2 * K)])
+
+    def widen(x, c0, c1, on, to="xe"):
+        out, win, off = V(to, 32 * c0, 32 * c1), V(x, c0, c1), V("cexp", 0, 2 * (c1 - c0))
+        if on == "v":
+            cp(out, win, off)
+        else:
+            act(out, win, off=off)
+
+    def turn(f, c0, c1):
+        tr(V(f, 32 * c0, 32 * c1), V("xe", 32 * c0, 32 * c1))
+
+    def run(f, a, b):
+        n0, n1, c, s = [r for r in RUNS if r[0] <= a and b <= r[1]][0]
+        return V(f, c + s * (a - n0), c + s * (b - n0), s)
+
+    def runs(a, b):
+        return [(max(a, r[0]), min(b, r[1])) for r in RUNS if r[0] < b and a < r[1]]
+
+    def turn_s(f, c0, c1):
+        for a, b in runs(32 * c0, 32 * c1):
+            tr(run(f, a, b), V("xb", a, b))
+
+    CF = lambda k: V("cf", k, k + 1)
+    SCL, HI, LO, SCOL, LCOL, BCOL, BETA, HCOL = [CF(k) for k in (0, 4, 11, 6, 7, 8, 3, 4)]
+
+    def lift(f, a, b):
+        for x, y in runs(a, b):
+            scan(V("sc", x, y), V("d0", 0, y - x), run(f, x, y), ALU.mult, ALU.add)
+
+    def listed(out, a, b):
+        ts(out, V("sc", a + 15, b, 16), SCL, ALU.mult, MID, ALU.add)
+
+    bank = lambda k, w: V("bl", 512 * k, 512 * k + w)
+
+    loads = []
+    for k in range(8):
+        o = V("nbe", 0, 48 - 2 * (k % 2), 1, 16 * k, 16 * k + 16)
+        loads.append(("ys"[k % 2], A(o), T.nb[:, 2 * (k % 2):48], [o], []))
+    dmas("dnb", loads)
+    dmas("dx", [("y", A(V("xt")), T.x[:], [V("xt")], [])])
+    dmas("du", [("s", A(V("ut")), T.u[:], [V("ut")], [])])
+    IP = lambda k: V("ip", k, k + 1)
+    iota(V("iu"), [[1, 3], [0, 8]], 0, 0)
+    iota(IP(0), [[0, 1]], 0, 1)
+    iota(V("iw"), [[1, 32], [0, 2]], 0, 0)
+    iota(V("id16"), [[1, 16]], 128, -1)
+    iota(V("ri"), [[1, 32]], 0, 0)
+    fill(V("one"), 1.0)
+    cp(V("cu"), V("iu"))
+    ts(IP(4), IP(0), 4, ALU.logical_shift_right, 1, ALU.bitwise_and)
+    ts(IP(1), IP(0), 15, ALU.bitwise_and)
+    ts(IP(2), IP(0), 31, ALU.bitwise_and)
+    ts(IP(3), IP(0), 5, ALU.logical_shift_right)
+    cp(V("cexp"), V("iw"))
+    cp(CF(4), IP(4))
+    cp(V("cf", 6, 9), V("ip", 1, 4))
+    ts(V("id16"), V("id16"), 15, ALU.bitwise_and)
+    ts(V("iw"), V("iw"), 0.0, ALU.mult)
+    ts(SCL, SCOL, 15.0, ALU.is_equal, 1.0 - 1.0 / UP, ALU.mult)
+    ts(V("d16"), V("id16"), 1.0, ALU.is_equal, UP, ALU.mult)
+    ts(V("d17"), V("id16"), 0.0, ALU.is_gt)
+    ts(V("crep"), V("iw"), SCOL, ALU.add)
+    ts(SCL, SCL, 1.0 / UP, ALU.max)
+    tt(V("d16"), V("d16"), V("d17"), ALU.add)
+    cp(V("twice", 0, 2), V("crep", 0, 2))
+    ts(V("twice", 2, 4), V("crep", 0, 2), 16.0, ALU.add)
+    o = 16 * rank
+    for e in (0, 1):
+        cp(V("nbl", o + e, o + 12, 2, 0, 64), V("nbe", e, 24, 4, 0, 64))
+        cp(V("nbl", o + e, o + 12, 2, 64, 128), V("nbe", 24 + e, 48, 4, 64, 128))
+    cp(V("nbl", o + 12, o + 16), V("nbe", 0, 4))
+    spread(V("nbl", o, o + 16), "nbr")
+    arrives("nbr", groups * len(others), [V("nbl", 16 * d, 16 * d + 16) for d in others])
+    quant(V("qu"), V("su"), V("ut"))
+    pick(V("qr", 0, 128), V("sr", 0, 128), V("qu"), V("su"), V("cu", 0, 8))
+    act(V("d0"), V("d16"), off=V("crep", 0, 32))
+
+    def height(k, t, q, s, a, n):
+        mm(bank(k, n), V("qr", 128 * t, 128 * t + 128), V("sr", 128 * t, 128 * t + 128), V(q, a, a + n), V(s, a, a + n), True, True)
+
+    def share(t):
+        spread(V("xh%d" % t, 8 * rank, 8 * rank + 8), "h%d" % t)
+        arrives("h%d" % t, groups * len(others), [V("xh%d" % t, 8 * d, 8 * d + 8) for d in others])
+
+    def own_f(t):
+        widen("xh%d" % t, 8 * rank, 8 * rank + 8, "v")
+        turn("fh", 8 * rank, 8 * rank + 8)
+
+    def others_f(t):
+        xh = "xh%d" % t
+        widen(xh, 8 * others[1], 8 * others[1] + 8, "s")
+        widen(xh, 8 * others[2], 8 * others[2] + 8, "s")
+        widen(xh, 8 * others[0], 8 * others[0] + 8, "v")
+        for d in others:
+            turn("fh", 8 * d, 8 * d + 8)
+
+    for h in (0, 1):
+        quant(V("qc0", H * h, H * h + H), V("scp0", H * h, H * h + H), V("xt", 4 * H * h, 4 * H * h + 4 * H))
+    for h in (0, 1):
+        height(h, 0, "qc0", "scp0", H * h, H)
+    for h in (0, 1):
+        tr(V("ht", H * h, H * h + H), bank(h, H))
+    cp(V("xh0", 8 * rank, 8 * rank + 8), V("ht", 0, M, 32))
+    share(0)
+    dmas("dw", [("y", A(V("wt")), T.w[:], [V("wt")], [])])
+
+    iota(V("sn"), [[16, 16]], M * rank, 0)
+    iota(V("ki"), [[16, 16]], 0, 0)
+    iota(V("s80"), [[16, 8]], 0, 0)
+    select(V("dg"), V("one"), [[1, 32], [-1, 32]], ALU.is_equal, 0.0, 0, 0)
+    iota(V("io2"), [[1, M]], NM, 0)
+    for n0, n1, c, s in RUNS:
+        iota(V("idn", c, c + s * (n1 - n0), s), [[1, n1 - n0]], n0, 0)
+    ts(CF(12), BCOL, -8.0, ALU.mult, LCOL, ALU.add)
+    own_f(0)
+    ts(CF(13), CF(12), 6.0, ALU.is_equal)
+    ts(CF(14), CF(12), 7.0, ALU.is_equal, 2048.0, ALU.mult)
+    for k in range(J):
+        for e in (0, 1):
+            a = 32 * k + 8 * rank
+            cp(V("lnb", a + e, a + 8, 2), V("nbe", 16 * k + e, 16 * k + 16, 4))
+    tt(CF(15), CF(13), CF(14), ALU.add)
+    ts(BETA, LCOL, float(NTS), ALU.is_lt, NM / 2.0, ALU.mult)
+    fill(V("one32"), 1.0)
+    fill(V("wb", NM, NM + 16), 0.0)
+    ts(IP(6), IP(2), 7, ALU.bitwise_and)
+    ts(IP(7), IP(1), 3, ALU.logical_shift_right)
+    ts(IP(8), IP(1), 7, ALU.bitwise_and)
+    ts(V("alp"), V("one32"), BETA, ALU.mult, -1.0 / NM, ALU.mult)
+    ts(CF(9), IP(6), 32.0, ALU.mult, float(BIGR), ALU.add)
+    tt(IP(9), IP(3), IP(7), ALU.subtract)
+    cp(CF(20), IP(8))
+    ts(V("alp"), V("alp"), 1.0, ALU.add)
+    ts(IP(10), IP(9), 4.0, ALU.add)
+    ts(IP(11), IP(9), 2.0, ALU.add)
+    ts(V("sn"), V("sn"), SCOL, ALU.add)
+    ts(V("ip", 12, 14), V("ip", 10, 12), 3, ALU.bitwise_and)
+    ts(LO, HI, -1.0, ALU.mult, 1.0, ALU.add)
+    ts(V("rotl"), V("ip", 12, 14), 8.0, ALU.mult, CF(20), ALU.add)
+    fill(V("ypd"), 0.0)
+    for h in (0, 1):
+        n0 = M * rank + H * h
+        step = place(n0 + 1) - place(n0)
+        ts(V("sn", 8 * h, 8 * h + 8), V("sn", 8 * h, 8 * h + 8), float(step), ALU.mult, float(place(n0) - step * n0), ALU.add)
+    ts(V("nn", 96, 128), V("ri"), 32.0, ALU.mult, LCOL, ALU.add)
+
+    def coded(a, b):
+        n1, n2, n3, n4, cn = [V(x, a, b) for x in ("n1", "n2", "n3", "n4", "cn")]
+        act(n3, V("nn", a, b), AF.Identity, scale=-4.0, bias=TOP + NM / 2)
+        ts(n1, V("nn", a, b), 896.0, ALU.min, 128.0, ALU.max)
+        ts(n2, V("nn", a, b), 768.0, ALU.min, 256.0, ALU.max)
+        act(n4, n1, scale=2.0)
+        tt(n2, n2, n3, ALU.add)
+        tt(cn, n2, n4, ALU.add)
+
+    coded(96, 128)
+
+    dmas("dswap", [("y", A(V("nbw", p0=0, p1=64)), A(V("nbl", p0=64, p1=128)), [V("nbw", p0=0, p1=64)], [V("nbl", p0=64, p1=128)]),
+                   ("y", A(V("nbw", p0=64, p1=128)), A(V("nbl", p0=0, p1=64)), [V("nbw", p0=64, p1=128)], [V("nbl", p0=0, p1=64)])])
+    first, second = ((0, 0, 8), (32, 8, 4)), ((36, 0, 4), (64, 4, 8))
+
+    def lists(src, a, b):
+        for d in others:
+            for p, parts in ((a, first), (b, second)):
+                for to, at, n in parts:
+                    cp(V("lnb", to + 8 * d, to + 8 * d + n, 1, p, p + 64), V(src, 16 * d + at, 16 * d + at + n, 1, p, p + 64))
+
+    lists("nbl", 0, 64)
+    others_f(0)
+    lists("nbw", 64, 0)
+    swaps = []
+    for k in range(8):
+        i = k ^ 1
+        w, r = V("lnw", 0, 96, 1, 16 * k, 16 * k + 16), V("lnb", 0, 96, 1, 16 * i, 16 * i + 16)
+        swaps.append(("y", A(w), A(r), [w], [r]))
+    dmas("dnum", swaps)
+
+    cuts = ((384, 896), (896, 1280), (1280, 1536))
+
+    def around(win, mid):
+        for a, b in cuts:
+            act(V("ra", a, b), win, off=V("lnb", a // 16, b // 16))
+        cp(V("ra", 0, 384), win, V("lnb", 0, 24))
+        for a, b in ((0, 384),) + cuts[:2]:
+            tr(V("rb", a, b), V("ra", a, b))
+        mid()
+        tr(V("rb", *cuts[2]), V("ra", *cuts[2]))
+
+    win3 = ["fa", "fb", "fc"]
+    lst3 = ["la", "lb", "lc"]
+    lo = M * rank
+    COL = lambda k: V("col", k, k + 1)
+    ACC = lambda k: V("acc", k, k + 1)
+    for t in range(R):
+        xh, qc, sp = "xh%d" % t, "qc%d" % t, "scp%d" % t
+        if t:
+            own_f(t)
+            others_f(t)
+        nbh = [V("rb", 512 * k, 512 * k + 512, 16) for k in range(J)] + [V(xh)]
+
+        def mid():
+            tt(V("m1"), nbh[0], nbh[1], ALU.max)
+            tt(V("m1"), V("m1"), nbh[3], ALU.max)
+
+        around(V("fh"), mid)
+        if not t:
+            act(V("dw"), V("dg"), scale=CF(15))
+            ts(V("nn", 0, 96, 2), V("lnb", 0, 96, 2), LO, ALU.mult)
+            ts(V("nn", 1, 96, 2), V("lnb", 1, 96, 2), HI, ALU.mult)
+            ts(V("nm", 0, 96, 2), V("lnw", 1, 96, 2), HI, ALU.mult)
+            ts(V("nm", 1, 96, 2), V("lnw", 0, 96, 2), LO, ALU.mult)
+            tt(V("nn", 0, 96), V("nn", 0, 96), V("nm"), ALU.add)
+            coded(0, 96)
+        tt(V("mm"), V("m1"), nbh[2], ALU.max)
+        for k in range(J + 1):
+            tt(V("eq4", 32 * k, 32 * k + 32), nbh[k], V("mm"), ALU.is_equal)
+        tt(V("b4"), V("eq4"), V("cn"), ALU.mult)
+        tt(V("b2"), V("b4", 0, 64), V("b4", 64, 128), ALU.max)
+        tt(V("b1"), V("b2", 0, 32), V("b2", 32, 64), ALU.max)
+        wide = lambda a, b: (V("xb", 32 * a, 32 * b), V("b1"), V("cexp", 2 * a, 2 * b))
+        for a, b in ((0, 8), (8, 16), (16, 24)):
+            out, win, off = wide(a, b)
+            act(out, win, AF.Identity, off=off, scale=-1.0, bias=TOP)
+        tr(V("tn"), V("b1"))
+        out, win, off = wide(24, 32)
+        ts(out, win, -1.0, ALU.mult, TOP, ALU.add, off)
+        cp(V("zz"), V("tn"), V("twice"))
+        turn_s("fa", 24, 32)
+        tr(V("zt"), V("zz"))
+        turn_s("fa", 0, 8)
+        for e in (0, 1):
+            ts(V("la", e, 64, 2), V("zt", 32 * e, 32 * e + 32), -1.0, ALU.mult, TOP + MID, ALU.add)
+        if not t:
+            tr(V("wb", 0, NM), V("dw"))
+        turn_s("fa", 8, 16)
+        turn_s("fa", 16, 24)
+        if not t:
+            for i in range(4):
+                for n0, n1, c, s in RUNS:
+                    select(V("w%d" % i, c, c + s * (n1 - n0), s), V("wb", n0 + 6 - 2 * i, n1 + 6 - 2 * i), [[0, n1 - n0]], ALU.is_gt, 0.0, 1, 0)
+            for b in range(4):
+                select(V("et", 512 * b, 512 * b + 512), V("one", 0, 512), [[1, 512]], ALU.is_equal, 0.0, -b, -4)
+        for k in range(10):
+            fi, fo, li = win3[k % 3], win3[(k + 1) % 3], lst3[k % 3]
+            lw = lst3[(k + 1) % 3] if k < 9 else "l0"
+            a, b = SPART[0]
+            act(run(fo, a, b), V(fi), off=V(li, a // 16, b // 16))
+            for j, (a, b) in enumerate(VPART):
+                cp(run(fo, a, b), V(fi), V(li, a // 16, b // 16))
+                if k and not j:
+                    listed(V(li, SCUT // 16, 64), SCUT, NM)
+            for a, b in SPART[1:]:
+                act(run(fo, a, b), V(fi), off=V(li, a // 16, b // 16))
+            for a, b in VPART + SPART[:1]:
+                lift(fo, a, b)
+            listed(V(lw, 0, SCUT // 16), 0, SCUT)
+            for a, b in SPART[1:]:
+                lift(fo, a, b)
+        act(V("trs", 0, SCUT), V("w0"), off=V("l0", 0, SCUT // 16), accum=ACC(0))
+        listed(V("l0", SCUT // 16, 64), SCUT, NM)
+        act(V("trs", 0, NM - SCUT), V("w0"), off=V("l0", SCUT // 16, 64), accum=ACC(4))
+        act(V("trs"), V("w1"), off=V("l0"), accum=ACC(1))
+        act(V("trs", 0, CUT3), V("w2"), off=V("l0", 0, CUT3 // 16), accum=ACC(2))
+        cp(V("dvs"), V("w3"), V("l0"))
+        cp(V("dvt"), V("w2"), V("l0", CUT3 // 16, 64))
+        red(ACC(3), V("dvs"), ALU.add)
+        red(ACC(6), V("dvt"), ALU.add)
+        tt(V("acc", 0, 4, 2), V("acc", 0, 4, 2), V("acc", 4, 8, 2), ALU.add)
+        ts(V("aci"), V("acc", 0, 4), 1.0 / 2048.0, ALU.mult, -0.499, ALU.add)
+        ts(V("t2", 0, 4), V("aci"), -2048.0, ALU.mult)
+        cp(V("sz8", 1, 8, 2), V("aci"))
+        tt(V("sz8", 0, 8, 2), V("t2", 0, 4), V("acc", 0, 4), ALU.add)
+        moves = []
+        for i in (1, 2, 3):
+            c = 32 * i
+            for qn, d0, d1, s0, s1 in (("y", c, 128, 0, 128 - c), ("s", 0, c, 128 - c, 128)):
+                o, s = V("rot", 8 * i, 8 * i + 8, 1, d0, d1), V("sz8", 0, 8, 1, s0, s1)
+                moves.append((qn, A(o), A(s), [o], [s]))
+        dmas("drot", moves)
+        cp(V("rot", 0, 8), V("sz8"))
+        listed(V("lro"), lo, lo + M)
+        listed(V("rho", 0, 16), lo, lo + M)
+        act(V("rtf"), V("idn"), off=V("lro"))
+        row = V("rtf", 0, M, 1, 0, 1)
+        dmas("drt", [("y", T.rt[0:1, M * t:M * t + M], A(row), [], [row])])
+        tt(V("rho", 16, 32), V("rho", 0, 16), V("sn"), ALU.not_equal)
+        fill(V("inv", 0, 96), 0.0)
+        far_in = [float(d in pair2) for d in range(N)]
+        terms = [(ALU.is_lt, M, far_in[0] * K)] + [(ALU.is_ge, M * d, (far_in[d] - (far_in[d - 1] if d > 1 else 0.0)) * K) for d in range(1, N)]
+        terms = [(op, float(place(n)), v) for op, n, v in terms if v]
+        parts = ("m1", "mm")
+        for j, (op, n, v) in enumerate(terms):
+            ts(V("rho", 32, 48) if not j else V(parts[j % 2], 0, 16), V("rho", 0, 16), n, op, v, ALU.mult)
+            if j:
+                tt(V("rho", 32, 48), V("rho", 32, 48), V(parts[j % 2], 0, 16), ALU.add)
+        if not t:
+            ts(V("rest"), V("ri"), CF(9), ALU.add)
+            ts(V("mlt"), V("ri"), LCOL, ALU.is_gt)
+            cp(V("rest2"), V("rest"), V("twice"))
+            ts(V("s80"), V("s80"), SCOL, ALU.add)
+            ts(V("ki"), V("ki"), SCOL, ALU.add)
+        for j in range(NTS):
+            act(V("trs", 32 * j, 32 * j + 32), V("rot"), AF.Sign, bias=-1.5 - j, accum=V("ypd", j, j + 1))
+        act(V("szs"), V("rot"), AF.Identity, off=V("rotl"), scale=2.0, bias=-34.0)
+        for j in range(NTS, NTH):
+            ts(V("cm", 32 * j, 32 * j + 32), V("rot"), float(j + 2), ALU.is_ge)
+        for j in range(NTS, NTH):
+            red(V("ypd", j, j + 1), V("cm", 32 * j, 32 * j + 32), ALU.add)
+        tr(V("ytr"), V("ypd"))
+        red(COL(0), V("ytr"), ALU.add)
+        ts(V("a1"), V("alp"), COL(0), ALU.mult, BETA, ALU.add)
+        tr(V("cs"), V("a1"))
+        act(V("trs", 0, 32), V("cs"), AF.Sign, bias=0.5 - K, accum=V("thr", 0, 1))
+        ts(V("f2"), V("cs"), float(K), ALU.is_ge, 2048.0, ALU.mult)
+        gt, eq, thr = V("ge", 0, 32), V("ge", 32, 64), V("thr", 0, 1)
+        ts(gt, V("szs"), thr, ALU.is_gt)
+        ts(eq, V("szs"), thr, ALU.is_equal)
+        tt(V("g1"), V("cs"), V("f2"), ALU.subtract)
+        scan(V("inc", 0, 32), V("one32"), gt, ALU.mult, ALU.add)
+        scan(V("inc", 32, 64), V("one32"), eq, ALU.mult, ALU.add)
+        red(COL(2), V("g1"), ALU.max)
+        ts(V("a2", 0, 32), V("mlt"), V("inc", 31, 32), ALU.mult)
+        ts(V("a2", 32, 64), V("mlt"), V("inc", 63, 64), ALU.mult)
+        ts(V("hh"), V("ge"), -BIG - 1.0, ALU.mult, BIG, ALU.add)
+        tr(V("a2t"), V("a2"))
+        tt(V("je"), V("inc"), V("hh"), ALU.add)
+        red(COL(3), V("a2t", 0, 32), ALU.add)
+        red(COL(5), V("a2t", 32, 64), ALU.add)
+        ts(V("ug"), V("je", 0, 32), COL(3), ALU.add)
+        ts(V("ue"), V("je", 32, 64), COL(5), ALU.add, COL(2), ALU.add)
+        tt(V("um"), V("ug"), V("ue"), ALU.min)
+        tt(V("zz"), V("um"), V("rest2"), ALU.min, V("twice"))
+        tr(V("zt"), V("zz"))
+        tt(V("slot"), V("um"), V("rest"), ALU.min)
+        for e in (0, 1):
+            cp(V("sll", e, 16, 2), V("zt", 32 * e + 8 * rank, 32 * e + 8 * rank + 8))
+        tr(V("sx"), V("slot"))
+        emit("v", lambda: g.vector.tensor_copy(ind(V("inv"), V("sll")), A(V("io2"))), [V("inv")], [V("io2"), V("sll")])
+        widen("sx", 0, 16, "s", "xb")
+        scan(V("scf", 0, K), V("d0", 0, K), V("inv", 0, K), ALU.mult, ALU.add)
+        k5 = V("scf", 15, K, 16)
+        ts(V("j1", 0, 5), k5, SCL, ALU.mult, float(-NM), ALU.add)
+        qa, sa, qb, sb = "qa%d" % t, "sa%d" % t, "qb%d" % t, "sb%d" % t
+        pick(V(qa, 0, K), V(sa, 0, K), V(qc, 0, M), V(sp, 0, M), V("j1", 0, 5))
+        widen("sx", 16, 32, "s", "xb")
+        swap(qa, sa, near, "ac%d" % t, "as%d" % t)
+        ts(V("j2f", 0, 5), k5, SCL, ALU.mult, NM - 0.5, ALU.is_lt)
+        turn_s("fs", 0, 16)
+        ts(V("j2f", 0, 5), V("j2f", 0, 5), float(K), ALU.mult)
+        tt(V("j2f", 0, 5), V("j2f", 0, 5), V("s80", 0, 5), ALU.add)
+        turn_s("fs", 16, 32)
+        cp(V("j2", 0, 5), V("j2f", 0, 5))
+        cp(V("rs"), V("fs"), V("lro"))
+        scan(V("sc", 0, M), V("d0", 0, M), V("rs"), ALU.mult, ALU.add)
+        so, me = V("rho", 0, 16), V("rho", 16, 32)
+        ts(so, V("sc", 15, M, 16), SCL, ALU.mult)
+        ts(V("rho", 48, 64), so, K - 0.5, ALU.is_lt)
+        tt(me, me, V("rho", 48, 64), ALU.mult)
+        tt(so, so, me, ALU.mult)
+        tt(V("rho", 32, 48), V("rho", 32, 48), so, ALU.add)
+        cp(V("pl"), V("rho", 32, 48))
+        pick(V(qb, 0, K), V(sb, 0, K), V(qa), V(sa), V("j2", 0, 5))
+        swap(qb, sb, far, "bc%d" % t, "bs%d" % t)
+        ts(V("rho", 48, 64), me, float(M), ALU.mult)
+        tt(V("rho", 48, 64), V("rho", 48, 64), V("ki"), ALU.add)
+        cp(V("kl"), V("rho", 48, 64))
+        if not t:
+            pick(V("qr", 128, 384), V("sr", 128, 384), V("qu"), V("su"), V("cu", 8, 24))
+            quant(V("qe"), V("se"), V("et"))
+            quant(V("qw"), V("sw"), V("wt"))
+        if t + 1 < R:
+            height(7, t + 1, qc, sp, 0, M)
+            tr(V("ho"), bank(7, M))
+            m0, m1 = V("rho", 16, 32, 2), V("rho", 17, 32, 2)
+            tt(V("mx"), m1, m0, ALU.subtract)
+            ts(V("mx"), V("mx"), HCOL, ALU.mult)
+            tt(V("mx"), V("mx"), m0, ALU.add)
+            ts(V("mx1"), V("mx"), -1.0, ALU.mult, 1.0, ALU.add)
+            tt(V("xo"), V("ho", 0, M, 32), V("mx1"), ALU.mult)
+        unpack = [(V("qe", 128 * b, 128 * b + 128), V("se", 128 * b, 128 * b + 128)) for b in range(4)]
+        half = [(H * h, H * h + H) for h in (0, 1)]
+        qp, pp = "qp%d" % t, "sp%d" % t
+        for h in (0, 1):
+            for b in range(4):
+                mm(bank(4 * h + b, H), *unpack[b], V(qc, *half[h]), V(sp, *half[h]), True, False)
+        for h in (0, 1):
+            pick(V(qp, *half[h]), V(pp, *half[h]), V(qb), V(sb), V("pl", 8 * h, 8 * h + 8))
+        for h in (0, 1):
+            for b in range(4):
+                mm(bank(4 * h + b, H), *unpack[b], V(qp, *half[h]), V(pp, *half[h]), False, True)
+        for h in (0, 1):
+            for b in range(4):
+                src, out = bank(4 * h + b, H), V("hb", 4 * H * h + b, 4 * H * h + 4 * H, 4)
+                if b % 2:
+                    act(out, src, scale=0.5)
+                else:
+                    ts(out, src, 0.5, ALU.mult)
+            quant(V(qc, M + H * h, M + H * h + H), V(sp, M + H * h, M + H * h + H), V("hb", 4 * H * h, 4 * H * h + 4 * H))
+            if t + 1 < R:
+                height(h, t + 1, qc, sp, M + H * h, H)
+        nq, ns = "qc%d" % (t + 1), "scp%d" % (t + 1)
+        if t + 1 < R:
+            for h in (0, 1):
+                tr(V("ht", *half[h]), bank(h, H))
+            tt(V("xm"), V("ht", 0, M, 32), V("mx"), ALU.mult)
+            tt(V("xh%d" % (t + 1), 8 * rank, 8 * rank + 8), V("xm"), V("xo"), ALU.add)
+            share(t + 1)
+            pick(V(nq, 0, M), V(ns, 0, M), V(qc), V(sp), V("kl"))
+
+    outs = []
+    for h in (0, 1):
+        pick(V(nq, *half[h]), V(ns, *half[h]), V(qc, 0, M + H * h + H), V(sp, 0, M + H * h + H), V("kl", 8 * h, 8 * h + 8))
+        mm(bank(h, H), V("qw"), V("sw"), V(nq, *half[h]), V(ns, *half[h]), True, True)
+        cp(V("ys", *half[h]), bank(h, H))
+        outs.append(("y", T.oc[:, 4 * H * h:4 * H * h + 4 * H], A(V(nq, *half[h])).bitcast(dt.uint8), [], [V(nq, *half[h])]))
+        outs.append(("s" if h else "y", T.y[:, H * h:H * h + H], A(V("ys", *half[h])), [], [V("ys", *half[h])]))
+    for k in range(4):
+        o = V(ns, 0, M, 1, 32 * k, 32 * k + 4)
+        outs.append(("y", T.osc[4 * k:4 * k + 4, 0:M], A(o), [], [o]))
+    dmas("dout", outs)
+    for sem in sorted(cnt):
+        g.sync.wait_ge(T.sem[sem], cnt[sem])

@@ -6,6 +6,7 @@ ALU = AluOpType
 AF = ActivationFunctionType
 N, M, K, J, R = 4, 256, 80, 3, 3
 NM = N * M
+HM = NM // 2
 H = M // 2
 SMAX = NM // K + 1
 NTH = SMAX - 1
@@ -13,50 +14,37 @@ NTS = 8
 BIG = 4.0 * NM
 BIGR = NM + K
 WINV = BIGR + M + K
-RUNS = ((0, 128, 0, 4), (128, 256, 512, 2), (256, 768, 768, 1), (768, 896, 1280, 2), (896, 1024, 1536, 4))
-WS, MID = 2048, 1024.0
+RUNS = ((0, 128, 4, 4), (128, 256, 516, 2), (256, 512, 772, 1), (512, 768, 1029, 1), (768, 896, 1286, 2), (896, 1024, 1544, 4))
+WS, MID = 2064, 1028.0
+R1, R2, R3 = [r[:2] for r in RUNS[:3]]
 TOP = 1100.0
 UP = float(2 ** 30)
-VPART = ((0, 128), (128, 256), (256, 288))
-SPART = ((288, 768), (768, 896), (896, 1024))
-SCUT = SPART[0][1]
 CUT3 = 512
 C8, U8, F32, B16, I32, U16 = "float8_e4m3fn_x4", "uint8", "float32", "bfloat16", "int32", "uint16"
 
-SCRATCH = {
-    "xt": ("sbuf", [128, 4 * M], B16), "ut": ("sbuf", [128, 512], B16), "wt": ("sbuf", [128, 512], B16),
-    "qu": ("sbuf", [128, 128], C8), "su": ("sbuf", [128, 128], U8),
-    "qw": ("sbuf", [128, 128], C8), "sw": ("sbuf", [128, 128], U8),
-    "qr": ("sbuf", [128, 384], C8), "sr": ("sbuf", [128, 384], U8),
-    "one": ("sbuf", [128, NM], B16), "et": ("sbuf", [128, 2048], B16),
-    "qe": ("sbuf", [128, 512], C8), "se": ("sbuf", [128, 512], U8),
-    "bl": ("psum", [128, 4096], F32),
-    "d0": ("sbuf", [128, 512], B16), "io2": ("sbuf", [128, M], F32),
-    "dg": ("sbuf", [128, NM], B16), "dw": ("sbuf", [128, NM], B16), "wb": ("sbuf", [128, NM + 16], B16),
-    "w0": ("sbuf", [128, WS], B16), "w1": ("sbuf", [128, WS], B16), "w2": ("sbuf", [128, WS], B16), "w3": ("sbuf", [128, WS], B16),
-    "idn": ("sbuf", [128, WS], F32), "rtf": ("sbuf", [128, M], F32),
-    "xe": ("sbuf", [128, NM], F32), "xb": ("sbuf", [128, NM], B16), "fh": ("sbuf", [128, NM], F32), "fs": ("sbuf", [128, WS], B16),
-    "fa": ("sbuf", [128, WS], B16), "fb": ("sbuf", [128, WS], B16), "fc": ("sbuf", [128, WS], B16),
-    "la": ("sbuf", [128, 64], U16), "lb": ("sbuf", [128, 64], U16), "lc": ("sbuf", [128, 64], U16), "l0": ("sbuf", [128, 64], U16),
-    "sc": ("sbuf", [128, NM], B16), "scf": ("sbuf", [128, 128], F32), "ra": ("sbuf", [128, 1536], F32), "rb": ("sbuf", [128, 1536], F32),
-    "trs": ("sbuf", [128, NM], F32), "dvs": ("sbuf", [128, NM], F32), "dvt": ("sbuf", [128, NM - CUT3], F32),
-    "ht": ("sbuf", [128, M], F32), "ho": ("sbuf", [128, M], F32), "rs": ("sbuf", [128, M], B16), "inv": ("sbuf", [128, WINV], F32),
-    "iw": ("sbuf", [128, 64], I32), "iu": ("sbuf", [128, 24], I32), "id16": ("sbuf", [128, 16], I32),
-    "cm": ("sbuf", [128, 32 * NTH], F32),
-    "nbe": ("sbuf", [128, 48], I32), "nbl": ("sbuf", [128, 64], U16), "nbw": ("sbuf", [128, 64], U16), "lnb": ("sbuf", [128, 96], U16),
-    "lnw": ("sbuf", [128, 96], U16),
-    "sz8": ("sbuf", [128, 8], F32), "rot": ("sbuf", [128, 32], F32), "acc": ("sbuf", [128, 8], F32), "ypd": ("sbuf", [128, 32], F32),
-    "szs": ("sbuf", [128, 32], F32), "hb": ("sbuf", [128, 4 * M], B16), "ys": ("sbuf", [128, M], F32),
+WIDTHS = {
+    B16: {"xt": 4 * M, "ut": 512, "wt": 512, "one": 512, "et": 2048, "d0": 512, "dw": NM, "wb": NM + 16, "w0": WS, "w1": WS, "w2": WS, "w3": WS,
+          "xb": NM, "fs": WS, "fa": WS, "fb": WS, "fc": WS, "sc": HM, "sc2": M, "rs": M, "hb": 4 * M},
+    C8: {"qu": 128, "qw": 128, "qr": 384, "qe": 512},
+    U8: {"su": 128, "sw": 128, "sr": 384, "se": 512},
+    F32: {"io2": M, "idn": WS, "rtf": M, "xe": NM, "fh": NM, "scf": 128, "ra": 768, "rb": 768, "trs": 3 * NM, "dvs": NM, "dvt": NM - CUT3,
+          "ht": M, "ho": M, "inv": WINV, "cm": 32 * NTH, "rot": 32, "acc": 8, "ypd": 32, "szs": 32, "ys": M},
+    U16: {"la": 32, "lb": 32, "lc": 32, "l0": 64, "nbl": 64, "lnb": 48, "lnw": 48},
+    I32: {"iw": 64, "iu": 24, "id16": 16, "nbe": 48},
 }
+SCRATCH = {"bl": ("psum", [128, 4096], F32)}
+for _d, _parts in WIDTHS.items():
+    for _n, _w in _parts.items():
+        SCRATCH[_n] = ("sbuf", [128, _w], _d)
 SMALL = {
-    "zf": (F32, {"d16": 16, "d17": 16, "cf": 32, "ri": 32, "mlt": 32, "rest": 32, "rest2": 64, "alp": 32, "one32": 32, "cn": 128, "sn": 16, "ki": 16, "s80": 8,
-                 "nn": 128, "nm": 96, "n1": 128, "n2": 128, "n3": 128, "n4": 128,
-                 "m1": 32, "mm": 32, "eq4": 128, "b4": 128, "b2": 64, "b1": 32, "tn": 32, "zz": 64, "zt": 64, "thr": 8, "t2": 8,
+    "zf": (F32, {"d16": 16, "d17": 16, "cf": 32, "ri": 32, "mlt": 32, "rest": 32, "rest2": 64, "alp": 32, "one32": 32, "cn": 64, "sn": 16, "ki": 16, "s80": 8,
+                 "nn": 64, "nm": 48, "n1": 64, "n2": 64, "n3": 64, "n4": 64, "xs": 16,
+                 "m1": 16, "mm": 16, "eq4": 64, "b4": 64, "b2": 32, "b1": 32, "b1x": 32, "tn": 32, "zz": 64, "zt": 64, "thr": 8, "t2": 16, "raw": 16,
                  "ytr": 32, "col": 8, "a1": 32, "cs": 32, "f2": 32, "g1": 32, "ge": 64, "inc": 64, "hh": 64, "je": 64, "a2": 64, "a2t": 64,
                  "ug": 32, "ue": 32, "um": 32, "slot": 32, "sx": 32,
                  "rho": 64, "j2f": 8, "mx": 8, "mx1": 8, "xo": 8, "xm": 8}),
-    "zi": (I32, {"ip": 16, "aci": 4}),
-    "zu": (U16, {"cexp": 64, "crep": 64, "cu": 24, "twice": 4, "rotl": 2, "lro": 16, "sll": 16, "j1": 6, "j2": 6, "pl": 16, "kl": 16}),
+    "zi": (I32, {"ip": 16, "aci": 16}),
+    "zu": (U16, {"cexp": 64, "cex2": 32, "crep": 64, "cu": 24, "twice": 4, "lro": 16, "sll": 16, "j1": 6, "j2": 6, "pl": 16, "kl": 16}),
 }
 AT = {}
 for _b, (_d, _parts) in SMALL.items():
@@ -78,7 +66,7 @@ for _t in range(R + 1):
 
 SEMAPHORES = (["ev", "es", "et", "eg", "loc", "nbr"] + ["h%d" % t for t in range(R)]
               + ["%s%d" % (k, t) for t in range(R) for k in ("ac", "as", "bc", "bs")]
-              + ["dx", "du", "dw", "dnb", "dswap", "dnum", "drot", "drt", "dout"])
+              + ["dx", "du", "dw", "dnb", "dnum", "drt", "dout"])
 
 
 def place(n):
@@ -100,7 +88,18 @@ def rank_program(g, core, T, topo):
         buf, off, w = AT[name] if name in AT else (name, 0, SCRATCH[name][1][1])
         return (buf, off + a, off + (w if b is None else b), step, p0, p1)
 
+    def on(r, p0, n=64):
+        return r[:4] + (p0, p0 + n) + r[6:]
+
+    def Z(name, a=0, b=None, step=1):
+        return V(name, a, b, step, 0, 32)
+
+    def back(r):
+        return r[:6] + (True,)
+
     def A(r):
+        if len(r) > 6:
+            return T[r[0]][r[4]:r[5], r[1] + (r[2] - r[1] - 1) // r[3] * r[3]:r[1] - 1:-r[3]]
         return T[r[0]][r[4]:r[5], r[1]:r[2]] if r[3] == 1 else T[r[0]][r[4]:r[5], r[1]:r[2]:r[3]]
 
     def meets(a, b):
@@ -202,13 +201,11 @@ def rank_program(g, core, T, topo):
     def fill(out, c):
         emit("v", lambda: g.vector.memset(A(out), c), [out], [])
 
-    def act(out, in_, func=AF.Copy, off=None, accum=None, scale=None, **kw):
+    def act(out, in_, func=AF.Copy, off=None, accum=None, **kw):
         src = lambda: A(in_) if off is None else ind(in_, off)
-        cols = [scale] if isinstance(scale, tuple) else []
+        cols = [v for v in kw.values() if isinstance(v, tuple)]
         def fn():
-            k2 = dict(kw)
-            if scale is not None:
-                k2["scale"] = A(scale) if cols else scale
+            k2 = {k: A(v) if isinstance(v, tuple) else v for k, v in kw.items()}
             if accum is not None:
                 k2["accum_out"] = A(accum)
             return g.scalar.activation(A(out), src(), func, **k2)
@@ -264,9 +261,9 @@ def rank_program(g, core, T, topo):
         arrives(semc, n, [V(q, K, 2 * K)])
         arrives(sems, n, [V(s, K, 2 * K)])
 
-    def widen(x, c0, c1, on, to="xe"):
+    def widen(x, c0, c1, by, to="xe"):
         out, win, off = V(to, 32 * c0, 32 * c1), V(x, c0, c1), V("cexp", 0, 2 * (c1 - c0))
-        if on == "v":
+        if by == "v":
             cp(out, win, off)
         else:
             act(out, win, off=off)
@@ -287,13 +284,27 @@ def rank_program(g, core, T, topo):
 
     CF = lambda k: V("cf", k, k + 1)
     SCL, HI, LO, SCOL, LCOL, BCOL, BETA, HCOL = [CF(k) for k in (0, 4, 11, 6, 7, 8, 3, 4)]
+    UPPER, SG, NSG, BI, H15, LH, SSCL = [CF(k) for k in (5, 16, 17, 18, 19, 20, 21)]
 
-    def lift(f, a, b):
-        for x, y in runs(a, b):
-            scan(V("sc", x, y), V("d0", 0, y - x), run(f, x, y), ALU.mult, ALU.add)
+    def lift(f, a, b, at):
+        scan(V("sc", at, at + b - a), V("d0", 0, b - a), run(f, a, b), ALU.mult, ALU.add)
 
-    def listed(out, a, b):
-        ts(out, V("sc", a + 15, b, 16), SCL, ALU.mult, MID, ALU.add)
+    def listed(l, a, b):
+        ts(V(l, a // 16, b // 16), V("sc", a + 15, b, 16), SCL, ALU.mult, MID, ALU.add)
+
+    def cross(f, a, b, by="v"):
+        for p in (0, 64):
+            out, src = on(run(f, NM - b, NM - a), 64 - p), on(back(run(f, a, b)), p)
+            if by == "v":
+                ts(out, src, -1.0, ALU.mult)
+            else:
+                act(out, src, scale=-1.0)
+
+    def counted(c, a, b):
+        src, n = V("sc", a + 15, b, 16), (b - a) // 16
+        ts(V("l0", c, c + n), src, SSCL, ALU.mult, MID, ALU.add)
+        for p in (0, 64):
+            ts(on(V("l0", c + n, c + 2 * n), 64 - p), on(src, p), on(SSCL, p), ALU.mult, MID, ALU.add)
 
     bank = lambda k, w: V("bl", 512 * k, 512 * k + w)
 
@@ -310,14 +321,15 @@ def rank_program(g, core, T, topo):
     iota(V("iw"), [[1, 32], [0, 2]], 0, 0)
     iota(V("id16"), [[1, 16]], 128, -1)
     iota(V("ri"), [[1, 32]], 0, 0)
-    fill(V("one"), 1.0)
+    fill(V("dw"), 0.0)
     cp(V("cu"), V("iu"))
     ts(IP(4), IP(0), 4, ALU.logical_shift_right, 1, ALU.bitwise_and)
+    ts(IP(5), IP(0), 6, ALU.logical_shift_right)
     ts(IP(1), IP(0), 15, ALU.bitwise_and)
     ts(IP(2), IP(0), 31, ALU.bitwise_and)
     ts(IP(3), IP(0), 5, ALU.logical_shift_right)
     cp(V("cexp"), V("iw"))
-    cp(CF(4), IP(4))
+    cp(V("cf", 4, 6), V("ip", 4, 6))
     cp(V("cf", 6, 9), V("ip", 1, 4))
     ts(V("id16"), V("id16"), 15, ALU.bitwise_and)
     ts(V("iw"), V("iw"), 0.0, ALU.mult)
@@ -356,6 +368,8 @@ def rank_program(g, core, T, topo):
         widen(xh, 8 * others[1], 8 * others[1] + 8, "s")
         widen(xh, 8 * others[2], 8 * others[2] + 8, "s")
         widen(xh, 8 * others[0], 8 * others[0] + 8, "v")
+        for p in (0, 64):
+            act(on(V("xs"), p), on(V(xh, p // 4, p // 4 + 16), p))
         for d in others:
             turn("fh", 8 * d, 8 * d + 8)
 
@@ -372,228 +386,206 @@ def rank_program(g, core, T, topo):
     iota(V("sn"), [[16, 16]], M * rank, 0)
     iota(V("ki"), [[16, 16]], 0, 0)
     iota(V("s80"), [[16, 8]], 0, 0)
-    select(V("dg"), V("one"), [[1, 32], [-1, 32]], ALU.is_equal, 0.0, 0, 0)
     iota(V("io2"), [[1, M]], NM, 0)
-    for n0, n1, c, s in RUNS:
-        iota(V("idn", c, c + s * (n1 - n0), s), [[1, n1 - n0]], n0, 0)
     ts(CF(12), BCOL, -8.0, ALU.mult, LCOL, ALU.add)
-    own_f(0)
-    ts(CF(13), CF(12), 6.0, ALU.is_equal)
-    ts(CF(14), CF(12), 7.0, ALU.is_equal, 2048.0, ALU.mult)
-    for k in range(J):
-        for e in (0, 1):
-            a = 32 * k + 8 * rank
-            cp(V("lnb", a + e, a + 8, 2), V("nbe", 16 * k + e, 16 * k + 16, 4))
-    tt(CF(15), CF(13), CF(14), ALU.add)
-    ts(BETA, LCOL, float(NTS), ALU.is_lt, NM / 2.0, ALU.mult)
     fill(V("one32"), 1.0)
     fill(V("wb", NM, NM + 16), 0.0)
+    ts(SG, UPPER, 2.0, ALU.mult, -1.0, ALU.add)
+    ts(CF(13), CF(12), 6.0, ALU.is_equal)
+    ts(CF(14), CF(12), 7.0, ALU.is_equal, 2048.0, ALU.mult)
+    ts(NSG, UPPER, -2.0, ALU.mult, 1.0, ALU.add)
+    ts(BI, UPPER, -2.0 * TOP, ALU.mult, TOP, ALU.add)
+    tt(CF(15), CF(13), CF(14), ALU.add)
+    ts(H15, UPPER, 15.0, ALU.mult)
+    ts(LH, UPPER, HM + 1.0, ALU.mult, LCOL, ALU.add)
+    ts(V("dw", 0, NM, 33), V("one32"), CF(15), ALU.mult)
+    ts(BETA, LCOL, float(NTS), ALU.is_lt, NM / 2.0, ALU.mult)
     ts(IP(6), IP(2), 7, ALU.bitwise_and)
-    ts(IP(7), IP(1), 3, ALU.logical_shift_right)
-    ts(IP(8), IP(1), 7, ALU.bitwise_and)
-    ts(V("alp"), V("one32"), BETA, ALU.mult, -1.0 / NM, ALU.mult)
-    ts(CF(9), IP(6), 32.0, ALU.mult, float(BIGR), ALU.add)
-    tt(IP(9), IP(3), IP(7), ALU.subtract)
-    cp(CF(20), IP(8))
-    ts(V("alp"), V("alp"), 1.0, ALU.add)
-    ts(IP(10), IP(9), 4.0, ALU.add)
-    ts(IP(11), IP(9), 2.0, ALU.add)
-    ts(V("sn"), V("sn"), SCOL, ALU.add)
-    ts(V("ip", 12, 14), V("ip", 10, 12), 3, ALU.bitwise_and)
-    ts(LO, HI, -1.0, ALU.mult, 1.0, ALU.add)
-    ts(V("rotl"), V("ip", 12, 14), 8.0, ALU.mult, CF(20), ALU.add)
-    fill(V("ypd"), 0.0)
-    for h in (0, 1):
-        n0 = M * rank + H * h
-        step = place(n0 + 1) - place(n0)
-        ts(V("sn", 8 * h, 8 * h + 8), V("sn", 8 * h, 8 * h + 8), float(step), ALU.mult, float(place(n0) - step * n0), ALU.add)
-    ts(V("nn", 96, 128), V("ri"), 32.0, ALU.mult, LCOL, ALU.add)
+    tr(V("wb", 0, NM), V("dw"))
+    fill(V("one"), 1.0)
+    for i in range(4):
+        for n0, n1, c, s in RUNS:
+            select(V("w%d" % i, c, c + s * (n1 - n0), s), V("wb", n0 + 6 - 2 * i, n1 + 6 - 2 * i), [[0, n1 - n0]], ALU.is_gt, 0.0, 1, 0)
+    for n0, n1, c, s in RUNS:
+        iota(V("idn", c, c + s * (n1 - n0), s), [[1, n1 - n0]], n0, 0)
+    for b in range(4):
+        select(V("et", 512 * b, 512 * b + 512), V("one"), [[1, 512]], ALU.is_equal, 0.0, -b, -4)
+    ts(V("nn", 48, 64), V("ri", 0, 16), 32.0, ALU.mult, LH, ALU.add)
+    own_f(0)
 
-    def coded(a, b):
+    def coded(step, a, b):
         n1, n2, n3, n4, cn = [V(x, a, b) for x in ("n1", "n2", "n3", "n4", "cn")]
-        act(n3, V("nn", a, b), AF.Identity, scale=-4.0, bias=TOP + NM / 2)
-        ts(n1, V("nn", a, b), 896.0, ALU.min, 128.0, ALU.max)
-        ts(n2, V("nn", a, b), 768.0, ALU.min, 256.0, ALU.max)
-        act(n4, n1, scale=2.0)
-        tt(n2, n2, n3, ALU.add)
-        tt(cn, n2, n4, ALU.add)
+        if step == 0:
+            ts(n1, V("nn", a, b), 896.0, ALU.min, 128.0, ALU.max)
+            ts(n2, V("nn", a, b), 768.0, ALU.min, 256.0, ALU.max)
+            ts(n3, V("nn", a, b), -4.0, ALU.mult, TOP + NM / 2, ALU.add)
+        elif step == 1:
+            ts(n4, n1, 2.0, ALU.mult)
+            tt(n2, n2, n3, ALU.add)
+        else:
+            tt(cn, n2, n4, ALU.add)
 
-    coded(96, 128)
+    def lists(d):
+        for to, p, at, n in ((0, 0, 0, 8), (16, 0, 8, 4), (20, 64, 0, 4), (32, 64, 4, 8)):
+            c = to + 8 * (d % 2)
+            cp(on(V("lnb", c, c + n), 64 * (d // 2)), on(V("nbl", 16 * d + at, 16 * d + at + n), p))
 
-    dmas("dswap", [("y", A(V("nbw", p0=0, p1=64)), A(V("nbl", p0=64, p1=128)), [V("nbw", p0=0, p1=64)], [V("nbl", p0=64, p1=128)]),
-                   ("y", A(V("nbw", p0=64, p1=128)), A(V("nbl", p0=0, p1=64)), [V("nbw", p0=64, p1=128)], [V("nbl", p0=0, p1=64)])])
-    first, second = ((0, 0, 8), (32, 8, 4)), ((36, 0, 4), (64, 4, 8))
-
-    def lists(src, a, b):
-        for d in others:
-            for p, parts in ((a, first), (b, second)):
-                for to, at, n in parts:
-                    cp(V("lnb", to + 8 * d, to + 8 * d + n, 1, p, p + 64), V(src, 16 * d + at, 16 * d + at + n, 1, p, p + 64))
-
-    lists("nbl", 0, 64)
-    others_f(0)
-    lists("nbw", 64, 0)
+    lists(rank)
+    for d in others:
+        lists(d)
     swaps = []
     for k in range(8):
         i = k ^ 1
-        w, r = V("lnw", 0, 96, 1, 16 * k, 16 * k + 16), V("lnb", 0, 96, 1, 16 * i, 16 * i + 16)
+        w, r = V("lnw", 0, 48, 1, 16 * k, 16 * k + 16), V("lnb", 0, 48, 1, 16 * i, 16 * i + 16)
         swaps.append(("y", A(w), A(r), [w], [r]))
     dmas("dnum", swaps)
+    ts(LO, HI, -1.0, ALU.mult, 1.0, ALU.add)
+    tt(SSCL, SCL, NSG, ALU.mult)
+    ts(V("cex2"), V("cexp", 0, 32), NSG, ALU.mult, H15, ALU.add)
+    fill(V("b1"), 0.0)
+    ts(V("nn", 0, 48, 2), V("lnb", 0, 48, 2), LO, ALU.mult)
+    ts(V("nn", 1, 48, 2), V("lnb", 1, 48, 2), HI, ALU.mult)
+    others_f(0)
 
-    cuts = ((384, 896), (896, 1280), (1280, 1536))
+    def numbers(step):
+        if step == 0:
+            ts(V("nm", 0, 48, 2), V("lnw", 1, 48, 2), HI, ALU.mult)
+            ts(V("nm", 1, 48, 2), V("lnw", 0, 48, 2), LO, ALU.mult)
+        elif step in (1, 3):
+            tt(V("nn", 0, 48), V("nn", 0, 48), V("nm"), ALU.add)
+        elif step == 2:
+            ts(V("nm"), V("nn", 0, 48), float(HM), ALU.is_ge)
+        else:
+            coded(step - 4, 0, 64)
 
-    def around(win, mid):
-        for a, b in cuts:
-            act(V("ra", a, b), win, off=V("lnb", a // 16, b // 16))
-        cp(V("ra", 0, 384), win, V("lnb", 0, 24))
-        for a, b in ((0, 384),) + cuts[:2]:
-            tr(V("rb", a, b), V("ra", a, b))
-        mid()
-        tr(V("rb", *cuts[2]), V("ra", *cuts[2]))
-
+    cuts = ((128, 384), (384, 640), (640, 768))
     win3 = ["fa", "fb", "fc"]
     lst3 = ["la", "lb", "lc"]
     lo = M * rank
-    COL = lambda k: V("col", k, k + 1)
+    COL = lambda k: Z("col", k, k + 1)
     ACC = lambda k: V("acc", k, k + 1)
     for t in range(R):
         xh, qc, sp = "xh%d" % t, "qc%d" % t, "scp%d" % t
         if t:
             own_f(t)
+            fill(V("inv", 0, 96), 0.0)
             others_f(t)
-        nbh = [V("rb", 512 * k, 512 * k + 512, 16) for k in range(J)] + [V(xh)]
-
-        def mid():
-            tt(V("m1"), nbh[0], nbh[1], ALU.max)
-            tt(V("m1"), V("m1"), nbh[3], ALU.max)
-
-        around(V("fh"), mid)
-        if not t:
-            act(V("dw"), V("dg"), scale=CF(15))
-            ts(V("nn", 0, 96, 2), V("lnb", 0, 96, 2), LO, ALU.mult)
-            ts(V("nn", 1, 96, 2), V("lnb", 1, 96, 2), HI, ALU.mult)
-            ts(V("nm", 0, 96, 2), V("lnw", 1, 96, 2), HI, ALU.mult)
-            ts(V("nm", 1, 96, 2), V("lnw", 0, 96, 2), LO, ALU.mult)
-            tt(V("nn", 0, 96), V("nn", 0, 96), V("nm"), ALU.add)
-            coded(0, 96)
+        nbh = [V("rb", M * k, M * k + M, 16) for k in range(J)] + [V("xs")]
+        once = (lambda step: None) if t else numbers
+        for a, b in cuts:
+            act(V("ra", a, b), V("fh"), off=V("lnb", a // 16, b // 16))
+        cp(V("ra", 0, 128), V("fh"), V("lnb", 0, 8))
+        for j, (a, b) in enumerate(((0, 128),) + cuts[:2]):
+            once(j)
+            tr(V("rb", a, b), V("ra", a, b))
+        once(3)
+        tt(V("m1"), nbh[0], nbh[1], ALU.max)
+        tr(V("rb", *cuts[2]), V("ra", *cuts[2]))
+        tt(V("m1"), V("m1"), nbh[3], ALU.max)
+        once(4)
         tt(V("mm"), V("m1"), nbh[2], ALU.max)
+        once(5)
         for k in range(J + 1):
-            tt(V("eq4", 32 * k, 32 * k + 32), nbh[k], V("mm"), ALU.is_equal)
+            tt(V("eq4", 16 * k, 16 * k + 16), nbh[k], V("mm"), ALU.is_equal)
+            if k == 1:
+                once(6)
         tt(V("b4"), V("eq4"), V("cn"), ALU.mult)
-        tt(V("b2"), V("b4", 0, 64), V("b4", 64, 128), ALU.max)
-        tt(V("b1"), V("b2", 0, 32), V("b2", 32, 64), ALU.max)
-        wide = lambda a, b: (V("xb", 32 * a, 32 * b), V("b1"), V("cexp", 2 * a, 2 * b))
-        for a, b in ((0, 8), (8, 16), (16, 24)):
+        tt(V("b2"), V("b4", 0, 32), V("b4", 32, 64), ALU.max)
+        tt(on(V("b1", 0, 16), 64), on(V("b2", 0, 16), 64), on(V("b2", 16, 32), 64), ALU.max)
+        tt(on(V("b1x", 0, 16), 0), on(V("b2", 0, 16), 0), on(V("b2", 16, 32), 0), ALU.max)
+        tr(on(V("tn"), 64), on(V("b1"), 64))
+        tr(on(V("b1x"), 64), on(back(V("tn")), 64))
+        wide = lambda a, b: (V("xb", a, b), V("b1x", 0, 16), V("cex2", a // 16, b // 16))
+        for a, b in (R3, R2):
             out, win, off = wide(a, b)
-            act(out, win, AF.Identity, off=off, scale=-1.0, bias=TOP)
-        tr(V("tn"), V("b1"))
-        out, win, off = wide(24, 32)
-        ts(out, win, -1.0, ALU.mult, TOP, ALU.add, off)
-        cp(V("zz"), V("tn"), V("twice"))
-        turn_s("fa", 24, 32)
-        tr(V("zt"), V("zz"))
-        turn_s("fa", 0, 8)
-        for e in (0, 1):
-            ts(V("la", e, 64, 2), V("zt", 32 * e, 32 * e + 32), -1.0, ALU.mult, TOP + MID, ALU.add)
-        if not t:
-            tr(V("wb", 0, NM), V("dw"))
-        turn_s("fa", 8, 16)
-        turn_s("fa", 16, 24)
-        if not t:
-            for i in range(4):
-                for n0, n1, c, s in RUNS:
-                    select(V("w%d" % i, c, c + s * (n1 - n0), s), V("wb", n0 + 6 - 2 * i, n1 + 6 - 2 * i), [[0, n1 - n0]], ALU.is_gt, 0.0, 1, 0)
-            for b in range(4):
-                select(V("et", 512 * b, 512 * b + 512), V("one", 0, 512), [[1, 512]], ALU.is_equal, 0.0, -b, -4)
+            act(out, win, AF.Identity, off=off, scale=SG, bias=BI)
+        out, win, off = wide(*R1)
+        ts(out, win, SG, ALU.mult, BI, ALU.add, off)
+        tr(run("fa", *R1), V("xb", *R1))
+        tr(run("fa", *R3), V("xb", *R3))
+        lift("fa", *R1, H)
+        tr(run("fa", *R2), V("xb", *R2))
+        lift("fa", *R3, M)
+        cross("fa", *R2, "s")
+        cross("fa", *R3)
+        listed("la", H, HM)
+        cross("fa", *R1)
         for k in range(10):
-            fi, fo, li = win3[k % 3], win3[(k + 1) % 3], lst3[k % 3]
-            lw = lst3[(k + 1) % 3] if k < 9 else "l0"
-            a, b = SPART[0]
-            act(run(fo, a, b), V(fi), off=V(li, a // 16, b // 16))
-            for j, (a, b) in enumerate(VPART):
-                cp(run(fo, a, b), V(fi), V(li, a // 16, b // 16))
-                if k and not j:
-                    listed(V(li, SCUT // 16, 64), SCUT, NM)
-            for a, b in SPART[1:]:
-                act(run(fo, a, b), V(fi), off=V(li, a // 16, b // 16))
-            for a, b in VPART + SPART[:1]:
-                lift(fo, a, b)
-            listed(V(lw, 0, SCUT // 16), 0, SCUT)
-            for a, b in SPART[1:]:
-                lift(fo, a, b)
-        act(V("trs", 0, SCUT), V("w0"), off=V("l0", 0, SCUT // 16), accum=ACC(0))
-        listed(V("l0", SCUT // 16, 64), SCUT, NM)
-        act(V("trs", 0, NM - SCUT), V("w0"), off=V("l0", SCUT // 16, 64), accum=ACC(4))
-        act(V("trs"), V("w1"), off=V("l0"), accum=ACC(1))
-        act(V("trs", 0, CUT3), V("w2"), off=V("l0", 0, CUT3 // 16), accum=ACC(2))
+            fi, fo, li, lw = win3[k % 3], win3[(k + 1) % 3], lst3[k % 3], lst3[(k + 1) % 3]
+            act(run(fo, *R3), V(fi), off=V(li, 16, 32))
+            lift(fi, *R2, 0)
+            cp(run(fo, *R1), V(fi), V(li, 8, 16))
+            listed(li, 0, H)
+            act(run(fo, *R2), V(fi), off=V(li, 0, 8))
+            if k < 9:
+                lift(fo, *R1, H)
+                cross(fo, *R1)
+                lift(fo, *R3, M)
+                cross(fo, *R3)
+                listed(lw, H, HM)
+                cross(fo, *R2, "s")
+        if not t:
+            fill(V("acc"), 0.0)
+        lift(fo, *R1, 0)
+        lift(fo, *R3, M)
+        counted(0, *R3)
+        act(V("trs", 0, HM), V("w0"), off=V("l0", 0, 32), accum=ACC(0))
+        lift(fo, *R2, H)
+        counted(32, 0, M)
+        act(V("trs", HM, NM), V("w0"), off=V("l0", 32, 64), accum=ACC(4))
+        act(V("trs", NM, 2 * NM), V("w1"), off=V("l0"), accum=ACC(1))
+        act(V("trs", 2 * NM, 2 * NM + CUT3), V("w2"), off=V("l0", 0, CUT3 // 16), accum=ACC(2))
         cp(V("dvs"), V("w3"), V("l0"))
         cp(V("dvt"), V("w2"), V("l0", CUT3 // 16, 64))
         red(ACC(3), V("dvs"), ALU.add)
         red(ACC(6), V("dvt"), ALU.add)
-        tt(V("acc", 0, 4, 2), V("acc", 0, 4, 2), V("acc", 4, 8, 2), ALU.add)
-        ts(V("aci"), V("acc", 0, 4), 1.0 / 2048.0, ALU.mult, -0.499, ALU.add)
-        ts(V("t2", 0, 4), V("aci"), -2048.0, ALU.mult)
-        cp(V("sz8", 1, 8, 2), V("aci"))
-        tt(V("sz8", 0, 8, 2), V("t2", 0, 4), V("acc", 0, 4), ALU.add)
-        moves = []
-        for i in (1, 2, 3):
-            c = 32 * i
-            for qn, d0, d1, s0, s1 in (("y", c, 128, 0, 128 - c), ("s", 0, c, 128 - c, 128)):
-                o, s = V("rot", 8 * i, 8 * i + 8, 1, d0, d1), V("sz8", 0, 8, 1, s0, s1)
-                moves.append((qn, A(o), A(s), [o], [s]))
-        dmas("drot", moves)
-        cp(V("rot", 0, 8), V("sz8"))
-        listed(V("lro"), lo, lo + M)
-        listed(V("rho", 0, 16), lo, lo + M)
-        act(V("rtf"), V("idn"), off=V("lro"))
-        row = V("rtf", 0, M, 1, 0, 1)
-        dmas("drt", [("y", T.rt[0:1, M * t:M * t + M], A(row), [], [row])])
-        tt(V("rho", 16, 32), V("rho", 0, 16), V("sn"), ALU.not_equal)
-        fill(V("inv", 0, 96), 0.0)
-        far_in = [float(d in pair2) for d in range(N)]
-        terms = [(ALU.is_lt, M, far_in[0] * K)] + [(ALU.is_ge, M * d, (far_in[d] - (far_in[d - 1] if d > 1 else 0.0)) * K) for d in range(1, N)]
-        terms = [(op, float(place(n)), v) for op, n, v in terms if v]
-        parts = ("m1", "mm")
-        for j, (op, n, v) in enumerate(terms):
-            ts(V("rho", 32, 48) if not j else V(parts[j % 2], 0, 16), V("rho", 0, 16), n, op, v, ALU.mult)
-            if j:
-                tt(V("rho", 32, 48), V("rho", 32, 48), V(parts[j % 2], 0, 16), ALU.add)
         if not t:
+            ts(CF(9), IP(6), 32.0, ALU.mult, float(BIGR), ALU.add)
+            ts(V("alp"), V("one32"), BETA, ALU.mult, -1.0 / NM, ALU.mult)
+            fill(V("inv", 0, 96), 0.0)
+            fill(V("ypd"), 0.0)
             ts(V("rest"), V("ri"), CF(9), ALU.add)
+            ts(V("alp"), V("alp"), 1.0, ALU.add)
             ts(V("mlt"), V("ri"), LCOL, ALU.is_gt)
+        for b in range(4):
+            tt(Z("raw", 4 * b, 4 * b + 4), on(V("acc", 0, 4), 32 * b, 32), on(V("acc", 4, 8), 32 * b, 32), ALU.add)
+        if not t:
             cp(V("rest2"), V("rest"), V("twice"))
-            ts(V("s80"), V("s80"), SCOL, ALU.add)
-            ts(V("ki"), V("ki"), SCOL, ALU.add)
+        ts(Z("aci"), Z("raw"), 1.0 / 2048.0, ALU.mult, -0.499, ALU.add)
+        ts(Z("t2"), Z("aci"), -2048.0, ALU.mult)
+        cp(Z("rot", 1, 32, 2), Z("aci"))
+        tt(Z("rot", 0, 32, 2), Z("t2"), Z("raw"), ALU.add)
         for j in range(NTS):
-            act(V("trs", 32 * j, 32 * j + 32), V("rot"), AF.Sign, bias=-1.5 - j, accum=V("ypd", j, j + 1))
-        act(V("szs"), V("rot"), AF.Identity, off=V("rotl"), scale=2.0, bias=-34.0)
+            act(Z("trs", 32 * j, 32 * j + 32), Z("rot"), AF.Sign, bias=-1.5 - j, accum=Z("ypd", j, j + 1))
+        act(Z("szs"), Z("rot"), AF.Identity, scale=2.0, bias=-34.0)
         for j in range(NTS, NTH):
-            ts(V("cm", 32 * j, 32 * j + 32), V("rot"), float(j + 2), ALU.is_ge)
+            ts(Z("cm", 32 * j, 32 * j + 32), Z("rot"), float(j + 2), ALU.is_ge)
         for j in range(NTS, NTH):
-            red(V("ypd", j, j + 1), V("cm", 32 * j, 32 * j + 32), ALU.add)
-        tr(V("ytr"), V("ypd"))
-        red(COL(0), V("ytr"), ALU.add)
-        ts(V("a1"), V("alp"), COL(0), ALU.mult, BETA, ALU.add)
-        tr(V("cs"), V("a1"))
-        act(V("trs", 0, 32), V("cs"), AF.Sign, bias=0.5 - K, accum=V("thr", 0, 1))
-        ts(V("f2"), V("cs"), float(K), ALU.is_ge, 2048.0, ALU.mult)
-        gt, eq, thr = V("ge", 0, 32), V("ge", 32, 64), V("thr", 0, 1)
-        ts(gt, V("szs"), thr, ALU.is_gt)
-        ts(eq, V("szs"), thr, ALU.is_equal)
-        tt(V("g1"), V("cs"), V("f2"), ALU.subtract)
-        scan(V("inc", 0, 32), V("one32"), gt, ALU.mult, ALU.add)
-        scan(V("inc", 32, 64), V("one32"), eq, ALU.mult, ALU.add)
-        red(COL(2), V("g1"), ALU.max)
-        ts(V("a2", 0, 32), V("mlt"), V("inc", 31, 32), ALU.mult)
-        ts(V("a2", 32, 64), V("mlt"), V("inc", 63, 64), ALU.mult)
-        ts(V("hh"), V("ge"), -BIG - 1.0, ALU.mult, BIG, ALU.add)
-        tr(V("a2t"), V("a2"))
-        tt(V("je"), V("inc"), V("hh"), ALU.add)
-        red(COL(3), V("a2t", 0, 32), ALU.add)
-        red(COL(5), V("a2t", 32, 64), ALU.add)
-        ts(V("ug"), V("je", 0, 32), COL(3), ALU.add)
-        ts(V("ue"), V("je", 32, 64), COL(5), ALU.add, COL(2), ALU.add)
-        tt(V("um"), V("ug"), V("ue"), ALU.min)
+            red(Z("ypd", j, j + 1), Z("cm", 32 * j, 32 * j + 32), ALU.add)
+        tr(Z("ytr"), Z("ypd"))
+        red(COL(0), Z("ytr"), ALU.add)
+        ts(Z("a1"), Z("alp"), COL(0), ALU.mult, on(BETA, 0, 32), ALU.add)
+        tr(Z("cs"), Z("a1"))
+        act(Z("trs", 512, 544), Z("cs"), AF.Sign, bias=0.5 - K, accum=Z("thr", 0, 1))
+        ts(Z("f2"), Z("cs"), float(K), ALU.is_ge, 2048.0, ALU.mult)
+        gt, eq, thr = Z("ge", 0, 32), Z("ge", 32, 64), Z("thr", 0, 1)
+        ts(gt, Z("szs"), thr, ALU.is_gt)
+        ts(eq, Z("szs"), thr, ALU.is_equal)
+        tt(Z("g1"), Z("cs"), Z("f2"), ALU.subtract)
+        scan(Z("inc", 0, 32), Z("one32"), gt, ALU.mult, ALU.add)
+        scan(Z("inc", 32, 64), Z("one32"), eq, ALU.mult, ALU.add)
+        red(COL(2), Z("g1"), ALU.max)
+        ts(Z("a2", 0, 32), Z("mlt"), Z("inc", 31, 32), ALU.mult)
+        ts(Z("a2", 32, 64), Z("mlt"), Z("inc", 63, 64), ALU.mult)
+        ts(Z("hh"), Z("ge"), -BIG - 1.0, ALU.mult, BIG, ALU.add)
+        tr(Z("a2t"), Z("a2"))
+        tt(Z("je"), Z("inc"), Z("hh"), ALU.add)
+        red(COL(3), Z("a2t", 0, 32), ALU.add)
+        red(COL(5), Z("a2t", 32, 64), ALU.add)
+        ts(Z("ug"), Z("je", 0, 32), COL(3), ALU.add)
+        ts(Z("ue"), Z("je", 32, 64), COL(5), ALU.add, COL(2), ALU.add)
+        for b in range(4):
+            tt(on(V("um"), 32 * b, 32), Z("ug"), Z("ue"), ALU.min)
         tt(V("zz"), V("um"), V("rest2"), ALU.min, V("twice"))
         tr(V("zt"), V("zz"))
         tt(V("slot"), V("um"), V("rest"), ALU.min)
@@ -609,13 +601,45 @@ def rank_program(g, core, T, topo):
         pick(V(qa, 0, K), V(sa, 0, K), V(qc, 0, M), V(sp, 0, M), V("j1", 0, 5))
         widen("sx", 16, 32, "s", "xb")
         swap(qa, sa, near, "ac%d" % t, "as%d" % t)
+        if not t:
+            ts(V("s80"), V("s80"), SCOL, ALU.add)
+            ts(V("ki"), V("ki"), SCOL, ALU.add)
+            ts(V("sn"), V("sn"), SCOL, ALU.add)
+            for h in (0, 1):
+                n0 = lo + H * h
+                step = place(n0 + 1) - place(n0)
+                ts(V("sn", 8 * h, 8 * h + 8), V("sn", 8 * h, 8 * h + 8), float(step), ALU.mult, float(place(n0) - step * n0), ALU.add)
         ts(V("j2f", 0, 5), k5, SCL, ALU.mult, NM - 0.5, ALU.is_lt)
-        turn_s("fs", 0, 16)
+        mine = 64 * (lo // HM)
+        if mine:
+            for a, b in runs(lo, lo + M):
+                scan(on(V("sc2", a - lo, b - lo), mine), on(V("d0", 0, b - a), mine), on(back(run(fo, NM - b, NM - a)), mine), ALU.mult, ALU.add)
+            last = V("sc2", 15, M, 16)
+        else:
+            last = V("sc", lo + 15, lo + M, 16)
         ts(V("j2f", 0, 5), V("j2f", 0, 5), float(K), ALU.mult)
+        for p in (0, 64):
+            ts(on(V("rho", 0, 16), p), on(last, mine), on(SSCL, mine), ALU.mult, MID, ALU.add)
+        turn_s("fs", 0, 16)
+        cp(V("lro"), V("rho", 0, 16))
         tt(V("j2f", 0, 5), V("j2f", 0, 5), V("s80", 0, 5), ALU.add)
+        tt(V("rho", 16, 32), V("rho", 0, 16), V("sn"), ALU.not_equal)
         turn_s("fs", 16, 32)
         cp(V("j2", 0, 5), V("j2f", 0, 5))
+        act(V("rtf"), V("idn"), off=V("lro"))
+        row = V("rtf", 0, M, 1, 0, 1)
+        dmas("drt", [("y", T.rt[0:1, M * t:M * t + M], A(row), [], [row])])
         cp(V("rs"), V("fs"), V("lro"))
+        far_in = [float(d in pair2) for d in range(N)]
+        terms = [(ALU.is_lt, M, far_in[0] * K)] + [(ALU.is_ge, M * d, (far_in[d] - (far_in[d - 1] if d > 1 else 0.0)) * K) for d in range(1, N)]
+        terms = [(op, float(place(n)), v) for op, n, v in terms if v]
+        parts = ("m1", "mm")
+        for j, (op, n, v) in enumerate(terms):
+            ts(V("rho", 32, 48) if not j else V(parts[j % 2], 0, 16), V("rho", 0, 16), n, op, v, ALU.mult)
+            if j:
+                tt(V("rho", 32, 48), V("rho", 32, 48), V(parts[j % 2], 0, 16), ALU.add)
+        pick(V(qb, 0, K), V(sb, 0, K), V(qa), V(sa), V("j2", 0, 5))
+        swap(qb, sb, far, "bc%d" % t, "bs%d" % t)
         scan(V("sc", 0, M), V("d0", 0, M), V("rs"), ALU.mult, ALU.add)
         so, me = V("rho", 0, 16), V("rho", 16, 32)
         ts(so, V("sc", 15, M, 16), SCL, ALU.mult)
@@ -624,8 +648,6 @@ def rank_program(g, core, T, topo):
         tt(so, so, me, ALU.mult)
         tt(V("rho", 32, 48), V("rho", 32, 48), so, ALU.add)
         cp(V("pl"), V("rho", 32, 48))
-        pick(V(qb, 0, K), V(sb, 0, K), V(qa), V(sa), V("j2", 0, 5))
-        swap(qb, sb, far, "bc%d" % t, "bs%d" % t)
         ts(V("rho", 48, 64), me, float(M), ALU.mult)
         tt(V("rho", 48, 64), V("rho", 48, 64), V("ki"), ALU.add)
         cp(V("kl"), V("rho", 48, 64))

@@ -10,26 +10,28 @@ HM = NM // 2
 H = M // 2
 SMAX = NM // K + 1
 NTH = SMAX - 1
-NTS = 8
+NTS = 7
 BIG = 4.0 * NM
 BIGR = NM + K
 WINV = BIGR + M + K
 RUNS = ((0, 128, 4, 4), (128, 256, 516, 2), (256, 512, 772, 1), (512, 768, 1029, 1), (768, 896, 1286, 2), (896, 1024, 1544, 4))
 WS, MID = 2064, 1028.0
 R1, R2, R3 = [r[:2] for r in RUNS[:3]]
+R3A, R3B = (M, M + H), (M + H, HM)
 TOP = 1100.0
 UP = float(2 ** 30)
-CUT3 = 512
+FR = 16
 C8, U8, F32, B16, I32, U16 = "float8_e4m3fn_x4", "uint8", "float32", "bfloat16", "int32", "uint16"
 
 WIDTHS = {
     B16: {"xt": 4 * M, "ut": 512, "wt": 512, "one": 512, "et": 2048, "d0": 512, "dw": NM, "wb": NM + 16, "w0": WS, "w1": WS, "w2": WS, "w3": WS,
-          "xb": NM, "fs": WS, "fa": WS, "fb": WS, "fc": WS, "sc": HM, "sc2": M, "rs": M, "hb": 4 * M},
+          "xb": NM, "fs": WS, "fa": WS, "fb": WS, "fc": WS, "sc": HM, "sc2": M, "rs": M, "hb": 4 * M,
+          "fr": FR + HM, "ee": 8 * HM, "so": 8 * M, "cv": 16},
     C8: {"qu": 128, "qw": 128, "qr": 384, "qe": 512},
     U8: {"su": 128, "sw": 128, "sr": 384, "se": 512},
-    F32: {"io2": M, "idn": WS, "rtf": M, "xe": NM, "fh": NM, "scf": 128, "ra": 768, "rb": 768, "trs": 3 * NM, "dvs": NM, "dvt": NM - CUT3,
-          "ht": M, "ho": M, "inv": WINV, "cm": 32 * NTH, "rot": 32, "acc": 8, "ypd": 32, "szs": 32, "ys": M},
-    U16: {"la": 32, "lb": 32, "lc": 32, "l0": 64, "nbl": 64, "lnb": 48, "lnw": 48},
+    F32: {"io2": M, "idn": WS, "rtf": M, "xe": NM, "fh": NM, "scf": 128, "ra": 384, "rb": 384, "trs": 2 * NM,
+          "ht": M, "ho": M, "inv": WINV, "cm": 32 * NTH, "rot": 32, "acc": 16, "ypd": 32, "szs": 32, "ys": M},
+    U16: {"la": 32, "lb": 32, "lc": 32, "l0": 32, "nbl": 64, "lnb": 24},
     I32: {"iw": 64, "iu": 24, "id16": 16, "nbe": 48},
 }
 SCRATCH = {"bl": ("psum", [128, 4096], F32)}
@@ -37,13 +39,13 @@ for _d, _parts in WIDTHS.items():
     for _n, _w in _parts.items():
         SCRATCH[_n] = ("sbuf", [128, _w], _d)
 SMALL = {
-    "zf": (F32, {"d16": 16, "d17": 16, "cf": 32, "ri": 32, "mlt": 32, "rest": 32, "rest2": 64, "alp": 32, "one32": 32, "cn": 64, "sn": 16, "ki": 16, "s80": 8,
-                 "nn": 64, "nm": 48, "n1": 64, "n2": 64, "n3": 64, "n4": 64, "xs": 16,
-                 "m1": 16, "mm": 16, "eq4": 64, "b4": 64, "b2": 32, "b1": 32, "b1x": 32, "tn": 32, "zz": 64, "zt": 64, "thr": 8, "t2": 16, "raw": 16,
+    "zf": (F32, {"d16": 16, "d17": 16, "cf": 32, "ri": 32, "mlt": 32, "rest": 32, "rest2": 64, "alp": 32, "one32": 32, "cn": 48, "sn": 16, "ki": 16, "s80": 8,
+                 "nn": 48, "nm": 24, "n1": 48, "n2": 48, "n3": 48, "n4": 48, "xs": 16,
+                 "m1": 16, "mm": 16, "eq4": 32, "b4": 32, "b2": 16, "b1": 32, "b1x": 32, "tn": 32, "zz": 64, "zt": 64, "thr": 8, "up": 8,
                  "ytr": 32, "col": 8, "a1": 32, "cs": 32, "f2": 32, "g1": 32, "ge": 64, "inc": 64, "hh": 64, "je": 64, "a2": 64, "a2t": 64,
                  "ug": 32, "ue": 32, "um": 32, "slot": 32, "sx": 32,
                  "rho": 64, "j2f": 8, "mx": 8, "mx1": 8, "xo": 8, "xm": 8}),
-    "zi": (I32, {"ip": 16, "aci": 16}),
+    "zi": (I32, {"ip": 16, "aci": 16, "roti": 16}),
     "zu": (U16, {"cexp": 64, "cex2": 32, "crep": 64, "cu": 24, "twice": 4, "lro": 16, "sll": 16, "j1": 6, "j2": 6, "pl": 16, "kl": 16}),
 }
 AT = {}
@@ -66,7 +68,7 @@ for _t in range(R + 1):
 
 SEMAPHORES = (["ev", "es", "et", "eg", "loc", "nbr"] + ["h%d" % t for t in range(R)]
               + ["%s%d" % (k, t) for t in range(R) for k in ("ac", "as", "bc", "bs")]
-              + ["dx", "du", "dw", "dnb", "dnum", "drt", "dout"])
+              + ["dx", "du", "dw", "dnb", "drt", "dout"])
 
 
 def place(n):
@@ -261,12 +263,12 @@ def rank_program(g, core, T, topo):
         arrives(semc, n, [V(q, K, 2 * K)])
         arrives(sems, n, [V(s, K, 2 * K)])
 
-    def widen(x, c0, c1, by, to="xe"):
-        out, win, off = V(to, 32 * c0, 32 * c1), V(x, c0, c1), V("cexp", 0, 2 * (c1 - c0))
-        if by == "v":
-            cp(out, win, off)
-        else:
-            act(out, win, off=off)
+    def widen(x, c0, c1, to):
+        act(V(to, 32 * c0, 32 * c1), V(x, c0, c1), off=V("cexp", 0, 2 * (c1 - c0)))
+
+    def spaced(x, c0, c1):
+        cp(V("xe", 32 * c0, 32 * c1, 32), V(x, c0, c1))
+        act(V("xe", 32 * c0 + 16, 32 * c1, 32), V(x, c0, c1))
 
     def turn(f, c0, c1):
         tr(V(f, 32 * c0, 32 * c1), V("xe", 32 * c0, 32 * c1))
@@ -283,7 +285,7 @@ def rank_program(g, core, T, topo):
             tr(run(f, a, b), V("xb", a, b))
 
     CF = lambda k: V("cf", k, k + 1)
-    SCL, HI, LO, SCOL, LCOL, BCOL, BETA, HCOL = [CF(k) for k in (0, 4, 11, 6, 7, 8, 3, 4)]
+    SCL, HI, SCOL, LCOL, BCOL, BETA, HCOL = [CF(k) for k in (0, 4, 6, 7, 8, 3, 4)]
     UPPER, SG, NSG, BI, H15, LH, SSCL = [CF(k) for k in (5, 16, 17, 18, 19, 20, 21)]
 
     def lift(f, a, b, at):
@@ -300,18 +302,13 @@ def rank_program(g, core, T, topo):
             else:
                 act(out, src, scale=-1.0)
 
-    def counted(c, a, b):
-        src, n = V("sc", a + 15, b, 16), (b - a) // 16
-        ts(V("l0", c, c + n), src, SSCL, ALU.mult, MID, ALU.add)
-        for p in (0, 64):
-            ts(on(V("l0", c + n, c + 2 * n), 64 - p), on(src, p), on(SSCL, p), ALU.mult, MID, ALU.add)
-
     bank = lambda k, w: V("bl", 512 * k, 512 * k + w)
 
     loads = []
     for k in range(8):
-        o = V("nbe", 0, 48 - 2 * (k % 2), 1, 16 * k, 16 * k + 16)
-        loads.append(("ys"[k % 2], A(o), T.nb[:, 2 * (k % 2):48], [o], []))
+        shift = (k % 2) * (2 - k // 4)
+        o = V("nbe", 0, 48 - shift, 1, 16 * k, 16 * k + 16)
+        loads.append(("ys"[k % 2], A(o), T.nb[:, shift:48], [o], []))
     dmas("dnb", loads)
     dmas("dx", [("y", A(V("xt")), T.x[:], [V("xt")], [])])
     dmas("du", [("s", A(V("ut")), T.u[:], [V("ut")], [])])
@@ -322,12 +319,14 @@ def rank_program(g, core, T, topo):
     iota(V("id16"), [[1, 16]], 128, -1)
     iota(V("ri"), [[1, 32]], 0, 0)
     fill(V("dw"), 0.0)
+    act(V("xe"), V("dw"))
     cp(V("cu"), V("iu"))
     ts(IP(4), IP(0), 4, ALU.logical_shift_right, 1, ALU.bitwise_and)
     ts(IP(5), IP(0), 6, ALU.logical_shift_right)
     ts(IP(1), IP(0), 15, ALU.bitwise_and)
     ts(IP(2), IP(0), 31, ALU.bitwise_and)
     ts(IP(3), IP(0), 5, ALU.logical_shift_right)
+    ts(IP(7), IP(0), 5, ALU.logical_shift_right, 1, ALU.bitwise_and)
     cp(V("cexp"), V("iw"))
     cp(V("cf", 4, 6), V("ip", 4, 6))
     cp(V("cf", 6, 9), V("ip", 1, 4))
@@ -341,10 +340,12 @@ def rank_program(g, core, T, topo):
     tt(V("d16"), V("d16"), V("d17"), ALU.add)
     cp(V("twice", 0, 2), V("crep", 0, 2))
     ts(V("twice", 2, 4), V("crep", 0, 2), 16.0, ALU.add)
+    fill(V("one"), 1.0)
     o = 16 * rank
-    for e in (0, 1):
-        cp(V("nbl", o + e, o + 12, 2, 0, 64), V("nbe", e, 24, 4, 0, 64))
-        cp(V("nbl", o + e, o + 12, 2, 64, 128), V("nbe", 24 + e, 48, 4, 64, 128))
+    for b in (0, 1):
+        for e in (0, 1):
+            cp(on(V("nbl", o + e, o + 12, 2), 32 * b, 32), on(V("nbe", 24 * b + e, 24 * b + 24, 4), 32 * b, 32))
+        cp(on(V("nbl", o, o + 12), 64 + 32 * b, 32), on(V("nbe", 24 * b, 24 * b + 24, 2), 64 + 32 * b, 32))
     cp(V("nbl", o + 12, o + 16), V("nbe", 0, 4))
     spread(V("nbl", o, o + 16), "nbr")
     arrives("nbr", groups * len(others), [V("nbl", 16 * d, 16 * d + 16) for d in others])
@@ -360,18 +361,17 @@ def rank_program(g, core, T, topo):
         arrives("h%d" % t, groups * len(others), [V("xh%d" % t, 8 * d, 8 * d + 8) for d in others])
 
     def own_f(t):
-        widen("xh%d" % t, 8 * rank, 8 * rank + 8, "v")
+        spaced("xh%d" % t, 8 * rank, 8 * rank + 8)
         turn("fh", 8 * rank, 8 * rank + 8)
 
     def others_f(t):
         xh = "xh%d" % t
-        widen(xh, 8 * others[1], 8 * others[1] + 8, "s")
-        widen(xh, 8 * others[2], 8 * others[2] + 8, "s")
-        widen(xh, 8 * others[0], 8 * others[0] + 8, "v")
-        for p in (0, 64):
-            act(on(V("xs"), p), on(V(xh, p // 4, p // 4 + 16), p))
-        for d in others:
-            turn("fh", 8 * d, 8 * d + 8)
+        spaced(xh, 0, 32)
+        for d in range(N):
+            act(on(V("xs", 0, 8), 32 * d, 32), on(V(xh, 8 * d, 8 * d + 8), 32 * d, 32))
+        for c0, c1 in ((0, 8 * rank), (8 * rank + 8, 32)):
+            if c1 > c0:
+                turn("fh", c0, c1)
 
     for h in (0, 1):
         quant(V("qc0", H * h, H * h + H), V("scp0", H * h, H * h + H), V("xt", 4 * H * h, 4 * H * h + 4 * H))
@@ -387,7 +387,10 @@ def rank_program(g, core, T, topo):
     iota(V("ki"), [[16, 16]], 0, 0)
     iota(V("s80"), [[16, 8]], 0, 0)
     iota(V("io2"), [[1, M]], NM, 0)
-    ts(CF(12), BCOL, -8.0, ALU.mult, LCOL, ALU.add)
+    ts(CF(12), IP(7), -8.0, ALU.mult, LCOL, ALU.add)
+    ts(CF(22), IP(7), 8.0, ALU.mult, HI, ALU.add)
+    ts(CF(23), LCOL, 32.0, ALU.mult, 16.0, ALU.add)
+    ts(CF(24), BCOL, float(M), ALU.mult, LCOL, ALU.add)
     fill(V("one32"), 1.0)
     fill(V("wb", NM, NM + 16), 0.0)
     ts(SG, UPPER, 2.0, ALU.mult, -1.0, ALU.add)
@@ -397,12 +400,12 @@ def rank_program(g, core, T, topo):
     ts(BI, UPPER, -2.0 * TOP, ALU.mult, TOP, ALU.add)
     tt(CF(15), CF(13), CF(14), ALU.add)
     ts(H15, UPPER, 15.0, ALU.mult)
-    ts(LH, UPPER, HM + 1.0, ALU.mult, LCOL, ALU.add)
+    tt(LH, UPPER, CF(24), ALU.add)
+    tt(CF(22), CF(22), CF(23), ALU.add)
     ts(V("dw", 0, NM, 33), V("one32"), CF(15), ALU.mult)
-    ts(BETA, LCOL, float(NTS), ALU.is_lt, NM / 2.0, ALU.mult)
-    ts(IP(6), IP(2), 7, ALU.bitwise_and)
+    ts(V("nn", 24, 32), V("ri", 0, 8), 32.0, ALU.mult, LH, ALU.add)
+    ts(V("nn", 32, 40), V("ri", 0, 8), CF(22), ALU.add)
     tr(V("wb", 0, NM), V("dw"))
-    fill(V("one"), 1.0)
     for i in range(4):
         for n0, n1, c, s in RUNS:
             select(V("w%d" % i, c, c + s * (n1 - n0), s), V("wb", n0 + 6 - 2 * i, n1 + 6 - 2 * i), [[0, n1 - n0]], ALU.is_gt, 0.0, 1, 0)
@@ -410,7 +413,6 @@ def rank_program(g, core, T, topo):
         iota(V("idn", c, c + s * (n1 - n0), s), [[1, n1 - n0]], n0, 0)
     for b in range(4):
         select(V("et", 512 * b, 512 * b + 512), V("one"), [[1, 512]], ALU.is_equal, 0.0, -b, -4)
-    ts(V("nn", 48, 64), V("ri", 0, 16), 32.0, ALU.mult, LH, ALU.add)
     own_f(0)
 
     def coded(step, a, b):
@@ -425,40 +427,27 @@ def rank_program(g, core, T, topo):
         else:
             tt(cn, n2, n4, ALU.add)
 
-    def lists(d):
-        for to, p, at, n in ((0, 0, 0, 8), (16, 0, 8, 4), (20, 64, 0, 4), (32, 64, 4, 8)):
-            c = to + 8 * (d % 2)
-            cp(on(V("lnb", c, c + n), 64 * (d // 2)), on(V("nbl", 16 * d + at, 16 * d + at + n), p))
+    def lists(to, p):
+        for d in [rank] + others:
+            for b in (0, 1):
+                cp(on(V(to, 12 * b, 12 * b + 12), 32 * d, 32), on(V("nbl", 16 * d, 16 * d + 12), p + 32 * b, 32))
 
-    lists(rank)
-    for d in others:
-        lists(d)
-    swaps = []
-    for k in range(8):
-        i = k ^ 1
-        w, r = V("lnw", 0, 48, 1, 16 * k, 16 * k + 16), V("lnb", 0, 48, 1, 16 * i, 16 * i + 16)
-        swaps.append(("y", A(w), A(r), [w], [r]))
-    dmas("dnum", swaps)
-    ts(LO, HI, -1.0, ALU.mult, 1.0, ALU.add)
     tt(SSCL, SCL, NSG, ALU.mult)
     ts(V("cex2"), V("cexp", 0, 32), NSG, ALU.mult, H15, ALU.add)
     fill(V("b1"), 0.0)
-    ts(V("nn", 0, 48, 2), V("lnb", 0, 48, 2), LO, ALU.mult)
-    ts(V("nn", 1, 48, 2), V("lnb", 1, 48, 2), HI, ALU.mult)
+    lists("lnb", 0)
     others_f(0)
 
     def numbers(step):
         if step == 0:
-            ts(V("nm", 0, 48, 2), V("lnw", 1, 48, 2), HI, ALU.mult)
-            ts(V("nm", 1, 48, 2), V("lnw", 0, 48, 2), LO, ALU.mult)
-        elif step in (1, 3):
-            tt(V("nn", 0, 48), V("nn", 0, 48), V("nm"), ALU.add)
+            lists("nn", 64)
+        elif step == 1:
+            ts(V("nm"), V("nn", 0, 24), float(HM), ALU.is_ge)
         elif step == 2:
-            ts(V("nm"), V("nn", 0, 48), float(HM), ALU.is_ge)
+            tt(V("nn", 0, 24), V("nn", 0, 24), V("nm"), ALU.add)
         else:
-            coded(step - 4, 0, 64)
+            coded(step - 3, 0, 40)
 
-    cuts = ((128, 384), (384, 640), (640, 768))
     win3 = ["fa", "fb", "fc"]
     lst3 = ["la", "lb", "lc"]
     lo = M * rank
@@ -470,30 +459,37 @@ def rank_program(g, core, T, topo):
             own_f(t)
             fill(V("inv", 0, 96), 0.0)
             others_f(t)
-        nbh = [V("rb", M * k, M * k + M, 16) for k in range(J)] + [V("xs")]
+        nbh = [V("rb", H * k, H * k + H, 16) for k in range(J)] + [V("xs", 0, 8)]
         once = (lambda step: None) if t else numbers
-        for a, b in cuts:
-            act(V("ra", a, b), V("fh"), off=V("lnb", a // 16, b // 16))
-        cp(V("ra", 0, 128), V("fh"), V("lnb", 0, 8))
-        for j, (a, b) in enumerate(((0, 128),) + cuts[:2]):
-            once(j)
-            tr(V("rb", a, b), V("ra", a, b))
+        act(V("ra", H, 3 * H), V("fh"), off=V("lnb", 8, 24))
+        cp(V("ra", 0, H), V("fh"), V("lnb", 0, 8))
+        once(0)
+        tr(V("rb", 0, H), V("ra", 0, H))
+        once(1)
+        tr(V("rb", H, 3 * H), V("ra", H, 3 * H))
+        m1, mx4 = V("m1", 0, 8), V("mm", 0, 8)
+        tt(m1, nbh[0], nbh[3], ALU.max)
+        once(2)
+        tt(mx4, nbh[1], nbh[2], ALU.max)
         once(3)
-        tt(V("m1"), nbh[0], nbh[1], ALU.max)
-        tr(V("rb", *cuts[2]), V("ra", *cuts[2]))
-        tt(V("m1"), V("m1"), nbh[3], ALU.max)
+        tt(mx4, mx4, m1, ALU.max)
         once(4)
-        tt(V("mm"), V("m1"), nbh[2], ALU.max)
-        once(5)
         for k in range(J + 1):
-            tt(V("eq4", 16 * k, 16 * k + 16), nbh[k], V("mm"), ALU.is_equal)
+            tt(V("eq4", 8 * k, 8 * k + 8), nbh[k], mx4, ALU.is_equal)
             if k == 1:
-                once(6)
-        tt(V("b4"), V("eq4"), V("cn"), ALU.mult)
-        tt(V("b2"), V("b4", 0, 32), V("b4", 32, 64), ALU.max)
-        tt(on(V("b1", 0, 16), 64), on(V("b2", 0, 16), 64), on(V("b2", 16, 32), 64), ALU.max)
-        tt(on(V("b1x", 0, 16), 0), on(V("b2", 0, 16), 0), on(V("b2", 16, 32), 0), ALU.max)
+                once(5)
+        tt(V("b4"), V("eq4"), V("cn", 0, 32), ALU.mult)
+        tt(V("b2"), V("b4", 0, 16), V("b4", 16, 32), ALU.max)
+        def handed(to, d, b):
+            tt(on(V(to, 8 * (d % 2), 8 * (d % 2) + 8), 32 * b, 32), on(V("b2", 0, 8), 32 * d, 32), on(V("b2", 8, 16), 32 * d, 32), ALU.max)
+        for d in (2, 3):
+            for b in (2, 3):
+                handed("b1", d, b)
+        handed("b1x", 0, 0)
+        handed("b1x", 0, 1)
         tr(on(V("tn"), 64), on(V("b1"), 64))
+        handed("b1x", 1, 0)
+        handed("b1x", 1, 1)
         tr(on(V("b1x"), 64), on(back(V("tn")), 64))
         wide = lambda a, b: (V("xb", a, b), V("b1x", 0, 16), V("cex2", a // 16, b // 16))
         for a, b in (R3, R2):
@@ -512,49 +508,54 @@ def rank_program(g, core, T, topo):
         cross("fa", *R1)
         for k in range(10):
             fi, fo, li, lw = win3[k % 3], win3[(k + 1) % 3], lst3[k % 3], lst3[(k + 1) % 3]
-            act(run(fo, *R3), V(fi), off=V(li, 16, 32))
+            to = (lambda a, b: run(fo, a, b)) if k < 9 else (lambda a, b: V("fr", FR + a, FR + b))
+            for a, b in (R3A, R3B) if k < 9 else (R3,):
+                act(to(a, b), V(fi), off=V(li, a // 16, b // 16))
             lift(fi, *R2, 0)
-            cp(run(fo, *R1), V(fi), V(li, 8, 16))
+            cp(to(*R1), V(fi), V(li, 8, 16))
             listed(li, 0, H)
-            act(run(fo, *R2), V(fi), off=V(li, 0, 8))
+            act(to(*R2), V(fi), off=V(li, 0, 8))
             if k < 9:
                 lift(fo, *R1, H)
-                cross(fo, *R1)
-                lift(fo, *R3, M)
-                cross(fo, *R3)
+                cross(fo, *R3A)
+                lift(fo, *R3A, R3A[0])
+                cross(fo, *R1, "s")
+                lift(fo, *R3B, R3B[0])
+                cross(fo, *R3B)
                 listed(lw, H, HM)
-                cross(fo, *R2, "s")
+                cross(fo, *R2)
         if not t:
-            fill(V("acc"), 0.0)
-        lift(fo, *R1, 0)
-        lift(fo, *R3, M)
-        counted(0, *R3)
-        act(V("trs", 0, HM), V("w0"), off=V("l0", 0, 32), accum=ACC(0))
-        lift(fo, *R2, H)
-        counted(32, 0, M)
-        act(V("trs", HM, NM), V("w0"), off=V("l0", 32, 64), accum=ACC(4))
-        act(V("trs", NM, 2 * NM), V("w1"), off=V("l0"), accum=ACC(1))
-        act(V("trs", 2 * NM, 2 * NM + CUT3), V("w2"), off=V("l0", 0, CUT3 // 16), accum=ACC(2))
-        cp(V("dvs"), V("w3"), V("l0"))
-        cp(V("dvt"), V("w2"), V("l0", CUT3 // 16, 64))
-        red(ACC(3), V("dvs"), ALU.add)
-        red(ACC(6), V("dvt"), ALU.add)
+            ts(V("cv", 0, 8), V("cn", 32, 40), SG, ALU.mult, BI, ALU.add)
+        same = lambda j: ts(V("ee", HM * j, HM * j + HM), V("fr", FR, FR + HM), V("cv", j, j + 1), ALU.is_equal)
+        summed = lambda j: scan(V("so", M * j, M * j + M), V("ee", HM * j, HM * j + M), V("ee", HM * j + M, HM * j + HM), ALU.add, ALU.add)
+        for a in (M, 0):
+            scan(V("sc", a, a + M), V("d0", 0, M), V("fr", FR + a, FR + a + M), ALU.mult, ALU.add)
+            if not a:
+                same(0)
+            ts(V("l0", a // 16, a // 16 + 16), V("sc", a + 15, a + M, 16), SSCL, ALU.mult, MID, ALU.add)
+            act(V("trs", a, a + M), V("w0"), off=V("l0", a // 16, a // 16 + 16), accum=ACC(a // 64))
+        for i in (1, 2, 3):
+            act(V("trs", HM * i, HM * i + HM), V("w%d" % i), off=V("l0"), accum=ACC(i))
+        for j in range(8):
+            if j < 7:
+                same(j + 1)
+            summed(j)
+            if j == 4:
+                tt(ACC(0), ACC(0), ACC(4), ALU.add)
+        ends = V("so", M - 1, 8 * M, M)
+        cp(on(V("up"), 0), on(ends, 64))
+        cp(on(V("acc", 8, 12), 0), on(V("acc", 0, 4), 64))
+        for b in (0, 1):
+            tt(Z("rot", 16 + 8 * b, 24 + 8 * b), on(ends, 32 * b, 32), on(V("up"), 32 * b, 32), ALU.add)
+        for b in (0, 1):
+            tt(Z("aci", 4 * b, 4 * b + 4), on(V("acc", 0, 4), 32 * b, 32), on(V("acc", 8, 12), 32 * b, 32), ALU.add)
         if not t:
-            ts(CF(9), IP(6), 32.0, ALU.mult, float(BIGR), ALU.add)
-            ts(V("alp"), V("one32"), BETA, ALU.mult, -1.0 / NM, ALU.mult)
-            fill(V("inv", 0, 96), 0.0)
+            ts(IP(6), IP(2), 7, ALU.bitwise_and)
+        ts(Z("roti", 0, 16, 2), Z("aci", 0, 8), 2047, ALU.bitwise_and)
+        ts(Z("roti", 1, 16, 2), Z("aci", 0, 8), 11, ALU.logical_shift_right)
+        if not t:
             fill(V("ypd"), 0.0)
-            ts(V("rest"), V("ri"), CF(9), ALU.add)
-            ts(V("alp"), V("alp"), 1.0, ALU.add)
-            ts(V("mlt"), V("ri"), LCOL, ALU.is_gt)
-        for b in range(4):
-            tt(Z("raw", 4 * b, 4 * b + 4), on(V("acc", 0, 4), 32 * b, 32), on(V("acc", 4, 8), 32 * b, 32), ALU.add)
-        if not t:
-            cp(V("rest2"), V("rest"), V("twice"))
-        ts(Z("aci"), Z("raw"), 1.0 / 2048.0, ALU.mult, -0.499, ALU.add)
-        ts(Z("t2"), Z("aci"), -2048.0, ALU.mult)
-        cp(Z("rot", 1, 32, 2), Z("aci"))
-        tt(Z("rot", 0, 32, 2), Z("t2"), Z("raw"), ALU.add)
+        cp(Z("rot", 0, 16), Z("roti"))
         for j in range(NTS):
             act(Z("trs", 32 * j, 32 * j + 32), Z("rot"), AF.Sign, bias=-1.5 - j, accum=Z("ypd", j, j + 1))
         act(Z("szs"), Z("rot"), AF.Identity, scale=2.0, bias=-34.0)
@@ -562,12 +563,26 @@ def rank_program(g, core, T, topo):
             ts(Z("cm", 32 * j, 32 * j + 32), Z("rot"), float(j + 2), ALU.is_ge)
         for j in range(NTS, NTH):
             red(Z("ypd", j, j + 1), Z("cm", 32 * j, 32 * j + 32), ALU.add)
+        if not t:
+            ts(BETA, LCOL, float(NTS), ALU.is_lt, NM / 2.0, ALU.mult)
+            ts(CF(9), IP(6), 32.0, ALU.mult, float(BIGR), ALU.add)
         tr(Z("ytr"), Z("ypd"))
+        if not t:
+            ts(V("alp"), V("one32"), BETA, ALU.mult, -1.0 / NM, ALU.mult)
+            ts(V("rest"), V("ri"), CF(9), ALU.add)
         red(COL(0), Z("ytr"), ALU.add)
+        if not t:
+            ts(V("alp"), V("alp"), 1.0, ALU.add)
         ts(Z("a1"), Z("alp"), COL(0), ALU.mult, on(BETA, 0, 32), ALU.add)
+        if not t:
+            ts(V("mlt"), V("ri"), LCOL, ALU.is_gt)
         tr(Z("cs"), Z("a1"))
         act(Z("trs", 512, 544), Z("cs"), AF.Sign, bias=0.5 - K, accum=Z("thr", 0, 1))
+        if not t:
+            cp(V("rest2"), V("rest"), V("twice"))
         ts(Z("f2"), Z("cs"), float(K), ALU.is_ge, 2048.0, ALU.mult)
+        if not t:
+            fill(V("inv", 0, 96), 0.0)
         gt, eq, thr = Z("ge", 0, 32), Z("ge", 32, 64), Z("thr", 0, 1)
         ts(gt, Z("szs"), thr, ALU.is_gt)
         ts(eq, Z("szs"), thr, ALU.is_equal)
@@ -587,19 +602,19 @@ def rank_program(g, core, T, topo):
         for b in range(4):
             tt(on(V("um"), 32 * b, 32), Z("ug"), Z("ue"), ALU.min)
         tt(V("zz"), V("um"), V("rest2"), ALU.min, V("twice"))
-        tr(V("zt"), V("zz"))
         tt(V("slot"), V("um"), V("rest"), ALU.min)
+        tr(V("zt"), V("zz"))
+        tr(V("sx"), V("slot"))
         for e in (0, 1):
             cp(V("sll", e, 16, 2), V("zt", 32 * e + 8 * rank, 32 * e + 8 * rank + 8))
-        tr(V("sx"), V("slot"))
         emit("v", lambda: g.vector.tensor_copy(ind(V("inv"), V("sll")), A(V("io2"))), [V("inv")], [V("io2"), V("sll")])
-        widen("sx", 0, 16, "s", "xb")
+        widen("sx", 0, 16, "xb")
         scan(V("scf", 0, K), V("d0", 0, K), V("inv", 0, K), ALU.mult, ALU.add)
         k5 = V("scf", 15, K, 16)
         ts(V("j1", 0, 5), k5, SCL, ALU.mult, float(-NM), ALU.add)
         qa, sa, qb, sb = "qa%d" % t, "sa%d" % t, "qb%d" % t, "sb%d" % t
+        widen("sx", 16, 32, "xb")
         pick(V(qa, 0, K), V(sa, 0, K), V(qc, 0, M), V(sp, 0, M), V("j1", 0, 5))
-        widen("sx", 16, 32, "s", "xb")
         swap(qa, sa, near, "ac%d" % t, "as%d" % t)
         if not t:
             ts(V("s80"), V("s80"), SCOL, ALU.add)
@@ -612,8 +627,7 @@ def rank_program(g, core, T, topo):
         ts(V("j2f", 0, 5), k5, SCL, ALU.mult, NM - 0.5, ALU.is_lt)
         mine = 64 * (lo // HM)
         if mine:
-            for a, b in runs(lo, lo + M):
-                scan(on(V("sc2", a - lo, b - lo), mine), on(V("d0", 0, b - a), mine), on(back(run(fo, NM - b, NM - a)), mine), ALU.mult, ALU.add)
+            scan(on(V("sc2"), mine), on(V("d0", 0, M), mine), on(back(V("fr", FR + NM - lo - M, FR + NM - lo)), mine), ALU.mult, ALU.add)
             last = V("sc2", 15, M, 16)
         else:
             last = V("sc", lo + 15, lo + M, 16)
@@ -646,10 +660,10 @@ def rank_program(g, core, T, topo):
         ts(V("rho", 48, 64), so, K - 0.5, ALU.is_lt)
         tt(me, me, V("rho", 48, 64), ALU.mult)
         tt(so, so, me, ALU.mult)
-        tt(V("rho", 32, 48), V("rho", 32, 48), so, ALU.add)
-        cp(V("pl"), V("rho", 32, 48))
         ts(V("rho", 48, 64), me, float(M), ALU.mult)
+        tt(V("rho", 32, 48), V("rho", 32, 48), so, ALU.add)
         tt(V("rho", 48, 64), V("rho", 48, 64), V("ki"), ALU.add)
+        cp(V("pl"), V("rho", 32, 48))
         cp(V("kl"), V("rho", 48, 64))
         if not t:
             pick(V("qr", 128, 384), V("sr", 128, 384), V("qu"), V("su"), V("cu", 8, 24))
@@ -657,9 +671,9 @@ def rank_program(g, core, T, topo):
             quant(V("qw"), V("sw"), V("wt"))
         if t + 1 < R:
             height(7, t + 1, qc, sp, 0, M)
-            tr(V("ho"), bank(7, M))
             m0, m1 = V("rho", 16, 32, 2), V("rho", 17, 32, 2)
             tt(V("mx"), m1, m0, ALU.subtract)
+            tr(V("ho"), bank(7, M))
             ts(V("mx"), V("mx"), HCOL, ALU.mult)
             tt(V("mx"), V("mx"), m0, ALU.add)
             ts(V("mx1"), V("mx"), -1.0, ALU.mult, 1.0, ALU.add)
@@ -698,9 +712,10 @@ def rank_program(g, core, T, topo):
     for h in (0, 1):
         pick(V(nq, *half[h]), V(ns, *half[h]), V(qc, 0, M + H * h + H), V(sp, 0, M + H * h + H), V("kl", 8 * h, 8 * h + 8))
         mm(bank(h, H), V("qw"), V("sw"), V(nq, *half[h]), V(ns, *half[h]), True, True)
-        cp(V("ys", *half[h]), bank(h, H))
         outs.append(("y", T.oc[:, 4 * H * h:4 * H * h + 4 * H], A(V(nq, *half[h])).bitcast(dt.uint8), [], [V(nq, *half[h])]))
-        outs.append(("s" if h else "y", T.y[:, H * h:H * h + H], A(V("ys", *half[h])), [], [V("ys", *half[h])]))
+    for h in (0, 1):
+        cp(V("ys", *half[h]), bank(h, H))
+        outs.append(("s", T.y[:, H * h:H * h + H], A(V("ys", *half[h])), [], [V("ys", *half[h])]))
     for k in range(4):
         o = V(ns, 0, M, 1, 32 * k, 32 * k + 4)
         outs.append(("y", T.osc[4 * k:4 * k + 4, 0:M], A(o), [], [o]))

@@ -9,44 +9,43 @@ NM = N * M
 HM = NM // 2
 H = M // 2
 SMAX = NM // K + 1
-NTH = SMAX - 1
 NTS = 7
 BIG = 4.0 * NM
 BIGR = NM + K
-WINV = BIGR + M + K
-RUNS = ((0, 128, 4, 4), (128, 256, 516, 2), (256, 512, 772, 1), (512, 768, 1029, 1), (768, 896, 1286, 2), (896, 1024, 1544, 4))
-WS, MID = 2064, 1028.0
-R1, R2, R3 = [r[:2] for r in RUNS[:3]]
-R3A, R3B = (M, M + H), (M + H, HM)
-TOP = 1100.0
+WINV = BIGR + NM + K + 16
+RUNS = ((-2048, 8), (-1024, 4), (-512, 2), (-256, 1), (128, 1), (256, 2), (512, 4), (1024, 8))
+UNIT = 1.0 / 4096
+OWN = ((2, 3, 4, 5), (0, 1, 6, 7))
+ALPHA = (4, 1)
+RK = (1, 2, 0, 3)
+GM, WM = 2048, 8192
 UP = float(2 ** 30)
-FR = 16
 C8, U8, F32, B16, I32, U16 = "float8_e4m3fn_x4", "uint8", "float32", "bfloat16", "int32", "uint16"
+XP = True
 
 WIDTHS = {
-    B16: {"xt": 4 * M, "ut": 512, "wt": 512, "one": 512, "et": 2048, "d0": 512, "dw": NM, "wb": NM + 16, "w0": WS, "w1": WS, "w2": WS, "w3": WS,
-          "xb": NM, "fs": WS, "fa": WS, "fb": WS, "fc": WS, "sc": HM, "sc2": M, "rs": M, "hb": 4 * M,
-          "fr": FR + HM, "ee": 8 * HM, "so": 8 * M, "cv": 16},
+    B16: {"xt": 4 * M, "ut": 512, "wt": 512, "one": 512, "et": 2048, "d0": 512, "dw": NM, "wb": NM + 16,
+          "w0": 2 * GM, "w1": 2 * GM, "w2": 2 * GM, "w3": 2 * GM, "xb": NM, "xz": HM, "d32": M, "cw": NM, "ca": 384, "cb": HM,
+          "fs": 2 * GM, "fa": 2 * WM, "fb": 2 * WM, "sc": HM, "rs": M, "hb": 4 * M,
+          "fr": HM, "ee": 8 * HM, "so": 8 * M, "cv": 16, "c2": 64},
     C8: {"qu": 128, "qw": 128, "qr": 384, "qe": 512},
     U8: {"su": 128, "sw": 128, "sr": 384, "se": 512},
-    F32: {"io2": M, "idn": WS, "rtf": M, "xe": NM, "fh": NM, "scf": 128, "ra": 384, "rb": 384, "trs": 2 * NM,
-          "ht": M, "ho": M, "inv": WINV, "cm": 32 * NTH, "rot": 32, "acc": 16, "ypd": 32, "szs": 32, "ys": M},
-    U16: {"la": 32, "lb": 32, "lc": 32, "l0": 32, "nbl": 64, "lnb": 24},
-    I32: {"iw": 64, "iu": 24, "id16": 16, "nbe": 48},
+    F32: {"io2": H, "i128": H, "idn": 2 * GM, "rtf": M, "xe": NM, "fh": NM, "scf": 128, "ra": 384, "rb": HM, "trs": 2 * NM,
+          "ht": M, "ho": M, "inv": WINV, "cm": 32 * SMAX, "rot": 32, "acc": 16, "ypd": 32, "szs": 32, "ys": M},
+    U16: {"la": 32, "lb": 32, "l0": 32, "nbl": 64, "lnb": 24},
+    I32: {"iw": 64, "iu": 24, "id16": 16, "nbe": 24},
 }
 SCRATCH = {"bl": ("psum", [128, 4096], F32)}
 for _d, _parts in WIDTHS.items():
     for _n, _w in _parts.items():
         SCRATCH[_n] = ("sbuf", [128, _w], _d)
 SMALL = {
-    "zf": (F32, {"d16": 16, "d17": 16, "cf": 32, "ri": 32, "mlt": 32, "rest": 32, "rest2": 64, "alp": 32, "one32": 32, "cn": 48, "sn": 16, "ki": 16, "s80": 8,
-                 "nn": 48, "nm": 24, "n1": 48, "n2": 48, "n3": 48, "n4": 48, "xs": 16,
-                 "m1": 16, "mm": 16, "eq4": 32, "b4": 32, "b2": 16, "b1": 32, "b1x": 32, "tn": 32, "zz": 64, "zt": 64, "thr": 8, "up": 8,
-                 "ytr": 32, "col": 8, "a1": 32, "cs": 32, "f2": 32, "g1": 32, "ge": 64, "inc": 64, "hh": 64, "je": 64, "a2": 64, "a2t": 64,
-                 "ug": 32, "ue": 32, "um": 32, "slot": 32, "sx": 32,
-                 "rho": 64, "j2f": 8, "mx": 8, "mx1": 8, "xo": 8, "xm": 8}),
+    "zf": (F32, {"d16": 16, "d17": 16, "cf": 32, "ri": 32, "nrest": 32, "dr": 32, "db": 32, "hs": 32, "s32": 32, "one32": 32,
+                 "sn": 16, "ki": 16, "s80": 8, "x0": 16, "m1": 16, "mm": 16, "neq": 32, "key": 32, "b2": 16, "zz": 96, "zt": 96,
+                 "thr": 8, "up": 8, "ytr": 32, "col": 8, "in2": 48, "a1": 32, "cs": 32, "suf": 32, "x3": 96, "c3": 96, "ge": 64,
+                 "inc": 64, "hh": 64, "je": 64, "jm": 8, "jx": 8, "rho": 64, "j2f": 8, "mx": 8, "mx1": 8, "xo": 8, "xm": 8}),
     "zi": (I32, {"ip": 16, "aci": 16, "roti": 16}),
-    "zu": (U16, {"cexp": 64, "cex2": 32, "crep": 64, "cu": 24, "twice": 4, "lro": 16, "sll": 16, "j1": 6, "j2": 6, "pl": 16, "kl": 16}),
+    "zu": (U16, {"cexp": 64, "crep": 64, "cu": 24, "rep8": 2, "lro": 16, "sll": 8, "j1": 6, "j2": 6, "pl": 16, "kl": 16}),
 }
 AT = {}
 for _b, (_d, _parts) in SMALL.items():
@@ -66,16 +65,13 @@ for _t in range(R + 1):
     SCRATCH["qc%d" % _t] = ("sbuf", [128, 2 * M if _t < R else M], C8)
     SCRATCH["scp%d" % _t] = ("sbuf", [128, 2 * M if _t < R else M], U8)
 
-SEMAPHORES = (["ev", "es", "et", "eg", "loc", "nbr"] + ["h%d" % t for t in range(R)]
+SEMAPHORES = (["ev", "es", "et", "eg", "loc"] + ["nb%d" % d for d in range(N)] + ["h%d_%d" % (t, d) for t in range(R) for d in range(N)]
               + ["%s%d" % (k, t) for t in range(R) for k in ("ac", "as", "bc", "bs")]
               + ["dx", "du", "dw", "dnb", "drt", "dout"])
 
 
 def place(n):
-    for n0, n1, c, s in RUNS:
-        if n0 <= n < n1:
-            return c + s * (n - n0)
-    return WS
+    return GM + RUNS[n // H][0] + RUNS[n // H][1] * (n % H)
 
 
 def rank_program(g, core, T, topo):
@@ -91,17 +87,12 @@ def rank_program(g, core, T, topo):
         return (buf, off + a, off + (w if b is None else b), step, p0, p1)
 
     def on(r, p0, n=64):
-        return r[:4] + (p0, p0 + n) + r[6:]
+        return r[:4] + (p0, p0 + n)
 
     def Z(name, a=0, b=None, step=1):
         return V(name, a, b, step, 0, 32)
 
-    def back(r):
-        return r[:6] + (True,)
-
     def A(r):
-        if len(r) > 6:
-            return T[r[0]][r[4]:r[5], r[1] + (r[2] - r[1] - 1) // r[3] * r[3]:r[1] - 1:-r[3]]
         return T[r[0]][r[4]:r[5], r[1]:r[2]] if r[3] == 1 else T[r[0]][r[4]:r[5], r[1]:r[2]:r[3]]
 
     def meets(a, b):
@@ -194,8 +185,9 @@ def rank_program(g, core, T, topo):
     def red(out, in_, op):
         emit("v", lambda: g.vector.tensor_reduce(A(out), A(in_), AxisListType.X, op), [out], [in_])
 
-    def scan(out, d0, d1, op0, op1):
-        emit("v", lambda: g.vector.tensor_tensor_scan(A(out), A(d0), A(d1), 0.0, op0, op1), [out], [d0, d1])
+    def scan(out, d0, d1, op0, op1, first=0.0):
+        col = isinstance(first, tuple)
+        emit("v", lambda: g.vector.tensor_tensor_scan(A(out), A(d0), A(d1), A(first) if col else first, op0, op1), [out], [d0, d1] + ([first] if col else []))
 
     def tr(out, in_):
         emit("v", lambda: g.vector.transpose(A(out), A(in_)), [out], [in_])
@@ -213,6 +205,12 @@ def rank_program(g, core, T, topo):
             return g.scalar.activation(A(out), src(), func, **k2)
         emit("s", fn, [out] + ([accum] if accum else []), [in_] + cols + ([off] if off else []))
 
+    def move(by, out, in_, off=None):
+        if by == "v":
+            cp(out, in_, off)
+        else:
+            act(out, in_, off=off)
+
     def iota(out, pattern, base, cm):
         if SCRATCH[out[0]][2] == I32:
             fn = lambda: g.iota(A(out), pattern, base, cm)
@@ -229,22 +227,38 @@ def rank_program(g, core, T, topo):
     def mm(out, lq, ls, rq, rs, start, stop):
         emit("t", lambda: g.tensor.matmul_mx(A(out), A(lq), A(ls), A(rq), A(rs), start, stop), [out], [lq, ls, rq, rs])
 
-    def pick(qo, so, qi, si, off):
+    def codes(qo, qi, off):
         emit("v", lambda: g.vector.tensor_copy(A(qo).bitcast(dt.uint32), A(qi).bitcast(dt.uint32).indirect(A(off))), [qo], [qi, off])
+
+    def pick(qo, so, qi, si, off):
+        codes(qo, qi, off)
         act(so, si, off=off)
 
-    others = [d for d in range(N) if d != rank]
+    def halves(outs, r, spare, op, p=0, n=64):
+        if XP:
+            for o in outs:
+                tt(o, on(r, p, n), on(r, 64 + p, n), op)
+        else:
+            cp(on(spare, p, n), on(r, 64 + p, n))
+            for o in outs:
+                tt(o, on(r, p, n), on(spare, p, n), op)
+
+    others = [(rank + k) % N for k in range(1, N)]
+    senders = others[::-1]
     mask3 = 0xFFFF
     for d in others:
         mask3 &= topo.mask(core, T.cores[d])
     groups = bin(mask3).count("1")
 
-    def spread(src, sem):
+    def spread(piece, sem):
+        src = piece(rank)
         use("g", [src], [])
         ids = [DstId(rid=topo.addr(T.cores[d])[0], pnc=topo.addr(T.cores[d])[1]) for d in others]
-        g.remote_dma_fused([RemoteDMATransfer(dst_ids=ids, dma_engine_mask=mask3, remote_sem=T.sem[sem], srcs=[A(src)], dsts=[A(src) for d in others])],
+        g.remote_dma_fused([RemoteDMATransfer(dst_ids=ids, dma_engine_mask=mask3, remote_sem=T.sem[sem % rank], srcs=[A(src)], dsts=[A(src) for d in others])],
                            local_sem=T.sem.loc)
         cnt["loc"] = cnt.get("loc", 0) + groups
+        for d in others:
+            arrives(sem % d, groups, [piece(d)])
 
     near = [d for d in others if topo.same_plane(topo.chip(core), topo.chip(T.cores[d]))][0]
     pair = sorted([rank, near])
@@ -263,73 +277,68 @@ def rank_program(g, core, T, topo):
         arrives(semc, n, [V(q, K, 2 * K)])
         arrives(sems, n, [V(s, K, 2 * K)])
 
-    def widen(x, c0, c1, to):
-        act(V(to, 32 * c0, 32 * c1), V(x, c0, c1), off=V("cexp", 0, 2 * (c1 - c0)))
+    def widen(c0, c1):
+        act(V("xb", 32 * c0, 32 * c1), V("zt", 64 + c0, 64 + c1), off=V("cexp", 0, 2 * (c1 - c0)))
 
-    def spaced(x, c0, c1):
-        cp(V("xe", 32 * c0, 32 * c1, 32), V(x, c0, c1))
-        act(V("xe", 32 * c0 + 16, 32 * c1, 32), V(x, c0, c1))
+    def turned(t, d, by):
+        for e in (0, 1):
+            move(by[e], V("xe", M * d + 16 * e, M * d + M, 32), V("xh%d" % t, 8 * d, 8 * d + 8))
+        b = 32 * RK.index(d)
+        act(on(V("rb", 3 * H, 4 * H, 16), b, 32), on(V("xh%d" % t, 8 * d, 8 * d + 8), b, 32))
+        tr(V("fh", M * d, M * d + M), V("xe", M * d, M * d + M))
 
-    def turn(f, c0, c1):
-        tr(V(f, 32 * c0, 32 * c1), V("xe", 32 * c0, 32 * c1))
+    def grun(f, k):
+        a, s = RUNS[k]
+        return V(f, GM + a, GM + a + s * H, s)
 
-    def run(f, a, b):
-        n0, n1, c, s = [r for r in RUNS if r[0] <= a and b <= r[1]][0]
-        return V(f, c + s * (a - n0), c + s * (b - n0), s)
+    def wrun(f, h, k):
+        a, s = RUNS[k]
+        return V(f, WM + ALPHA[h] * a, WM + ALPHA[h] * (a + s * H), ALPHA[h] * s)
 
-    def runs(a, b):
-        return [(max(a, r[0]), min(b, r[1])) for r in RUNS if r[0] < b and a < r[1]]
-
-    def turn_s(f, c0, c1):
-        for a, b in runs(32 * c0, 32 * c1):
-            tr(run(f, a, b), V("xb", a, b))
-
+    piece = lambda f, i: wrun(f, 0, OWN[0][i])
     CF = lambda k: V("cf", k, k + 1)
-    SCL, HI, SCOL, LCOL, BCOL, BETA, HCOL = [CF(k) for k in (0, 4, 6, 7, 8, 3, 4)]
-    UPPER, SG, NSG, BI, H15, LH, SSCL = [CF(k) for k in (5, 16, 17, 18, 19, 20, 21)]
+    SCL, HI, UPPER, SCOL, LCOL, GSCL, WSCL, NHS, KT = [CF(k) for k in (0, 4, 5, 6, 7, 16, 17, 19, 20)]
 
-    def lift(f, a, b, at):
-        scan(V("sc", at, at + b - a), V("d0", 0, b - a), run(f, a, b), ALU.mult, ALU.add)
+    def lift(f, i):
+        scan(V("sc", H * i, H * i + H), V("d0", 0, H), piece(f, i), ALU.mult, ALU.add)
 
-    def listed(l, a, b):
-        ts(V(l, a // 16, b // 16), V("sc", a + 15, b, 16), SCL, ALU.mult, MID, ALU.add)
+    def listed(l, i, j):
+        ts(V(l, 8 * i, 8 * j), V("sc", H * i + 15, H * j, 16), WSCL, ALU.mult, float(WM), ALU.add)
 
-    def cross(f, a, b, by="v"):
-        for p in (0, 64):
-            out, src = on(run(f, NM - b, NM - a), 64 - p), on(back(run(f, a, b)), p)
-            if by == "v":
-                ts(out, src, -1.0, ALU.mult)
-            else:
-                act(out, src, scale=-1.0)
+    def cross(f, i, h, by):
+        move(by, on(wrun(f, 1 - h, OWN[h][i]), 64 - 64 * h), on(piece(f, i), 64 * h))
 
     bank = lambda k, w: V("bl", 512 * k, 512 * k + w)
 
     loads = []
-    for k in range(8):
-        shift = (k % 2) * (2 - k // 4)
-        o = V("nbe", 0, 48 - shift, 1, 16 * k, 16 * k + 16)
-        loads.append(("ys"[k % 2], A(o), T.nb[:, shift:48], [o], []))
-    dmas("dnb", loads)
+    for k in range(4):
+        shift = 2 * (k % 2)
+        o = V("nbe", 0, 24 - shift, 1, 16 * k, 16 * k + 16)
+        loads.append(("s", A(o), T.nb[:, 24 * (k // 2) + shift:24 * (k // 2) + 24], [o], []))
     dmas("dx", [("y", A(V("xt")), T.x[:], [V("xt")], [])])
-    dmas("du", [("s", A(V("ut")), T.u[:], [V("ut")], [])])
+    dmas("dnb", loads)
+    dmas("du", [("y", A(V("ut")), T.u[:], [V("ut")], [])])
     IP = lambda k: V("ip", k, k + 1)
     iota(V("iu"), [[1, 3], [0, 8]], 0, 0)
     iota(IP(0), [[0, 1]], 0, 1)
     iota(V("iw"), [[1, 32], [0, 2]], 0, 0)
     iota(V("id16"), [[1, 16]], 128, -1)
     iota(V("ri"), [[1, 32]], 0, 0)
+    iota(V("i128"), [[1, H]], 0, 0)
+    o = 16 * rank
     fill(V("dw"), 0.0)
+    fill(on(V("nbl", o, o + 12), 64), 0)
     act(V("xe"), V("dw"))
     cp(V("cu"), V("iu"))
     ts(IP(4), IP(0), 4, ALU.logical_shift_right, 1, ALU.bitwise_and)
     ts(IP(5), IP(0), 6, ALU.logical_shift_right)
     ts(IP(1), IP(0), 15, ALU.bitwise_and)
     ts(IP(2), IP(0), 31, ALU.bitwise_and)
-    ts(IP(3), IP(0), 5, ALU.logical_shift_right)
+    ts(IP(6), IP(0), 7, ALU.bitwise_and)
     ts(IP(7), IP(0), 5, ALU.logical_shift_right, 1, ALU.bitwise_and)
     cp(V("cexp"), V("iw"))
     cp(V("cf", 4, 6), V("ip", 4, 6))
-    cp(V("cf", 6, 9), V("ip", 1, 4))
+    cp(V("cf", 6, 8), V("ip", 1, 3))
     ts(V("id16"), V("id16"), 15, ALU.bitwise_and)
     ts(V("iw"), V("iw"), 0.0, ALU.mult)
     ts(SCL, SCOL, 15.0, ALU.is_equal, 1.0 - 1.0 / UP, ALU.mult)
@@ -338,17 +347,10 @@ def rank_program(g, core, T, topo):
     ts(V("crep"), V("iw"), SCOL, ALU.add)
     ts(SCL, SCL, 1.0 / UP, ALU.max)
     tt(V("d16"), V("d16"), V("d17"), ALU.add)
-    cp(V("twice", 0, 2), V("crep", 0, 2))
-    ts(V("twice", 2, 4), V("crep", 0, 2), 16.0, ALU.add)
     fill(V("one"), 1.0)
-    o = 16 * rank
-    for b in (0, 1):
-        for e in (0, 1):
-            cp(on(V("nbl", o + e, o + 12, 2), 32 * b, 32), on(V("nbe", 24 * b + e, 24 * b + 24, 4), 32 * b, 32))
-        cp(on(V("nbl", o, o + 12), 64 + 32 * b, 32), on(V("nbe", 24 * b, 24 * b + 24, 2), 64 + 32 * b, 32))
-    cp(V("nbl", o + 12, o + 16), V("nbe", 0, 4))
-    spread(V("nbl", o, o + 16), "nbr")
-    arrives("nbr", groups * len(others), [V("nbl", 16 * d, 16 * d + 16) for d in others])
+    for e in (0, 1):
+        cp(on(V("nbl", o + e, o + 12, 2), 0), on(V("nbe", e, 24, 4), 0))
+    spread(lambda d: V("nbl", 16 * d, 16 * d + 12), "nb%d")
     quant(V("qu"), V("su"), V("ut"))
     pick(V("qr", 0, 128), V("sr", 0, 128), V("qu"), V("su"), V("cu", 0, 8))
     act(V("d0"), V("d16"), off=V("crep", 0, 32))
@@ -357,21 +359,7 @@ def rank_program(g, core, T, topo):
         mm(bank(k, n), V("qr", 128 * t, 128 * t + 128), V("sr", 128 * t, 128 * t + 128), V(q, a, a + n), V(s, a, a + n), True, True)
 
     def share(t):
-        spread(V("xh%d" % t, 8 * rank, 8 * rank + 8), "h%d" % t)
-        arrives("h%d" % t, groups * len(others), [V("xh%d" % t, 8 * d, 8 * d + 8) for d in others])
-
-    def own_f(t):
-        spaced("xh%d" % t, 8 * rank, 8 * rank + 8)
-        turn("fh", 8 * rank, 8 * rank + 8)
-
-    def others_f(t):
-        xh = "xh%d" % t
-        spaced(xh, 0, 32)
-        for d in range(N):
-            act(on(V("xs", 0, 8), 32 * d, 32), on(V(xh, 8 * d, 8 * d + 8), 32 * d, 32))
-        for c0, c1 in ((0, 8 * rank), (8 * rank + 8, 32)):
-            if c1 > c0:
-                turn("fh", c0, c1)
+        spread(lambda d: V("xh%d" % t, 8 * d, 8 * d + 8), "h%d_" % t + "%d")
 
     for h in (0, 1):
         quant(V("qc0", H * h, H * h + H), V("scp0", H * h, H * h + H), V("xt", 4 * H * h, 4 * H * h + 4 * H))
@@ -383,156 +371,158 @@ def rank_program(g, core, T, topo):
     share(0)
     dmas("dw", [("y", A(V("wt")), T.w[:], [V("wt")], [])])
 
+    fill(V("one32"), 1.0)
     iota(V("sn"), [[16, 16]], M * rank, 0)
     iota(V("ki"), [[16, 16]], 0, 0)
     iota(V("s80"), [[16, 8]], 0, 0)
-    iota(V("io2"), [[1, M]], NM, 0)
+    for h in (0, 1):
+        iota(on(V("io2"), 64 * h), [[32, 8], [1, 16]], NM + 16 * h, 0)
+    iota(Z("nrest"), [[-1, 32]], -BIGR - 1, -32)
+    iota(Z("dr", 0, 1), [[0, 1]], BIGR, 32)
+    iota(Z("dr", 1, 32), [[0, 31]], 1, 0)
+    iota(Z("db", 0, 1), [[0, 1]], int(BIG), 0)
+    iota(Z("db", 1, 32), [[0, 31]], 0, 0)
+    iota(Z("in2", 0, 1), [[0, 1]], 0, 0)
+    iota(Z("ypd", 0, 1), [[0, 1]], 32, 0)
+    iota(Z("ypd", SMAX, 32), [[0, 32 - SMAX]], 0, 0)
+    select(Z("s32"), Z("one32"), [[0, 32]], ALU.is_gt, 0.0, 0, 1)
+    select(Z("s32"), Z("s32"), [[0, 32]], ALU.is_ge, 0.0, NTS, -1)
     ts(CF(12), IP(7), -8.0, ALU.mult, LCOL, ALU.add)
-    ts(CF(22), IP(7), 8.0, ALU.mult, HI, ALU.add)
-    ts(CF(23), LCOL, 32.0, ALU.mult, 16.0, ALU.add)
-    ts(CF(24), BCOL, float(M), ALU.mult, LCOL, ALU.add)
-    fill(V("one32"), 1.0)
+    ts(CF(22), IP(7), 8.0, ALU.mult)
     fill(V("wb", NM, NM + 16), 0.0)
-    ts(SG, UPPER, 2.0, ALU.mult, -1.0, ALU.add)
     ts(CF(13), CF(12), 6.0, ALU.is_equal)
     ts(CF(14), CF(12), 7.0, ALU.is_equal, 2048.0, ALU.mult)
-    ts(NSG, UPPER, -2.0, ALU.mult, 1.0, ALU.add)
-    ts(BI, UPPER, -2.0 * TOP, ALU.mult, TOP, ALU.add)
+    ts(CF(23), UPPER, float(ALPHA[1] - ALPHA[0]), ALU.mult, float(ALPHA[0]), ALU.add)
+    ts(GSCL, SCL, 1.0 / UNIT, ALU.mult)
     tt(CF(15), CF(13), CF(14), ALU.add)
-    ts(H15, UPPER, 15.0, ALU.mult)
-    tt(LH, UPPER, CF(24), ALU.add)
-    tt(CF(22), CF(22), CF(23), ALU.add)
+    ts(V("x0", 0, 4), V("ri", 0, 4), 32.0, ALU.mult, LCOL, ALU.add)
+    tt(WSCL, GSCL, CF(23), ALU.mult)
     ts(V("dw", 0, NM, 33), V("one32"), CF(15), ALU.mult)
-    ts(V("nn", 24, 32), V("ri", 0, 8), 32.0, ALU.mult, LH, ALU.add)
-    ts(V("nn", 32, 40), V("ri", 0, 8), CF(22), ALU.add)
+    for e in (0, 1):
+        cp(V("rep8", e, e + 1), IP(6))
     tr(V("wb", 0, NM), V("dw"))
-    for i in range(4):
-        for n0, n1, c, s in RUNS:
-            select(V("w%d" % i, c, c + s * (n1 - n0), s), V("wb", n0 + 6 - 2 * i, n1 + 6 - 2 * i), [[0, n1 - n0]], ALU.is_gt, 0.0, 1, 0)
-    for n0, n1, c, s in RUNS:
-        iota(V("idn", c, c + s * (n1 - n0), s), [[1, n1 - n0]], n0, 0)
+    for i in range(1, 4):
+        for k in range(8):
+            select(grun("w%d" % i, k), V("wb", H * k + 6 - 2 * i, H * k + H + 6 - 2 * i), [[0, H]], ALU.is_gt, 0.0, 1, 0)
+    for k in range(8):
+        iota(grun("idn", k), [[1, H]], H * k, 0)
     for b in range(4):
         select(V("et", 512 * b, 512 * b + 512), V("one"), [[1, 512]], ALU.is_equal, 0.0, -b, -4)
-    own_f(0)
+    for k, (a, s) in enumerate(RUNS):
+        act(V("cw", H * k, H * k + H), V("i128"), AF.Identity, scale=s * UNIT, bias=a * UNIT)
+    turned(0, rank, "vs")
+    for k in range(8):
+        act(grun("w0", k), V("wb", H * k + 6, H * k + H + 6))
+    fill(V("xz"), 0.0)
+    fill(V("d32"), 1.0)
+    for b in range(4):
+        for e in (0, 1):
+            a, s = RUNS[2 * RK[b] + e]
+            ts(on(V("cb", 3 * H + 64 * e, 3 * H + 64 * e + 64, 16), 32 * b, 32), on(V("x0", 0, 4), 32 * b, 32), s * UNIT, ALU.mult, a * UNIT, ALU.add)
+    fill(V("d32", 0, M, 32), 0.0)
+    for d in [rank] + senders:
+        for b in (0, 1):
+            cp(on(V("lnb", 12 * b, 12 * b + 12), 32 * RK.index(d), 32), on(V("nbl", 16 * d, 16 * d + 12), 32 * b, 32))
 
-    def coded(step, a, b):
-        n1, n2, n3, n4, cn = [V(x, a, b) for x in ("n1", "n2", "n3", "n4", "cn")]
-        if step == 0:
-            ts(n1, V("nn", a, b), 896.0, ALU.min, 128.0, ALU.max)
-            ts(n2, V("nn", a, b), 768.0, ALU.min, 256.0, ALU.max)
-            ts(n3, V("nn", a, b), -4.0, ALU.mult, TOP + NM / 2, ALU.add)
-        elif step == 1:
-            ts(n4, n1, 2.0, ALU.mult)
-            tt(n2, n2, n3, ALU.add)
-        else:
-            tt(cn, n2, n4, ALU.add)
-
-    def lists(to, p):
-        for d in [rank] + others:
-            for b in (0, 1):
-                cp(on(V(to, 12 * b, 12 * b + 12), 32 * d, 32), on(V("nbl", 16 * d, 16 * d + 12), p + 32 * b, 32))
-
-    tt(SSCL, SCL, NSG, ALU.mult)
-    ts(V("cex2"), V("cexp", 0, 32), NSG, ALU.mult, H15, ALU.add)
-    fill(V("b1"), 0.0)
-    lists("lnb", 0)
-    others_f(0)
-
-    def numbers(step):
-        if step == 0:
-            lists("nn", 64)
-        elif step == 1:
-            ts(V("nm"), V("nn", 0, 24), float(HM), ALU.is_ge)
-        elif step == 2:
-            tt(V("nn", 0, 24), V("nn", 0, 24), V("nm"), ALU.add)
-        else:
-            coded(step - 3, 0, 40)
-
-    win3 = ["fa", "fb", "fc"]
-    lst3 = ["la", "lb", "lc"]
     lo = M * rank
     COL = lambda k: Z("col", k, k + 1)
     ACC = lambda k: V("acc", k, k + 1)
+    z = lambda r: on(r, 0, 32)
+    HS = Z("hs", 0, 1)
     for t in range(R):
-        xh, qc, sp = "xh%d" % t, "qc%d" % t, "scp%d" % t
+        qc, sp = "qc%d" % t, "scp%d" % t
         if t:
-            own_f(t)
+            turned(t, rank, "vs")
             fill(V("inv", 0, 96), 0.0)
-            others_f(t)
-        nbh = [V("rb", H * k, H * k + H, 16) for k in range(J)] + [V("xs", 0, 8)]
-        once = (lambda step: None) if t else numbers
-        act(V("ra", H, 3 * H), V("fh"), off=V("lnb", 8, 24))
-        cp(V("ra", 0, H), V("fh"), V("lnb", 0, 8))
-        once(0)
-        tr(V("rb", 0, H), V("ra", 0, H))
-        once(1)
-        tr(V("rb", H, 3 * H), V("ra", H, 3 * H))
-        m1, mx4 = V("m1", 0, 8), V("mm", 0, 8)
-        tt(m1, nbh[0], nbh[3], ALU.max)
-        once(2)
-        tt(mx4, nbh[1], nbh[2], ALU.max)
-        once(3)
-        tt(mx4, mx4, m1, ALU.max)
-        once(4)
-        for k in range(J + 1):
-            tt(V("eq4", 8 * k, 8 * k + 8), nbh[k], mx4, ALU.is_equal)
-            if k == 1:
-                once(5)
-        tt(V("b4"), V("eq4"), V("cn", 0, 32), ALU.mult)
-        tt(V("b2"), V("b4", 0, 16), V("b4", 16, 32), ALU.max)
-        def handed(to, d, b):
-            tt(on(V(to, 8 * (d % 2), 8 * (d % 2) + 8), 32 * b, 32), on(V("b2", 0, 8), 32 * d, 32), on(V("b2", 8, 16), 32 * d, 32), ALU.max)
-        for d in (2, 3):
-            for b in (2, 3):
-                handed("b1", d, b)
-        handed("b1x", 0, 0)
-        handed("b1x", 0, 1)
-        tr(on(V("tn"), 64), on(V("b1"), 64))
-        handed("b1x", 1, 0)
-        handed("b1x", 1, 1)
-        tr(on(V("b1x"), 64), on(back(V("tn")), 64))
-        wide = lambda a, b: (V("xb", a, b), V("b1x", 0, 16), V("cex2", a // 16, b // 16))
-        for a, b in (R3, R2):
-            out, win, off = wide(a, b)
-            act(out, win, AF.Identity, off=off, scale=SG, bias=BI)
-        out, win, off = wide(*R1)
-        ts(out, win, SG, ALU.mult, BI, ALU.add, off)
-        tr(run("fa", *R1), V("xb", *R1))
-        tr(run("fa", *R3), V("xb", *R3))
-        lift("fa", *R1, H)
-        tr(run("fa", *R2), V("xb", *R2))
-        lift("fa", *R3, M)
-        cross("fa", *R2, "s")
-        cross("fa", *R3)
-        listed("la", H, HM)
-        cross("fa", *R1)
-        for k in range(10):
-            fi, fo, li, lw = win3[k % 3], win3[(k + 1) % 3], lst3[k % 3], lst3[(k + 1) % 3]
-            to = (lambda a, b: run(fo, a, b)) if k < 9 else (lambda a, b: V("fr", FR + a, FR + b))
-            for a, b in (R3A, R3B) if k < 9 else (R3,):
-                act(to(a, b), V(fi), off=V(li, a // 16, b // 16))
-            lift(fi, *R2, 0)
-            cp(to(*R1), V(fi), V(li, 8, 16))
-            listed(li, 0, H)
-            act(to(*R2), V(fi), off=V(li, 0, 8))
-            if k < 9:
-                lift(fo, *R1, H)
-                cross(fo, *R3A)
-                lift(fo, *R3A, R3A[0])
-                cross(fo, *R1, "s")
-                lift(fo, *R3B, R3B[0])
-                cross(fo, *R3B)
-                listed(lw, H, HM)
-                cross(fo, *R2)
+        turned(t, senders[0], "vs")
+        turned(t, senders[1], "ss")
         if not t:
-            ts(V("cv", 0, 8), V("cn", 32, 40), SG, ALU.mult, BI, ALU.add)
-        same = lambda j: ts(V("ee", HM * j, HM * j + HM), V("fr", FR, FR + HM), V("cv", j, j + 1), ALU.is_equal)
+            act(V("ca"), V("cw"), off=V("lnb"))
+        turned(t, senders[2], "vs" if t else "vv")
+        act(V("ra", H, 2 * H + 32), V("fh"), off=V("lnb", 8, 18))
+        cp(V("ra", 0, H), V("fh"), V("lnb", 0, 8))
+        act(V("ra", 2 * H + 32, 3 * H), V("fh"), off=V("lnb", 18, 24))
+        tr(V("rb", 0, H), V("ra", 0, H))
+        tr(V("rb", H, 2 * H + 32), V("ra", H, 2 * H + 32))
+        tr(V("rb", 2 * H + 32, 3 * H), V("ra", 2 * H + 32, 3 * H))
+        if not t:
+            tr(V("cb", 0, H), V("ca", 0, H))
+        tt(V("m1"), V("rb", 0, M, 16), V("rb", M, HM, 16), ALU.max)
+        if not t:
+            tr(V("cb", H, 2 * H), V("ca", H, 2 * H))
+        tt(V("mm", 0, 8), V("m1", 0, 8), V("m1", 8, 16), ALU.max)
+        if not t:
+            tr(V("cb", 2 * H, 3 * H), V("ca", 2 * H, 3 * H))
+        tt(V("neq"), V("mm", 0, 8), V("rb", 0, HM, 16), ALU.not_equal, V("rep8"))
+        if not t:
+            ts(Z("hs"), Z("s32"), -0.5, ALU.mult, 1.0, ALU.add)
+            ts(z(NHS), Z("s32", 0, 1), 0.5, ALU.mult, -1.0, ALU.add)
+        tt(V("key"), V("neq"), V("cb", 0, HM, 16), ALU.add)
+        if not t:
+            ts(z(KT), Z("s32", 0, 1), float(K), ALU.mult, float(K), ALU.add)
+            ts(Z("s32"), Z("s32"), 32.0, ALU.mult)
+        tt(V("b2"), V("key", 0, 16), V("key", 16, 32), ALU.min)
+        if not t:
+            fill(V("inv", 0, 96), 0.0)
+        spot = lambda e: V("xz", M * e, M * e + M, 32)
+        for e in (0, 1):
+            tt(spot(e), V("b2", 0, 8), V("b2", 8, 16), ALU.min)
+        for e in (0, 1):
+            for h in (0, 1):
+                src = 64 * h + 32 * e
+                tt(on(spot(e), 64 * h + 32 - 32 * e, 32), on(V("b2", 0, 8), src, 32), on(V("b2", 8, 16), src, 32), ALU.min)
+        for e in (0, 1):
+            scan(V("xb", M * e, M * e + M), V("d32"), V("xz", M * e, M * e + M), ALU.mult, ALU.add)
+        for i in range(4):
+            tr(piece("fa", i), V("xb", H * i, H * i + H))
+        for i in (0, 1):
+            cross("fa", i, 0, "s")
+            cross("fa", i, 1, "s")
+            lift("fa", i)
+        cross("fa", 3, 0, "s")
+        lift("fa", 3)
+        cross("fa", 2, 0, "v")
+        lift("fa", 2)
+        listed("la", 0, 2)
+        cross("fa", 2, 1, "v")
+        cross("fa", 3, 1, "v")
+        listed("la", 2, 4)
+        for k in range(9):
+            fi, fo, li, lw = ("fa", "fb", "la", "lb") if k % 2 == 0 else ("fb", "fa", "lb", "la")
+            for i, by in ((0, "v"), (1, "s"), (3, "v"), (2, "s")):
+                move(by, piece(fo, i), V(fi), V(li, 8 * i, 8 * i + 8))
+            lift(fo, 0)
+            cross(fo, 1, 0, "s")
+            lift(fo, 1)
+            cross(fo, 0, 0, "s")
+            cross(fo, 0, 1, "v")
+            cross(fo, 1, 1, "v")
+            lift(fo, 3)
+            cross(fo, 3, 1, "s")
+            cross(fo, 2, 0, "v")
+            lift(fo, 2)
+            cross(fo, 2, 1, "s")
+            listed(lw, 0, 2)
+            cross(fo, 3, 0, "v")
+            listed(lw, 2, 4)
+        act(V("fr", 0, M), V("fb"), off=V("lb", 0, 16))
+        cp(V("fr", 3 * H, HM), V("fb"), V("lb", 24, 32))
+        act(V("fr", M, 3 * H), V("fb"), off=V("lb", 16, 24))
+        if not t:
+            for e in (0, 1):
+                tr(V("c2", 32 * e, 32 * e + 32), V("cw", 16 + e, NM, 32))
+            ts(V("x0", 8, 16), V("ri", 0, 8), CF(22), ALU.add)
+            tt(CF(24), V("c2", 32, 33), V("c2", 0, 1), ALU.subtract)
+            cp(CF(25), V("c2", 0, 1))
+        same = lambda j: ts(V("ee", HM * j, HM * j + HM), V("fr"), V("cv", j, j + 1), ALU.is_equal)
         summed = lambda j: scan(V("so", M * j, M * j + M), V("ee", HM * j, HM * j + M), V("ee", HM * j + M, HM * j + HM), ALU.add, ALU.add)
-        for a in (M, 0):
-            scan(V("sc", a, a + M), V("d0", 0, M), V("fr", FR + a, FR + a + M), ALU.mult, ALU.add)
-            if not a:
+        for a in (0, M):
+            scan(V("sc", a, a + M), V("d0", 0, M), V("fr", a, a + M), ALU.mult, ALU.add)
+            if a:
                 same(0)
-            ts(V("l0", a // 16, a // 16 + 16), V("sc", a + 15, a + M, 16), SSCL, ALU.mult, MID, ALU.add)
+            elif not t:
+                ts(V("cv", 0, 8), V("x0", 8, 16), CF(24), ALU.mult, CF(25), ALU.add)
+            ts(V("l0", a // 16, a // 16 + 16), V("sc", a + 15, a + M, 16), GSCL, ALU.mult, float(GM), ALU.add)
             act(V("trs", a, a + M), V("w0"), off=V("l0", a // 16, a // 16 + 16), accum=ACC(a // 64))
         for i in (1, 2, 3):
             act(V("trs", HM * i, HM * i + HM), V("w%d" % i), off=V("l0"), accum=ACC(i))
@@ -543,79 +533,64 @@ def rank_program(g, core, T, topo):
             if j == 4:
                 tt(ACC(0), ACC(0), ACC(4), ALU.add)
         ends = V("so", M - 1, 8 * M, M)
-        cp(on(V("up"), 0), on(ends, 64))
-        cp(on(V("acc", 8, 12), 0), on(V("acc", 0, 4), 64))
         for b in (0, 1):
-            tt(Z("rot", 16 + 8 * b, 24 + 8 * b), on(ends, 32 * b, 32), on(V("up"), 32 * b, 32), ALU.add)
+            halves([Z("rot", 16 + 8 * b, 24 + 8 * b)], ends, V("up"), ALU.add, 32 * b, 32)
         for b in (0, 1):
-            tt(Z("aci", 4 * b, 4 * b + 4), on(V("acc", 0, 4), 32 * b, 32), on(V("acc", 8, 12), 32 * b, 32), ALU.add)
-        if not t:
-            ts(IP(6), IP(2), 7, ALU.bitwise_and)
+            halves([Z("aci", 4 * b, 4 * b + 4)], V("acc", 0, 4), V("acc", 8, 12), ALU.add, 32 * b, 32)
         ts(Z("roti", 0, 16, 2), Z("aci", 0, 8), 2047, ALU.bitwise_and)
         ts(Z("roti", 1, 16, 2), Z("aci", 0, 8), 11, ALU.logical_shift_right)
-        if not t:
-            fill(V("ypd"), 0.0)
         cp(Z("rot", 0, 16), Z("roti"))
-        for j in range(NTS):
-            act(Z("trs", 32 * j, 32 * j + 32), Z("rot"), AF.Sign, bias=-1.5 - j, accum=Z("ypd", j, j + 1))
-        act(Z("szs"), Z("rot"), AF.Identity, scale=2.0, bias=-34.0)
-        for j in range(NTS, NTH):
-            ts(Z("cm", 32 * j, 32 * j + 32), Z("rot"), float(j + 2), ALU.is_ge)
-        for j in range(NTS, NTH):
+        for j in range(1, NTS + 1):
+            act(Z("trs", 32 * j, 32 * j + 32), Z("rot"), AF.Sign, bias=-0.5 - j, accum=Z("ypd", j, j + 1))
+        act(Z("szs"), Z("rot"), AF.Relu, scale=2.0, bias=-2.0)
+        for j in range(NTS + 1, SMAX):
+            ts(Z("cm", 32 * j, 32 * j + 32), Z("rot"), float(j + 1), ALU.is_ge)
+        for j in range(NTS + 1, SMAX):
             red(Z("ypd", j, j + 1), Z("cm", 32 * j, 32 * j + 32), ALU.add)
-        if not t:
-            ts(BETA, LCOL, float(NTS), ALU.is_lt, NM / 2.0, ALU.mult)
-            ts(CF(9), IP(6), 32.0, ALU.mult, float(BIGR), ALU.add)
         tr(Z("ytr"), Z("ypd"))
-        if not t:
-            ts(V("alp"), V("one32"), BETA, ALU.mult, -1.0 / NM, ALU.mult)
-            ts(V("rest"), V("ri"), CF(9), ALU.add)
-        red(COL(0), Z("ytr"), ALU.add)
-        if not t:
-            ts(V("alp"), V("alp"), 1.0, ALU.add)
-        ts(Z("a1"), Z("alp"), COL(0), ALU.mult, on(BETA, 0, 32), ALU.add)
-        if not t:
-            ts(V("mlt"), V("ri"), LCOL, ALU.is_gt)
+        scan(Z("in2", 1, 33), Z("s32"), Z("ytr"), ALU.add, ALU.add)
+        tot, before = Z("in2", 32, 33), Z("in2", 0, 32)
+        act(Z("a1"), Z("hs"), AF.Identity, scale=tot)
+        ts(COL(0), tot, z(KT), ALU.is_ge, -2048.0, ALU.mult)
+        ts(COL(1), tot, z(KT), ALU.is_lt, 2048.0, ALU.mult)
+        ts(Z("suf"), before, tot, ALU.subtract, z(NHS), ALU.mult)
         tr(Z("cs"), Z("a1"))
+        act(Z("x3", 0, 32), before, AF.Identity, scale=HS, bias=COL(0))
+        ts(Z("x3", 64, 96), before, HS, ALU.mult, COL(1), ALU.add)
+        ts(Z("x3", 32, 64), Z("suf"), COL(0), ALU.add)
         act(Z("trs", 512, 544), Z("cs"), AF.Sign, bias=0.5 - K, accum=Z("thr", 0, 1))
-        if not t:
-            cp(V("rest2"), V("rest"), V("twice"))
-        ts(Z("f2"), Z("cs"), float(K), ALU.is_ge, 2048.0, ALU.mult)
-        if not t:
-            fill(V("inv", 0, 96), 0.0)
+        tr(Z("c3"), Z("x3"))
         gt, eq, thr = Z("ge", 0, 32), Z("ge", 32, 64), Z("thr", 0, 1)
-        ts(gt, Z("szs"), thr, ALU.is_gt)
-        ts(eq, Z("szs"), thr, ALU.is_equal)
-        tt(Z("g1"), Z("cs"), Z("f2"), ALU.subtract)
-        scan(Z("inc", 0, 32), Z("one32"), gt, ALU.mult, ALU.add)
-        scan(Z("inc", 32, 64), Z("one32"), eq, ALU.mult, ALU.add)
-        red(COL(2), Z("g1"), ALU.max)
-        ts(Z("a2", 0, 32), Z("mlt"), Z("inc", 31, 32), ALU.mult)
-        ts(Z("a2", 32, 64), Z("mlt"), Z("inc", 63, 64), ALU.mult)
-        ts(Z("hh"), Z("ge"), -BIG - 1.0, ALU.mult, BIG, ALU.add)
-        tr(Z("a2t"), Z("a2"))
-        tt(Z("je"), Z("inc"), Z("hh"), ALU.add)
-        red(COL(3), Z("a2t", 0, 32), ALU.add)
-        red(COL(5), Z("a2t", 32, 64), ALU.add)
-        ts(Z("ug"), Z("je", 0, 32), COL(3), ALU.add)
-        ts(Z("ue"), Z("je", 32, 64), COL(5), ALU.add, COL(2), ALU.add)
-        for b in range(4):
-            tt(on(V("um"), 32 * b, 32), Z("ug"), Z("ue"), ALU.min)
-        tt(V("zz"), V("um"), V("rest2"), ALU.min, V("twice"))
-        tt(V("slot"), V("um"), V("rest"), ALU.min)
-        tr(V("zt"), V("zz"))
-        tr(V("sx"), V("slot"))
+        ts(gt, Z("szs"), -30.0, ALU.add, thr, ALU.is_gt)
+        ts(eq, Z("szs"), -30.0, ALU.add, thr, ALU.is_equal)
+        red(COL(2), Z("c3", 0, 32), ALU.max)
+        red(COL(3), Z("c3", 32, 64), ALU.max)
+        red(COL(4), Z("c3", 64, 96), ALU.min)
+        tt(Z("hh", 0, 32), gt, Z("nrest"), ALU.mult)
+        scan(Z("inc", 0, 32), Z("dr"), gt, ALU.add, ALU.add, COL(2))
+        act(Z("hh", 32, 64), eq, AF.Identity, scale=-BIG - 1.0, bias=COL(3))
+        scan(Z("inc", 32, 64), Z("db"), eq, ALU.add, ALU.add, COL(4))
         for e in (0, 1):
-            cp(V("sll", e, 16, 2), V("zt", 32 * e + 8 * rank, 32 * e + 8 * rank + 8))
+            tt(Z("je", 32 * e, 32 * e + 32), Z("inc", 32 * e, 32 * e + 32), Z("hh", 32 * e, 32 * e + 32), ALU.add)
+        for e in range(4):
+            tt(Z("zz", 16 * e, 16 * e + 16), Z("je", 16 * (e // 2), 16 * (e // 2) + 16), Z("je", 32 + 16 * (e // 2), 48 + 16 * (e // 2)), ALU.min)
+        tt(Z("zz", 64, 96), Z("je", 0, 32), Z("je", 32, 64), ALU.min)
+        tr(Z("zt", 0, 64), Z("zz", 0, 64))
+        tr(Z("zt", 64, 96), Z("zz", 64, 96))
+        for b in range(4):
+            cp(on(V("sll"), 32 * b, 32), Z("zt", 32 * (b // 2) + 8 * rank, 32 * (b // 2) + 8 * rank + 8))
         emit("v", lambda: g.vector.tensor_copy(ind(V("inv"), V("sll")), A(V("io2"))), [V("inv")], [V("io2"), V("sll")])
-        widen("sx", 0, 16, "xb")
+        for b in (1, 2, 3):
+            act(on(V("zt", 64, 96), 32 * b, 32), Z("zt", 64, 96))
+        widen(0, 16)
         scan(V("scf", 0, K), V("d0", 0, K), V("inv", 0, K), ALU.mult, ALU.add)
-        k5 = V("scf", 15, K, 16)
-        ts(V("j1", 0, 5), k5, SCL, ALU.mult, float(-NM), ALU.add)
+        jm = V("jm", 0, 5)
+        halves([on(jm, 0), on(jm, 64)], V("scf", 15, K, 16), V("jx", 0, 5), ALU.max)
+        ts(V("j1", 0, 5), jm, SCL, ALU.mult, float(-NM), ALU.add)
         qa, sa, qb, sb = "qa%d" % t, "sa%d" % t, "qb%d" % t, "sb%d" % t
-        widen("sx", 16, 32, "xb")
         pick(V(qa, 0, K), V(sa, 0, K), V(qc, 0, M), V(sp, 0, M), V("j1", 0, 5))
         swap(qa, sa, near, "ac%d" % t, "as%d" % t)
+        widen(16, 32)
         if not t:
             ts(V("s80"), V("s80"), SCOL, ALU.add)
             ts(V("ki"), V("ki"), SCOL, ALU.add)
@@ -624,58 +599,63 @@ def rank_program(g, core, T, topo):
                 n0 = lo + H * h
                 step = place(n0 + 1) - place(n0)
                 ts(V("sn", 8 * h, 8 * h + 8), V("sn", 8 * h, 8 * h + 8), float(step), ALU.mult, float(place(n0) - step * n0), ALU.add)
-        ts(V("j2f", 0, 5), k5, SCL, ALU.mult, NM - 0.5, ALU.is_lt)
-        mine = 64 * (lo // HM)
-        if mine:
-            scan(on(V("sc2"), mine), on(V("d0", 0, M), mine), on(back(V("fr", FR + NM - lo - M, FR + NM - lo)), mine), ALU.mult, ALU.add)
-            last = V("sc2", 15, M, 16)
-        else:
-            last = V("sc", lo + 15, lo + M, 16)
-        ts(V("j2f", 0, 5), V("j2f", 0, 5), float(K), ALU.mult)
+        ts(V("j2f", 0, 5), jm, SCL, ALU.mult, NM - 0.5, ALU.is_lt)
+        blk = RK.index(rank)
+        mine, last = 64 * (blk // 2), V("sc", M * (blk % 2) + 15, M * (blk % 2) + M, 16)
         for p in (0, 64):
-            ts(on(V("rho", 0, 16), p), on(last, mine), on(SSCL, mine), ALU.mult, MID, ALU.add)
-        turn_s("fs", 0, 16)
+            ts(on(V("rho", 0, 16), p), on(last, mine), on(GSCL, mine), ALU.mult, float(GM), ALU.add)
+        ts(V("j2f", 0, 5), V("j2f", 0, 5), float(K), ALU.mult)
+        for k in range(4):
+            tr(grun("fs", k), V("xb", H * k, H * k + H))
         cp(V("lro"), V("rho", 0, 16))
         tt(V("j2f", 0, 5), V("j2f", 0, 5), V("s80", 0, 5), ALU.add)
         tt(V("rho", 16, 32), V("rho", 0, 16), V("sn"), ALU.not_equal)
-        turn_s("fs", 16, 32)
+        far_in = [float(d in pair2) for d in range(N)]
+        terms = [(ALU.is_lt, M, far_in[0] * K)] + [(ALU.is_ge, M * d, (far_in[d] - (far_in[d - 1] if d > 1 else 0.0)) * K) for d in range(1, N)]
+        terms = [(op, float(place(n)), v) for op, n, v in terms if v]
+        parts = [V("rho", 32, 48), V("m1"), V("mm")]
+        for j, (op, n, v) in enumerate(terms):
+            ts(parts[j], V("rho", 0, 16), n, op, v, ALU.mult)
         cp(V("j2", 0, 5), V("j2f", 0, 5))
         act(V("rtf"), V("idn"), off=V("lro"))
         row = V("rtf", 0, M, 1, 0, 1)
         dmas("drt", [("y", T.rt[0:1, M * t:M * t + M], A(row), [], [row])])
+        for k in range(4, 8):
+            tr(grun("fs", k), V("xb", H * k, H * k + H))
+            if k - 3 < len(terms):
+                tt(parts[0], parts[0], parts[k - 3], ALU.add)
         cp(V("rs"), V("fs"), V("lro"))
-        far_in = [float(d in pair2) for d in range(N)]
-        terms = [(ALU.is_lt, M, far_in[0] * K)] + [(ALU.is_ge, M * d, (far_in[d] - (far_in[d - 1] if d > 1 else 0.0)) * K) for d in range(1, N)]
-        terms = [(op, float(place(n)), v) for op, n, v in terms if v]
-        parts = ("m1", "mm")
-        for j, (op, n, v) in enumerate(terms):
-            ts(V("rho", 32, 48) if not j else V(parts[j % 2], 0, 16), V("rho", 0, 16), n, op, v, ALU.mult)
-            if j:
-                tt(V("rho", 32, 48), V("rho", 32, 48), V(parts[j % 2], 0, 16), ALU.add)
         pick(V(qb, 0, K), V(sb, 0, K), V(qa), V(sa), V("j2", 0, 5))
         swap(qb, sb, far, "bc%d" % t, "bs%d" % t)
         scan(V("sc", 0, M), V("d0", 0, M), V("rs"), ALU.mult, ALU.add)
+        if t + 1 < R:
+            if not t:
+                pick(V("qr", 128, 384), V("sr", 128, 384), V("qu"), V("su"), V("cu", 8, 24))
+            height(7, t + 1, qc, sp, 0, M)
         so, me = V("rho", 0, 16), V("rho", 16, 32)
+        ts(V("rho", 48, 64), V("sc", 15, M, 16), SCL, ALU.mult, K - 0.5, ALU.is_lt)
         ts(so, V("sc", 15, M, 16), SCL, ALU.mult)
-        ts(V("rho", 48, 64), so, K - 0.5, ALU.is_lt)
+        if not t:
+            quant(V("qe"), V("se"), V("et"))
         tt(me, me, V("rho", 48, 64), ALU.mult)
+        if t + 1 < R:
+            tr(V("ho"), bank(7, M))
         tt(so, so, me, ALU.mult)
         ts(V("rho", 48, 64), me, float(M), ALU.mult)
+        m0, m1 = V("rho", 16, 32, 2), V("rho", 17, 32, 2)
+        if t + 1 < R:
+            tt(V("mx"), m1, m0, ALU.subtract)
         tt(V("rho", 32, 48), V("rho", 32, 48), so, ALU.add)
         tt(V("rho", 48, 64), V("rho", 48, 64), V("ki"), ALU.add)
+        if t + 1 < R:
+            ts(V("mx"), V("mx"), HI, ALU.mult)
         cp(V("pl"), V("rho", 32, 48))
         cp(V("kl"), V("rho", 48, 64))
+        if t + 1 < R:
+            tt(V("mx"), V("mx"), m0, ALU.add)
         if not t:
-            pick(V("qr", 128, 384), V("sr", 128, 384), V("qu"), V("su"), V("cu", 8, 24))
-            quant(V("qe"), V("se"), V("et"))
             quant(V("qw"), V("sw"), V("wt"))
         if t + 1 < R:
-            height(7, t + 1, qc, sp, 0, M)
-            m0, m1 = V("rho", 16, 32, 2), V("rho", 17, 32, 2)
-            tt(V("mx"), m1, m0, ALU.subtract)
-            tr(V("ho"), bank(7, M))
-            ts(V("mx"), V("mx"), HCOL, ALU.mult)
-            tt(V("mx"), V("mx"), m0, ALU.add)
             ts(V("mx1"), V("mx"), -1.0, ALU.mult, 1.0, ALU.add)
             tt(V("xo"), V("ho", 0, M, 32), V("mx1"), ALU.mult)
         unpack = [(V("qe", 128 * b, 128 * b + 128), V("se", 128 * b, 128 * b + 128)) for b in range(4)]
@@ -685,20 +665,31 @@ def rank_program(g, core, T, topo):
             for b in range(4):
                 mm(bank(4 * h + b, H), *unpack[b], V(qc, *half[h]), V(sp, *half[h]), True, False)
         for h in (0, 1):
-            pick(V(qp, *half[h]), V(pp, *half[h]), V(qb), V(sb), V("pl", 8 * h, 8 * h + 8))
+            codes(V(qp, *half[h]), V(qb), V("pl", 8 * h, 8 * h + 8))
+        for h in (0, 1):
+            move("sv"[h], V(pp, *half[h]), V(sb), V("pl", 8 * h, 8 * h + 8))
         for h in (0, 1):
             for b in range(4):
                 mm(bank(4 * h + b, H), *unpack[b], V(qp, *half[h]), V(pp, *half[h]), False, True)
-        for h in (0, 1):
-            for b in range(4):
-                src, out = bank(4 * h + b, H), V("hb", 4 * H * h + b, 4 * H * h + 4 * H, 4)
-                if b % 2:
-                    act(out, src, scale=0.5)
-                else:
-                    ts(out, src, 0.5, ALU.mult)
+
+        def cast(h, b):
+            src, out = bank(4 * h + b, H), V("hb", 4 * H * h + b, 4 * H * h + 4 * H, 4)
+            if b % 2:
+                act(out, src, scale=0.5)
+            else:
+                ts(out, src, 0.5, ALU.mult)
+
+        def anew(h):
             quant(V(qc, M + H * h, M + H * h + H), V(sp, M + H * h, M + H * h + H), V("hb", 4 * H * h, 4 * H * h + 4 * H))
             if t + 1 < R:
                 height(h, t + 1, qc, sp, M + H * h, H)
+
+        for b in range(6):
+            cast(b // 4, b % 4)
+        anew(0)
+        cast(1, 2)
+        cast(1, 3)
+        anew(1)
         nq, ns = "qc%d" % (t + 1), "scp%d" % (t + 1)
         if t + 1 < R:
             for h in (0, 1):

@@ -10,6 +10,7 @@ HM = NM // 2
 H = M // 2
 SMAX = NM // K + 1
 NTS = 7
+NS, NV = 6, 10
 BIG = 4.0 * NM
 BIGR = NM + K
 WINV = BIGR + NM + K + 16
@@ -21,31 +22,30 @@ RK = (1, 2, 0, 3)
 GM, WM = 2048, 8192
 UP = float(2 ** 30)
 C8, U8, F32, B16, I32, U16 = "float8_e4m3fn_x4", "uint8", "float32", "bfloat16", "int32", "uint16"
-XP = True
 
 WIDTHS = {
-    B16: {"xt": 4 * M, "ut": 512, "wt": 512, "one": 512, "et": 2048, "d0": 512, "dw": NM, "wb": NM + 16,
-          "w0": 2 * GM, "w1": 2 * GM, "w2": 2 * GM, "w3": 2 * GM, "xb": NM, "xz": HM, "d32": M, "cw": NM, "ca": 384, "cb": HM,
-          "fs": 2 * GM, "fa": 2 * WM, "fb": 2 * WM, "sc": HM, "rs": M, "hb": 4 * M,
-          "fr": HM, "ee": 8 * HM, "so": 8 * M, "cv": 16, "c2": 64},
+    B16: {"xt": 4 * M, "ut": 512, "wt": 512, "one": 528, "et": 2 * 528, "d0": 512, "dw": NM, "wb": NM + 16,
+          "w0": 2 * GM, "w1": 2 * GM, "w2": 2 * GM, "xb": NM, "xz": NM, "d32": M, "cw": NM, "ca": 384, "cb": HM,
+          "fs": 2 * GM, "fa": 2 * WM, "fb": 2 * WM, "sc": HM, "rs": M, "rx": M, "hb": 4 * M,
+          "fr": HM, "ee": 4 * HM, "so": NV * M, "cv": 16, "c2": 64},
     C8: {"qu": 128, "qw": 128, "qr": 384, "qe": 512},
     U8: {"su": 128, "sw": 128, "sr": 384, "se": 512},
     F32: {"io2": H, "i128": H, "idn": 2 * GM, "rtf": M, "xe": NM, "fh": NM, "scf": 128, "ra": 384, "rb": HM, "trs": 2 * NM,
-          "ht": M, "ho": M, "inv": WINV, "cm": 32 * SMAX, "rot": 32, "acc": 16, "ypd": 32, "szs": 32, "ys": M},
+          "ht": M, "ho": M, "inv": WINV, "cm": 32 * SMAX, "rot": 64, "acc": 16, "szs": 32, "ys": M, "bg": 96},
     U16: {"la": 32, "lb": 32, "l0": 32, "nbl": 64, "lnb": 24},
-    I32: {"iw": 64, "iu": 24, "id16": 16, "nbe": 24},
+    I32: {"iu": 24, "id16": 16, "nbe": 24},
 }
 SCRATCH = {"bl": ("psum", [128, 4096], F32)}
 for _d, _parts in WIDTHS.items():
     for _n, _w in _parts.items():
         SCRATCH[_n] = ("sbuf", [128, _w], _d)
 SMALL = {
-    "zf": (F32, {"d16": 16, "d17": 16, "cf": 32, "ri": 32, "nrest": 32, "dr": 32, "db": 32, "hs": 32, "s32": 32, "one32": 32,
-                 "sn": 16, "ki": 16, "s80": 8, "x0": 16, "m1": 16, "mm": 16, "neq": 32, "key": 32, "b2": 16, "zz": 96, "zt": 96,
-                 "thr": 8, "up": 8, "ytr": 32, "col": 8, "in2": 48, "a1": 32, "cs": 32, "suf": 32, "x3": 96, "c3": 96, "ge": 64,
-                 "inc": 64, "hh": 64, "je": 64, "jm": 8, "jx": 8, "rho": 64, "j2f": 8, "mx": 8, "mx1": 8, "xo": 8, "xm": 8}),
+    "zf": (F32, {"d16": 16, "d17": 16, "cf": 32, "nrest": 32, "dr": 32, "dt": 64, "db": 32, "ypd": 32, "ytr": 64, "in2": 80, "one32": 32,
+                 "sn": 16, "ki": 16, "x0": 32, "m1": 16, "neq": 32, "lost": 32, "key": 32, "b2": 16, "zz": 96, "zt": 96, "thr": 8,
+                 "sfx": 48, "col": 8, "cs": 32, "x3": 96, "c3": 96, "ge": 64, "inc": 64, "hh": 64, "je": 64, "um": 80,
+                 "jm": 8, "rho": 32, "mx": 8, "mx1": 8, "xo": 8}),
     "zi": (I32, {"ip": 16, "aci": 16, "roti": 16}),
-    "zu": (U16, {"cexp": 64, "crep": 64, "cu": 24, "rep8": 2, "lro": 16, "sll": 8, "j1": 6, "j2": 6, "pl": 16, "kl": 16}),
+    "zu": (U16, {"crep": 32, "cu": 24, "lro": 16, "lrm": 16, "sll": 8, "j1": 6, "j2": 6, "pl": 16, "kl": 16}),
 }
 AT = {}
 for _b, (_d, _parts) in SMALL.items():
@@ -56,18 +56,16 @@ for _b, (_d, _parts) in SMALL.items():
     SCRATCH[_b] = ("sbuf", [128, _o], _d)
 for _t in range(R):
     SCRATCH["xh%d" % _t] = ("sbuf", [128, 32], F32)
-    for _n in ("a", "b"):
-        SCRATCH["q%s%d" % (_n, _t)] = ("sbuf", [128, 2 * K], C8)
-        SCRATCH["s%s%d" % (_n, _t)] = ("sbuf", [128, 2 * K], U8)
-    SCRATCH["qp%d" % _t] = ("sbuf", [128, M], C8)
-    SCRATCH["sp%d" % _t] = ("sbuf", [128, M], U8)
+    for _n, _w in (("a", K), ("z", M + K), ("b", 2 * K), ("p", M)):
+        SCRATCH["q%s%d" % (_n, _t)] = ("sbuf", [128, _w], C8)
+        SCRATCH["s%s%d" % (_n, _t)] = ("sbuf", [128, _w], U8)
 for _t in range(R + 1):
     SCRATCH["qc%d" % _t] = ("sbuf", [128, 2 * M if _t < R else M], C8)
     SCRATCH["scp%d" % _t] = ("sbuf", [128, 2 * M if _t < R else M], U8)
 
 SEMAPHORES = (["ev", "es", "et", "eg", "loc"] + ["nb%d" % d for d in range(N)] + ["h%d_%d" % (t, d) for t in range(R) for d in range(N)]
               + ["%s%d" % (k, t) for t in range(R) for k in ("ac", "as", "bc", "bs")]
-              + ["dx", "du", "dw", "dnb", "drt", "dout"])
+              + ["dx0", "dx1", "du", "dw", "dz", "dnb", "drt", "dout"])
 
 
 def place(n):
@@ -92,7 +90,12 @@ def rank_program(g, core, T, topo):
     def Z(name, a=0, b=None, step=1):
         return V(name, a, b, step, 0, 32)
 
+    def back(r):
+        return r[:6] + (True,)
+
     def A(r):
+        if len(r) > 6:
+            return T[r[0]][r[4]:r[5], r[2] - 1:r[1] - 1:-1]
         return T[r[0]][r[4]:r[5], r[1]:r[2]] if r[3] == 1 else T[r[0]][r[4]:r[5], r[1]:r[2]:r[3]]
 
     def meets(a, b):
@@ -169,18 +172,17 @@ def rank_program(g, core, T, topo):
     def cp(out, in_, off=None):
         emit("v", lambda: g.vector.tensor_copy(A(out), A(in_) if off is None else ind(in_, off)), [out], [in_] + ([off] if off else []))
 
-    def ts(out, in0, s1, op0, s2=None, op1=None, off=None):
+    def ts(out, in0, s1, op0, s2=None, op1=None):
         cols = [s for s in (s1, s2) if isinstance(s, tuple)]
         val = lambda s: A(s) if isinstance(s, tuple) else s
-        src = lambda: A(in0) if off is None else ind(in0, off)
         if op1 is None:
-            fn = lambda: g.vector.tensor_scalar(A(out), src(), val(s1), None, op0)
+            fn = lambda: g.vector.tensor_scalar(A(out), A(in0), val(s1), None, op0)
         else:
-            fn = lambda: g.vector.tensor_scalar(A(out), src(), val(s1), val(s2), op0, op1)
-        emit("v", fn, [out], [in0] + cols + ([off] if off else []))
+            fn = lambda: g.vector.tensor_scalar(A(out), A(in0), val(s1), val(s2), op0, op1)
+        emit("v", fn, [out], [in0] + cols)
 
-    def tt(out, a, b, op, off=None):
-        emit("v", lambda: g.vector.tensor_tensor(A(out), A(a) if off is None else ind(a, off), A(b), op), [out], [a, b] + ([off] if off else []))
+    def tt(out, a, b, op):
+        emit("v", lambda: g.vector.tensor_tensor(A(out), A(a), A(b), op), [out], [a, b])
 
     def red(out, in_, op):
         emit("v", lambda: g.vector.tensor_reduce(A(out), A(in_), AxisListType.X, op), [out], [in_])
@@ -218,6 +220,9 @@ def rank_program(g, core, T, topo):
             fn = lambda: g.iota(A(out), pattern, base, cm, allow_small_or_imprecise_dtypes=True)
         emit("g", fn, [out], [])
 
+    def const(out, c):
+        iota(out, [[0, out[2] - out[1]]], int(c), 0)
+
     def select(out, in_, pattern, cmp, fillv, base, cm):
         emit("g", lambda: g.affine_select(A(out), A(in_), pattern, cmp, fillv, base, cm), [out], [in_])
 
@@ -234,14 +239,8 @@ def rank_program(g, core, T, topo):
         codes(qo, qi, off)
         act(so, si, off=off)
 
-    def halves(outs, r, spare, op, p=0, n=64):
-        if XP:
-            for o in outs:
-                tt(o, on(r, p, n), on(r, 64 + p, n), op)
-        else:
-            cp(on(spare, p, n), on(r, 64 + p, n))
-            for o in outs:
-                tt(o, on(r, p, n), on(spare, p, n), op)
+    def halves(out, r, op, p=0, n=64):
+        tt(out, on(r, p, n), on(r, 64 + p, n), op)
 
     others = [(rank + k) % N for k in range(1, N)]
     senders = others[::-1]
@@ -265,27 +264,29 @@ def rank_program(g, core, T, topo):
     pair2 = [d for d in range(N) if d not in pair]
     far = pair2[pair.index(rank)]
 
-    def swap(q, s, d, semc, sems):
+    def swap(q, s, q2, s2, at, d, semc, sems):
         dst = T.cores[d]
         rid, pid = topo.addr(dst)[:2]
         mask, n = topo.mask(core, dst), len(topo.engines(core, dst))
         use("g", [V(q, 0, K)], [])
-        g.remote_dma(A(V(q, K, 2 * K)).bitcast(dt.uint8), A(V(q, 0, K)).bitcast(dt.uint8), T.sem[semc], T.sem.loc, pid, rid, mask)
+        g.remote_dma(A(V(q2, at, at + K)).bitcast(dt.uint8), A(V(q, 0, K)).bitcast(dt.uint8), T.sem[semc], T.sem.loc, pid, rid, mask)
         use("g", [V(s, 0, K)], [])
-        g.remote_dma(A(V(s, K, 2 * K)), A(V(s, 0, K)), T.sem[sems], T.sem.loc, pid, rid, mask)
+        g.remote_dma(A(V(s2, at, at + K)), A(V(s, 0, K)), T.sem[sems], T.sem.loc, pid, rid, mask)
         cnt["loc"] = cnt.get("loc", 0) + 2 * n
-        arrives(semc, n, [V(q, K, 2 * K)])
-        arrives(sems, n, [V(s, K, 2 * K)])
+        arrives(semc, n, [V(q2, at, at + K)])
+        arrives(sems, n, [V(s2, at, at + K)])
 
-    def widen(c0, c1):
-        act(V("xb", 32 * c0, 32 * c1), V("zt", 64 + c0, 64 + c1), off=V("cexp", 0, 2 * (c1 - c0)))
-
-    def turned(t, d, by):
+    def turned(t, d, by, between=None):
         for e in (0, 1):
             move(by[e], V("xe", M * d + 16 * e, M * d + M, 32), V("xh%d" % t, 8 * d, 8 * d + 8))
         b = 32 * RK.index(d)
         act(on(V("rb", 3 * H, 4 * H, 16), b, 32), on(V("xh%d" % t, 8 * d, 8 * d + 8), b, 32))
+        if between:
+            between()
         tr(V("fh", M * d, M * d + M), V("xe", M * d, M * d + M))
+
+    def repeated(e):
+        scan(V("xb", M * e, M * e + M), V("d32"), V("xz", M * e, M * e + M), ALU.mult, ALU.add)
 
     def grun(f, k):
         a, s = RUNS[k]
@@ -297,7 +298,7 @@ def rank_program(g, core, T, topo):
 
     piece = lambda f, i: wrun(f, 0, OWN[0][i])
     CF = lambda k: V("cf", k, k + 1)
-    SCL, HI, UPPER, SCOL, LCOL, GSCL, WSCL, NHS, KT = [CF(k) for k in (0, 4, 5, 6, 7, 16, 17, 19, 20)]
+    SCL, UPPER, SCOL, LCOL, GSCL, WSCL = [CF(k) for k in (0, 5, 6, 7, 16, 17)]
 
     def lift(f, i):
         scan(V("sc", H * i, H * i + H), V("d0", 0, H), piece(f, i), ALU.mult, ALU.add)
@@ -309,51 +310,44 @@ def rank_program(g, core, T, topo):
         move(by, on(wrun(f, 1 - h, OWN[h][i]), 64 - 64 * h), on(piece(f, i), 64 * h))
 
     bank = lambda k, w: V("bl", 512 * k, 512 * k + w)
+    half = [(H * h, H * h + H) for h in (0, 1)]
 
     loads = []
     for k in range(4):
         shift = 2 * (k % 2)
         o = V("nbe", 0, 24 - shift, 1, 16 * k, 16 * k + 16)
         loads.append(("s", A(o), T.nb[:, 24 * (k // 2) + shift:24 * (k // 2) + 24], [o], []))
-    dmas("dx", [("y", A(V("xt")), T.x[:], [V("xt")], [])])
-    dmas("dnb", loads)
     dmas("du", [("y", A(V("ut")), T.u[:], [V("ut")], [])])
+    dmas("dnb", loads)
+    for h in (0, 1):
+        o = V("xt", 4 * H * h, 4 * H * h + 4 * H)
+        dmas("dx%d" % h, [("y", A(o), T.x[:, 4 * H * h:4 * H * h + 4 * H], [o], [])])
     IP = lambda k: V("ip", k, k + 1)
+    RI = lambda n: V("i128", 0, n)
     iota(V("iu"), [[1, 3], [0, 8]], 0, 0)
     iota(IP(0), [[0, 1]], 0, 1)
-    iota(V("iw"), [[1, 32], [0, 2]], 0, 0)
     iota(V("id16"), [[1, 16]], 128, -1)
-    iota(V("ri"), [[1, 32]], 0, 0)
     iota(V("i128"), [[1, H]], 0, 0)
     o = 16 * rank
-    fill(V("dw"), 0.0)
     fill(on(V("nbl", o, o + 12), 64), 0)
+    fill(V("dw"), 0.0)
     act(V("xe"), V("dw"))
     cp(V("cu"), V("iu"))
-    ts(IP(4), IP(0), 4, ALU.logical_shift_right, 1, ALU.bitwise_and)
-    ts(IP(5), IP(0), 6, ALU.logical_shift_right)
-    ts(IP(1), IP(0), 15, ALU.bitwise_and)
-    ts(IP(2), IP(0), 31, ALU.bitwise_and)
-    ts(IP(6), IP(0), 7, ALU.bitwise_and)
+    fill(V("d32"), 1.0)
+    ts(IP(1), IP(0), 6, ALU.logical_shift_right)
+    ts(IP(2), IP(0), 15, ALU.bitwise_and)
+    ts(IP(3), IP(0), 31, ALU.bitwise_and)
     ts(IP(7), IP(0), 5, ALU.logical_shift_right, 1, ALU.bitwise_and)
-    cp(V("cexp"), V("iw"))
-    cp(V("cf", 4, 6), V("ip", 4, 6))
-    cp(V("cf", 6, 8), V("ip", 1, 3))
-    ts(V("id16"), V("id16"), 15, ALU.bitwise_and)
-    ts(V("iw"), V("iw"), 0.0, ALU.mult)
-    ts(SCL, SCOL, 15.0, ALU.is_equal, 1.0 - 1.0 / UP, ALU.mult)
-    ts(V("d16"), V("id16"), 1.0, ALU.is_equal, UP, ALU.mult)
-    ts(V("d17"), V("id16"), 0.0, ALU.is_gt)
-    ts(V("crep"), V("iw"), SCOL, ALU.add)
-    ts(SCL, SCL, 1.0 / UP, ALU.max)
-    tt(V("d16"), V("d16"), V("d17"), ALU.add)
-    fill(V("one"), 1.0)
+    fill(V("xz", 0, HM), 0.0)
+    cp(V("cf", 5, 8), V("ip", 1, 4))
     for e in (0, 1):
         cp(on(V("nbl", o + e, o + 12, 2), 0), on(V("nbe", e, 24, 4), 0))
     spread(lambda d: V("nbl", 16 * d, 16 * d + 12), "nb%d")
     quant(V("qu"), V("su"), V("ut"))
+    ts(CF(12), IP(7), -float(NS), ALU.mult, LCOL, ALU.add)
+    fill(V("d32", 0, M, 32), 0.0)
+    ts(V("id16"), V("id16"), 15, ALU.bitwise_and)
     pick(V("qr", 0, 128), V("sr", 0, 128), V("qu"), V("su"), V("cu", 0, 8))
-    act(V("d0"), V("d16"), off=V("crep", 0, 32))
 
     def height(k, t, q, s, a, n):
         mm(bank(k, n), V("qr", 128 * t, 128 * t + 128), V("sr", 128 * t, 128 * t + 128), V(q, a, a + n), V(s, a, a + n), True, True)
@@ -362,117 +356,153 @@ def rank_program(g, core, T, topo):
         spread(lambda d: V("xh%d" % t, 8 * d, 8 * d + 8), "h%d_" % t + "%d")
 
     for h in (0, 1):
-        quant(V("qc0", H * h, H * h + H), V("scp0", H * h, H * h + H), V("xt", 4 * H * h, 4 * H * h + 4 * H))
+        quant(V("qc0", *half[h]), V("scp0", *half[h]), V("xt", 4 * H * h, 4 * H * h + 4 * H))
     for h in (0, 1):
         height(h, 0, "qc0", "scp0", H * h, H)
+    ts(SCL, SCOL, 15.0, ALU.is_equal, 1.0 - 1.0 / UP, ALU.mult)
+    ts(V("d16"), V("id16"), 1.0, ALU.is_equal, UP, ALU.mult)
+    ts(V("d17"), V("id16"), 0.0, ALU.is_gt)
+    ts(V("crep"), RI(32), 0.0, ALU.mult, SCOL, ALU.add)
     for h in (0, 1):
-        tr(V("ht", H * h, H * h + H), bank(h, H))
+        tr(V("ht", *half[h]), bank(h, H))
+    ts(SCL, SCL, 1.0 / UP, ALU.max)
+    tt(V("d16"), V("d16"), V("d17"), ALU.add)
+    fill(V("one32"), 1.0)
     cp(V("xh0", 8 * rank, 8 * rank + 8), V("ht", 0, M, 32))
     share(0)
     dmas("dw", [("y", A(V("wt")), T.w[:], [V("wt")], [])])
 
-    fill(V("one32"), 1.0)
     iota(V("sn"), [[16, 16]], M * rank, 0)
     iota(V("ki"), [[16, 16]], 0, 0)
-    iota(V("s80"), [[16, 8]], 0, 0)
+    for d in range(N):
+        const(Z("um", 64 + d, 65 + d), K * ((d in pair2) - (d - 1 in pair2)))
+    select(Z("um", 64, 64 + N), Z("um", 64, 64 + N), [[-8, N]], ALU.is_ge, 0.0, 0, 1)
+    iota(V("bg"), [[1, 96]], M, 0)
+    const(V("fs", 2 * GM - 16, 2 * GM), NM)
     for h in (0, 1):
-        iota(on(V("io2"), 64 * h), [[32, 8], [1, 16]], NM + 16 * h, 0)
+        iota(on(V("io2"), 64 * h), [[32, 8], [1, 16]], 16 * h, 0)
     iota(Z("nrest"), [[-1, 32]], -BIGR - 1, -32)
+    for name, a, b, c in (("dr", 0, 96, 1), ("db", 0, 144, 0), ("db", 0, 1, BIG), ("ypd", 0, 1, 64), ("rot", 32, 64, NM),
+                          ("dt", 32, 33, -BIG), ("ytr", 32, 33, BIG * (2 * K - 1))):
+        const(Z(name, a, b), c)
     iota(Z("dr", 0, 1), [[0, 1]], BIGR, 32)
-    iota(Z("dr", 1, 32), [[0, 31]], 1, 0)
-    iota(Z("db", 0, 1), [[0, 1]], int(BIG), 0)
-    iota(Z("db", 1, 32), [[0, 31]], 0, 0)
-    iota(Z("in2", 0, 1), [[0, 1]], 0, 0)
-    iota(Z("ypd", 0, 1), [[0, 1]], 32, 0)
-    iota(Z("ypd", SMAX, 32), [[0, 32 - SMAX]], 0, 0)
-    select(Z("s32"), Z("one32"), [[0, 32]], ALU.is_gt, 0.0, 0, 1)
-    select(Z("s32"), Z("s32"), [[0, 32]], ALU.is_ge, 0.0, NTS, -1)
-    ts(CF(12), IP(7), -8.0, ALU.mult, LCOL, ALU.add)
-    ts(CF(22), IP(7), 8.0, ALU.mult)
-    fill(V("wb", NM, NM + 16), 0.0)
-    ts(CF(13), CF(12), 6.0, ALU.is_equal)
-    ts(CF(14), CF(12), 7.0, ALU.is_equal, 2048.0, ALU.mult)
-    ts(CF(23), UPPER, float(ALPHA[1] - ALPHA[0]), ALU.mult, float(ALPHA[0]), ALU.add)
-    ts(GSCL, SCL, 1.0 / UNIT, ALU.mult)
-    tt(CF(15), CF(13), CF(14), ALU.add)
-    ts(V("x0", 0, 4), V("ri", 0, 4), 32.0, ALU.mult, LCOL, ALU.add)
-    tt(WSCL, GSCL, CF(23), ALU.mult)
-    ts(V("dw", 0, NM, 33), V("one32"), CF(15), ALU.mult)
-    for e in (0, 1):
-        cp(V("rep8", e, e + 1), IP(6))
-    tr(V("wb", 0, NM), V("dw"))
-    for i in range(1, 4):
-        for k in range(8):
-            select(grun("w%d" % i, k), V("wb", H * k + 6 - 2 * i, H * k + H + 6 - 2 * i), [[0, H]], ALU.is_gt, 0.0, 1, 0)
-    for k in range(8):
-        iota(grun("idn", k), [[1, H]], H * k, 0)
-    for b in range(4):
-        select(V("et", 512 * b, 512 * b + 512), V("one"), [[1, 512]], ALU.is_equal, 0.0, -b, -4)
     for k, (a, s) in enumerate(RUNS):
         act(V("cw", H * k, H * k + H), V("i128"), AF.Identity, scale=s * UNIT, bias=a * UNIT)
-    turned(0, rank, "vs")
-    for k in range(8):
-        act(grun("w0", k), V("wb", H * k + 6, H * k + H + 6))
-    fill(V("xz"), 0.0)
-    fill(V("d32"), 1.0)
+    ts(V("x0", 0, 4), RI(4), 32.0, ALU.mult, LCOL, ALU.add)
+    turned(0, rank, "vs", lambda: (ts(CF(13), CF(12), NS - 2.0, ALU.is_equal), ts(CF(14), CF(12), NS - 1.0, ALU.is_equal, 2048.0, ALU.mult)))
+    act(V("d0"), V("d16"), off=V("crep"))
+    tt(CF(15), CF(13), CF(14), ALU.add)
     for b in range(4):
         for e in (0, 1):
             a, s = RUNS[2 * RK[b] + e]
             ts(on(V("cb", 3 * H + 64 * e, 3 * H + 64 * e + 64, 16), 32 * b, 32), on(V("x0", 0, 4), 32 * b, 32), s * UNIT, ALU.mult, a * UNIT, ALU.add)
-    fill(V("d32", 0, M, 32), 0.0)
+    ts(V("dw", 0, NM, 33), V("one32"), CF(15), ALU.mult)
+    fill(V("wb", NM, NM + 16), 0.0)
     for d in [rank] + senders:
         for b in (0, 1):
             cp(on(V("lnb", 12 * b, 12 * b + 12), 32 * RK.index(d), 32), on(V("nbl", 16 * d, 16 * d + 12), 32 * b, 32))
+        if d == rank:
+            tr(V("wb", 0, NM), V("dw"))
+            fill(V("xz", HM, NM), 0.0)
 
-    lo = M * rank
+    def tables():
+        act(V("one"), V("dw", 0, 528), AF.Identity, scale=0.0, bias=1.0)
+        for i in range(NS // 2):
+            for k in range(8):
+                src = V("wb", H * k + NS - 2 - 2 * i, H * k + H + NS - 2 - 2 * i)
+                if i:
+                    select(grun("w%d" % i, k), src, [[0, H]], ALU.is_gt, 0.0, 1, 0)
+                else:
+                    act(grun("w0", k), src)
+        for k in range(8):
+            iota(grun("idn", k), [[1, H]], H * k, 0)
+        for e in (0, 1):
+            select(V("et", 528 * e, 528 * e + 528), V("one"), [[1, 528]], ALU.is_equal, 0.0, -2 - e, -4)
+
+    def unpacking(b):
+        a = 528 * (b % 2) + 2 - b // 2 * 2
+        quant(V("qe", 128 * b, 128 * b + 128), V("se", 128 * b, 128 * b + 128), V("et", a, a + 512))
+
+    def parked(t):
+        q, s = V("qz%d" % t, 0, M), V("sz%d" % t, 0, M)
+        qi, si = V("qc%d" % t, 0, M), V("scp%d" % t, 0, M)
+        dmas("dz", [("y", A(q).bitcast(dt.uint8), A(qi).bitcast(dt.uint8), [q], [qi]), ("y", A(s), A(si), [s], [si])])
+
+    def own_place(h):
+        n0 = M * rank + H * h
+        step = place(n0 + 1) - place(n0)
+        ts(V("sn", 8 * h, 8 * h + 8), V("sn", 8 * h, 8 * h + 8), float(step), ALU.mult, float(place(n0) - step * n0), ALU.add)
+
+    later = [
+        lambda: ts(CF(23), UPPER, float(ALPHA[1] - ALPHA[0]), ALU.mult, float(ALPHA[0]), ALU.add),
+        lambda: ts(GSCL, SCL, 1.0 / UNIT, ALU.mult),
+        lambda: ts(CF(22), IP(7), float(NV), ALU.mult, 2.0 * NS - 16, ALU.add),
+        lambda: tr(V("c2", 0, 32), V("cw", 16, NM, 32)),
+        lambda: tr(V("c2", 32, 64), V("cw", 17, NM, 32)),
+        lambda: tt(WSCL, GSCL, CF(23), ALU.mult),
+        lambda: ts(V("x0", 16, 32), RI(16), CF(22), ALU.add),
+        lambda: tt(CF(24), V("c2", 32, 33), V("c2", 0, 1), ALU.subtract),
+        lambda: cp(CF(25), V("c2", 0, 1)),
+        lambda: ts(V("sn"), V("sn"), SCOL, ALU.add),
+        lambda: ts(V("cv"), V("x0", 16, 32), CF(24), ALU.mult, CF(25), ALU.add),
+        lambda: ts(V("ki"), V("ki"), SCOL, ALU.add),
+        lambda: red(Z("um", 72, 73), Z("um", 64, 64 + N), ALU.add),
+        lambda: own_place(0),
+        lambda: own_place(1),
+    ]
+
+    def meanwhile(n=2):
+        for f in later[:n]:
+            f()
+        del later[:n]
+
     COL = lambda k: Z("col", k, k + 1)
     ACC = lambda k: V("acc", k, k + 1)
-    z = lambda r: on(r, 0, 32)
-    HS = Z("hs", 0, 1)
     for t in range(R):
         qc, sp = "qc%d" % t, "scp%d" % t
+        final = t + 1 == R
         if t:
             turned(t, rank, "vs")
-            fill(V("inv", 0, 96), 0.0)
-        turned(t, senders[0], "vs")
+            if final:
+                quant(V("qw"), V("sw"), V("wt"))
+            else:
+                height(7, t + 1, qc, sp, 0, M)
+                tr(V("ho"), bank(7, M))
+        parked(t)
+        turned(t, senders[0], "vs", meanwhile)
         turned(t, senders[1], "ss")
         if not t:
             act(V("ca"), V("cw"), off=V("lnb"))
-        turned(t, senders[2], "vs" if t else "vv")
+        turned(t, senders[2], "vs" if t else "vv", meanwhile)
+        meanwhile()
         act(V("ra", H, 2 * H + 32), V("fh"), off=V("lnb", 8, 18))
         cp(V("ra", 0, H), V("fh"), V("lnb", 0, 8))
         act(V("ra", 2 * H + 32, 3 * H), V("fh"), off=V("lnb", 18, 24))
+        if not t:
+            tr(V("cb", 0, 3 * H), V("ca"))
+            tables()
         tr(V("rb", 0, H), V("ra", 0, H))
         tr(V("rb", H, 2 * H + 32), V("ra", H, 2 * H + 32))
         tr(V("rb", 2 * H + 32, 3 * H), V("ra", 2 * H + 32, 3 * H))
-        if not t:
-            tr(V("cb", 0, H), V("ca", 0, H))
-        tt(V("m1"), V("rb", 0, M, 16), V("rb", M, HM, 16), ALU.max)
-        if not t:
-            tr(V("cb", H, 2 * H), V("ca", H, 2 * H))
-        tt(V("mm", 0, 8), V("m1", 0, 8), V("m1", 8, 16), ALU.max)
-        if not t:
-            tr(V("cb", 2 * H, 3 * H), V("ca", 2 * H, 3 * H))
-        tt(V("neq"), V("mm", 0, 8), V("rb", 0, HM, 16), ALU.not_equal, V("rep8"))
-        if not t:
-            ts(Z("hs"), Z("s32"), -0.5, ALU.mult, 1.0, ALU.add)
-            ts(z(NHS), Z("s32", 0, 1), 0.5, ALU.mult, -1.0, ALU.add)
-        tt(V("key"), V("neq"), V("cb", 0, HM, 16), ALU.add)
-        if not t:
-            ts(z(KT), Z("s32", 0, 1), float(K), ALU.mult, float(K), ALU.add)
-            ts(Z("s32"), Z("s32"), 32.0, ALU.mult)
+        four = lambda a, b: V("rb", H * a, H * b, 16)
+        for e in (0, 1):
+            tt(V("m1", 8 * e, 8 * e + 8), four(1 - e, 2 - e), four(3 - e, 4 - e), ALU.max)
+        for e in (0, 1):
+            tt(V("neq", 16 * e, 16 * e + 16), four(2 - 2 * e, 4 - 2 * e), four(2 * e, 2 * e + 2), ALU.is_gt)
+        for e in (0, 1):
+            tt(V("lost", 16 * e, 16 * e + 16), V("m1"), four(2 * e, 2 * e + 2), ALU.is_gt)
+        tt(V("neq"), V("neq"), V("cb", 0, HM, 16), ALU.add)
+        meanwhile()
+        tt(V("key"), V("neq"), V("lost"), ALU.add)
+        meanwhile()
         tt(V("b2"), V("key", 0, 16), V("key", 16, 32), ALU.min)
-        if not t:
-            fill(V("inv", 0, 96), 0.0)
-        spot = lambda e: V("xz", M * e, M * e + M, 32)
+        meanwhile()
         for e in (0, 1):
-            tt(spot(e), V("b2", 0, 8), V("b2", 8, 16), ALU.min)
+            for b in range(4):
+                src = 64 * (b // 2) + 32 * e
+                tt(on(V("xz", M * e, M * e + M, 32), 32 * b, 32), on(V("b2", 0, 8), src, 32), on(V("b2", 8, 16), src, 32), ALU.min)
         for e in (0, 1):
-            for h in (0, 1):
-                src = 64 * h + 32 * e
-                tt(on(spot(e), 64 * h + 32 - 32 * e, 32), on(V("b2", 0, 8), src, 32), on(V("b2", 8, 16), src, 32), ALU.min)
-        for e in (0, 1):
-            scan(V("xb", M * e, M * e + M), V("d32"), V("xz", M * e, M * e + M), ALU.mult, ALU.add)
+            repeated(e)
         for i in range(4):
             tr(piece("fa", i), V("xb", H * i, H * i + H))
         for i in (0, 1):
@@ -505,60 +535,63 @@ def rank_program(g, core, T, topo):
             listed(lw, 0, 2)
             cross(fo, 3, 0, "v")
             listed(lw, 2, 4)
-        act(V("fr", 0, M), V("fb"), off=V("lb", 0, 16))
-        cp(V("fr", 3 * H, HM), V("fb"), V("lb", 24, 32))
-        act(V("fr", M, 3 * H), V("fb"), off=V("lb", 16, 24))
-        if not t:
-            for e in (0, 1):
-                tr(V("c2", 32 * e, 32 * e + 32), V("cw", 16 + e, NM, 32))
-            ts(V("x0", 8, 16), V("ri", 0, 8), CF(22), ALU.add)
-            tt(CF(24), V("c2", 32, 33), V("c2", 0, 1), ALU.subtract)
-            cp(CF(25), V("c2", 0, 1))
-        same = lambda j: ts(V("ee", HM * j, HM * j + HM), V("fr"), V("cv", j, j + 1), ALU.is_equal)
-        summed = lambda j: scan(V("so", M * j, M * j + M), V("ee", HM * j, HM * j + M), V("ee", HM * j + M, HM * j + HM), ALU.add, ALU.add)
+        for by, a, b in (("v", 0, H), ("s", H, M), ("s", M, HM)):
+            move(by, V("fr", a, b), V("fb"), V("lb", a // 16, b // 16))
+        meanwhile(3)
+        EE = lambda j, a, b: V("ee", HM * (j % 4) + a, HM * (j % 4) + b)
+        same = lambda j, a, b: ts(EE(j, a, b), V("fr", a, b), V("cv", j, j + 1), ALU.is_equal)
         for a in (0, M):
             scan(V("sc", a, a + M), V("d0", 0, M), V("fr", a, a + M), ALU.mult, ALU.add)
-            if a:
-                same(0)
-            elif not t:
-                ts(V("cv", 0, 8), V("x0", 8, 16), CF(24), ALU.mult, CF(25), ALU.add)
+            same(0, a, a + M)
+            same(1, a, a + M)
             ts(V("l0", a // 16, a // 16 + 16), V("sc", a + 15, a + M, 16), GSCL, ALU.mult, float(GM), ALU.add)
             act(V("trs", a, a + M), V("w0"), off=V("l0", a // 16, a // 16 + 16), accum=ACC(a // 64))
-        for i in (1, 2, 3):
+        for i in range(1, NS // 2):
             act(V("trs", HM * i, HM * i + HM), V("w%d" % i), off=V("l0"), accum=ACC(i))
-        for j in range(8):
-            if j < 7:
-                same(j + 1)
-            summed(j)
+        blk = RK.index(rank)
+        mine, last = 64 * (blk // 2), V("sc", M * (blk % 2) + 15, M * (blk % 2) + M, 16)
+        rho, itself = V("rho", 0, 16), V("rho", 16, 32)
+        for p in (0, 64):
+            act(on(rho, p), on(last, mine), AF.Identity, scale=on(GSCL, mine), bias=float(GM))
+        act(V("inv", 0, 96), V("bg"))
+        for j in range(NV):
+            if 0 < j < NV - 1:
+                same(j + 1, 0, HM)
+            scan(V("so", M * j, M * j + M), EE(j, 0, M), EE(j, M, HM), ALU.add, ALU.add)
             if j == 4:
                 tt(ACC(0), ACC(0), ACC(4), ALU.add)
-        ends = V("so", M - 1, 8 * M, M)
+            if j == NV - 3:
+                for b in (0, 1):
+                    halves(Z("aci", NS // 2 * b, NS // 2 * b + NS // 2), V("acc", 0, NS // 2), ALU.add, 32 * b, 32)
+            if j == NV - 2:
+                ts(Z("roti", 0, 2 * NS, 2), Z("aci", 0, NS), 2047, ALU.bitwise_and)
+                ts(Z("roti", 1, 2 * NS, 2), Z("aci", 0, NS), 11, ALU.logical_shift_right)
+        cp(Z("rot", 0, 2 * NS), Z("roti", 0, 2 * NS))
         for b in (0, 1):
-            halves([Z("rot", 16 + 8 * b, 24 + 8 * b)], ends, V("up"), ALU.add, 32 * b, 32)
-        for b in (0, 1):
-            halves([Z("aci", 4 * b, 4 * b + 4)], V("acc", 0, 4), V("acc", 8, 12), ALU.add, 32 * b, 32)
-        ts(Z("roti", 0, 16, 2), Z("aci", 0, 8), 2047, ALU.bitwise_and)
-        ts(Z("roti", 1, 16, 2), Z("aci", 0, 8), 11, ALU.logical_shift_right)
-        cp(Z("rot", 0, 16), Z("roti"))
+            halves(Z("rot", 2 * NS + NV * b, 2 * NS + NV * b + NV), V("so", M - 1, NV * M, M), ALU.add, 32 * b, 32)
+        cp(V("lro"), rho)
+        tt(itself, rho, V("sn"), ALU.is_equal)
         for j in range(1, NTS + 1):
-            act(Z("trs", 32 * j, 32 * j + 32), Z("rot"), AF.Sign, bias=-0.5 - j, accum=Z("ypd", j, j + 1))
-        act(Z("szs"), Z("rot"), AF.Relu, scale=2.0, bias=-2.0)
+            act(Z("trs", 64 * j, 64 * j + 64), Z("rot"), AF.Sign, bias=-0.5 - j, accum=Z("ypd", j, j + 1))
+        act(Z("szs"), Z("rot", 0, 32), AF.Relu, scale=2.0, bias=-2.0)
         for j in range(NTS + 1, SMAX):
-            ts(Z("cm", 32 * j, 32 * j + 32), Z("rot"), float(j + 1), ALU.is_ge)
+            ts(Z("cm", 32 * j, 32 * j + 32), Z("rot", 0, 32), float(j + 1), ALU.is_ge, 2.0, ALU.mult)
         for j in range(NTS + 1, SMAX):
             red(Z("ypd", j, j + 1), Z("cm", 32 * j, 32 * j + 32), ALU.add)
-        tr(Z("ytr"), Z("ypd"))
-        scan(Z("in2", 1, 33), Z("s32"), Z("ytr"), ALU.add, ALU.add)
-        tot, before = Z("in2", 32, 33), Z("in2", 0, 32)
-        act(Z("a1"), Z("hs"), AF.Identity, scale=tot)
-        ts(COL(0), tot, z(KT), ALU.is_ge, -2048.0, ALU.mult)
-        ts(COL(1), tot, z(KT), ALU.is_lt, 2048.0, ALU.mult)
-        ts(Z("suf"), before, tot, ALU.subtract, z(NHS), ALU.mult)
-        tr(Z("cs"), Z("a1"))
-        act(Z("x3", 0, 32), before, AF.Identity, scale=HS, bias=COL(0))
-        ts(Z("x3", 64, 96), before, HS, ALU.mult, COL(1), ALU.add)
-        ts(Z("x3", 32, 64), Z("suf"), COL(0), ALU.add)
-        act(Z("trs", 512, 544), Z("cs"), AF.Sign, bias=0.5 - K, accum=Z("thr", 0, 1))
+        act(itself, itself, scale=2.0 * GM - 1)
+        act(V("rtf"), V("idn"), off=V("lro"))
+        row = V("rtf", 0, M, 1, 0, 1)
+        dmas("drt", [("y", T.rt[0:1, M * t:M * t + M], A(row), [], [row])])
+        tr(Z("ytr", 0, 32), Z("ypd"))
+        scan(Z("in2", 1, 65), Z("dt"), Z("ytr"), ALU.mult, ALU.add)
+        scan(back(Z("sfx", 16, 48)), Z("dt", 0, 32), back(Z("ytr", 0, 32)), ALU.mult, ALU.add)
+        short, before = Z("in2", 33, 34), Z("in2", 0, 32)
+        tr(Z("cs"), Z("in2", 33, 65))
+        ts(Z("x3", 0, 32), before, short, ALU.min, 0.5, ALU.mult)
+        ts(Z("x3", 64, 96), before, short, ALU.max, 0.5, ALU.mult)
+        ts(Z("x3", 32, 64), Z("sfx", 16, 48), short, ALU.min, 0.5, ALU.mult)
+        act(Z("trs", NM, NM + 32), Z("cs"), AF.Sign, scale=-1.0, accum=Z("thr", 0, 1))
+        tt(itself, itself, rho, ALU.max)
         tr(Z("c3"), Z("x3"))
         gt, eq, thr = Z("ge", 0, 32), Z("ge", 32, 64), Z("thr", 0, 1)
         ts(gt, Z("szs"), -30.0, ALU.add, thr, ALU.is_gt)
@@ -570,132 +603,97 @@ def rank_program(g, core, T, topo):
         scan(Z("inc", 0, 32), Z("dr"), gt, ALU.add, ALU.add, COL(2))
         act(Z("hh", 32, 64), eq, AF.Identity, scale=-BIG - 1.0, bias=COL(3))
         scan(Z("inc", 32, 64), Z("db"), eq, ALU.add, ALU.add, COL(4))
+        cp(V("lrm"), itself)
         for e in (0, 1):
             tt(Z("je", 32 * e, 32 * e + 32), Z("inc", 32 * e, 32 * e + 32), Z("hh", 32 * e, 32 * e + 32), ALU.add)
+        if not t:
+            unpacking(0)
         for e in range(4):
             tt(Z("zz", 16 * e, 16 * e + 16), Z("je", 16 * (e // 2), 16 * (e // 2) + 16), Z("je", 32 + 16 * (e // 2), 48 + 16 * (e // 2)), ALU.min)
         tt(Z("zz", 64, 96), Z("je", 0, 32), Z("je", 32, 64), ALU.min)
         tr(Z("zt", 0, 64), Z("zz", 0, 64))
-        tr(Z("zt", 64, 96), Z("zz", 64, 96))
+        act(Z("um", 0, 32), Z("zz", 64, 96), AF.Identity, bias=Z("um", 72, 73))
+        act(Z("um", 32, 64), Z("zz", 64, 96), AF.Identity, scale=float(NM), bias=(0.5 - K) * NM)
         for b in range(4):
             cp(on(V("sll"), 32 * b, 32), Z("zt", 32 * (b // 2) + 8 * rank, 32 * (b // 2) + 8 * rank + 8))
+        tt(Z("zz", 64, 96), Z("um", 0, 32), Z("um", 32, 64), ALU.max)
         emit("v", lambda: g.vector.tensor_copy(ind(V("inv"), V("sll")), A(V("io2"))), [V("inv")], [V("io2"), V("sll")])
-        for b in (1, 2, 3):
-            act(on(V("zt", 64, 96), 32 * b, 32), Z("zt", 64, 96))
-        widen(0, 16)
+        tr(Z("zt", 64, 96), Z("zz", 64, 96))
+        for b in range(4):
+            act(on(V("xz", 0, NM, 32), 32 * b, 32), Z("zt", 64, 96))
         scan(V("scf", 0, K), V("d0", 0, K), V("inv", 0, K), ALU.mult, ALU.add)
         jm = V("jm", 0, 5)
-        halves([on(jm, 0), on(jm, 64)], V("scf", 15, K, 16), V("jx", 0, 5), ALU.max)
-        ts(V("j1", 0, 5), jm, SCL, ALU.mult, float(-NM), ALU.add)
-        qa, sa, qb, sb = "qa%d" % t, "sa%d" % t, "qb%d" % t, "sb%d" % t
-        pick(V(qa, 0, K), V(sa, 0, K), V(qc, 0, M), V(sp, 0, M), V("j1", 0, 5))
-        swap(qa, sa, near, "ac%d" % t, "as%d" % t)
-        widen(16, 32)
-        if not t:
-            ts(V("s80"), V("s80"), SCOL, ALU.add)
-            ts(V("ki"), V("ki"), SCOL, ALU.add)
-            ts(V("sn"), V("sn"), SCOL, ALU.add)
-            for h in (0, 1):
-                n0 = lo + H * h
-                step = place(n0 + 1) - place(n0)
-                ts(V("sn", 8 * h, 8 * h + 8), V("sn", 8 * h, 8 * h + 8), float(step), ALU.mult, float(place(n0) - step * n0), ALU.add)
-        ts(V("j2f", 0, 5), jm, SCL, ALU.mult, NM - 0.5, ALU.is_lt)
-        blk = RK.index(rank)
-        mine, last = 64 * (blk // 2), V("sc", M * (blk % 2) + 15, M * (blk % 2) + M, 16)
         for p in (0, 64):
-            ts(on(V("rho", 0, 16), p), on(last, mine), on(GSCL, mine), ALU.mult, float(GM), ALU.add)
-        ts(V("j2f", 0, 5), V("j2f", 0, 5), float(K), ALU.mult)
-        for k in range(4):
+            halves(on(jm, p), V("scf", 15, K, 16), ALU.min)
+        if not t:
+            unpacking(1)
+        ts(V("j1", 0, 5), jm, SCL, ALU.mult, M - 1.0, ALU.min)
+        ts(V("j2", 0, 5), jm, SCL, ALU.mult)
+        repeated(0)
+        qa, sa, qz, sz, qb, sb = [n + str(t) for n in ("qa", "sa", "qz", "sz", "qb", "sb")]
+        pick(V(qa), V(sa), V(qc, 0, M), V(sp, 0, M), V("j1", 0, 5))
+        swap(qa, sa, qz, sz, M, near, "ac%d" % t, "as%d" % t)
+        for e in (1, 2, 3):
+            repeated(e)
+        for k in range(8):
             tr(grun("fs", k), V("xb", H * k, H * k + H))
-        cp(V("lro"), V("rho", 0, 16))
-        tt(V("j2f", 0, 5), V("j2f", 0, 5), V("s80", 0, 5), ALU.add)
-        tt(V("rho", 16, 32), V("rho", 0, 16), V("sn"), ALU.not_equal)
-        far_in = [float(d in pair2) for d in range(N)]
-        terms = [(ALU.is_lt, M, far_in[0] * K)] + [(ALU.is_ge, M * d, (far_in[d] - (far_in[d - 1] if d > 1 else 0.0)) * K) for d in range(1, N)]
-        terms = [(op, float(place(n)), v) for op, n, v in terms if v]
-        parts = [V("rho", 32, 48), V("m1"), V("mm")]
-        for j, (op, n, v) in enumerate(terms):
-            ts(parts[j], V("rho", 0, 16), n, op, v, ALU.mult)
-        cp(V("j2", 0, 5), V("j2f", 0, 5))
-        act(V("rtf"), V("idn"), off=V("lro"))
-        row = V("rtf", 0, M, 1, 0, 1)
-        dmas("drt", [("y", T.rt[0:1, M * t:M * t + M], A(row), [], [row])])
-        for k in range(4, 8):
-            tr(grun("fs", k), V("xb", H * k, H * k + H))
-            if k - 3 < len(terms):
-                tt(parts[0], parts[0], parts[k - 3], ALU.add)
-        cp(V("rs"), V("fs"), V("lro"))
-        pick(V(qb, 0, K), V(sb, 0, K), V(qa), V(sa), V("j2", 0, 5))
-        swap(qb, sb, far, "bc%d" % t, "bs%d" % t)
+        if not t:
+            unpacking(2)
+            unpacking(3)
+        cp(V("rs"), V("fs"), V("lrm"))
+        pick(V(qb, 0, K), V(sb, 0, K), V(qz), V(sz), V("j2", 0, 5))
+        swap(qb, sb, qb, sb, K, far, "bc%d" % t, "bs%d" % t)
         scan(V("sc", 0, M), V("d0", 0, M), V("rs"), ALU.mult, ALU.add)
-        if t + 1 < R:
-            if not t:
-                pick(V("qr", 128, 384), V("sr", 128, 384), V("qu"), V("su"), V("cu", 8, 24))
+        if not final:
+            tr(V("rx"), V("rs"))
+        if not t:
+            pick(V("qr", 128, 384), V("sr", 128, 384), V("qu"), V("su"), V("cu", 8, 24))
             height(7, t + 1, qc, sp, 0, M)
-        so, me = V("rho", 0, 16), V("rho", 16, 32)
-        ts(V("rho", 48, 64), V("sc", 15, M, 16), SCL, ALU.mult, K - 0.5, ALU.is_lt)
-        ts(so, V("sc", 15, M, 16), SCL, ALU.mult)
+        me, at = V("rho", 16, 32), V("sc", 15, M, 16)
+        ts(V("pl"), at, SCL, ALU.mult, 2.0 * K - 1, ALU.min)
+        ts(me, at, SCL, ALU.mult, 2 * K - 0.5, ALU.is_lt)
+        if not final:
+            ts(V("mx1"), V("rx", 0, M, 32), 2 * K - 0.5, ALU.is_ge)
+            ts(V("mx"), V("rx", 0, M, 32), 2 * K - 0.5, ALU.is_lt)
         if not t:
-            quant(V("qe"), V("se"), V("et"))
-        tt(me, me, V("rho", 48, 64), ALU.mult)
-        if t + 1 < R:
             tr(V("ho"), bank(7, M))
-        tt(so, so, me, ALU.mult)
-        ts(V("rho", 48, 64), me, float(M), ALU.mult)
-        m0, m1 = V("rho", 16, 32, 2), V("rho", 17, 32, 2)
-        if t + 1 < R:
-            tt(V("mx"), m1, m0, ALU.subtract)
-        tt(V("rho", 32, 48), V("rho", 32, 48), so, ALU.add)
-        tt(V("rho", 48, 64), V("rho", 48, 64), V("ki"), ALU.add)
-        if t + 1 < R:
-            ts(V("mx"), V("mx"), HI, ALU.mult)
-        cp(V("pl"), V("rho", 32, 48))
-        cp(V("kl"), V("rho", 48, 64))
-        if t + 1 < R:
-            tt(V("mx"), V("mx"), m0, ALU.add)
-        if not t:
-            quant(V("qw"), V("sw"), V("wt"))
-        if t + 1 < R:
-            ts(V("mx1"), V("mx"), -1.0, ALU.mult, 1.0, ALU.add)
-            tt(V("xo"), V("ho", 0, M, 32), V("mx1"), ALU.mult)
+        ts(me, me, float(M), ALU.mult)
         unpack = [(V("qe", 128 * b, 128 * b + 128), V("se", 128 * b, 128 * b + 128)) for b in range(4)]
-        half = [(H * h, H * h + H) for h in (0, 1)]
         qp, pp = "qp%d" % t, "sp%d" % t
         for h in (0, 1):
             for b in range(4):
                 mm(bank(4 * h + b, H), *unpack[b], V(qc, *half[h]), V(sp, *half[h]), True, False)
-        for h in (0, 1):
-            codes(V(qp, *half[h]), V(qb), V("pl", 8 * h, 8 * h + 8))
+        codes(V(qp, *half[0]), V(qb), V("pl", 0, 8))
+        tt(me, me, V("ki"), ALU.add)
+        if not final:
+            tt(V("xo"), V("ho", 0, M, 32), V("mx1"), ALU.mult)
+        codes(V(qp, *half[1]), V(qb), V("pl", 8, 16))
         for h in (0, 1):
             move("sv"[h], V(pp, *half[h]), V(sb), V("pl", 8 * h, 8 * h + 8))
+        cp(V("kl"), me)
         for h in (0, 1):
             for b in range(4):
                 mm(bank(4 * h + b, H), *unpack[b], V(qp, *half[h]), V(pp, *half[h]), False, True)
-
-        def cast(h, b):
-            src, out = bank(4 * h + b, H), V("hb", 4 * H * h + b, 4 * H * h + 4 * H, 4)
+        for b in range(8):
+            src, out = bank(b, H), V("hb", 4 * H * (b // 4) + b % 4, 4 * H * (b // 4) + 4 * H, 4)
             if b % 2:
                 act(out, src, scale=0.5)
             else:
                 ts(out, src, 0.5, ALU.mult)
-
-        def anew(h):
+        for h in (0, 1):
             quant(V(qc, M + H * h, M + H * h + H), V(sp, M + H * h, M + H * h + H), V("hb", 4 * H * h, 4 * H * h + 4 * H))
-            if t + 1 < R:
+            if not final:
                 height(h, t + 1, qc, sp, M + H * h, H)
-
-        for b in range(6):
-            cast(b // 4, b % 4)
-        anew(0)
-        cast(1, 2)
-        cast(1, 3)
-        anew(1)
         nq, ns = "qc%d" % (t + 1), "scp%d" % (t + 1)
-        if t + 1 < R:
+        if not final:
             for h in (0, 1):
                 tr(V("ht", *half[h]), bank(h, H))
-            tt(V("xm"), V("ht", 0, M, 32), V("mx"), ALU.mult)
-            tt(V("xh%d" % (t + 1), 8 * rank, 8 * rank + 8), V("xm"), V("xo"), ALU.add)
+                for c in range(4 * h, 4 * h + 4):
+                    out, new = V("xh%d" % (t + 1), 8 * rank + c, 8 * rank + c + 1), V("ht", 32 * c, 32 * c + 1)
+                    if h and c % 2 == 0:
+                        ts(out, new, V("mx", c, c + 1), ALU.mult, V("xo", c, c + 1), ALU.add)
+                    else:
+                        act(out, new, AF.Identity, scale=V("mx", c, c + 1), bias=V("xo", c, c + 1))
             share(t + 1)
             pick(V(nq, 0, M), V(ns, 0, M), V(qc), V(sp), V("kl"))
 
@@ -704,12 +702,12 @@ def rank_program(g, core, T, topo):
         pick(V(nq, *half[h]), V(ns, *half[h]), V(qc, 0, M + H * h + H), V(sp, 0, M + H * h + H), V("kl", 8 * h, 8 * h + 8))
         mm(bank(h, H), V("qw"), V("sw"), V(nq, *half[h]), V(ns, *half[h]), True, True)
         outs.append(("y", T.oc[:, 4 * H * h:4 * H * h + 4 * H], A(V(nq, *half[h])).bitcast(dt.uint8), [], [V(nq, *half[h])]))
-    for h in (0, 1):
-        cp(V("ys", *half[h]), bank(h, H))
-        outs.append(("s", T.y[:, H * h:H * h + H], A(V("ys", *half[h])), [], [V("ys", *half[h])]))
     for k in range(4):
         o = V(ns, 0, M, 1, 32 * k, 32 * k + 4)
-        outs.append(("y", T.osc[4 * k:4 * k + 4, 0:M], A(o), [], [o]))
+        outs.append(("s", T.osc[4 * k:4 * k + 4, 0:M], A(o), [], [o]))
+    for h in (0, 1):
+        cp(V("ys", *half[h]), bank(h, H))
+        outs.append(("y", T.y[:, H * h:H * h + H], A(V("ys", *half[h])), [], [V("ys", *half[h])]))
     dmas("dout", outs)
     for sem in sorted(cnt):
         g.sync.wait_ge(T.sem[sem], cnt[sem])

@@ -8,12 +8,8 @@ N, M, K, J, R = 4, 256, 80, 3, 3
 NM = N * M
 HM = NM // 2
 H = M // 2
-SMAX = NM // K + 1
-NTS = 7
-NS, NV = 6, 10
-BIG = 4.0 * NM
-BIGR = NM + K
-WINV = BIGR + NM + K + 16
+KC = K // 16
+SEG = 65
 RUNS = ((-2048, 8), (-1024, 4), (-512, 2), (-256, 1), (128, 1), (256, 2), (512, 4), (1024, 8))
 UNIT = 1.0 / 4096
 OWN = ((2, 3, 4, 5), (0, 1, 6, 7))
@@ -24,28 +20,28 @@ UP = float(2 ** 30)
 C8, U8, F32, B16, I32, U16 = "float8_e4m3fn_x4", "uint8", "float32", "bfloat16", "int32", "uint16"
 
 WIDTHS = {
-    B16: {"xt": 4 * M, "ut": 512, "wt": 512, "one": 528, "et": 2 * 528, "d0": 512, "dw": NM, "wb": NM + 16,
-          "w0": 2 * GM, "w1": 2 * GM, "w2": 2 * GM, "xb": NM, "xz": NM, "d32": M, "cw": NM, "ca": 384, "cb": HM,
+    B16: {"xt": 4 * M, "ut": 512, "wt": 512, "one": 528, "et": 2 * 528, "d0": 512, "dw": NM,
+          "xb": NM, "xz": NM, "d32": M, "cw": NM, "ca": 384, "cb": HM,
           "fs": 2 * GM, "fa": 2 * WM, "fb": 2 * WM, "sc": HM, "rs": M, "rx": M, "hb": 4 * M,
-          "fr": HM, "ee": 4 * HM, "so": NV * M, "cv": 16, "c2": 64},
+          "fr": HM, "ee": 4 * HM, "so": 4 * M, "cv": 16, "ea": 2 * (H + 32), "pb": H + 64, "ps": 64, "dd": 336, "di": 336, "de": 336,
+          "sg": 3 * M, "kr": 64, "km": 160, "kt": 160, "kw": 16, "uu": 32},
     C8: {"qu": 128, "qw": 128, "qr": 384, "qe": 512},
     U8: {"su": 128, "sw": 128, "sr": 384, "se": 512},
-    F32: {"io2": H, "i128": H, "idn": 2 * GM, "rtf": M, "xe": NM, "fh": NM, "scf": 128, "ra": 384, "rb": HM, "trs": 2 * NM,
-          "ht": M, "ho": M, "inv": WINV, "cm": 32 * SMAX, "rot": 64, "acc": 16, "szs": 32, "ys": M, "bg": 96},
-    U16: {"la": 32, "lb": 32, "l0": 32, "nbl": 64, "lnb": 24},
-    I32: {"iu": 24, "id16": 16, "nbe": 24},
+    F32: {"i128": H, "idn": 2 * GM, "rtf": M, "xe": NM, "fh": NM, "ra": 384, "rb": HM,
+          "ht": M, "ho": M, "acc": 16, "ys": M, "xk": M, "xr": M, "kf": M},
+    U16: {"la": 32, "lb": 32, "nbl": 64, "lnb": 24},
+    I32: {"iu": 24, "id16": 16, "nbe": 16},
 }
 SCRATCH = {"bl": ("psum", [128, 4096], F32)}
 for _d, _parts in WIDTHS.items():
     for _n, _w in _parts.items():
         SCRATCH[_n] = ("sbuf", [128, _w], _d)
 SMALL = {
-    "zf": (F32, {"d16": 16, "d17": 16, "cf": 32, "nrest": 32, "dr": 32, "dt": 64, "db": 32, "ypd": 32, "ytr": 64, "in2": 80, "one32": 32,
-                 "sn": 16, "ki": 16, "x0": 32, "m1": 16, "neq": 32, "lost": 32, "key": 32, "b2": 16, "zz": 96, "zt": 96, "thr": 8,
-                 "sfx": 48, "col": 8, "cs": 32, "x3": 96, "c3": 96, "ge": 64, "inc": 64, "hh": 64, "je": 64, "um": 80,
-                 "jm": 8, "rho": 32, "mx": 8, "mx1": 8, "xo": 8}),
-    "zi": (I32, {"ip": 16, "aci": 16, "roti": 16}),
-    "zu": (U16, {"crep": 32, "cu": 24, "lro": 16, "lrm": 16, "sll": 8, "j1": 6, "j2": 6, "pl": 16, "kl": 16}),
+    "zf": (F32, {"d16": 16, "d17": 16, "cf": 32, "sn": 16, "ki": 16, "x0": 32, "m1": 16, "neq": 32, "lost": 32, "key": 32, "b2": 16,
+                 "nn": 4, "fq": 4, "aa": 4, "want": 16, "e1": 8, "e2": 8, "kk": 8, "fl": 16, "um": 16, "mh": 32,
+                 "rho": 32, "mx": 8, "mx1": 8, "xo": 8}),
+    "zi": (I32, {"ip": 16}),
+    "zu": (U16, {"crep": 32, "cu": 24, "lro": 16, "lrm": 16, "j1": 6, "j2": 6, "pl": 16, "kl": 16}),
 }
 AT = {}
 for _b, (_d, _parts) in SMALL.items():
@@ -56,16 +52,17 @@ for _b, (_d, _parts) in SMALL.items():
     SCRATCH[_b] = ("sbuf", [128, _o], _d)
 for _t in range(R):
     SCRATCH["xh%d" % _t] = ("sbuf", [128, 32], F32)
-    for _n, _w in (("a", K), ("z", M + K), ("b", 2 * K), ("p", M)):
+    SCRATCH["ms%d" % _t] = ("sbuf", [128, 32], B16)
+    for _n, _w in (("z", 2 * K), ("b", 2 * K), ("p", M)):
         SCRATCH["q%s%d" % (_n, _t)] = ("sbuf", [128, _w], C8)
         SCRATCH["s%s%d" % (_n, _t)] = ("sbuf", [128, _w], U8)
 for _t in range(R + 1):
     SCRATCH["qc%d" % _t] = ("sbuf", [128, 2 * M if _t < R else M], C8)
     SCRATCH["scp%d" % _t] = ("sbuf", [128, 2 * M if _t < R else M], U8)
 
-SEMAPHORES = (["ev", "es", "et", "eg", "loc"] + ["nb%d" % d for d in range(N)] + ["h%d_%d" % (t, d) for t in range(R) for d in range(N)]
+SEMAPHORES = (["ev", "es", "et", "eg", "loc"] + ["nb%d" % d for d in range(N)] + ["%s%d_%d" % (k, t, d) for k in "hm" for t in range(R) for d in range(N)]
               + ["%s%d" % (k, t) for t in range(R) for k in ("ac", "as", "bc", "bs")]
-              + ["dx0", "dx1", "du", "dw", "dz", "dnb", "drt", "dout"])
+              + ["dx0", "dx1", "du", "dw", "dnb", "drt", "dout"])
 
 
 def place(n):
@@ -221,7 +218,7 @@ def rank_program(g, core, T, topo):
         emit("g", fn, [out], [])
 
     def const(out, c):
-        iota(out, [[0, out[2] - out[1]]], int(c), 0)
+        iota(out, [[0, len(range(*out[1:4]))]], int(c), 0)
 
     def select(out, in_, pattern, cmp, fillv, base, cm):
         emit("g", lambda: g.affine_select(A(out), A(in_), pattern, cmp, fillv, base, cm), [out], [in_])
@@ -249,10 +246,10 @@ def rank_program(g, core, T, topo):
         mask3 &= topo.mask(core, T.cores[d])
     groups = bin(mask3).count("1")
 
-    def spread(piece, sem):
+    def spread(piece, sem, order=others):
         src = piece(rank)
         use("g", [src], [])
-        ids = [DstId(rid=topo.addr(T.cores[d])[0], pnc=topo.addr(T.cores[d])[1]) for d in others]
+        ids = [DstId(rid=topo.addr(T.cores[d])[0], pnc=topo.addr(T.cores[d])[1]) for d in order]
         g.remote_dma_fused([RemoteDMATransfer(dst_ids=ids, dma_engine_mask=mask3, remote_sem=T.sem[sem % rank], srcs=[A(src)], dsts=[A(src) for d in others])],
                            local_sem=T.sem.loc)
         cnt["loc"] = cnt.get("loc", 0) + groups
@@ -262,19 +259,20 @@ def rank_program(g, core, T, topo):
     near = [d for d in others if topo.same_plane(topo.chip(core), topo.chip(T.cores[d]))][0]
     pair = sorted([rank, near])
     pair2 = [d for d in range(N) if d not in pair]
-    far = pair2[pair.index(rank)]
+    second = pair.index(rank)
+    far = pair2[second]
 
-    def swap(q, s, q2, s2, at, d, semc, sems):
+    def swap(q, s, a, at, lands, d, semc, sems):
         dst = T.cores[d]
         rid, pid = topo.addr(dst)[:2]
         mask, n = topo.mask(core, dst), len(topo.engines(core, dst))
-        use("g", [V(q, 0, K)], [])
-        g.remote_dma(A(V(q2, at, at + K)).bitcast(dt.uint8), A(V(q, 0, K)).bitcast(dt.uint8), T.sem[semc], T.sem.loc, pid, rid, mask)
-        use("g", [V(s, 0, K)], [])
-        g.remote_dma(A(V(s2, at, at + K)), A(V(s, 0, K)), T.sem[sems], T.sem.loc, pid, rid, mask)
+        use("g", [V(q, a, a + K)], [])
+        g.remote_dma(A(V(q, at, at + K)).bitcast(dt.uint8), A(V(q, a, a + K)).bitcast(dt.uint8), T.sem[semc], T.sem.loc, pid, rid, mask)
+        use("g", [V(s, a, a + K)], [])
+        g.remote_dma(A(V(s, at, at + K)), A(V(s, a, a + K)), T.sem[sems], T.sem.loc, pid, rid, mask)
         cnt["loc"] = cnt.get("loc", 0) + 2 * n
-        arrives(semc, n, [V(q2, at, at + K)])
-        arrives(sems, n, [V(s2, at, at + K)])
+        arrives(semc, n, [V(q, lands, lands + K)])
+        arrives(sems, n, [V(s, lands, lands + K)])
 
     def turned(t, d, by, between=None):
         for e in (0, 1):
@@ -313,10 +311,10 @@ def rank_program(g, core, T, topo):
     half = [(H * h, H * h + H) for h in (0, 1)]
 
     loads = []
-    for k in range(4):
+    for k in range(2 * J):
         shift = 2 * (k % 2)
-        o = V("nbe", 0, 24 - shift, 1, 16 * k, 16 * k + 16)
-        loads.append(("s", A(o), T.nb[:, 24 * (k // 2) + shift:24 * (k // 2) + 24], [o], []))
+        o = V("nbe", 0, 16 - shift, 1, 16 * k, 16 * k + 16)
+        loads.append(("s", A(o), T.nb[:, 16 * (k // 2) + shift:16 * (k // 2) + 16], [o], []))
     dmas("du", [("y", A(V("ut")), T.u[:], [V("ut")], [])])
     dmas("dnb", loads)
     for h in (0, 1):
@@ -329,7 +327,7 @@ def rank_program(g, core, T, topo):
     iota(V("id16"), [[1, 16]], 128, -1)
     iota(V("i128"), [[1, H]], 0, 0)
     o = 16 * rank
-    fill(on(V("nbl", o, o + 12), 64), 0)
+    fill(on(V("nbl", o, o + 8), 96, 32), 0)
     fill(V("dw"), 0.0)
     act(V("xe"), V("dw"))
     cp(V("cu"), V("iu"))
@@ -337,14 +335,12 @@ def rank_program(g, core, T, topo):
     ts(IP(1), IP(0), 6, ALU.logical_shift_right)
     ts(IP(2), IP(0), 15, ALU.bitwise_and)
     ts(IP(3), IP(0), 31, ALU.bitwise_and)
-    ts(IP(7), IP(0), 5, ALU.logical_shift_right, 1, ALU.bitwise_and)
     fill(V("xz", 0, HM), 0.0)
     cp(V("cf", 5, 8), V("ip", 1, 4))
     for e in (0, 1):
-        cp(on(V("nbl", o + e, o + 12, 2), 0), on(V("nbe", e, 24, 4), 0))
-    spread(lambda d: V("nbl", 16 * d, 16 * d + 12), "nb%d")
+        cp(on(V("nbl", o + e, o + 8, 2), 0, 96), on(V("nbe", e, 16, 4), 0, 96))
+    spread(lambda d: V("nbl", 16 * d, 16 * d + 8), "nb%d")
     quant(V("qu"), V("su"), V("ut"))
-    ts(CF(12), IP(7), -float(NS), ALU.mult, LCOL, ALU.add)
     fill(V("d32", 0, M, 32), 0.0)
     ts(V("id16"), V("id16"), 15, ALU.bitwise_and)
     pick(V("qr", 0, 128), V("sr", 0, 128), V("qu"), V("su"), V("cu", 0, 8))
@@ -367,53 +363,42 @@ def rank_program(g, core, T, topo):
         tr(V("ht", *half[h]), bank(h, H))
     ts(SCL, SCL, 1.0 / UP, ALU.max)
     tt(V("d16"), V("d16"), V("d17"), ALU.add)
-    fill(V("one32"), 1.0)
     cp(V("xh0", 8 * rank, 8 * rank + 8), V("ht", 0, M, 32))
     share(0)
     dmas("dw", [("y", A(V("wt")), T.w[:], [V("wt")], [])])
 
     iota(V("sn"), [[16, 16]], M * rank, 0)
     iota(V("ki"), [[16, 16]], 0, 0)
-    for d in range(N):
-        const(Z("um", 64 + d, 65 + d), K * ((d in pair2) - (d - 1 in pair2)))
-    select(Z("um", 64, 64 + N), Z("um", 64, 64 + N), [[-8, N]], ALU.is_ge, 0.0, 0, 1)
-    iota(V("bg"), [[1, 96]], M, 0)
     const(V("fs", 2 * GM - 16, 2 * GM), NM)
-    for h in (0, 1):
-        iota(on(V("io2"), 64 * h), [[32, 8], [1, 16]], 16 * h, 0)
-    iota(Z("nrest"), [[-1, 32]], -BIGR - 1, -32)
-    for name, a, b, c in (("dr", 0, 96, 1), ("db", 0, 144, 0), ("db", 0, 1, BIG), ("ypd", 0, 1, 64), ("rot", 32, 64, NM),
-                          ("dt", 32, 33, -BIG), ("ytr", 32, 33, BIG * (2 * K - 1))):
-        const(Z(name, a, b), c)
-    iota(Z("dr", 0, 1), [[0, 1]], BIGR, 32)
+    for p in (0, 64):
+        iota(on(V("nn", 0, 2), p), [[H, 2]], 0, 1)
+        iota(on(V("nn", 2, 4), p), [[-H, 2]], H + 64, 1)
+    const(V("di", 0, SEG * KC), 1)
+    const(V("di", 0, SEG * KC, SEG), 2 * M)
+    const(V("di", 32, SEG * KC, SEG), H - 31)
+    const(V("kr", 0, 32), K - 1)
+    const(V("kr", 32, 64), K - 2)
     for k, (a, s) in enumerate(RUNS):
         act(V("cw", H * k, H * k + H), V("i128"), AF.Identity, scale=s * UNIT, bias=a * UNIT)
     ts(V("x0", 0, 4), RI(4), 32.0, ALU.mult, LCOL, ALU.add)
-    turned(0, rank, "vs", lambda: (ts(CF(13), CF(12), NS - 2.0, ALU.is_equal), ts(CF(14), CF(12), NS - 1.0, ALU.is_equal, 2048.0, ALU.mult)))
+    turned(0, rank, "vs")
     act(V("d0"), V("d16"), off=V("crep"))
-    tt(CF(15), CF(13), CF(14), ALU.add)
     for b in range(4):
         for e in (0, 1):
             a, s = RUNS[2 * RK[b] + e]
             ts(on(V("cb", 3 * H + 64 * e, 3 * H + 64 * e + 64, 16), 32 * b, 32), on(V("x0", 0, 4), 32 * b, 32), s * UNIT, ALU.mult, a * UNIT, ALU.add)
-    ts(V("dw", 0, NM, 33), V("one32"), CF(15), ALU.mult)
-    fill(V("wb", NM, NM + 16), 0.0)
     for d in [rank] + senders:
-        for b in (0, 1):
-            cp(on(V("lnb", 12 * b, 12 * b + 12), 32 * RK.index(d), 32), on(V("nbl", 16 * d, 16 * d + 12), 32 * b, 32))
+        for b in range(J):
+            cp(on(V("lnb", 8 * b, 8 * b + 8), 32 * RK.index(d), 32), on(V("nbl", 16 * d, 16 * d + 8), 32 * b, 32))
         if d == rank:
-            tr(V("wb", 0, NM), V("dw"))
             fill(V("xz", HM, NM), 0.0)
+            fill(V("xk"), 0.0)
 
     def tables():
         act(V("one"), V("dw", 0, 528), AF.Identity, scale=0.0, bias=1.0)
-        for i in range(NS // 2):
-            for k in range(8):
-                src = V("wb", H * k + NS - 2 - 2 * i, H * k + H + NS - 2 - 2 * i)
-                if i:
-                    select(grun("w%d" % i, k), src, [[0, H]], ALU.is_gt, 0.0, 1, 0)
-                else:
-                    act(grun("w0", k), src)
+        act(V("ea"), V("dw", 0, 2 * (H + 32)))
+        act(V("dd", 0, SEG * KC, SEG), V("dw", 0, KC))
+        act(V("mh"), V("dw", 0, 32), AF.Identity, scale=0.0, bias=-0.5)
         for k in range(8):
             iota(grun("idn", k), [[1, H]], H * k, 0)
         for e in (0, 1):
@@ -423,10 +408,10 @@ def rank_program(g, core, T, topo):
         a = 528 * (b % 2) + 2 - b // 2 * 2
         quant(V("qe", 128 * b, 128 * b + 128), V("se", 128 * b, 128 * b + 128), V("et", a, a + 512))
 
-    def parked(t):
-        q, s = V("qz%d" % t, 0, M), V("sz%d" % t, 0, M)
-        qi, si = V("qc%d" % t, 0, M), V("scp%d" % t, 0, M)
-        dmas("dz", [("y", A(q).bitcast(dt.uint8), A(qi).bitcast(dt.uint8), [q], [qi]), ("y", A(s), A(si), [s], [si])])
+    def own_codes(e):
+        a, s = RUNS[2 * rank + e]
+        cols = (0, 4, 3) if e == 0 else (1, 3, 1)
+        ts(V("cv", *cols), V("nn", *cols), s * UNIT, ALU.mult, (a - s * H * e) * UNIT, ALU.add)
 
     def own_place(h):
         n0 = M * rank + H * h
@@ -436,17 +421,20 @@ def rank_program(g, core, T, topo):
     later = [
         lambda: ts(CF(23), UPPER, float(ALPHA[1] - ALPHA[0]), ALU.mult, float(ALPHA[0]), ALU.add),
         lambda: ts(GSCL, SCL, 1.0 / UNIT, ALU.mult),
-        lambda: ts(CF(22), IP(7), float(NV), ALU.mult, 2.0 * NS - 16, ALU.add),
-        lambda: tr(V("c2", 0, 32), V("cw", 16, NM, 32)),
-        lambda: tr(V("c2", 32, 64), V("cw", 17, NM, 32)),
-        lambda: tt(WSCL, GSCL, CF(23), ALU.mult),
-        lambda: ts(V("x0", 16, 32), RI(16), CF(22), ALU.add),
-        lambda: tt(CF(24), V("c2", 32, 33), V("c2", 0, 1), ALU.subtract),
-        lambda: cp(CF(25), V("c2", 0, 1)),
-        lambda: ts(V("sn"), V("sn"), SCOL, ALU.add),
-        lambda: ts(V("cv"), V("x0", 16, 32), CF(24), ALU.mult, CF(25), ALU.add),
         lambda: ts(V("ki"), V("ki"), SCOL, ALU.add),
-        lambda: red(Z("um", 72, 73), Z("um", 64, 64 + N), ALU.add),
+        lambda: ts(CF(22), IP(0), -1.0, ALU.mult, LCOL, ALU.add),
+        lambda: own_codes(0),
+        lambda: tt(WSCL, GSCL, CF(23), ALU.mult),
+        lambda: own_codes(1),
+        lambda: ts(V("sn"), V("sn"), SCOL, ALU.add),
+        lambda: ts(V("want", 0, KC), V("ki", 0, KC), 1.0 - 2.0 * second, ALU.mult, (K - 1.0) * second, ALU.add),
+        lambda: ts(V("di", SEG - 1, SEG * KC, SEG), RI(KC), 0.0, ALU.mult, CF(22), ALU.add),
+        lambda: ts(on(V("fq"), 0), on(V("nn"), 0), -1.0 / M, ALU.mult),
+        lambda: ts(back(on(V("fq"), 64)), on(V("nn"), 64), -1.0 / M, ALU.mult),
+        lambda: ts(V("want", 8, 8 + KC), V("want", 0, KC), -float(NM), ALU.mult),
+        lambda: ts(V("di", SEG - 1, SEG * KC, SEG), V("di", SEG - 1, SEG * KC, SEG), H - 31.0, ALU.add),
+        lambda: ts(CF(24), LCOL, 0.5 / M - 1.0, ALU.add),
+        lambda: ts(CF(25), LCOL, 0.5 / M, ALU.add),
         lambda: own_place(0),
         lambda: own_place(1),
     ]
@@ -456,7 +444,6 @@ def rank_program(g, core, T, topo):
             f()
         del later[:n]
 
-    COL = lambda k: Z("col", k, k + 1)
     ACC = lambda k: V("acc", k, k + 1)
     for t in range(R):
         qc, sp = "qc%d" % t, "scp%d" % t
@@ -468,7 +455,6 @@ def rank_program(g, core, T, topo):
             else:
                 height(7, t + 1, qc, sp, 0, M)
                 tr(V("ho"), bank(7, M))
-        parked(t)
         turned(t, senders[0], "vs", meanwhile)
         turned(t, senders[1], "ss")
         if not t:
@@ -537,118 +523,118 @@ def rank_program(g, core, T, topo):
             listed(lw, 2, 4)
         for by, a, b in (("v", 0, H), ("s", H, M), ("s", M, HM)):
             move(by, V("fr", a, b), V("fb"), V("lb", a // 16, b // 16))
-        meanwhile(3)
-        EE = lambda j, a, b: V("ee", HM * (j % 4) + a, HM * (j % 4) + b)
+        meanwhile(len(later))
+        EE = lambda j, a, b: V("ee", HM * j + a, HM * j + b)
         same = lambda j, a, b: ts(EE(j, a, b), V("fr", a, b), V("cv", j, j + 1), ALU.is_equal)
-        for a in (0, M):
-            scan(V("sc", a, a + M), V("d0", 0, M), V("fr", a, a + M), ALU.mult, ALU.add)
-            same(0, a, a + M)
-            same(1, a, a + M)
-            ts(V("l0", a // 16, a // 16 + 16), V("sc", a + 15, a + M, 16), GSCL, ALU.mult, float(GM), ALU.add)
-            act(V("trs", a, a + M), V("w0"), off=V("l0", a // 16, a // 16 + 16), accum=ACC(a // 64))
-        for i in range(1, NS // 2):
-            act(V("trs", HM * i, HM * i + HM), V("w%d" % i), off=V("l0"), accum=ACC(i))
+        count = lambda j: scan(V("so", M * j, M * j + M), EE(j, 0, M), EE(j, M, HM), ALU.add, ALU.add)
+        for j in range(4):
+            same(j, 0, M)
+        for j in range(4):
+            same(j, M, HM)
+            if j:
+                count(j - 1)
+        count(3)
+        ends = V("so", M - 1, 4 * M, M)
+        halves(on(V("aa"), 0), ends, ALU.add)
+        halves(back(on(V("aa"), 64)), ends, ALU.add)
+        tt(V("xk", 0, H, 32), V("aa"), V("fq"), ALU.add)
+        for b in range(4):
+            tt(on(V("xk", H, M, 32), 32 * b, 32), on(V("aa"), 32 * (b ^ 1), 32), on(V("fq"), 32 * (b ^ 1), 32), ALU.add)
+        for h in (0, 1):
+            scan(V("xr", *half[h]), V("d32", 0, H), V("xk", *half[h]), ALU.mult, ALU.add)
+        for h in (0, 1):
+            tr(V("kf", *half[h]), V("xr", *half[h]))
+        ms = "ms%d" % t
+        MS = lambda d, a, b: V(ms, 8 * d + a, 8 * d + b)
+        signs = lambda k, col: act(V("sg", M * k, M * k + M), V("kf"), AF.Sign, scale=-1.0, bias=col, accum=ACC(k))
+        signs(0, V("xk", 32, 33))
+        for h in (0, 1):
+            ts(V("ea", (H + 32) * h, (H + 32) * h + H), V("kf", *half[h]), V("xk", 0, 1), ALU.is_gt)
+        act(V("pb", H + 32, H + 64), V("mh"), AF.Identity, scale=ACC(0), bias=(M - 1) / 2)
+        scan(V("pb", 0, H + 32), V("ea", 0, H + 32), V("ea", H + 32, 2 * H + 64), ALU.add, ALU.add)
+        signs(1, CF(24))
         blk = RK.index(rank)
-        mine, last = 64 * (blk // 2), V("sc", M * (blk % 2) + 15, M * (blk % 2) + M, 16)
+        mine, at0 = 64 * (blk // 2), M * (blk % 2)
+        tr(V("ps"), V("pb", H, H + 64))
+        for k in range(KC):
+            out = V("dd", SEG * k + 1, SEG * k + SEG)
+            if k < 3:
+                ts(out, V("ps"), V("want", k, k + 1), ALU.not_equal, float(NM), ALU.mult)
+            else:
+                act(out, V("ps"), AF.Abs, scale=float(NM), bias=V("want", 8 + k, 9 + k))
+        signs(2, CF(25))
+        scan(V("de", 0, SEG * KC), V("dd", 0, SEG * KC), V("di", 0, SEG * KC), ALU.min, ALU.add)
+        act(MS(rank, 0, 2), V("pb", H, H + 64, 32))
+        act(MS(rank, 2, 4), V("acc", 1, 3), AF.Identity, scale=-0.5, bias=(M - 1) / 2)
+        spread(lambda d: MS(d, 0, 4), "m%d_" % t + "%d", [near, far] + [d for d in pair2 if d != far])
+        for p in (0, 64):
+            halves(on(V("e1", 0, KC), p), V("de", SEG - 1, SEG * KC, SEG), ALU.min)
+        for b in range(4):
+            tt(on(V("e2", 0, KC), 32 * b, 32), on(V("e1", 0, KC), 32 * b, 32), on(V("e1", 0, KC), 32 * (b ^ 1), 32), ALU.min)
+        scan(on(V("sc", 0, M), mine), on(V("d0", 0, M), mine), on(V("fr", at0, at0 + M), mine), ALU.mult, ALU.add)
+        ts(V("j1", 0, KC), V("e2", 0, KC), -1.0, ALU.mult, float(M), ALU.add)
+        qz, sz, qb, sb = [n + str(t) for n in ("qz", "sz", "qb", "sb")]
+        a = K * second
+        pick(V(qz, a, a + K), V(sz, a, a + K), V(qc, 0, M), V(sp, 0, M), V("j1", 0, KC))
+        swap(qz, sz, a, a, K - a, near, "ac%d" % t, "as%d" % t)
         rho, itself = V("rho", 0, 16), V("rho", 16, 32)
         for p in (0, 64):
-            act(on(rho, p), on(last, mine), AF.Identity, scale=on(GSCL, mine), bias=float(GM))
-        act(V("inv", 0, 96), V("bg"))
-        for j in range(NV):
-            if 0 < j < NV - 1:
-                same(j + 1, 0, HM)
-            scan(V("so", M * j, M * j + M), EE(j, 0, M), EE(j, M, HM), ALU.add, ALU.add)
-            if j == 4:
-                tt(ACC(0), ACC(0), ACC(4), ALU.add)
-            if j == NV - 3:
-                for b in (0, 1):
-                    halves(Z("aci", NS // 2 * b, NS // 2 * b + NS // 2), V("acc", 0, NS // 2), ALU.add, 32 * b, 32)
-            if j == NV - 2:
-                ts(Z("roti", 0, 2 * NS, 2), Z("aci", 0, NS), 2047, ALU.bitwise_and)
-                ts(Z("roti", 1, 2 * NS, 2), Z("aci", 0, NS), 11, ALU.logical_shift_right)
-        cp(Z("rot", 0, 2 * NS), Z("roti", 0, 2 * NS))
-        for b in (0, 1):
-            halves(Z("rot", 2 * NS + NV * b, 2 * NS + NV * b + NV), V("so", M - 1, NV * M, M), ALU.add, 32 * b, 32)
+            act(on(rho, p), on(V("sc", 15, M, 16), mine), AF.Identity, scale=on(GSCL, mine), bias=float(GM))
+        if not t:
+            unpacking(0)
+            unpacking(1)
         cp(V("lro"), rho)
         tt(itself, rho, V("sn"), ALU.is_equal)
-        for j in range(1, NTS + 1):
-            act(Z("trs", 64 * j, 64 * j + 64), Z("rot"), AF.Sign, bias=-0.5 - j, accum=Z("ypd", j, j + 1))
-        act(Z("szs"), Z("rot", 0, 32), AF.Relu, scale=2.0, bias=-2.0)
-        for j in range(NTS + 1, SMAX):
-            ts(Z("cm", 32 * j, 32 * j + 32), Z("rot", 0, 32), float(j + 1), ALU.is_ge, 2.0, ALU.mult)
-        for j in range(NTS + 1, SMAX):
-            red(Z("ypd", j, j + 1), Z("cm", 32 * j, 32 * j + 32), ALU.add)
         act(itself, itself, scale=2.0 * GM - 1)
         act(V("rtf"), V("idn"), off=V("lro"))
         row = V("rtf", 0, M, 1, 0, 1)
         dmas("drt", [("y", T.rt[0:1, M * t:M * t + M], A(row), [], [row])])
-        tr(Z("ytr", 0, 32), Z("ypd"))
-        scan(Z("in2", 1, 65), Z("dt"), Z("ytr"), ALU.mult, ALU.add)
-        scan(back(Z("sfx", 16, 48)), Z("dt", 0, 32), back(Z("ytr", 0, 32)), ALU.mult, ALU.add)
-        short, before = Z("in2", 33, 34), Z("in2", 0, 32)
-        tr(Z("cs"), Z("in2", 33, 65))
-        ts(Z("x3", 0, 32), before, short, ALU.min, 0.5, ALU.mult)
-        ts(Z("x3", 64, 96), before, short, ALU.max, 0.5, ALU.mult)
-        ts(Z("x3", 32, 64), Z("sfx", 16, 48), short, ALU.min, 0.5, ALU.mult)
-        act(Z("trs", NM, NM + 32), Z("cs"), AF.Sign, scale=-1.0, accum=Z("thr", 0, 1))
+        ts(V("km", 0, 32), V("kr", 0, 32), MS(pair[1], 3, 4), ALU.subtract, MS(pair[0], 2, 3), ALU.min)
         tt(itself, itself, rho, ALU.max)
-        tr(Z("c3"), Z("x3"))
-        gt, eq, thr = Z("ge", 0, 32), Z("ge", 32, 64), Z("thr", 0, 1)
-        ts(gt, Z("szs"), -30.0, ALU.add, thr, ALU.is_gt)
-        ts(eq, Z("szs"), -30.0, ALU.add, thr, ALU.is_equal)
-        red(COL(2), Z("c3", 0, 32), ALU.max)
-        red(COL(3), Z("c3", 32, 64), ALU.max)
-        red(COL(4), Z("c3", 64, 96), ALU.min)
-        tt(Z("hh", 0, 32), gt, Z("nrest"), ALU.mult)
-        scan(Z("inc", 0, 32), Z("dr"), gt, ALU.add, ALU.add, COL(2))
-        act(Z("hh", 32, 64), eq, AF.Identity, scale=-BIG - 1.0, bias=COL(3))
-        scan(Z("inc", 32, 64), Z("db"), eq, ALU.add, ALU.add, COL(4))
+        tr(V("kt", 0, 32), V("km", 0, 32))
         cp(V("lrm"), itself)
-        for e in (0, 1):
-            tt(Z("je", 32 * e, 32 * e + 32), Z("inc", 32 * e, 32 * e + 32), Z("hh", 32 * e, 32 * e + 32), ALU.add)
+        red(V("kk", 4, 5), V("kt", 0, 32), ALU.max)
+        for d in range(N):
+            down = d in (pair[1], pair2[1])
+            act(V("um", 2 * d, 2 * d + 2), MS(d, 0, 2), AF.Identity, scale=1.0 - 2.0 * down, bias=float(K * (d in pair2) + (K - 1) * down))
+        for d in range(N):
+            c = [MS(e, 2, 3) if e < d else MS(e, 3, 4) for e in range(N) if e != d]
+            ts(V("kw", d, d + 1), c[0], c[1], ALU.add, c[2], ALU.add)
+            if d == 0:
+                ts(V("fl", 0, KC), V("ki", 0, KC), V("kk", 4, 5), ALU.is_gt, float(K), ALU.mult)
+            if d == 2:
+                tt(V("fl", 8, 8 + KC), V("fl", 0, KC), V("ki", 0, KC), ALU.add)
+        for d in range(N):
+            ts(V("km", 32 + 32 * d, 64 + 32 * d), V("kr", 32, 64), V("kw", d, d + 1), ALU.subtract, MS(d, 2, 3), ALU.min)
+            if d == 0:
+                cp(V("j2", 0, KC), V("fl", 8, 8 + KC))
+        tr(V("kt", 32, 160), V("km", 32, 160))
         if not t:
-            unpacking(0)
+            unpacking(2)
+        for d in range(N):
+            red(V("kk", d, d + 1), V("kt", 32 + 32 * d, 64 + 32 * d), ALU.max)
+        pick(V(qb, 0, K), V(sb, 0, K), V(qz), V(sz), V("j2", 0, KC))
+        swap(qb, sb, 0, K, K, far, "bc%d" % t, "bs%d" % t)
+        for d in range(N):
+            ts(V("um", 8 + 2 * d, 10 + 2 * d), MS(d, 0, 2), V("kk", d, d + 1), ALU.subtract, float(NM), ALU.mult)
+        if not t:
+            unpacking(3)
+        tt(V("uu", 0, 8), V("um", 0, 8), V("um", 8, 16), ALU.max)
+        for s in range(4):
+            for b in range(4):
+                move("vs"[(b + s) % 2], on(V("xz", 32 * s, NM, H), 32 * b, 32), on(V("uu", 0, 8), 32 * s, 32))
         for e in range(4):
-            tt(Z("zz", 16 * e, 16 * e + 16), Z("je", 16 * (e // 2), 16 * (e // 2) + 16), Z("je", 32 + 16 * (e // 2), 48 + 16 * (e // 2)), ALU.min)
-        tt(Z("zz", 64, 96), Z("je", 0, 32), Z("je", 32, 64), ALU.min)
-        tr(Z("zt", 0, 64), Z("zz", 0, 64))
-        act(Z("um", 0, 32), Z("zz", 64, 96), AF.Identity, bias=Z("um", 72, 73))
-        act(Z("um", 32, 64), Z("zz", 64, 96), AF.Identity, scale=float(NM), bias=(0.5 - K) * NM)
-        for b in range(4):
-            cp(on(V("sll"), 32 * b, 32), Z("zt", 32 * (b // 2) + 8 * rank, 32 * (b // 2) + 8 * rank + 8))
-        tt(Z("zz", 64, 96), Z("um", 0, 32), Z("um", 32, 64), ALU.max)
-        emit("v", lambda: g.vector.tensor_copy(ind(V("inv"), V("sll")), A(V("io2"))), [V("inv")], [V("io2"), V("sll")])
-        tr(Z("zt", 64, 96), Z("zz", 64, 96))
-        for b in range(4):
-            act(on(V("xz", 0, NM, 32), 32 * b, 32), Z("zt", 64, 96))
-        scan(V("scf", 0, K), V("d0", 0, K), V("inv", 0, K), ALU.mult, ALU.add)
-        jm = V("jm", 0, 5)
-        for p in (0, 64):
-            halves(on(jm, p), V("scf", 15, K, 16), ALU.min)
-        if not t:
-            unpacking(1)
-        ts(V("j1", 0, 5), jm, SCL, ALU.mult, M - 1.0, ALU.min)
-        ts(V("j2", 0, 5), jm, SCL, ALU.mult)
-        repeated(0)
-        qa, sa, qz, sz, qb, sb = [n + str(t) for n in ("qa", "sa", "qz", "sz", "qb", "sb")]
-        pick(V(qa), V(sa), V(qc, 0, M), V(sp, 0, M), V("j1", 0, 5))
-        swap(qa, sa, qz, sz, M, near, "ac%d" % t, "as%d" % t)
-        for e in (1, 2, 3):
             repeated(e)
         for k in range(8):
             tr(grun("fs", k), V("xb", H * k, H * k + H))
-        if not t:
-            unpacking(2)
-            unpacking(3)
-        cp(V("rs"), V("fs"), V("lrm"))
-        pick(V(qb, 0, K), V(sb, 0, K), V(qz), V(sz), V("j2", 0, 5))
-        swap(qb, sb, qb, sb, K, far, "bc%d" % t, "bs%d" % t)
-        scan(V("sc", 0, M), V("d0", 0, M), V("rs"), ALU.mult, ALU.add)
-        if not final:
-            tr(V("rx"), V("rs"))
+        cp(V("rs", 0, H), V("fs"), V("lrm", 0, 8))
+        act(V("rs", H, M), V("fs"), off=V("lrm", 8, 16))
         if not t:
             pick(V("qr", 128, 384), V("sr", 128, 384), V("qu"), V("su"), V("cu", 8, 24))
             height(7, t + 1, qc, sp, 0, M)
+        scan(V("sc", 0, M), V("d0", 0, M), V("rs"), ALU.mult, ALU.add)
+        if not final:
+            tr(V("rx"), V("rs"))
         me, at = V("rho", 16, 32), V("sc", 15, M, 16)
         ts(V("pl"), at, SCL, ALU.mult, 2.0 * K - 1, ALU.min)
         ts(me, at, SCL, ALU.mult, 2 * K - 0.5, ALU.is_lt)

@@ -9,6 +9,7 @@ NM = N * M
 HM = NM // 2
 H = M // 2
 KC = K // 16
+PAD = 16
 SEG = 65
 RUNS = ((-2048, 8), (-1024, 4), (-512, 2), (-256, 1), (128, 1), (256, 2), (512, 4), (1024, 8))
 UNIT = 1.0 / 4096
@@ -22,9 +23,9 @@ C8, U8, F32, B16, I32, U16 = "float8_e4m3fn_x4", "uint8", "float32", "bfloat16",
 WIDTHS = {
     B16: {"xt": 4 * M, "ut": 512, "wt": 512, "one": 528, "et": 2 * 528, "d0": 512, "dw": NM,
           "xb": NM, "xz": NM, "d32": M, "cw": NM, "ca": 384, "cb": HM,
-          "fs": 2 * GM, "fa": 2 * WM, "fb": 2 * WM, "sc": HM, "rs": M, "rx": M, "hb": 4 * M,
-          "fr": HM, "ee": 4 * HM, "so": 4 * M, "cv": 16, "ea": 2 * (H + 32), "pb": H + 64, "ps": 64, "dd": 336, "di": 336, "de": 336,
-          "sg": 3 * M, "kr": 64, "km": 160, "kt": 160, "kw": 16, "uu": 32},
+          "fs": 2 * GM, "fa": 2 * WM, "fb": 2 * WM, "sc": HM, "rs": M, "hb": 4 * M,
+          "fr": HM, "ee": 4 * HM, "so": 4 * M, "cv": 16, "ea": 4 * (H + 32), "pb": 2 * H + 64, "ps": 64, "dd": 336, "di": 336, "de": 336,
+          "sg": 2 * M, "kr": 64, "km": 160, "kt": 160, "kw": 16, "uu": 16, "iv": H, "iw": H, "d8": H},
     C8: {"qu": 128, "qw": 128, "qr": 384, "qe": 512},
     U8: {"su": 128, "sw": 128, "sr": 384, "se": 512},
     F32: {"i128": H, "idn": 2 * GM, "rtf": M, "xe": NM, "fh": NM, "ra": 384, "rb": HM,
@@ -38,7 +39,7 @@ for _d, _parts in WIDTHS.items():
         SCRATCH[_n] = ("sbuf", [128, _w], _d)
 SMALL = {
     "zf": (F32, {"d16": 16, "d17": 16, "cf": 32, "sn": 16, "ki": 16, "x0": 32, "m1": 16, "neq": 32, "lost": 32, "key": 32, "b2": 16,
-                 "nn": 4, "fq": 4, "aa": 4, "want": 16, "e1": 8, "e2": 8, "kk": 8, "fl": 16, "um": 16, "mh": 32,
+                 "nn": 4, "fq": 4, "aa": 4, "want": 16, "e1": 8, "e2": 8, "kk": 8, "fl": 16, "um": 16, "sgn": 32, "px": 16, "pd": 16,
                  "rho": 32, "mx": 8, "mx1": 8, "xo": 8}),
     "zi": (I32, {"ip": 16}),
     "zu": (U16, {"crep": 32, "cu": 24, "lro": 16, "lrm": 16, "j1": 6, "j2": 6, "pl": 16, "kl": 16}),
@@ -53,7 +54,7 @@ for _b, (_d, _parts) in SMALL.items():
 for _t in range(R):
     SCRATCH["xh%d" % _t] = ("sbuf", [128, 32], F32)
     SCRATCH["ms%d" % _t] = ("sbuf", [128, 32], B16)
-    for _n, _w in (("z", 2 * K), ("b", 2 * K), ("p", M)):
+    for _n, _w in (("z", 2 * K), ("b", PAD + 2 * K), ("p", M)):
         SCRATCH["q%s%d" % (_n, _t)] = ("sbuf", [128, _w], C8)
         SCRATCH["s%s%d" % (_n, _t)] = ("sbuf", [128, _w], U8)
 for _t in range(R + 1):
@@ -261,15 +262,17 @@ def rank_program(g, core, T, topo):
     pair2 = [d for d in range(N) if d not in pair]
     second = pair.index(rank)
     far = pair2[second]
+    seconds = (pair[1], pair2[1])
+    stand = [PAD + K * ((d in pair) != (0 in pair)) for d in range(N)]
 
-    def swap(q, s, a, at, lands, d, semc, sems):
+    def swap(q, s, a, lands, d, semc, sems):
         dst = T.cores[d]
         rid, pid = topo.addr(dst)[:2]
         mask, n = topo.mask(core, dst), len(topo.engines(core, dst))
         use("g", [V(q, a, a + K)], [])
-        g.remote_dma(A(V(q, at, at + K)).bitcast(dt.uint8), A(V(q, a, a + K)).bitcast(dt.uint8), T.sem[semc], T.sem.loc, pid, rid, mask)
+        g.remote_dma(A(V(q, a, a + K)).bitcast(dt.uint8), A(V(q, a, a + K)).bitcast(dt.uint8), T.sem[semc], T.sem.loc, pid, rid, mask)
         use("g", [V(s, a, a + K)], [])
-        g.remote_dma(A(V(s, at, at + K)), A(V(s, a, a + K)), T.sem[sems], T.sem.loc, pid, rid, mask)
+        g.remote_dma(A(V(s, a, a + K)), A(V(s, a, a + K)), T.sem[sems], T.sem.loc, pid, rid, mask)
         cnt["loc"] = cnt.get("loc", 0) + 2 * n
         arrives(semc, n, [V(q, lands, lands + K)])
         arrives(sems, n, [V(s, lands, lands + K)])
@@ -393,12 +396,16 @@ def rank_program(g, core, T, topo):
         if d == rank:
             fill(V("xz", HM, NM), 0.0)
             fill(V("xk"), 0.0)
+            pick(V("qr", 128, 384), V("sr", 128, 384), V("qu"), V("su"), V("cu", 8, 24))
 
     def tables():
         act(V("one"), V("dw", 0, 528), AF.Identity, scale=0.0, bias=1.0)
-        act(V("ea"), V("dw", 0, 2 * (H + 32)))
-        act(V("dd", 0, SEG * KC, SEG), V("dw", 0, KC))
-        act(V("mh"), V("dw", 0, 32), AF.Identity, scale=0.0, bias=-0.5)
+        for k in range(4):
+            const(V("ea", (H + 32) * k + H, (H + 32) * (k + 1)), 0)
+        const(V("dd", 0, SEG * KC, SEG), 0)
+        const(V("d8"), 1)
+        const(V("d8", 0, H, 8), 0)
+        const(V("pd", 0, 16, 2), -8)
         for k in range(8):
             iota(grun("idn", k), [[1, H]], H * k, 0)
         for e in (0, 1):
@@ -427,7 +434,9 @@ def rank_program(g, core, T, topo):
         lambda: tt(WSCL, GSCL, CF(23), ALU.mult),
         lambda: own_codes(1),
         lambda: ts(V("sn"), V("sn"), SCOL, ALU.add),
-        lambda: ts(V("want", 0, KC), V("ki", 0, KC), 1.0 - 2.0 * second, ALU.mult, (K - 1.0) * second, ALU.add),
+        lambda: ts(V("want", 0, KC), V("ki", 0, KC), (1.0 - K) * second, ALU.add),
+        lambda: ts(CF(26), LCOL, 16.0, ALU.is_lt, 12.0, ALU.mult),
+        lambda: ts(CF(27), LCOL, 16.0, ALU.is_lt, 4.0, ALU.mult),
         lambda: ts(V("di", SEG - 1, SEG * KC, SEG), RI(KC), 0.0, ALU.mult, CF(22), ALU.add),
         lambda: ts(on(V("fq"), 0), on(V("nn"), 0), -1.0 / M, ALU.mult),
         lambda: ts(back(on(V("fq"), 64)), on(V("nn"), 64), -1.0 / M, ALU.mult),
@@ -435,6 +444,8 @@ def rank_program(g, core, T, topo):
         lambda: ts(V("di", SEG - 1, SEG * KC, SEG), V("di", SEG - 1, SEG * KC, SEG), H - 31.0, ALU.add),
         lambda: ts(CF(24), LCOL, 0.5 / M - 1.0, ALU.add),
         lambda: ts(CF(25), LCOL, 0.5 / M, ALU.add),
+        lambda: ts(V("pd", 1, 16, 2), V("dw", 0, 8), -8.0, ALU.add, CF(26), ALU.add),
+        lambda: ts(CF(27), CF(27), 0.5, ALU.add),
         lambda: own_place(0),
         lambda: own_place(1),
     ]
@@ -467,6 +478,7 @@ def rank_program(g, core, T, topo):
         if not t:
             tr(V("cb", 0, 3 * H), V("ca"))
             tables()
+            height(7, 1, qc, sp, 0, M)
         tr(V("rb", 0, H), V("ra", 0, H))
         tr(V("rb", H, 2 * H + 32), V("ra", H, 2 * H + 32))
         tr(V("rb", 2 * H + 32, 3 * H), V("ra", 2 * H + 32, 3 * H))
@@ -529,151 +541,181 @@ def rank_program(g, core, T, topo):
         count = lambda j: scan(V("so", M * j, M * j + M), EE(j, 0, M), EE(j, M, HM), ALU.add, ALU.add)
         for j in range(4):
             same(j, 0, M)
-        for j in range(4):
+        for j in range(3):
             same(j, M, HM)
-            if j:
-                count(j - 1)
-        count(3)
+        count(0)
+        same(3, M, HM)
+        for j in (1, 2, 3):
+            count(j)
+        blk = RK.index(rank)
+        mine, at0 = 64 * (blk // 2), M * (blk % 2)
+        scan(on(V("sc", 0, M), mine), on(V("d0", 0, M), mine), on(V("fr", at0, at0 + M), mine), ALU.mult, ALU.add)
+        rho, itself = V("rho", 0, 16), V("rho", 16, 32)
+        for p in (0, 64):
+            act(on(rho, p), on(V("sc", 15, M, 16), mine), AF.Identity, scale=on(GSCL, mine), bias=float(GM))
         ends = V("so", M - 1, 4 * M, M)
         halves(on(V("aa"), 0), ends, ALU.add)
         halves(back(on(V("aa"), 64)), ends, ALU.add)
+        if not t:
+            unpacking(0)
         tt(V("xk", 0, H, 32), V("aa"), V("fq"), ALU.add)
         for b in range(4):
             tt(on(V("xk", H, M, 32), 32 * b, 32), on(V("aa"), 32 * (b ^ 1), 32), on(V("fq"), 32 * (b ^ 1), 32), ALU.add)
-        for h in (0, 1):
-            scan(V("xr", *half[h]), V("d32", 0, H), V("xk", *half[h]), ALU.mult, ALU.add)
-        for h in (0, 1):
-            tr(V("kf", *half[h]), V("xr", *half[h]))
+        keys = lambda h: scan(V("xr", *half[h]), V("d32", 0, H), V("xk", *half[h]), ALU.mult, ALU.add)
+        keys(0)
+        cp(V("lro"), rho)
+        tt(itself, rho, V("sn"), ALU.is_equal)
+        keys(1)
+        act(V("rtf"), V("idn"), off=V("lro"))
+        row = V("rtf", 0, M, 1, 0, 1)
+        dmas("drt", [("y", T.rt[0:1, M * t:M * t + M], A(row), [], [row])])
+        tr(V("kf", *half[0]), V("xr", *half[0]))
+        ts(itself, itself, 2.0 * GM - 1, ALU.mult)
+        tr(V("kf", *half[1]), V("xr", *half[1]))
         ms = "ms%d" % t
         MS = lambda d, a, b: V(ms, 8 * d + a, 8 * d + b)
-        signs = lambda k, col: act(V("sg", M * k, M * k + M), V("kf"), AF.Sign, scale=-1.0, bias=col, accum=ACC(k))
-        signs(0, V("xk", 32, 33))
+        EA = lambda i, h, n: V("ea", (H + 32) * (2 * i + h), (H + 32) * (2 * i + h) + n)
+        for k in (0, 1):
+            act(V("sg", M * k, M * k + M), V("kf"), AF.Sign, scale=-1.0, bias=CF(24 + k), accum=ACC(k))
         for h in (0, 1):
-            ts(V("ea", (H + 32) * h, (H + 32) * h + H), V("kf", *half[h]), V("xk", 0, 1), ALU.is_gt)
-        act(V("pb", H + 32, H + 64), V("mh"), AF.Identity, scale=ACC(0), bias=(M - 1) / 2)
-        scan(V("pb", 0, H + 32), V("ea", 0, H + 32), V("ea", H + 32, 2 * H + 64), ALU.add, ALU.add)
-        signs(1, CF(24))
-        blk = RK.index(rank)
-        mine, at0 = 64 * (blk // 2), M * (blk % 2)
+            for i in (0, 1):
+                ts(EA(i, h, H), V("kf", *half[h]), V("xk", 32 * i, 32 * i + 1), ALU.is_gt, 1.0 - 2.0 * second, ALU.mult)
+        act(MS(rank, 2, 4), V("acc", 0, 2), AF.Identity, scale=-0.5, bias=(M - 1) / 2)
+        tt(itself, itself, rho, ALU.max)
+        scan(V("pb", 0, H + 32), EA(0, 0, H + 32), EA(0, 1, H + 32), ALU.add, ALU.add)
+        scan(back(V("pb", H + 32, 2 * H + 64)), EA(1, 0, H + 32), EA(1, 1, H + 32), ALU.add, ALU.add)
+        cp(V("lrm"), itself)
+        if not t:
+            unpacking(1)
+        if second:
+            ts(MS(rank, 0, 2), V("pb", H, H + 64, 32), 0.5 - K, ALU.max, float(stand[rank] + K - 1), ALU.add)
+        else:
+            ts(MS(rank, 0, 2), V("pb", H, H + 64, 32), K - 0.5, ALU.min, float(stand[rank]), ALU.add)
         tr(V("ps"), V("pb", H, H + 64))
+        spread(lambda d: MS(d, 0, 4), "m%d_" % t + "%d", [near, far] + [d for d in pair2 if d != far])
+        flips = [d for d in range(1, N) if (d in seconds) != (d - 1 in seconds)]
+        for i, d in enumerate(flips):
+            o = V("sgn", 16 * min(i, 1), 16 * min(i, 1) + 16)
+            ts(o, rho, place(M * d) - 0.5, ALU.is_lt, 2.0, ALU.mult)
+            if i:
+                ts(o, o, -1.0, ALU.add)
+                tt(V("sgn", 0, 16), V("sgn", 0, 16), o, ALU.mult)
+            elif len(flips) > 1:
+                ts(o, o, -1.0, ALU.add, SCL, ALU.mult)
+        if not t:
+            unpacking(2)
         for k in range(KC):
             out = V("dd", SEG * k + 1, SEG * k + SEG)
             if k < 3:
                 ts(out, V("ps"), V("want", k, k + 1), ALU.not_equal, float(NM), ALU.mult)
             else:
                 act(out, V("ps"), AF.Abs, scale=float(NM), bias=V("want", 8 + k, 9 + k))
-        signs(2, CF(25))
+        if len(flips) == 1:
+            ts(V("sgn", 0, 16), V("sgn", 0, 16), -1.0, ALU.add, SCL, ALU.mult)
+        if not t:
+            unpacking(3)
         scan(V("de", 0, SEG * KC), V("dd", 0, SEG * KC), V("di", 0, SEG * KC), ALU.min, ALU.add)
-        act(MS(rank, 0, 2), V("pb", H, H + 64, 32))
-        act(MS(rank, 2, 4), V("acc", 1, 3), AF.Identity, scale=-0.5, bias=(M - 1) / 2)
-        spread(lambda d: MS(d, 0, 4), "m%d_" % t + "%d", [near, far] + [d for d in pair2 if d != far])
         for p in (0, 64):
             halves(on(V("e1", 0, KC), p), V("de", SEG - 1, SEG * KC, SEG), ALU.min)
+        if not t:
+            tr(V("ho"), bank(7, M))
         for b in range(4):
             tt(on(V("e2", 0, KC), 32 * b, 32), on(V("e1", 0, KC), 32 * b, 32), on(V("e1", 0, KC), 32 * (b ^ 1), 32), ALU.min)
-        scan(on(V("sc", 0, M), mine), on(V("d0", 0, M), mine), on(V("fr", at0, at0 + M), mine), ALU.mult, ALU.add)
         ts(V("j1", 0, KC), V("e2", 0, KC), -1.0, ALU.mult, float(M), ALU.add)
         qz, sz, qb, sb = [n + str(t) for n in ("qz", "sz", "qb", "sb")]
         a = K * second
         pick(V(qz, a, a + K), V(sz, a, a + K), V(qc, 0, M), V(sp, 0, M), V("j1", 0, KC))
-        swap(qz, sz, a, a, K - a, near, "ac%d" % t, "as%d" % t)
-        rho, itself = V("rho", 0, 16), V("rho", 16, 32)
-        for p in (0, 64):
-            act(on(rho, p), on(V("sc", 15, M, 16), mine), AF.Identity, scale=on(GSCL, mine), bias=float(GM))
-        if not t:
-            unpacking(0)
-            unpacking(1)
-        cp(V("lro"), rho)
-        tt(itself, rho, V("sn"), ALU.is_equal)
-        act(itself, itself, scale=2.0 * GM - 1)
-        act(V("rtf"), V("idn"), off=V("lro"))
-        row = V("rtf", 0, M, 1, 0, 1)
-        dmas("drt", [("y", T.rt[0:1, M * t:M * t + M], A(row), [], [row])])
-        ts(V("km", 0, 32), V("kr", 0, 32), MS(pair[1], 3, 4), ALU.subtract, MS(pair[0], 2, 3), ALU.min)
-        tt(itself, itself, rho, ALU.max)
-        tr(V("kt", 0, 32), V("km", 0, 32))
-        cp(V("lrm"), itself)
-        red(V("kk", 4, 5), V("kt", 0, 32), ALU.max)
-        for d in range(N):
-            down = d in (pair[1], pair2[1])
-            act(V("um", 2 * d, 2 * d + 2), MS(d, 0, 2), AF.Identity, scale=1.0 - 2.0 * down, bias=float(K * (d in pair2) + (K - 1) * down))
-        for d in range(N):
-            c = [MS(e, 2, 3) if e < d else MS(e, 3, 4) for e in range(N) if e != d]
-            ts(V("kw", d, d + 1), c[0], c[1], ALU.add, c[2], ALU.add)
-            if d == 0:
-                ts(V("fl", 0, KC), V("ki", 0, KC), V("kk", 4, 5), ALU.is_gt, float(K), ALU.mult)
-            if d == 2:
-                tt(V("fl", 8, 8 + KC), V("fl", 0, KC), V("ki", 0, KC), ALU.add)
-        for d in range(N):
-            ts(V("km", 32 + 32 * d, 64 + 32 * d), V("kr", 32, 64), V("kw", d, d + 1), ALU.subtract, MS(d, 2, 3), ALU.min)
-            if d == 0:
-                cp(V("j2", 0, KC), V("fl", 8, 8 + KC))
-        tr(V("kt", 32, 160), V("km", 32, 160))
-        if not t:
-            unpacking(2)
-        for d in range(N):
-            red(V("kk", d, d + 1), V("kt", 32 + 32 * d, 64 + 32 * d), ALU.max)
-        pick(V(qb, 0, K), V(sb, 0, K), V(qz), V(sz), V("j2", 0, KC))
-        swap(qb, sb, 0, K, K, far, "bc%d" % t, "bs%d" % t)
-        for d in range(N):
-            ts(V("um", 8 + 2 * d, 10 + 2 * d), MS(d, 0, 2), V("kk", d, d + 1), ALU.subtract, float(NM), ALU.mult)
-        if not t:
-            unpacking(3)
-        tt(V("uu", 0, 8), V("um", 0, 8), V("um", 8, 16), ALU.max)
-        for s in range(4):
-            for b in range(4):
-                move("vs"[(b + s) % 2], on(V("xz", 32 * s, NM, H), 32 * b, 32), on(V("uu", 0, 8), 32 * s, 32))
-        for e in range(4):
-            repeated(e)
-        for k in range(8):
-            tr(grun("fs", k), V("xb", H * k, H * k + H))
-        cp(V("rs", 0, H), V("fs"), V("lrm", 0, 8))
-        act(V("rs", H, M), V("fs"), off=V("lrm", 8, 16))
-        if not t:
-            pick(V("qr", 128, 384), V("sr", 128, 384), V("qu"), V("su"), V("cu", 8, 24))
-            height(7, t + 1, qc, sp, 0, M)
-        scan(V("sc", 0, M), V("d0", 0, M), V("rs"), ALU.mult, ALU.add)
-        if not final:
-            tr(V("rx"), V("rs"))
-        me, at = V("rho", 16, 32), V("sc", 15, M, 16)
-        ts(V("pl"), at, SCL, ALU.mult, 2.0 * K - 1, ALU.min)
-        ts(me, at, SCL, ALU.mult, 2 * K - 0.5, ALU.is_lt)
-        if not final:
-            ts(V("mx1"), V("rx", 0, M, 32), 2 * K - 0.5, ALU.is_ge)
-            ts(V("mx"), V("rx", 0, M, 32), 2 * K - 0.5, ALU.is_lt)
-        if not t:
-            tr(V("ho"), bank(7, M))
-        ts(me, me, float(M), ALU.mult)
+        swap(qz, sz, a, K - a, near, "ac%d" % t, "as%d" % t)
         unpack = [(V("qe", 128 * b, 128 * b + 128), V("se", 128 * b, 128 * b + 128)) for b in range(4)]
-        qp, pp = "qp%d" % t, "sp%d" % t
         for h in (0, 1):
             for b in range(4):
                 mm(bank(4 * h + b, H), *unpack[b], V(qc, *half[h]), V(sp, *half[h]), True, False)
+        for d in [rank, near, far] + [d for d in pair2 if d != far]:
+            act(V("uu", 2 * d, 2 * d + 2), MS(d, 0, 2))
+        spaced = lambda by, s, b: move(by, on(V("xz", 32 * s, NM, H), 32 * b, 32), on(V("uu", 0, 8), 32 * s, 32))
+        ts(V("km", 0, 32), V("kr", 0, 32), MS(pair[1], 3, 4), ALU.subtract, MS(pair[0], 2, 3), ALU.min)
+        for s in range(4):
+            for b in (0, 1):
+                spaced("s", s, b)
+        tr(V("kt", 0, 32), V("km", 0, 32))
+        red(V("kk", 4, 5), V("kt", 0, 32), ALU.max)
+        ts(V("fl", 0, KC), V("ki", 0, KC), V("kk", 4, 5), ALU.is_gt, float(K), ALU.mult)
+        for s in range(4):
+            spaced("v", s, 2)
+        tt(V("fl", 8, 8 + KC), V("fl", 0, KC), V("ki", 0, KC), ALU.add)
+        for s in range(4):
+            spaced("v", s, 3)
+        cp(V("j2", 0, KC), V("fl", 8, 8 + KC))
+        for d in range(N):
+            c = [MS(e, 2, 3) if e < d else MS(e, 3, 4) for e in range(N) if e != d]
+            ts(V("kw", d, d + 1), c[0], c[1], ALU.add, c[2], ALU.add)
+        repeated(0)
+        repeated(1)
+        a = stand[rank]
+        pick(V(qb, a, a + K), V(sb, a, a + K), V(qz), V(sz), V("j2", 0, KC))
+        swap(qb, sb, a, stand[far], far, "bc%d" % t, "bs%d" % t)
+        repeated(2)
+        repeated(3)
+        for k in range(8):
+            tr(grun("fs", k), V("xb", H * k, H * k + H))
+        for d in range(N):
+            ts(V("km", 32 + 32 * d, 64 + 32 * d), V("kr", 32, 64), V("kw", d, d + 1), ALU.subtract, MS(d, 2, 3), ALU.min)
+        act(V("rs", H, M), V("fs"), off=V("lrm", 8, 16))
+        cp(V("rs", 0, H), V("fs"), V("lrm", 0, 8))
+        tr(V("kt", 32, 160), V("km", 32, 160))
+        scan(V("sc", 0, H), V("d0", 0, H), V("rs", 0, H), ALU.mult, ALU.add)
+        scan(V("sc", H, M), V("d0", 0, H), V("rs", H, M), ALU.mult, ALU.add)
+        for d in range(N):
+            red(V("kk", d, d + 1), V("kt", 32 + 32 * d, 64 + 32 * d), ALU.max)
+        at, us, me = V("sc", 15, M, 16), V("um", 0, 16), V("rho", 16, 32)
+        ts(V("pl"), at, SCL, ALU.mult, float(PAD + 2 * K - 1), ALU.min)
+        tt(us, at, V("sgn", 0, 16), ALU.mult)
+        qp, pp = "qp%d" % t, "sp%d" % t
+        lows = [-(stand[d] + K - 1.0) if d in seconds else float(stand[d]) for d in range(N)]
+        for d in (0, 1):
+            ts(V("iv", d, H, 8), us, lows[d] - 0.25, ALU.is_ge, -1.0, ALU.add)
         codes(V(qp, *half[0]), V(qb), V("pl", 0, 8))
-        tt(me, me, V("ki"), ALU.add)
-        if not final:
-            tt(V("xo"), V("ho", 0, M, 32), V("mx1"), ALU.mult)
         codes(V(qp, *half[1]), V(qb), V("pl", 8, 16))
         for h in (0, 1):
             move("sv"[h], V(pp, *half[h]), V(sb), V("pl", 8 * h, 8 * h + 8))
-        cp(V("kl"), me)
         for h in (0, 1):
             for b in range(4):
                 mm(bank(4 * h + b, H), *unpack[b], V(qp, *half[h]), V(pp, *half[h]), False, True)
+        for d in (2, 3):
+            ts(V("iv", d, H, 8), us, lows[d] - 0.25, ALU.is_ge, -1.0, ALU.add)
+        for d in range(N):
+            ts(V("iv", 4 + d, H, 8), us, lows[d], ALU.subtract, V("kk", d, d + 1), ALU.is_lt)
+        member = V("iw", 7, H, 8)
         for b in range(8):
             src, out = bank(b, H), V("hb", 4 * H * (b // 4) + b % 4, 4 * H * (b // 4) + 4 * H, 4)
             if b % 2:
                 act(out, src, scale=0.5)
             else:
                 ts(out, src, 0.5, ALU.mult)
+            if b == 2:
+                scan(V("iw"), V("d8"), V("iv"), ALU.mult, ALU.add)
         for h in (0, 1):
             quant(V(qc, M + H * h, M + H * h + H), V(sp, M + H * h, M + H * h + H), V("hb", 4 * H * h, 4 * H * h + 4 * H))
             if not final:
                 height(h, t + 1, qc, sp, M + H * h, H)
+            if not h:
+                if not final:
+                    scan(V("px"), V("pd"), member, ALU.add, ALU.max)
+                ts(me, member, 0.5, ALU.is_gt, float(M), ALU.mult)
         nq, ns = "qc%d" % (t + 1), "scp%d" % (t + 1)
         if not final:
+            ts(V("mx1"), V("px", 1, 16, 2), CF(27), ALU.is_lt)
+            ts(V("mx"), V("px", 1, 16, 2), CF(27), ALU.is_gt)
+        tt(me, me, V("ki"), ALU.add)
+        if final:
+            cp(V("kl"), me)
+        else:
             for h in (0, 1):
                 tr(V("ht", *half[h]), bank(h, H))
+                if h:
+                    cp(V("kl"), me)
+                else:
+                    tt(V("xo"), V("ho", 0, M, 32), V("mx1"), ALU.mult)
                 for c in range(4 * h, 4 * h + 4):
                     out, new = V("xh%d" % (t + 1), 8 * rank + c, 8 * rank + c + 1), V("ht", 32 * c, 32 * c + 1)
                     if h and c % 2 == 0:

@@ -18,18 +18,19 @@ ALPHA = (4, 1)
 RK = (1, 2, 0, 3)
 GM, WM = 2048, 8192
 UP = float(2 ** 30)
+OPT = {"early": 0, "nv": 6, "nr": 1}
 C8, U8, F32, B16, I32, U16 = "float8_e4m3fn_x4", "uint8", "float32", "bfloat16", "int32", "uint16"
 
 WIDTHS = {
-    B16: {"xt": 4 * M, "ut": 512, "wt": 512, "one": 528, "et": 2 * 528, "d0": 512, "dw": NM,
+    B16: {"xt": 4 * M, "ut": 512, "wt": 512, "one": 528, "et": 2 * 528, "d0": M, "dw": 16,
           "xb": NM, "xz": NM, "d32": M, "cw": NM, "ca": 384, "cb": HM,
           "fs": 2 * GM, "fa": 2 * WM, "fb": 2 * WM, "sc": HM, "rs": M, "hb": 4 * M,
           "fr": HM, "ee": 4 * HM, "so": 4 * M, "cv": 16, "ea": 4 * (H + 32), "pb": 2 * H + 64, "ps": 64, "dd": 336, "di": 336, "de": 336,
-          "sg": 2 * M, "kr": 64, "km": 160, "kt": 160, "kw": 16, "uu": 16, "iv": H, "iw": H, "d8": H},
+          "sg": 2 * M, "kr": 32, "km": 160, "kt": 160, "ku": H, "iv": H, "iw": H, "d8": H, "d4": H, "lost": H, "key": H},
     C8: {"qu": 128, "qw": 128, "qr": 384, "qe": 512},
     U8: {"su": 128, "sw": 128, "sr": 384, "se": 512},
     F32: {"i128": H, "idn": 2 * GM, "rtf": M, "xe": NM, "fh": NM, "ra": 384, "rb": HM,
-          "ht": M, "ho": M, "acc": 16, "ys": M, "xk": M, "xr": M, "kf": M},
+          "ht": M, "ho": M, "acc": 16, "ys": M, "fq": M, "xr": M, "kf": M},
     U16: {"la": 32, "lb": 32, "nbl": 64, "lnb": 24},
     I32: {"iu": 24, "id16": 16, "nbe": 16},
 }
@@ -38,11 +39,11 @@ for _d, _parts in WIDTHS.items():
     for _n, _w in _parts.items():
         SCRATCH[_n] = ("sbuf", [128, _w], _d)
 SMALL = {
-    "zf": (F32, {"d16": 16, "d17": 16, "cf": 32, "sn": 16, "ki": 16, "x0": 32, "m1": 16, "neq": 32, "lost": 32, "key": 32, "b2": 16,
-                 "nn": 4, "fq": 4, "aa": 4, "want": 16, "e1": 8, "e2": 8, "kk": 8, "fl": 16, "um": 16, "sgn": 32, "px": 16, "pd": 16,
+    "zf": (F32, {"d16": 16, "d17": 16, "cf": 32, "sn": 16, "ki": 16, "x0": 16, "b2": 16,
+                 "nn": 4, "aa": 4, "ab": 4, "kw": 4, "low": 4, "want": 16, "e1": 8, "e2": 8, "kk": 8, "fl": 16, "um": 16, "sgn": 32, "px": 16, "pd": 16,
                  "rho": 32, "mx": 8, "mx1": 8, "xo": 8}),
     "zi": (I32, {"ip": 16}),
-    "zu": (U16, {"crep": 32, "cu": 24, "lro": 16, "lrm": 16, "j1": 6, "j2": 6, "pl": 16, "kl": 16}),
+    "zu": (U16, {"crep": 16, "cu": 24, "lro": 16, "lrm": 16, "j1": 6, "j2": 6, "pl": 16, "kl": 16}),
 }
 AT = {}
 for _b, (_d, _parts) in SMALL.items():
@@ -63,7 +64,7 @@ for _t in range(R + 1):
 
 SEMAPHORES = (["ev", "es", "et", "eg", "loc"] + ["nb%d" % d for d in range(N)] + ["%s%d_%d" % (k, t, d) for k in "hm" for t in range(R) for d in range(N)]
               + ["%s%d" % (k, t) for t in range(R) for k in ("ac", "as", "bc", "bs")]
-              + ["dx0", "dx1", "du", "dw", "dnb", "drt", "dout"])
+              + ["dx0", "dx1", "du", "dw", "dnb", "dm", "drt", "dout"])
 
 
 def place(n):
@@ -182,8 +183,8 @@ def rank_program(g, core, T, topo):
     def tt(out, a, b, op):
         emit("v", lambda: g.vector.tensor_tensor(A(out), A(a), A(b), op), [out], [a, b])
 
-    def red(out, in_, op):
-        emit("v", lambda: g.vector.tensor_reduce(A(out), A(in_), AxisListType.X, op), [out], [in_])
+    def red(out, in_, op, negate=False):
+        emit("v", lambda: g.vector.tensor_reduce(A(out), A(in_), AxisListType.X, op, negate=negate), [out], [in_])
 
     def scan(out, d0, d1, op0, op1, first=0.0):
         col = isinstance(first, tuple)
@@ -208,8 +209,10 @@ def rank_program(g, core, T, topo):
     def move(by, out, in_, off=None):
         if by == "v":
             cp(out, in_, off)
-        else:
+        elif by == "s":
             act(out, in_, off=off)
+        else:
+            select(out, in_, [[0, len(range(*out[1:4]))]], ALU.is_gt, 0.0, 1, 0)
 
     def iota(out, pattern, base, cm):
         if SCRATCH[out[0]][2] == I32:
@@ -240,30 +243,34 @@ def rank_program(g, core, T, topo):
     def halves(out, r, op, p=0, n=64):
         tt(out, on(r, p, n), on(r, 64 + p, n), op)
 
-    others = [(rank + k) % N for k in range(1, N)]
-    senders = others[::-1]
+    beside = lambda a, b: topo.same_plane(topo.chip(T.cores[a]), topo.chip(T.cores[b]))
+    turn = lambda r: sorted([(r + k) % N for k in range(1, N)], key=lambda d: beside(r, d))
+    others = turn(rank)
+    senders = sorted(others, key=lambda d: turn(d).index(rank))
     mask3 = 0xFFFF
     for d in others:
         mask3 &= topo.mask(core, T.cores[d])
     groups = bin(mask3).count("1")
 
-    def spread(piece, sem, order=others):
-        src = piece(rank)
+    def spread(piece, sem, order=others, src=None):
+        src = src or piece(rank)
         use("g", [src], [])
         ids = [DstId(rid=topo.addr(T.cores[d])[0], pnc=topo.addr(T.cores[d])[1]) for d in order]
-        g.remote_dma_fused([RemoteDMATransfer(dst_ids=ids, dma_engine_mask=mask3, remote_sem=T.sem[sem % rank], srcs=[A(src)], dsts=[A(src) for d in others])],
+        g.remote_dma_fused([RemoteDMATransfer(dst_ids=ids, dma_engine_mask=mask3, remote_sem=T.sem[sem % rank], srcs=[A(src)], dsts=[A(piece(rank)) for d in others])],
                            local_sem=T.sem.loc)
         cnt["loc"] = cnt.get("loc", 0) + groups
         for d in others:
             arrives(sem % d, groups, [piece(d)])
 
-    near = [d for d in others if topo.same_plane(topo.chip(core), topo.chip(T.cores[d]))][0]
+    near = [d for d in others if beside(rank, d)][0]
     pair = sorted([rank, near])
     pair2 = [d for d in range(N) if d not in pair]
     second = pair.index(rank)
     far = pair2[second]
     seconds = (pair[1], pair2[1])
     stand = [PAD + K * ((d in pair) != (0 in pair)) for d in range(N)]
+    lows = [1 - stand[d] - K if d in seconds else stand[d] for d in range(N)]
+    beyond = [sum(low > lows[d] for low in lows) for d in range(N)]
 
     def swap(q, s, a, lands, d, semc, sems):
         dst = T.cores[d]
@@ -280,11 +287,13 @@ def rank_program(g, core, T, topo):
     def turned(t, d, by, between=None):
         for e in (0, 1):
             move(by[e], V("xe", M * d + 16 * e, M * d + M, 32), V("xh%d" % t, 8 * d, 8 * d + 8))
-        b = 32 * RK.index(d)
-        act(on(V("rb", 3 * H, 4 * H, 16), b, 32), on(V("xh%d" % t, 8 * d, 8 * d + 8), b, 32))
         if between:
             between()
         tr(V("fh", M * d, M * d + M), V("xe", M * d, M * d + M))
+
+    def themselves(t, d):
+        b = 32 * RK.index(d)
+        act(on(V("rb", 3 * H, 4 * H, 16), b, 32), on(V("xh%d" % t, 8 * d, 8 * d + 8), b, 32))
 
     def repeated(e):
         scan(V("xb", M * e, M * e + M), V("d32"), V("xz", M * e, M * e + M), ALU.mult, ALU.add)
@@ -317,36 +326,35 @@ def rank_program(g, core, T, topo):
     for k in range(2 * J):
         shift = 2 * (k % 2)
         o = V("nbe", 0, 16 - shift, 1, 16 * k, 16 * k + 16)
-        loads.append(("s", A(o), T.nb[:, 16 * (k // 2) + shift:16 * (k // 2) + 16], [o], []))
-    dmas("du", [("y", A(V("ut")), T.u[:], [V("ut")], [])])
+        loads.append(("ys"[k % 2], A(o), T.nb[:, 16 * (k // 2) + shift:16 * (k // 2) + 16], [o], []))
     dmas("dnb", loads)
+    dmas("du", [("s", A(V("ut", 0, 16)), T.u[:, 0:16], [V("ut", 0, 16)], [])])
     for h in (0, 1):
         o = V("xt", 4 * H * h, 4 * H * h + 4 * H)
-        dmas("dx%d" % h, [("y", A(o), T.x[:, 4 * H * h:4 * H * h + 4 * H], [o], [])])
+        dmas("dx%d" % h, [("ys"[h], A(o), T.x[:, 4 * H * h:4 * H * h + 4 * H], [o], [])])
     IP = lambda k: V("ip", k, k + 1)
     RI = lambda n: V("i128", 0, n)
     iota(V("iu"), [[1, 3], [0, 8]], 0, 0)
     iota(IP(0), [[0, 1]], 0, 1)
-    iota(V("id16"), [[1, 16]], 128, -1)
     iota(V("i128"), [[1, H]], 0, 0)
     o = 16 * rank
+    fill(V("xe", 0, M), 0.0)
+    for d in range(1, N):
+        act(V("xe", M * d, M * d + M), V("xe", 0, M))
+    fill(V("ut", 16, 512), 0.0)
     fill(on(V("nbl", o, o + 8), 96, 32), 0)
-    fill(V("dw"), 0.0)
-    act(V("xe"), V("dw"))
     cp(V("cu"), V("iu"))
-    fill(V("d32"), 1.0)
     ts(IP(1), IP(0), 6, ALU.logical_shift_right)
     ts(IP(2), IP(0), 15, ALU.bitwise_and)
-    ts(IP(3), IP(0), 31, ALU.bitwise_and)
-    fill(V("xz", 0, HM), 0.0)
-    cp(V("cf", 5, 8), V("ip", 1, 4))
     for e in (0, 1):
         cp(on(V("nbl", o + e, o + 8, 2), 0, 96), on(V("nbe", e, 16, 4), 0, 96))
     spread(lambda d: V("nbl", 16 * d, 16 * d + 8), "nb%d")
     quant(V("qu"), V("su"), V("ut"))
-    fill(V("d32", 0, M, 32), 0.0)
-    ts(V("id16"), V("id16"), 15, ALU.bitwise_and)
+    ts(IP(3), IP(0), 31, ALU.bitwise_and)
+    fill(V("dw"), 0.0)
     pick(V("qr", 0, 128), V("sr", 0, 128), V("qu"), V("su"), V("cu", 0, 8))
+    for k, (a, s) in enumerate(RUNS):
+        act(V("cw", H * k, H * k + H), V("i128"), AF.Identity, scale=s * UNIT, bias=a * UNIT)
 
     def height(k, t, q, s, a, n):
         mm(bank(k, n), V("qr", 128 * t, 128 * t + 128), V("sr", 128 * t, 128 * t + 128), V(q, a, a + n), V(s, a, a + n), True, True)
@@ -358,96 +366,99 @@ def rank_program(g, core, T, topo):
         quant(V("qc0", *half[h]), V("scp0", *half[h]), V("xt", 4 * H * h, 4 * H * h + 4 * H))
     for h in (0, 1):
         height(h, 0, "qc0", "scp0", H * h, H)
-    ts(SCL, SCOL, 15.0, ALU.is_equal, 1.0 - 1.0 / UP, ALU.mult)
-    ts(V("d16"), V("id16"), 1.0, ALU.is_equal, UP, ALU.mult)
-    ts(V("d17"), V("id16"), 0.0, ALU.is_gt)
-    ts(V("crep"), RI(32), 0.0, ALU.mult, SCOL, ALU.add)
+    def gathered(d):
+        for j in range(J):
+            cp(on(V("lnb", 8 * j, 8 * j + 8), 32 * RK.index(d), 32), on(V("nbl", 16 * d, 16 * d + 8), 32 * j, 32))
+
+    cp(V("cf", 5, 8), V("ip", 1, 4))
+    gathered(rank)
     for h in (0, 1):
         tr(V("ht", *half[h]), bank(h, H))
-    ts(SCL, SCL, 1.0 / UP, ALU.max)
-    tt(V("d16"), V("d16"), V("d17"), ALU.add)
+    ts(V("x0", 0, 4), RI(4), 32.0, ALU.mult, LCOL, ALU.add)
+    ts(SCL, SCOL, 15.0, ALU.is_equal, 1.0 - 1.0 / UP, ALU.mult)
     cp(V("xh0", 8 * rank, 8 * rank + 8), V("ht", 0, M, 32))
     share(0)
-    dmas("dw", [("y", A(V("wt")), T.w[:], [V("wt")], [])])
 
-    iota(V("sn"), [[16, 16]], M * rank, 0)
+    iota(V("id16"), [[1, 16]], 128, -1)
+    fill(V("one"), 1.0)
     iota(V("ki"), [[16, 16]], 0, 0)
-    const(V("fs", 2 * GM - 16, 2 * GM), NM)
+    runs = lambda d, n, k: select(V(d), V("one", 0, n), [[0, n // k], [1, k]], ALU.is_gt, 0.0, 0, 0)
+    runs("d4", H, 4)
+    const(V("xz", 0, HM), 0)
+    runs("d32", M, 32)
+    for i, first in enumerate((0, H + 64)):
+        iota(on(V("fq", 64 * i, 64 * i + 64), 0), [[M * (2 * i - 1), 2], [0, 32]], -2 * first - 1, -2)
     for p in (0, 64):
         iota(on(V("nn", 0, 2), p), [[H, 2]], 0, 1)
         iota(on(V("nn", 2, 4), p), [[-H, 2]], H + 64, 1)
+    for i, first in enumerate((64, H)):
+        iota(on(V("fq", 64 * i, 64 * i + 64), 64), [[M * (2 * i - 1), 2], [0, 32]], -2 * first - 1, -2)
+    for b in range(4):
+        iota(on(V("cf", 24, 26), 32 * b, 32), [[HM, 2]], -HM, HM)
+    for k in range(4):
+        const(V("ea", (H + 32) * k + H, (H + 32) * (k + 1)), 0)
+    for e in (0, 1):
+        select(V("et", 528 * e, 528 * e + 528), V("one"), [[1, 528]], ALU.is_equal, 0.0, -2 - e, -4)
+    const(V("dd", 0, SEG * KC, SEG), 0)
     const(V("di", 0, SEG * KC), 1)
     const(V("di", 0, SEG * KC, SEG), 2 * M)
     const(V("di", 32, SEG * KC, SEG), H - 31)
+    iota(V("di", SEG - 1, SEG * KC, SEG), [[0, KC]], H - 31, -1)
+    const(V("iv", 0, H, 8), -beyond[0])
     const(V("kr", 0, 32), K - 1)
-    const(V("kr", 32, 64), K - 2)
-    for k, (a, s) in enumerate(RUNS):
-        act(V("cw", H * k, H * k + H), V("i128"), AF.Identity, scale=s * UNIT, bias=a * UNIT)
-    ts(V("x0", 0, 4), RI(4), 32.0, ALU.mult, LCOL, ALU.add)
-    turned(0, rank, "vs")
-    act(V("d0"), V("d16"), off=V("crep"))
+    const(V("xz", HM, NM), 0)
+    const(V("km", 32, 160), 0)
+    for d in range(N):
+        const(V("low", d, d + 1), lows[d])
+    runs("d8", H, 8)
+    const(V("pd", 0, 16, 2), -8)
+
+    ts(V("crep"), RI(16), 0.0, ALU.mult, SCOL, ALU.add)
+    ts(SCL, SCL, 1.0 / UP, ALU.max)
+    ts(CF(23), UPPER, float(ALPHA[1] - ALPHA[0]), ALU.mult, float(ALPHA[0]), ALU.add)
+    turned(0, rank, "ss")
     for b in range(4):
         for e in (0, 1):
             a, s = RUNS[2 * RK[b] + e]
-            ts(on(V("cb", 3 * H + 64 * e, 3 * H + 64 * e + 64, 16), 32 * b, 32), on(V("x0", 0, 4), 32 * b, 32), s * UNIT, ALU.mult, a * UNIT, ALU.add)
-    for d in [rank] + senders:
-        for b in range(J):
-            cp(on(V("lnb", 8 * b, 8 * b + 8), 32 * RK.index(d), 32), on(V("nbl", 16 * d, 16 * d + 8), 32 * b, 32))
-        if d == rank:
-            fill(V("xz", HM, NM), 0.0)
-            fill(V("xk"), 0.0)
-            pick(V("qr", 128, 384), V("sr", 128, 384), V("qu"), V("su"), V("cu", 8, 24))
+            act(on(V("cb", 3 * H + 64 * e, 3 * H + 64 * e + 64, 16), 32 * b, 32), on(V("x0", 0, 4), 32 * b, 32), AF.Identity, scale=s * UNIT, bias=a * UNIT)
+    ts(V("id16"), V("id16"), 15, ALU.bitwise_and)
+    ts(GSCL, SCL, 1.0 / UNIT, ALU.mult)
+    for d in senders:
+        gathered(d)
 
     def tables():
-        act(V("one"), V("dw", 0, 528), AF.Identity, scale=0.0, bias=1.0)
-        for k in range(4):
-            const(V("ea", (H + 32) * k + H, (H + 32) * (k + 1)), 0)
-        const(V("dd", 0, SEG * KC, SEG), 0)
-        const(V("d8"), 1)
-        const(V("d8", 0, H, 8), 0)
-        const(V("pd", 0, 16, 2), -8)
+        act(V("d0"), V("d16"), off=V("crep"))
+        act(V("ki"), V("ki"), AF.Identity, bias=SCOL)
         for k in range(8):
-            iota(grun("idn", k), [[1, H]], H * k, 0)
-        for e in (0, 1):
-            select(V("et", 528 * e, 528 * e + 528), V("one"), [[1, 528]], ALU.is_equal, 0.0, -2 - e, -4)
-
-    def unpacking(b):
-        a = 528 * (b % 2) + 2 - b // 2 * 2
-        quant(V("qe", 128 * b, 128 * b + 128), V("se", 128 * b, 128 * b + 128), V("et", a, a + 512))
+            act(grun("idn", k), V("i128"), AF.Identity, bias=float(H * k))
+        for h in (0, 1):
+            n0 = M * rank + H * h
+            act(V("sn", 8 * h, 8 * h + 8), V("ki", 0, 8), AF.Identity, scale=float(place(n0 + 1) - place(n0)), bias=float(place(n0)))
+        act(V("want", 0, KC), V("ki", 0, KC), AF.Identity, bias=(1.0 - K) * second)
+        act(V("want", 8, 8 + KC), V("ki", 0, KC), AF.Identity, scale=-float(NM), bias=(K - 1.0) * second * NM)
+        for b in range(4):
+            act(on(V("fq", H, M), 32 * b, 32), on(V("fq", 0, H), 32 * ((b + 1) % 2), 32))
 
     def own_codes(e):
         a, s = RUNS[2 * rank + e]
         cols = (0, 4, 3) if e == 0 else (1, 3, 1)
         ts(V("cv", *cols), V("nn", *cols), s * UNIT, ALU.mult, (a - s * H * e) * UNIT, ALU.add)
 
-    def own_place(h):
-        n0 = M * rank + H * h
-        step = place(n0 + 1) - place(n0)
-        ts(V("sn", 8 * h, 8 * h + 8), V("sn", 8 * h, 8 * h + 8), float(step), ALU.mult, float(place(n0) - step * n0), ALU.add)
+    def unpacking(b):
+        a = 528 * (b % 2) + 2 - b // 2 * 2
+        quant(V("qe", 128 * b, 128 * b + 128), V("se", 128 * b, 128 * b + 128), V("et", a, a + 512))
 
     later = [
-        lambda: ts(CF(23), UPPER, float(ALPHA[1] - ALPHA[0]), ALU.mult, float(ALPHA[0]), ALU.add),
-        lambda: ts(GSCL, SCL, 1.0 / UNIT, ALU.mult),
-        lambda: ts(V("ki"), V("ki"), SCOL, ALU.add),
-        lambda: ts(CF(22), IP(0), -1.0, ALU.mult, LCOL, ALU.add),
-        lambda: own_codes(0),
+        lambda: ts(V("d16"), V("id16"), 1.0, ALU.is_equal, UP, ALU.mult),
+        lambda: ts(V("d17"), V("id16"), 0.0, ALU.is_gt),
+        lambda: tt(V("d16"), V("d16"), V("d17"), ALU.add),
         lambda: tt(WSCL, GSCL, CF(23), ALU.mult),
-        lambda: own_codes(1),
-        lambda: ts(V("sn"), V("sn"), SCOL, ALU.add),
-        lambda: ts(V("want", 0, KC), V("ki", 0, KC), (1.0 - K) * second, ALU.add),
         lambda: ts(CF(26), LCOL, 16.0, ALU.is_lt, 12.0, ALU.mult),
         lambda: ts(CF(27), LCOL, 16.0, ALU.is_lt, 4.0, ALU.mult),
-        lambda: ts(V("di", SEG - 1, SEG * KC, SEG), RI(KC), 0.0, ALU.mult, CF(22), ALU.add),
-        lambda: ts(on(V("fq"), 0), on(V("nn"), 0), -1.0 / M, ALU.mult),
-        lambda: ts(back(on(V("fq"), 64)), on(V("nn"), 64), -1.0 / M, ALU.mult),
-        lambda: ts(V("want", 8, 8 + KC), V("want", 0, KC), -float(NM), ALU.mult),
-        lambda: ts(V("di", SEG - 1, SEG * KC, SEG), V("di", SEG - 1, SEG * KC, SEG), H - 31.0, ALU.add),
-        lambda: ts(CF(24), LCOL, 0.5 / M - 1.0, ALU.add),
-        lambda: ts(CF(25), LCOL, 0.5 / M, ALU.add),
-        lambda: ts(V("pd", 1, 16, 2), V("dw", 0, 8), -8.0, ALU.add, CF(26), ALU.add),
+        lambda: fill(V("fs", 2 * GM - 16, 2 * GM), stand[N - 1] - 0.5 + K * (N - 1 not in seconds)),
         lambda: ts(CF(27), CF(27), 0.5, ALU.add),
-        lambda: own_place(0),
-        lambda: own_place(1),
+        lambda: ts(V("pd", 1, 16, 2), V("dw", 0, 8), -8.0, ALU.add, CF(26), ALU.add),
+        lambda: ts(CF(22), LCOL, -float(M), ALU.add),
     ]
 
     def meanwhile(n=2):
@@ -459,61 +470,57 @@ def rank_program(g, core, T, topo):
     for t in range(R):
         qc, sp = "qc%d" % t, "scp%d" % t
         final = t + 1 == R
-        if t:
-            turned(t, rank, "vs")
-            if final:
-                quant(V("qw"), V("sw"), V("wt"))
-            else:
-                height(7, t + 1, qc, sp, 0, M)
-                tr(V("ho"), bank(7, M))
-        turned(t, senders[0], "vs", meanwhile)
+        if final:
+            quant(V("qw"), V("sw"), V("wt"))
+        turned(t, senders[0], "vs" if t else "ss", meanwhile)
         turned(t, senders[1], "ss")
+        turned(t, senders[2], "ss")
+        for d in range(N):
+            themselves(t, d)
         if not t:
             act(V("ca"), V("cw"), off=V("lnb"))
-        turned(t, senders[2], "vs" if t else "vv", meanwhile)
         meanwhile()
         act(V("ra", H, 2 * H + 32), V("fh"), off=V("lnb", 8, 18))
         cp(V("ra", 0, H), V("fh"), V("lnb", 0, 8))
         act(V("ra", 2 * H + 32, 3 * H), V("fh"), off=V("lnb", 18, 24))
         if not t:
-            tr(V("cb", 0, 3 * H), V("ca"))
             tables()
-            height(7, 1, qc, sp, 0, M)
+            tr(V("cb", 0, 3 * H), V("ca"))
+            dmas("dw", [("y", A(V("wt")), T.w[:], [V("wt")], [V("fh")])])
         tr(V("rb", 0, H), V("ra", 0, H))
         tr(V("rb", H, 2 * H + 32), V("ra", H, 2 * H + 32))
         tr(V("rb", 2 * H + 32, 3 * H), V("ra", 2 * H + 32, 3 * H))
         four = lambda a, b: V("rb", H * a, H * b, 16)
-        for e in (0, 1):
-            tt(V("m1", 8 * e, 8 * e + 8), four(1 - e, 2 - e), four(3 - e, 4 - e), ALU.max)
-        for e in (0, 1):
-            tt(V("neq", 16 * e, 16 * e + 16), four(2 - 2 * e, 4 - 2 * e), four(2 * e, 2 * e + 2), ALU.is_gt)
-        for e in (0, 1):
-            tt(V("lost", 16 * e, 16 * e + 16), V("m1"), four(2 * e, 2 * e + 2), ALU.is_gt)
-        tt(V("neq"), V("neq"), V("cb", 0, HM, 16), ALU.add)
-        meanwhile()
-        tt(V("key"), V("neq"), V("lost"), ALU.add)
-        meanwhile()
-        tt(V("b2"), V("key", 0, 16), V("key", 16, 32), ALU.min)
-        meanwhile()
+        for r, a, b in ((1, 3, 4), (3, 0, 1), (1, 0, 3), (2, 0, 2), (2, 2, 4), (3, 1, 4)):
+            tt(V("lost", 32 * a + r, 32 * b, 4), four((a + r) % 4, (b - 1 + r) % 4 + 1), four(a, b), ALU.is_gt)
+        if not t:
+            cp(V("lost", 0, H, 4), V("cb", 0, HM, 16))
+        meanwhile(3)
+        scan(V("key"), V("d4"), V("lost"), ALU.mult, ALU.add)
+        meanwhile(3)
+        tt(V("b2"), V("key", 3, 64, 4), V("key", 67, H, 4), ALU.min)
+        meanwhile(3)
         for e in (0, 1):
             for b in range(4):
                 src = 64 * (b // 2) + 32 * e
                 tt(on(V("xz", M * e, M * e + M, 32), 32 * b, 32), on(V("b2", 0, 8), src, 32), on(V("b2", 8, 16), src, 32), ALU.min)
         for e in (0, 1):
             repeated(e)
-        for i in range(4):
+        for i in (0, 1, 3, 2):
             tr(piece("fa", i), V("xb", H * i, H * i + H))
-        for i in (0, 1):
-            cross("fa", i, 0, "s")
-            cross("fa", i, 1, "s")
-            lift("fa", i)
-        cross("fa", 3, 0, "s")
+        cross("fa", 0, 0, "s")
+        cross("fa", 0, 1, "g" if t else "v")
+        lift("fa", 1)
+        cross("fa", 1, 0, "s")
+        cross("fa", 1, 1, "v")
+        lift("fa", 0)
         lift("fa", 3)
-        cross("fa", 2, 0, "v")
+        cross("fa", 3, 1, "s")
         lift("fa", 2)
+        cross("fa", 3, 0, "v")
+        cross("fa", 2, 0, "v")
+        cross("fa", 2, 1, "s")
         listed("la", 0, 2)
-        cross("fa", 2, 1, "v")
-        cross("fa", 3, 1, "v")
         listed("la", 2, 4)
         for k in range(9):
             fi, fo, li, lw = ("fa", "fb", "la", "lb") if k % 2 == 0 else ("fb", "fa", "lb", "la")
@@ -523,21 +530,31 @@ def rank_program(g, core, T, topo):
             cross(fo, 1, 0, "s")
             lift(fo, 1)
             cross(fo, 0, 0, "s")
-            cross(fo, 0, 1, "v")
+            cross(fo, 0, 1, "g" if t else "v")
             cross(fo, 1, 1, "v")
             lift(fo, 3)
             cross(fo, 3, 1, "s")
-            cross(fo, 2, 0, "v")
-            lift(fo, 2)
-            cross(fo, 2, 1, "s")
-            listed(lw, 0, 2)
-            cross(fo, 3, 0, "v")
+            if t:
+                lift(fo, 2)
+                cross(fo, 2, 0, "v")
+                cross(fo, 3, 0, "v")
+                cross(fo, 2, 1, "s")
+                listed(lw, 0, 2)
+            else:
+                cross(fo, 2, 0, "v")
+                lift(fo, 2)
+                cross(fo, 2, 1, "s")
+                listed(lw, 0, 2)
+                cross(fo, 3, 0, "v")
             listed(lw, 2, 4)
         for by, a, b in (("v", 0, H), ("s", H, M), ("s", M, HM)):
             move(by, V("fr", a, b), V("fb"), V("lb", a // 16, b // 16))
         meanwhile(len(later))
+        if not t:
+            own_codes(0)
+            own_codes(1)
         EE = lambda j, a, b: V("ee", HM * j + a, HM * j + b)
-        same = lambda j, a, b: ts(EE(j, a, b), V("fr", a, b), V("cv", j, j + 1), ALU.is_equal)
+        same = lambda j, a, b: ts(EE(j, a, b), V("fr", a, b), V("cv", j, j + 1), ALU.is_equal, float(HM), ALU.mult)
         count = lambda j: scan(V("so", M * j, M * j + M), EE(j, 0, M), EE(j, M, HM), ALU.add, ALU.add)
         for j in range(4):
             same(j, 0, M)
@@ -556,174 +573,205 @@ def rank_program(g, core, T, topo):
         ends = V("so", M - 1, 4 * M, M)
         halves(on(V("aa"), 0), ends, ALU.add)
         halves(back(on(V("aa"), 64)), ends, ALU.add)
-        if not t:
-            unpacking(0)
-        tt(V("xk", 0, H, 32), V("aa"), V("fq"), ALU.add)
         for b in range(4):
-            tt(on(V("xk", H, M, 32), 32 * b, 32), on(V("aa"), 32 * (b ^ 1), 32), on(V("fq"), 32 * (b ^ 1), 32), ALU.add)
-        keys = lambda h: scan(V("xr", *half[h]), V("d32", 0, H), V("xk", *half[h]), ALU.mult, ALU.add)
-        keys(0)
-        cp(V("lro"), rho)
+            halves(on(V("ab"), 32 * b, 32), ends, ALU.add, 32 * ((b + 1) % 2), 32)
+        for j in range(8):
+            out, less, size = V("xr", 32 * j, 32 * j + 32), V("fq", 32 * j, 32 * j + 32), V("aa" if j < 4 else "ab", j % 4, j % 4 + 1)
+            if j in (0, 1, 6, 7):
+                ts(out, less, size, ALU.add)
+            else:
+                act(out, less, AF.Identity, bias=size)
+            if j == 1:
+                cp(V("lro"), rho)
         tt(itself, rho, V("sn"), ALU.is_equal)
-        keys(1)
-        act(V("rtf"), V("idn"), off=V("lro"))
-        row = V("rtf", 0, M, 1, 0, 1)
-        dmas("drt", [("y", T.rt[0:1, M * t:M * t + M], A(row), [], [row])])
         tr(V("kf", *half[0]), V("xr", *half[0]))
-        ts(itself, itself, 2.0 * GM - 1, ALU.mult)
         tr(V("kf", *half[1]), V("xr", *half[1]))
+        ts(itself, itself, 2.0 * GM - 1, ALU.mult)
         ms = "ms%d" % t
-        MS = lambda d, a, b: V(ms, 8 * d + a, 8 * d + b)
+        MS = lambda d: V(ms, 4 * d, 4 * d + 4)
         EA = lambda i, h, n: V("ea", (H + 32) * (2 * i + h), (H + 32) * (2 * i + h) + n)
         for k in (0, 1):
             act(V("sg", M * k, M * k + M), V("kf"), AF.Sign, scale=-1.0, bias=CF(24 + k), accum=ACC(k))
         for h in (0, 1):
             for i in (0, 1):
-                ts(EA(i, h, H), V("kf", *half[h]), V("xk", 32 * i, 32 * i + 1), ALU.is_gt, 1.0 - 2.0 * second, ALU.mult)
-        act(MS(rank, 2, 4), V("acc", 0, 2), AF.Identity, scale=-0.5, bias=(M - 1) / 2)
+                ts(EA(i, h, H), V("kf", *half[h]), V("xr", 32 * i, 32 * i + 1), ALU.is_gt, 1.0 - 2.0 * second, ALU.mult)
+        act(V(ms, 4 * N + 1, 4 * N + 4, 2), V("acc", 0, 2), AF.Identity, scale=-0.5, bias=(M - 1) / 2)
         tt(itself, itself, rho, ALU.max)
+        if not t:
+            unpacking(0)
         scan(V("pb", 0, H + 32), EA(0, 0, H + 32), EA(0, 1, H + 32), ALU.add, ALU.add)
         scan(back(V("pb", H + 32, 2 * H + 64)), EA(1, 0, H + 32), EA(1, 1, H + 32), ALU.add, ALU.add)
         cp(V("lrm"), itself)
         if not t:
             unpacking(1)
-        if second:
-            ts(MS(rank, 0, 2), V("pb", H, H + 64, 32), 0.5 - K, ALU.max, float(stand[rank] + K - 1), ALU.add)
-        else:
-            ts(MS(rank, 0, 2), V("pb", H, H + 64, 32), K - 0.5, ALU.min, float(stand[rank]), ALU.add)
         tr(V("ps"), V("pb", H, H + 64))
-        spread(lambda d: MS(d, 0, 4), "m%d_" % t + "%d", [near, far] + [d for d in pair2 if d != far])
+        if second:
+            ts(V(ms, 4 * N, 4 * N + 4, 2), V("pb", H, H + 64, 32), 0.5 - K, ALU.max, float(stand[rank] + K - 1), ALU.add)
+        else:
+            ts(V(ms, 4 * N, 4 * N + 4, 2), V("pb", H, H + 64, 32), K - 0.5, ALU.min, float(stand[rank]), ALU.add)
+        spread(MS, "m%d_" % t + "%d", [near, far] + [d for d in pair2 if d != far], MS(N))
+        dmas("dm", [("y", A(MS(rank)), A(MS(N)), [MS(rank)], [MS(N)])])
         flips = [d for d in range(1, N) if (d in seconds) != (d - 1 in seconds)]
         for i, d in enumerate(flips):
             o = V("sgn", 16 * min(i, 1), 16 * min(i, 1) + 16)
-            ts(o, rho, place(M * d) - 0.5, ALU.is_lt, 2.0, ALU.mult)
+            ts(o, itself, place(M * d) - 0.5, ALU.is_lt, 2.0, ALU.mult)
             if i:
                 ts(o, o, -1.0, ALU.add)
                 tt(V("sgn", 0, 16), V("sgn", 0, 16), o, ALU.mult)
             elif len(flips) > 1:
                 ts(o, o, -1.0, ALU.add, SCL, ALU.mult)
-        if not t:
-            unpacking(2)
         for k in range(KC):
             out = V("dd", SEG * k + 1, SEG * k + SEG)
             if k < 3:
                 ts(out, V("ps"), V("want", k, k + 1), ALU.not_equal, float(NM), ALU.mult)
             else:
                 act(out, V("ps"), AF.Abs, scale=float(NM), bias=V("want", 8 + k, 9 + k))
+        act(V("rtf"), V("idn"), off=V("lro"))
+        row = V("rtf", 0, M, 1, 0, 1)
+        dmas("drt", [("y", T.rt[0:1, M * t:M * t + M], A(row), [], [row])])
         if len(flips) == 1:
             ts(V("sgn", 0, 16), V("sgn", 0, 16), -1.0, ALU.add, SCL, ALU.mult)
         if not t:
-            unpacking(3)
+            unpacking(2)
         scan(V("de", 0, SEG * KC), V("dd", 0, SEG * KC), V("di", 0, SEG * KC), ALU.min, ALU.add)
+        if not final:
+            a = H * (t + 1)
+            pick(V("qr", a, a + H), V("sr", a, a + H), V("qu"), V("su"), V("cu", a // 16, a // 16 + 8))
+            height(7, t + 1, qc, sp, 0, M)
         for p in (0, 64):
             halves(on(V("e1", 0, KC), p), V("de", SEG - 1, SEG * KC, SEG), ALU.min)
         if not t:
-            tr(V("ho"), bank(7, M))
+            unpacking(3)
         for b in range(4):
             tt(on(V("e2", 0, KC), 32 * b, 32), on(V("e1", 0, KC), 32 * b, 32), on(V("e1", 0, KC), 32 * (b ^ 1), 32), ALU.min)
-        ts(V("j1", 0, KC), V("e2", 0, KC), -1.0, ALU.mult, float(M), ALU.add)
+        for d in range(1, N):
+            ts(V("iv", d, H, 8), itself, place(M * d) - 0.5, ALU.is_gt, float(beyond[d - 1] - beyond[d]), ALU.mult)
+        ts(V("j1", 0, KC), V("e2", 0, KC), CF(22), ALU.add, -1.0, ALU.mult)
+        spaced = lambda by, s, b: move(by, on(V("xz", 32 * s, NM, H), 32 * b, 32), on(V(ms, 0, 4 * N, 2), 32 * s, 32))
+        col = lambda d, c: V(ms, 4 * (N if d == rank else d) + c, 4 * (N if d == rank else d) + c + 1)
+        ge, gt = V(ms, 1, 4 * N, 4), V(ms, 3, 4 * N, 4)
+        allows = lambda: ts(V("km", 0, 32), V("kr", 0, 32), col(pair[1], 3), ALU.subtract, col(pair[0], 1), ALU.min)
+        if not final:
+            tr(V("ho", 0, H), bank(7, H))
+        if OPT["early"]:
+            allows()
         qz, sz, qb, sb = [n + str(t) for n in ("qz", "sz", "qb", "sb")]
         a = K * second
         pick(V(qz, a, a + K), V(sz, a, a + K), V(qc, 0, M), V(sp, 0, M), V("j1", 0, KC))
         swap(qz, sz, a, K - a, near, "ac%d" % t, "as%d" % t)
+        todo = [(s, b) for b in range(4) for s in range(4)]
+        for s, b in todo[OPT["nv"]:]:
+            spaced("s", s, b)
+        todo = todo[:OPT["nv"]]
+
+        def some(n):
+            for s, b in todo[:n]:
+                spaced("v", s, b)
+            del todo[:n]
+
+        if not OPT["early"]:
+            allows()
+        else:
+            tr(V("kt", 0, 32), V("km", 0, 32))
+        if not final:
+            tr(V("ho", H, M), V("bl", 512 * 7 + H, 512 * 7 + M))
         unpack = [(V("qe", 128 * b, 128 * b + 128), V("se", 128 * b, 128 * b + 128)) for b in range(4)]
         for h in (0, 1):
             for b in range(4):
                 mm(bank(4 * h + b, H), *unpack[b], V(qc, *half[h]), V(sp, *half[h]), True, False)
-        for d in [rank, near, far] + [d for d in pair2 if d != far]:
-            act(V("uu", 2 * d, 2 * d + 2), MS(d, 0, 2))
-        spaced = lambda by, s, b: move(by, on(V("xz", 32 * s, NM, H), 32 * b, 32), on(V("uu", 0, 8), 32 * s, 32))
-        ts(V("km", 0, 32), V("kr", 0, 32), MS(pair[1], 3, 4), ALU.subtract, MS(pair[0], 2, 3), ALU.min)
-        for s in range(4):
-            for b in (0, 1):
-                spaced("s", s, b)
-        tr(V("kt", 0, 32), V("km", 0, 32))
+        if not OPT["early"]:
+            tr(V("kt", 0, 32), V("km", 0, 32))
+            some(2)
         red(V("kk", 4, 5), V("kt", 0, 32), ALU.max)
+        some(2)
         ts(V("fl", 0, KC), V("ki", 0, KC), V("kk", 4, 5), ALU.is_gt, float(K), ALU.mult)
-        for s in range(4):
-            spaced("v", s, 2)
+        some(2)
+        red(V("kk", 5, 6), gt, ALU.add, True)
         tt(V("fl", 8, 8 + KC), V("fl", 0, KC), V("ki", 0, KC), ALU.add)
-        for s in range(4):
-            spaced("v", s, 3)
+        scan(V("kw", 0, N), gt, ge, ALU.add, ALU.subtract, V("kk", 5, 6))
+        some(16)
         cp(V("j2", 0, KC), V("fl", 8, 8 + KC))
-        for d in range(N):
-            c = [MS(e, 2, 3) if e < d else MS(e, 3, 4) for e in range(N) if e != d]
-            ts(V("kw", d, d + 1), c[0], c[1], ALU.add, c[2], ALU.add)
-        repeated(0)
-        repeated(1)
+        ts(V("kw", 0, N), V("kw", 0, N), K - 0.5 * N, ALU.add, 0.0, ALU.min)
+        for e in range(OPT["nr"]):
+            repeated(e)
         a = stand[rank]
         pick(V(qb, a, a + K), V(sb, a, a + K), V(qz), V(sz), V("j2", 0, KC))
         swap(qb, sb, a, stand[far], far, "bc%d" % t, "bs%d" % t)
-        repeated(2)
-        repeated(3)
+        for e in range(OPT["nr"], 4):
+            repeated(e)
+        tt(V("km", 32, 160, 32), V("kw", 0, N), ge, ALU.add)
         for k in range(8):
             tr(grun("fs", k), V("xb", H * k, H * k + H))
-        for d in range(N):
-            ts(V("km", 32 + 32 * d, 64 + 32 * d), V("kr", 32, 64), V("kw", d, d + 1), ALU.subtract, MS(d, 2, 3), ALU.min)
+        scan(V("kt", 32, 160), V("d32", 0, H), V("km", 32, 160), ALU.mult, ALU.add)
         act(V("rs", H, M), V("fs"), off=V("lrm", 8, 16))
         cp(V("rs", 0, H), V("fs"), V("lrm", 0, 8))
-        tr(V("kt", 32, 160), V("km", 32, 160))
-        scan(V("sc", 0, H), V("d0", 0, H), V("rs", 0, H), ALU.mult, ALU.add)
-        scan(V("sc", H, M), V("d0", 0, H), V("rs", H, M), ALU.mult, ALU.add)
-        for d in range(N):
-            red(V("kk", d, d + 1), V("kt", 32 + 32 * d, 64 + 32 * d), ALU.max)
+        tr(V("ku"), V("kt", 32, 160))
         at, us, me = V("sc", 15, M, 16), V("um", 0, 16), V("rho", 16, 32)
+        qp, pp = "qp%d" % t, "sp%d" % t
+        scan(V("sc", 0, M), V("d0", 0, M), V("rs"), ALU.mult, ALU.add)
+        scan(V("kt", 32, 160), V("d32", 0, H), V("ku"), ALU.mult, ALU.max)
         ts(V("pl"), at, SCL, ALU.mult, float(PAD + 2 * K - 1), ALU.min)
         tt(us, at, V("sgn", 0, 16), ALU.mult)
-        qp, pp = "qp%d" % t, "sp%d" % t
-        lows = [-(stand[d] + K - 1.0) if d in seconds else float(stand[d]) for d in range(N)]
-        for d in (0, 1):
-            ts(V("iv", d, H, 8), us, lows[d] - 0.25, ALU.is_ge, -1.0, ALU.add)
-        codes(V(qp, *half[0]), V(qb), V("pl", 0, 8))
-        codes(V(qp, *half[1]), V(qb), V("pl", 8, 16))
+        tt(V("kk", 0, N), V("kt", 63, 160, 32), V("low"), ALU.add)
         for h in (0, 1):
-            move("sv"[h], V(pp, *half[h]), V(sb), V("pl", 8 * h, 8 * h + 8))
+            pick(V(qp, *half[h]), V(pp, *half[h]), V(qb), V(sb), V("pl", 8 * h, 8 * h + 8))
         for h in (0, 1):
             for b in range(4):
                 mm(bank(4 * h + b, H), *unpack[b], V(qp, *half[h]), V(pp, *half[h]), False, True)
-        for d in (2, 3):
-            ts(V("iv", d, H, 8), us, lows[d] - 0.25, ALU.is_ge, -1.0, ALU.add)
         for d in range(N):
-            ts(V("iv", 4 + d, H, 8), us, lows[d], ALU.subtract, V("kk", d, d + 1), ALU.is_lt)
+            ts(V("iv", 4 + d, H, 8), us, V("kk", d, d + 1), ALU.is_lt)
         member = V("iw", 7, H, 8)
-        for b in range(8):
+
+        def cast(b, by):
             src, out = bank(b, H), V("hb", 4 * H * (b // 4) + b % 4, 4 * H * (b // 4) + 4 * H, 4)
-            if b % 2:
-                act(out, src, scale=0.5)
-            else:
+            if by == "v":
                 ts(out, src, 0.5, ALU.mult)
-            if b == 2:
-                scan(V("iw"), V("d8"), V("iv"), ALU.mult, ALU.add)
-        for h in (0, 1):
+            else:
+                act(out, src, scale=0.5)
+
+        def anew(h):
             quant(V(qc, M + H * h, M + H * h + H), V(sp, M + H * h, M + H * h + H), V("hb", 4 * H * h, 4 * H * h + 4 * H))
             if not final:
                 height(h, t + 1, qc, sp, M + H * h, H)
-            if not h:
-                if not final:
-                    scan(V("px"), V("pd"), member, ALU.add, ALU.max)
-                ts(me, member, 0.5, ALU.is_gt, float(M), ALU.mult)
-        nq, ns = "qc%d" % (t + 1), "scp%d" % (t + 1)
-        if not final:
-            ts(V("mx1"), V("px", 1, 16, 2), CF(27), ALU.is_lt)
-            ts(V("mx"), V("px", 1, 16, 2), CF(27), ALU.is_gt)
-        tt(me, me, V("ki"), ALU.add)
+
+        for b in (0, 2, 4, 6):
+            cast(b, "s")
+        cast(1, "v")
+        scan(V("iw"), V("d8"), V("iv"), ALU.mult, ALU.add)
+        cast(3, "v")
+        if final:
+            ts(me, member, 0.5, ALU.is_gt, float(M), ALU.mult)
+        cast(5, "v")
+        if final:
+            tt(me, me, V("ki"), ALU.add)
+        else:
+            scan(V("px"), V("pd"), member, ALU.add, ALU.max)
+        cast(7, "v")
+        anew(0)
         if final:
             cp(V("kl"), me)
         else:
+            ts(V("mx1"), V("px", 1, 16, 2), CF(27), ALU.is_lt)
+        anew(1)
+        nq, ns = "qc%d" % (t + 1), "scp%d" % (t + 1)
+        if not final:
+            tt(V("xo"), V("ho", 0, M, 32), V("mx1"), ALU.mult)
+            ts(V("mx"), V("px", 1, 16, 2), CF(27), ALU.is_gt)
             for h in (0, 1):
                 tr(V("ht", *half[h]), bank(h, H))
                 if h:
-                    cp(V("kl"), me)
+                    tt(me, me, V("ki"), ALU.add)
                 else:
-                    tt(V("xo"), V("ho", 0, M, 32), V("mx1"), ALU.mult)
+                    ts(me, member, 0.5, ALU.is_gt, float(M), ALU.mult)
                 for c in range(4 * h, 4 * h + 4):
                     out, new = V("xh%d" % (t + 1), 8 * rank + c, 8 * rank + c + 1), V("ht", 32 * c, 32 * c + 1)
-                    if h and c % 2 == 0:
+                    if c > 5:
                         ts(out, new, V("mx", c, c + 1), ALU.mult, V("xo", c, c + 1), ALU.add)
                     else:
                         act(out, new, AF.Identity, scale=V("mx", c, c + 1), bias=V("xo", c, c + 1))
             share(t + 1)
-            pick(V(nq, 0, M), V(ns, 0, M), V(qc), V(sp), V("kl"))
+            cp(V("kl"), me)
+            turned(t + 1, rank, "ss", lambda: pick(V(nq, 0, M), V(ns, 0, M), V(qc), V(sp), V("kl")))
 
     outs = []
     for h in (0, 1):
@@ -735,7 +783,8 @@ def rank_program(g, core, T, topo):
         outs.append(("s", T.osc[4 * k:4 * k + 4, 0:M], A(o), [], [o]))
     for h in (0, 1):
         cp(V("ys", *half[h]), bank(h, H))
-        outs.append(("y", T.y[:, H * h:H * h + H], A(V("ys", *half[h])), [], [V("ys", *half[h])]))
+        outs.append(("ys"[h], T.y[:, H * h:H * h + H], A(V("ys", *half[h])), [], [V("ys", *half[h])]))
     dmas("dout", outs)
     for sem in sorted(cnt):
-        g.sync.wait_ge(T.sem[sem], cnt[sem])
+        if max(known[q].get(sem, 0) for q in known) < cnt[sem]:
+            queue["y" if sem == "dout" else "g"].wait_ge(T.sem[sem], cnt[sem])

@@ -11,6 +11,7 @@ H = M // 2
 KC = K // 16
 PAD = 16
 SEG = 65
+EARLY = 3
 RUNS = ((-2048, 8), (-1024, 4), (-512, 2), (-256, 1), (128, 1), (256, 2), (512, 4), (1024, 8))
 UNIT = 1.0 / 4096
 OWN = ((2, 3, 4, 5), (0, 1, 6, 7))
@@ -18,15 +19,15 @@ ALPHA = (4, 1)
 RK = (1, 2, 0, 3)
 GM, WM = 2048, 8192
 UP = float(2 ** 30)
-OPT = {"early": 0, "nv": 6, "nr": 1}
 C8, U8, F32, B16, I32, U16 = "float8_e4m3fn_x4", "uint8", "float32", "bfloat16", "int32", "uint16"
+PLAN = {"wake": 300, "gather": 1.3, "call": 360, "way": 1000, "row": 20, "load": 1300, "v": 60, "g": 150}
 
 WIDTHS = {
     B16: {"xt": 4 * M, "ut": 512, "wt": 512, "one": 528, "et": 2 * 528, "d0": M, "dw": 16,
           "xb": NM, "xz": NM, "d32": M, "cw": NM, "ca": 384, "cb": HM,
-          "fs": 2 * GM, "fa": 2 * WM, "fb": 2 * WM, "sc": HM, "rs": M, "hb": 4 * M,
-          "fr": HM, "ee": 4 * HM, "so": 4 * M, "cv": 16, "ea": 4 * (H + 32), "pb": 2 * H + 64, "ps": 64, "dd": 336, "di": 336, "de": 336,
-          "sg": 2 * M, "kr": 32, "km": 160, "kt": 160, "ku": H, "iv": H, "iw": H, "d8": H, "d4": H, "lost": H, "key": H},
+          "fs": 2 * GM, "fa": 2 * WM, "fb": 2 * WM, "sc": HM, "s2": M, "s3": M, "rs": M, "hb": 4 * M,
+          "fr": M, "ee": 4 * HM, "so": 4 * M, "cv": 16, "ea": 4 * (H + 32), "pb": 2 * H + 64, "ps": 64, "dd": 336, "di": 336, "de": 336,
+          "sg": 2 * M, "kr": 32, "km": 160, "kt": 160, "ku": H, "kv": H, "iv": H, "iw": H, "d8": H, "d4": H, "lost": H, "key": H},
     C8: {"qu": 128, "qw": 128, "qr": 384, "qe": 512},
     U8: {"su": 128, "sw": 128, "sr": 384, "se": 512},
     F32: {"i128": H, "idn": 2 * GM, "rtf": M, "xe": NM, "fh": NM, "ra": 384, "rb": HM,
@@ -39,11 +40,11 @@ for _d, _parts in WIDTHS.items():
     for _n, _w in _parts.items():
         SCRATCH[_n] = ("sbuf", [128, _w], _d)
 SMALL = {
-    "zf": (F32, {"d16": 16, "d17": 16, "cf": 32, "sn": 16, "ki": 16, "x0": 16, "b2": 16,
-                 "nn": 4, "aa": 4, "ab": 4, "kw": 4, "low": 4, "want": 16, "e1": 8, "e2": 8, "kk": 8, "fl": 16, "um": 16, "sgn": 32, "px": 16, "pd": 16,
-                 "rho": 32, "mx": 8, "mx1": 8, "xo": 8}),
+    "zf": (F32, {"d16": 16, "d17": 16, "cf": 32, "sn": 16, "ki": 16, "x0": 16, "b2": 16, "nn": 4, "nr": 4, "aa": 4, "ab": 4, "kw": 4,
+                 "low": 4, "want": 16, "e1": 8, "e2": 8, "kk": 8, "fl": 16, "us": 16, "sgn": 32, "px": 16, "pd": 16,
+                 "rho": 16, "self": 16, "me": 16, "mx": 8, "mx1": 8, "xo": 8}),
     "zi": (I32, {"ip": 16}),
-    "zu": (U16, {"crep": 16, "cu": 24, "lro": 16, "lrm": 16, "j1": 6, "j2": 6, "pl": 16, "kl": 16}),
+    "zu": (U16, {"crep": 16, "cu": 24, "lro": 16, "j1": 6, "j2": 6, "pl": 16, "kl": 16}),
 }
 AT = {}
 for _b, (_d, _parts) in SMALL.items():
@@ -63,12 +64,88 @@ for _t in range(R + 1):
     SCRATCH["scp%d" % _t] = ("sbuf", [128, 2 * M if _t < R else M], U8)
 
 SEMAPHORES = (["ev", "es", "et", "eg", "loc"] + ["nb%d" % d for d in range(N)] + ["%s%d_%d" % (k, t, d) for k in "hm" for t in range(R) for d in range(N)]
-              + ["%s%d" % (k, t) for t in range(R) for k in ("ac", "as", "bc", "bs")]
-              + ["dx0", "dx1", "du", "dw", "dnb", "dm", "drt", "dout"])
+              + ["%s%d" % (k, t) for t in range(R) for k in ("ac", "as", "bc", "bs", "dm", "drt")]
+              + ["dx0", "dx1", "du", "dw", "dnb", "dout"])
+BYTES = {C8: 4, U8: 1, F32: 4, B16: 2, I32: 4, U16: 2}
 
 
 def place(n):
     return GM + RUNS[n // H][0] + RUNS[n // H][1] * (n % H)
+
+
+def meets(a, b):
+    if a[1] >= b[2] or b[1] >= a[2] or a[4] >= b[5] or b[4] >= a[5]:
+        return False
+    return not (a[3] == b[3] and a[3] > 1 and (a[1] - b[1]) % a[3])
+
+
+def split(reads, writes):
+    ps = [r for r in list(reads) + list(writes) if SCRATCH[r[0]][0] == "psum"]
+    return ([r for r in reads if SCRATCH[r[0]][0] != "psum"],
+            [r for r in writes if SCRATCH[r[0]][0] != "psum"] + [(r[0], r[1] // 512 * 512, -(-r[2] // 512) * 512, 1, 0, 128) for r in ps])
+
+
+def noted(hist, reads, writes, tag):
+    for r in writes:
+        hist[r[0]] = [h for h in hist.get(r[0], [])
+                      if not ((r[3] == 1 or h[0] == r) and r[1] <= h[0][1] and h[0][2] <= r[2] and r[4] <= h[0][4] and h[0][5] <= r[5])]
+    for r, w in [(r, False) for r in reads] + [(r, True) for r in writes]:
+        hist.setdefault(r[0], []).append((r, w, tag))
+
+
+def behind(hist, reads, writes):
+    return [tag for r, w in [(r, False) for r in reads] + [(r, True) for r in writes]
+            for e, ew, tag in hist.get(r[0], []) if (w or ew) and meets(r, e)]
+
+
+def ordered(calls):
+    wake, n = PLAN["wake"], len(calls)
+    hist, before, after = {}, [], [[] for _ in calls]
+    for i, (cost, run, reads, writes, follows, kind) in enumerate(calls):
+        reads, writes = split(reads, writes)
+        before.append([(j, wake) for j in set(behind(hist, reads, writes))] if follows is None else [(follows, 0)])
+        for j, w in before[i]:
+            after[j].append((i, w))
+        noted(hist, reads, writes, i)
+    chain = [0.0] * n
+    for i in range(n - 1, -1, -1):
+        chain[i] = min(calls[i][0].values()) + max([w + chain[j] for j, w in after[i]], default=0)
+    left = [len(b) for b in before]
+    ready = {i: 0.0 for i in range(n) if not left[i]}
+    free, crossed, out, due = {}, -wake, [], [0.0] * n
+
+    def start(i, q):
+        t = max(ready[i], free.get(q, 0.0))
+        if q == "g" and calls[i][5] != "remote":
+            t = max(t, free.get("gc", -wake) + wake)
+        if q == "v" and calls[i][5] == "port":
+            t = max(t, crossed + wake)
+        return t
+
+    while ready:
+        best = {}
+        for i in ready:
+            cost = calls[i][0]
+            q = min(cost, key=lambda q: start(i, q) + cost[q] + (PLAN.get(q, 0) if len(cost) > 1 else 0))
+            best[i] = (q, start(i, q), cost[q])
+        first = min(best, key=lambda i: (best[i][1] + best[i][2], i))
+        q, end = best[first][0], best[first][1] + best[first][2]
+        i = first if q is None else max([j for j in best if best[j][0] == q and (best[j][1] < end or j == first)], key=lambda j: (chain[j] - best[j][1], -j))
+        q, t, c = best[i]
+        out.append((t, len(out), i, q))
+        if q is not None:
+            free[q] = t + c
+        if q == "g" and calls[i][5] != "remote":
+            free["gc"] = t + c
+        if q == "v" and calls[i][5] == "cross":
+            crossed = t + c
+        del ready[i]
+        for j, w in after[i]:
+            left[j] -= 1
+            due[j] = max(due[j], t + c + w)
+            if not left[j]:
+                ready[j] = due[j]
+    return [(i, q) for t, k, i, q in sorted(out)]
 
 
 def rank_program(g, core, T, topo):
@@ -77,7 +154,7 @@ def rank_program(g, core, T, topo):
         return
     queue = {"v": g.vector, "s": g.scalar, "t": g.tensor, "g": g, "y": g.sync}
     esem = {"v": "ev", "s": "es", "t": "et", "g": "eg"}
-    cnt, known, clock, hist = {}, {k: {} for k in queue}, {}, {}
+    cnt, known, clock, hist, calls, crossed = {}, {k: {} for k in queue}, {}, {}, [], [0]
 
     def V(name, a=0, b=None, step=1, p0=0, p1=128):
         buf, off, w = AT[name] if name in AT else (name, 0, SCRATCH[name][1][1])
@@ -85,9 +162,6 @@ def rank_program(g, core, T, topo):
 
     def on(r, p0, n=64):
         return r[:4] + (p0, p0 + n)
-
-    def Z(name, a=0, b=None, step=1):
-        return V(name, a, b, step, 0, 32)
 
     def back(r):
         return r[:6] + (True,)
@@ -97,26 +171,15 @@ def rank_program(g, core, T, topo):
             return T[r[0]][r[4]:r[5], r[2] - 1:r[1] - 1:-1]
         return T[r[0]][r[4]:r[5], r[1]:r[2]] if r[3] == 1 else T[r[0]][r[4]:r[5], r[1]:r[2]:r[3]]
 
-    def meets(a, b):
-        if a[1] >= b[2] or b[1] >= a[2] or a[4] >= b[5] or b[4] >= a[5]:
-            return False
-        return not (a[3] == b[3] and a[3] > 1 and (a[1] - b[1]) % a[3])
-
-    def grown(r):
-        return (r[0], r[1] // 512 * 512, -(-r[2] // 512) * 512, 1, 0, 128)
-
-    def split(reads, writes):
-        ps = [r for r in list(reads) + list(writes) if SCRATCH[r[0]][0] == "psum"]
-        return ([r for r in reads if SCRATCH[r[0]][0] != "psum"],
-                [r for r in writes if SCRATCH[r[0]][0] != "psum"] + [grown(r) for r in ps])
+    size = lambda r: len(range(*r[1:4]))
+    kind = lambda r: SCRATCH[r[0]][2]
 
     def use(qn, reads, writes):
         reads, writes = split(reads, writes)
         need = {}
-        for r, w in [(r, False) for r in reads] + [(r, True) for r in writes]:
-            for e, ew, sem, val in hist.get(r[0], []):
-                if (w or ew) and meets(r, e) and known[qn].get(sem, 0) < val:
-                    need[sem] = max(need.get(sem, 0), val)
+        for sem, val in behind(hist, reads, writes):
+            if known[qn].get(sem, 0) < val:
+                need[sem] = max(need.get(sem, 0), val)
         for sem in sorted(need):
             if any(o != sem and clock[(o, need[o])].get(sem, 0) >= need[sem] for o in need):
                 continue
@@ -126,174 +189,188 @@ def rank_program(g, core, T, topo):
                 known[qn][s2] = max(known[qn].get(s2, 0), v2)
             known[qn][sem] = max(known[qn].get(sem, 0), need[sem])
 
-    def mark(sem, val, reads, writes):
-        reads, writes = split(reads, writes)
-        for r in writes:
-            hist[r[0]] = [h for h in hist.get(r[0], [])
-                          if not ((r[3] == 1 or h[0] == r) and r[1] <= h[0][1] and h[0][2] <= r[2] and r[4] <= h[0][4] and h[0][5] <= r[5])]
-        for r, w in [(r, False) for r in reads] + [(r, True) for r in writes]:
-            hist.setdefault(r[0], []).append((r, w, sem, val))
-
-    def done(qn, inst, sem, n, reads, writes):
+    def counted(sem, n, reads, writes, before):
         cnt[sem] = cnt.get(sem, 0) + n
-        inst.then_inc(T.sem[sem], n)
-        clock[(sem, cnt[sem])] = dict(known[qn])
-        mark(sem, cnt[sem], reads, writes)
+        clock[(sem, cnt[sem])] = dict(before)
+        noted(hist, *split(reads, writes), (sem, cnt[sem]))
 
-    def emit(qn, fn, outs, ins):
-        use(qn, ins, outs)
-        if qn == "g" and known["g"].get("eg", 0) < cnt.get("eg", 0):
-            g.wait_ge(T.sem.eg, cnt["eg"])
-            known["g"]["eg"] = cnt["eg"]
-        done(qn, fn(), esem[qn], 1, ins, outs)
+    def upto(qn, sem, val):
+        if known[qn].get(sem, 0) < val:
+            queue[qn].wait_ge(T.sem[sem], val)
+            known[qn][sem] = val
 
-    def dmas(sem, items):
-        tot = cnt.get(sem, 0) + 16 * len(items)
-        merged = {}
-        for qn, out, in_, outs, ins in items:
+    def put(ways, outs, ins, how=None):
+        def run(qn):
             use(qn, ins, outs)
-            queue[qn].dma_start(out, in_).then_inc(T.sem[sem], 16)
-            for s, v in known[qn].items():
-                merged[s] = max(merged.get(s, 0), v)
-        cnt[sem] = tot
-        clock[(sem, tot)] = merged
-        for qn, out, in_, outs, ins in items:
-            mark(sem, tot, ins, outs)
+            if qn == "g":
+                upto("g", "eg", cnt.get("eg", 0))
+            if qn == "v" and how == "port":
+                upto("v", "ev", crossed[0])
+            ways[qn][1]().then_inc(T.sem[esem[qn]], 1)
+            counted(esem[qn], 1, ins, outs, known[qn])
+            if how == "cross":
+                crossed[0] = cnt["ev"]
+        calls.append(({q: w[0] for q, w in ways.items()}, [run], ins, outs, None, how))
 
-    def arrives(sem, n, writes):
-        cnt[sem] = cnt.get(sem, 0) + n
-        clock[(sem, cnt[sem])] = {}
-        mark(sem, cnt[sem], [], writes)
+    def lands(cycles, outs):
+        calls.append(({None: cycles}, [lambda qn: None], [], outs, len([c for c in calls]) - 1 - lands_behind[0], None))
+        lands_behind[0] += 1
 
-    def ind(win, off):
-        return A(win).indirect(A(off))
+    lands_behind = [0]
+
+    def dmas(sem, items, cycles=PLAN["load"]):
+        def run(qn):
+            merged = {}
+            for q, out, in_, outs, ins in items:
+                use(q, ins, outs)
+                queue[q].dma_start(out, in_).then_inc(T.sem[sem], 16)
+                for s, v in known[q].items():
+                    merged[s] = max(merged.get(s, 0), v)
+            counted(sem, 16 * len(items), [r for i in items for r in i[4]], [r for i in items for r in i[3]], merged)
+        calls.append(({items[0][0]: 60.0 * len(items)}, [run], [r for i in items for r in i[4]], [r for i in items for r in i[3]], None, None))
+        lands_behind[0] = 0
+        lands(cycles, [r for i in items for r in i[3]])
+
+    def cycles(n, *sides):
+        return max(64.0, n * (0.5 if all(BYTES[kind(r)] == 2 for r in sides) else 1.0))
+
+    gather = lambda off, fixed: fixed + PLAN["gather"] * 16 * size(off)
+    ind = lambda win, off: A(win).indirect(A(off))
+
+    def move(by, out, in_, off=None):
+        ways = {}
+        if "v" in by:
+            ways["v"] = (gather(off, 60) if off else cycles(size(out), out, in_),
+                         lambda: g.vector.tensor_copy(A(out), A(in_) if off is None else ind(in_, off)))
+        if "s" in by:
+            ways["s"] = (gather(off, 80) if off else max(64.0, size(out)),
+                         lambda: g.scalar.activation(A(out), A(in_) if off is None else ind(in_, off), AF.Copy))
+        if "g" in by:
+            ways["g"] = (200.0 + 2 * size(out), lambda: g.affine_select(A(out), A(in_), [[0, size(out)]], ALU.is_gt, 0.0, 1, 0))
+        put(ways, [out], [in_] + ([off] if off else []), "port" if off or kind(out) == kind(in_) else None)
 
     def cp(out, in_, off=None):
-        emit("v", lambda: g.vector.tensor_copy(A(out), A(in_) if off is None else ind(in_, off)), [out], [in_] + ([off] if off else []))
+        move("v", out, in_, off)
 
-    def ts(out, in0, s1, op0, s2=None, op1=None):
-        cols = [s for s in (s1, s2) if isinstance(s, tuple)]
-        val = lambda s: A(s) if isinstance(s, tuple) else s
+    val = lambda s: A(s) if isinstance(s, tuple) else s
+
+    def ts(out, in0, s1, op0, s2=None, op1=None, also=None):
         if op1 is None:
             fn = lambda: g.vector.tensor_scalar(A(out), A(in0), val(s1), None, op0)
         else:
             fn = lambda: g.vector.tensor_scalar(A(out), A(in0), val(s1), val(s2), op0, op1)
-        emit("v", fn, [out], [in0] + cols)
+        ways = {"v": (cycles(size(out), out, in0), fn)}
+        if also:
+            ways["s"] = (max(64.0, size(out)), lambda: g.scalar.activation(A(out), A(in0), also[0], scale=val(also[1]), bias=val(also[2])))
+        cols = [s for s in (s1, s2) + tuple(also or ()) if isinstance(s, tuple)]
+        put(ways, [out], [in0] + cols, "port" if kind(in0) == B16 else None)
+
+    def affine(out, in_, scale, bias):
+        ts(out, in_, scale, ALU.mult, bias, ALU.add, (AF.Identity, scale, bias))
 
     def tt(out, a, b, op):
-        emit("v", lambda: g.vector.tensor_tensor(A(out), A(a), A(b), op), [out], [a, b])
+        put({"v": (max(64.0, 2.0 * size(out)), lambda: g.vector.tensor_tensor(A(out), A(a), A(b), op))}, [out], [a, b], "cross" if a[4] != b[4] else None)
 
     def red(out, in_, op, negate=False):
-        emit("v", lambda: g.vector.tensor_reduce(A(out), A(in_), AxisListType.X, op, negate=negate), [out], [in_])
+        put({"v": (max(64.0, size(in_)), lambda: g.vector.tensor_reduce(A(out), A(in_), AxisListType.X, op, negate=negate))}, [out], [in_])
 
     def scan(out, d0, d1, op0, op1, first=0.0):
-        col = isinstance(first, tuple)
-        emit("v", lambda: g.vector.tensor_tensor_scan(A(out), A(d0), A(d1), A(first) if col else first, op0, op1), [out], [d0, d1] + ([first] if col else []))
+        put({"v": (cycles(size(out), out, d0, d1), lambda: g.vector.tensor_tensor_scan(A(out), A(d0), A(d1), val(first), op0, op1))},
+            [out], [d0, d1] + ([first] if isinstance(first, tuple) else []))
 
     def tr(out, in_):
-        emit("v", lambda: g.vector.transpose(A(out), A(in_)), [out], [in_])
+        put({"v": (cycles(size(out), out, in_), lambda: g.vector.transpose(A(out), A(in_)))}, [out], [in_], "port" if in_[0] != "bl" else None)
 
-    def fill(out, c):
-        emit("v", lambda: g.vector.memset(A(out), c), [out], [])
-
-    def act(out, in_, func=AF.Copy, off=None, accum=None, **kw):
-        src = lambda: A(in_) if off is None else ind(in_, off)
-        cols = [v for v in kw.values() if isinstance(v, tuple)]
+    def act(out, in_, func, accum=None, **kw):
         def fn():
-            k2 = {k: A(v) if isinstance(v, tuple) else v for k, v in kw.items()}
+            k2 = {k: val(v) for k, v in kw.items()}
             if accum is not None:
                 k2["accum_out"] = A(accum)
-            return g.scalar.activation(A(out), src(), func, **k2)
-        emit("s", fn, [out] + ([accum] if accum else []), [in_] + cols + ([off] if off else []))
+            return g.scalar.activation(A(out), A(in_), func, **k2)
+        put({"s": (max(64.0, size(out)) + (24 if accum else 0), fn)}, [out] + ([accum] if accum else []), [in_] + [v for v in kw.values() if isinstance(v, tuple)])
 
-    def move(by, out, in_, off=None):
-        if by == "v":
-            cp(out, in_, off)
-        elif by == "s":
-            act(out, in_, off=off)
-        else:
-            select(out, in_, [[0, len(range(*out[1:4]))]], ALU.is_gt, 0.0, 1, 0)
+    def counting(out, pattern, base, cm):
+        if kind(out) == I32:
+            return lambda: g.iota(A(out), pattern, base, cm)
+        return lambda: g.iota(A(out), pattern, base, cm, allow_small_or_imprecise_dtypes=True)
 
     def iota(out, pattern, base, cm):
-        if SCRATCH[out[0]][2] == I32:
-            fn = lambda: g.iota(A(out), pattern, base, cm)
-        else:
-            fn = lambda: g.iota(A(out), pattern, base, cm, allow_small_or_imprecise_dtypes=True)
-        emit("g", fn, [out], [])
+        put({"g": (160.0 + 2 * size(out), counting(out, pattern, base, cm))}, [out], [])
 
-    def const(out, c):
-        iota(out, [[0, len(range(*out[1:4]))]], int(c), 0)
+    def fill(out, c, by="vg"):
+        ways = {"v": (cycles(size(out), out), lambda: g.vector.memset(A(out), c))}
+        if "g" in by:
+            ways["g"] = (160.0 + 2 * size(out), counting(out, [[0, size(out)]], int(c), 0))
+        put(ways, [out], [])
 
     def select(out, in_, pattern, cmp, fillv, base, cm):
-        emit("g", lambda: g.affine_select(A(out), A(in_), pattern, cmp, fillv, base, cm), [out], [in_])
+        put({"g": (200.0 + 2 * size(out), lambda: g.affine_select(A(out), A(in_), pattern, cmp, fillv, base, cm))}, [out], [in_])
 
     def quant(q, s, in_):
-        emit("v", lambda: g.vector.quantize_mx(A(q), A(s), A(in_)), [q, s], [in_])
+        put({"v": (15 + 0.27 * size(in_), lambda: g.vector.quantize_mx(A(q), A(s), A(in_)))}, [q, s], [in_])
 
     def mm(out, lq, ls, rq, rs, start, stop):
-        emit("t", lambda: g.tensor.matmul_mx(A(out), A(lq), A(ls), A(rq), A(rs), start, stop), [out], [lq, ls, rq, rs])
-
-    def codes(qo, qi, off):
-        emit("v", lambda: g.vector.tensor_copy(A(qo).bitcast(dt.uint32), A(qi).bitcast(dt.uint32).indirect(A(off))), [qo], [qi, off])
+        put({"t": (0.75 * (size(out) + 16), lambda: g.tensor.matmul_mx(A(out), A(lq), A(ls), A(rq), A(rs), start, stop))}, [out], [lq, ls, rq, rs])
 
     def pick(qo, so, qi, si, off):
-        codes(qo, qi, off)
-        act(so, si, off=off)
+        put({"v": (gather(off, 60), lambda: g.vector.tensor_copy(A(qo).bitcast(dt.uint32), A(qi).bitcast(dt.uint32).indirect(A(off))))}, [qo], [qi, off], "port")
+        move("s", so, si, off)
 
     def halves(out, r, op, p=0, n=64):
         tt(out, on(r, p, n), on(r, 64 + p, n), op)
 
     beside = lambda a, b: topo.same_plane(topo.chip(T.cores[a]), topo.chip(T.cores[b]))
-    turn = lambda r: sorted([(r + k) % N for k in range(1, N)], key=lambda d: beside(r, d))
-    others = turn(rank)
-    senders = sorted(others, key=lambda d: turn(d).index(rank))
+    farthest = lambda r: sorted([(r + k) % N for k in range(1, N)], key=lambda d: beside(r, d))
+    pair_of = lambda r: sorted([r] + [d for d in range(N) if d != r and beside(r, d)])
+    far_of = lambda r: [d for d in range(N) if d not in pair_of(r)][pair_of(r).index(r)]
+    nearest = lambda r: sorted([d for d in range(N) if d != r], key=lambda d: (not beside(r, d), d != far_of(r)))
+    others = farthest(rank)
     mask3 = 0xFFFF
     for d in others:
         mask3 &= topo.mask(core, T.cores[d])
     groups = bin(mask3).count("1")
 
-    def spread(piece, sem, order=others, src=None):
-        src = src or piece(rank)
-        use("g", [src], [])
-        ids = [DstId(rid=topo.addr(T.cores[d])[0], pnc=topo.addr(T.cores[d])[1]) for d in order]
-        g.remote_dma_fused([RemoteDMATransfer(dst_ids=ids, dma_engine_mask=mask3, remote_sem=T.sem[sem % rank], srcs=[A(src)], dsts=[A(piece(rank)) for d in others])],
-                           local_sem=T.sem.loc)
-        cnt["loc"] = cnt.get("loc", 0) + groups
-        for d in others:
-            arrives(sem % d, groups, [piece(d)])
+    def remote(src, call, n, landings):
+        def run(qn):
+            use("g", [src], [])
+            call()
+            cnt["loc"] = cnt.get("loc", 0) + n
+            for sem, r in landings:
+                counted(sem, n, [], [r], {})
+        calls.append(({"g": float(PLAN["call"])}, [run], [src], [], None, "remote"))
+        lands_behind[0] = 0
+        for i, (sem, r) in enumerate(landings):
+            lands(PLAN["way"] + (i + 1) * 128 // n * (PLAN["row"] + size(r) * BYTES[kind(r)] // 20), [r])
 
-    near = [d for d in others if beside(rank, d)][0]
-    pair = sorted([rank, near])
-    pair2 = [d for d in range(N) if d not in pair]
-    second = pair.index(rank)
-    far = pair2[second]
-    seconds = (pair[1], pair2[1])
-    stand = [PAD + K * ((d in pair) != (0 in pair)) for d in range(N)]
+    def spread(piece, sem, turn=farthest, src=None):
+        src = src or piece(rank)
+        ids = [DstId(rid=topo.addr(T.cores[d])[0], pnc=topo.addr(T.cores[d])[1]) for d in turn(rank)]
+        call = lambda: g.remote_dma_fused([RemoteDMATransfer(dst_ids=ids, dma_engine_mask=mask3, remote_sem=T.sem[sem % rank], srcs=[A(src)],
+                                                             dsts=[A(piece(rank)) for d in others])], local_sem=T.sem.loc)
+        remote(src, call, groups, [(sem % d, piece(d)) for d in sorted(others, key=lambda d: turn(d).index(rank))])
+
+    pair, far = pair_of(rank), far_of(rank)
+    near, second = sum(pair) - rank, pair.index(rank)
+    seconds = (pair[1], pair_of(far)[1])
+    stand = [PAD + K * (0 not in pair_of(d)) for d in range(N)]
     lows = [1 - stand[d] - K if d in seconds else stand[d] for d in range(N)]
     beyond = [sum(low > lows[d] for low in lows) for d in range(N)]
 
-    def swap(q, s, a, lands, d, semc, sems):
+    def swap(q, s, a, there, d, semc, sems):
         dst = T.cores[d]
         rid, pid = topo.addr(dst)[:2]
         mask, n = topo.mask(core, dst), len(topo.engines(core, dst))
-        use("g", [V(q, a, a + K)], [])
-        g.remote_dma(A(V(q, a, a + K)).bitcast(dt.uint8), A(V(q, a, a + K)).bitcast(dt.uint8), T.sem[semc], T.sem.loc, pid, rid, mask)
-        use("g", [V(s, a, a + K)], [])
-        g.remote_dma(A(V(s, a, a + K)), A(V(s, a, a + K)), T.sem[sems], T.sem.loc, pid, rid, mask)
-        cnt["loc"] = cnt.get("loc", 0) + 2 * n
-        arrives(semc, n, [V(q, lands, lands + K)])
-        arrives(sems, n, [V(s, lands, lands + K)])
+        qa, sa = V(q, a, a + K), V(s, a, a + K)
+        remote(qa, lambda: g.remote_dma(A(qa).bitcast(dt.uint8), A(qa).bitcast(dt.uint8), T.sem[semc], T.sem.loc, pid, rid, mask), n, [(semc, V(q, there, there + K))])
+        remote(sa, lambda: g.remote_dma(A(sa), A(sa), T.sem[sems], T.sem.loc, pid, rid, mask), n, [(sems, V(s, there, there + K))])
 
-    def turned(t, d, by, between=None):
+    def turned(t, d):
+        h = V("xh%d" % t, 8 * d, 8 * d + 8)
         for e in (0, 1):
-            move(by[e], V("xe", M * d + 16 * e, M * d + M, 32), V("xh%d" % t, 8 * d, 8 * d + 8))
-        if between:
-            between()
+            move("vs", V("xe", M * d + 16 * e, M * d + M, 32), h)
         tr(V("fh", M * d, M * d + M), V("xe", M * d, M * d + M))
-
-    def themselves(t, d):
         b = 32 * RK.index(d)
-        act(on(V("rb", 3 * H, 4 * H, 16), b, 32), on(V("xh%d" % t, 8 * d, 8 * d + 8), b, 32))
+        move("vs", on(V("rb", 3 * H, 4 * H, 16), b, 32), on(h, b, 32))
 
     def repeated(e):
         scan(V("xb", M * e, M * e + M), V("d32"), V("xz", M * e, M * e + M), ALU.mult, ALU.add)
@@ -310,51 +387,42 @@ def rank_program(g, core, T, topo):
     CF = lambda k: V("cf", k, k + 1)
     SCL, UPPER, SCOL, LCOL, GSCL, WSCL = [CF(k) for k in (0, 5, 6, 7, 16, 17)]
 
-    def lift(f, i):
-        scan(V("sc", H * i, H * i + H), V("d0", 0, H), piece(f, i), ALU.mult, ALU.add)
+    def handed(f, l, pieces=range(4), to=(0, 1)):
+        for i in pieces:
+            scan(V("sc", H * i, H * i + H), V("d0", 0, H), piece(f, i), ALU.mult, ALU.add)
+        for i in range(4):
+            for h in to:
+                move("vsg", on(wrun(f, h, OWN[1 - h][i]), 64 * h), on(piece(f, i), 64 - 64 * h))
+        for i in list(pieces)[::2]:
+            ts(V(l, 8 * i, 8 * i + 16), V("sc", H * i + 15, H * i + M, 16), WSCL, ALU.mult, float(WM), ALU.add)
 
-    def listed(l, i, j):
-        ts(V(l, 8 * i, 8 * j), V("sc", H * i + 15, H * j, 16), WSCL, ALU.mult, float(WM), ALU.add)
-
-    def cross(f, i, h, by):
-        move(by, on(wrun(f, 1 - h, OWN[h][i]), 64 - 64 * h), on(piece(f, i), 64 * h))
-
-    bank = lambda k, w: V("bl", 512 * k, 512 * k + w)
+    bank = lambda k, w, a=0: V("bl", 512 * k + a, 512 * k + a + w)
     half = [(H * h, H * h + H) for h in (0, 1)]
+    blk = RK.index(rank)
+    mine, own = 64 * (blk // 2), 2 * (blk % 2)
 
-    loads = []
-    for k in range(2 * J):
-        shift = 2 * (k % 2)
-        o = V("nbe", 0, 16 - shift, 1, 16 * k, 16 * k + 16)
-        loads.append(("ys"[k % 2], A(o), T.nb[:, 16 * (k // 2) + shift:16 * (k // 2) + 16], [o], []))
-    dmas("dnb", loads)
-    dmas("du", [("s", A(V("ut", 0, 16)), T.u[:, 0:16], [V("ut", 0, 16)], [])])
+    for q in (0, 1):
+        loads = []
+        for k in range(q, 2 * J, 2):
+            o = V("nbe", 0, 16 - 2 * q, 1, 16 * k, 16 * k + 16)
+            loads.append(("ys"[q], A(o), T.nb[:, 16 * (k // 2) + 2 * q:16 * (k // 2) + 16], [o], []))
+        dmas(("dnb", "du")[q], loads + [("s", A(V("ut", 0, 16)), T.u[:, 0:16], [V("ut", 0, 16)], [])] * q)
     for h in (0, 1):
         o = V("xt", 4 * H * h, 4 * H * h + 4 * H)
-        dmas("dx%d" % h, [("ys"[h], A(o), T.x[:, 4 * H * h:4 * H * h + 4 * H], [o], [])])
+        dmas("dx%d" % h, [("ys"[h], A(o), T.x[:, 4 * H * h:4 * H * h + 4 * H], [o], [])], PLAN["load"] * (1.4 + 0.3 * h))
     IP = lambda k: V("ip", k, k + 1)
     RI = lambda n: V("i128", 0, n)
     iota(V("iu"), [[1, 3], [0, 8]], 0, 0)
     iota(IP(0), [[0, 1]], 0, 1)
     iota(V("i128"), [[1, H]], 0, 0)
     o = 16 * rank
-    fill(V("xe", 0, M), 0.0)
-    for d in range(1, N):
-        act(V("xe", M * d, M * d + M), V("xe", 0, M))
-    fill(V("ut", 16, 512), 0.0)
-    fill(on(V("nbl", o, o + 8), 96, 32), 0)
-    cp(V("cu"), V("iu"))
-    ts(IP(1), IP(0), 6, ALU.logical_shift_right)
-    ts(IP(2), IP(0), 15, ALU.bitwise_and)
+    fill(V("ut", 16, 512), 0.0, "v")
+    fill(on(V("nbl", o, o + 8), 96, 32), 0, "v")
     for e in (0, 1):
         cp(on(V("nbl", o + e, o + 8, 2), 0, 96), on(V("nbe", e, 16, 4), 0, 96))
     spread(lambda d: V("nbl", 16 * d, 16 * d + 8), "nb%d")
+    cp(V("cu"), V("iu"))
     quant(V("qu"), V("su"), V("ut"))
-    ts(IP(3), IP(0), 31, ALU.bitwise_and)
-    fill(V("dw"), 0.0)
-    pick(V("qr", 0, 128), V("sr", 0, 128), V("qu"), V("su"), V("cu", 0, 8))
-    for k, (a, s) in enumerate(RUNS):
-        act(V("cw", H * k, H * k + H), V("i128"), AF.Identity, scale=s * UNIT, bias=a * UNIT)
 
     def height(k, t, q, s, a, n):
         mm(bank(k, n), V("qr", 128 * t, 128 * t + 128), V("sr", 128 * t, 128 * t + 128), V(q, a, a + n), V(s, a, a + n), True, True)
@@ -362,429 +430,289 @@ def rank_program(g, core, T, topo):
     def share(t):
         spread(lambda d: V("xh%d" % t, 8 * d, 8 * d + 8), "h%d_" % t + "%d")
 
+    for t in range(R):
+        pick(V("qr", H * t, H * t + H), V("sr", H * t, H * t + H), V("qu"), V("su"), V("cu", 8 * t, 8 * t + 8))
     for h in (0, 1):
         quant(V("qc0", *half[h]), V("scp0", *half[h]), V("xt", 4 * H * h, 4 * H * h + 4 * H))
-    for h in (0, 1):
         height(h, 0, "qc0", "scp0", H * h, H)
-    def gathered(d):
-        for j in range(J):
-            cp(on(V("lnb", 8 * j, 8 * j + 8), 32 * RK.index(d), 32), on(V("nbl", 16 * d, 16 * d + 8), 32 * j, 32))
-
-    cp(V("cf", 5, 8), V("ip", 1, 4))
-    gathered(rank)
-    for h in (0, 1):
         tr(V("ht", *half[h]), bank(h, H))
-    ts(V("x0", 0, 4), RI(4), 32.0, ALU.mult, LCOL, ALU.add)
-    ts(SCL, SCOL, 15.0, ALU.is_equal, 1.0 - 1.0 / UP, ALU.mult)
-    cp(V("xh0", 8 * rank, 8 * rank + 8), V("ht", 0, M, 32))
+    move("vs", V("xh0", 8 * rank, 8 * rank + 8), V("ht", 0, M, 32))
     share(0)
 
-    iota(V("id16"), [[1, 16]], 128, -1)
-    fill(V("one"), 1.0)
-    iota(V("ki"), [[16, 16]], 0, 0)
-    runs = lambda d, n, k: select(V(d), V("one", 0, n), [[0, n // k], [1, k]], ALU.is_gt, 0.0, 0, 0)
-    runs("d4", H, 4)
-    const(V("xz", 0, HM), 0)
-    runs("d32", M, 32)
-    for i, first in enumerate((0, H + 64)):
-        iota(on(V("fq", 64 * i, 64 * i + 64), 0), [[M * (2 * i - 1), 2], [0, 32]], -2 * first - 1, -2)
-    for p in (0, 64):
-        iota(on(V("nn", 0, 2), p), [[H, 2]], 0, 1)
-        iota(on(V("nn", 2, 4), p), [[-H, 2]], H + 64, 1)
-    for i, first in enumerate((64, H)):
-        iota(on(V("fq", 64 * i, 64 * i + 64), 64), [[M * (2 * i - 1), 2], [0, 32]], -2 * first - 1, -2)
-    for b in range(4):
-        iota(on(V("cf", 24, 26), 32 * b, 32), [[HM, 2]], -HM, HM)
-    for k in range(4):
-        const(V("ea", (H + 32) * k + H, (H + 32) * (k + 1)), 0)
-    for e in (0, 1):
-        select(V("et", 528 * e, 528 * e + 528), V("one"), [[1, 528]], ALU.is_equal, 0.0, -2 - e, -4)
-    const(V("dd", 0, SEG * KC, SEG), 0)
-    const(V("di", 0, SEG * KC), 1)
-    const(V("di", 0, SEG * KC, SEG), 2 * M)
-    const(V("di", 32, SEG * KC, SEG), H - 31)
-    iota(V("di", SEG - 1, SEG * KC, SEG), [[0, KC]], H - 31, -1)
-    const(V("iv", 0, H, 8), -beyond[0])
-    const(V("kr", 0, 32), K - 1)
-    const(V("xz", HM, NM), 0)
-    const(V("km", 32, 160), 0)
+    fill(V("xe", 0, M), 0.0, "v")
+    for d in range(1, N):
+        move("vs", V("xe", M * d, M * d + M), V("xe", 0, M))
+    ts(IP(1), IP(0), 6, ALU.logical_shift_right)
+    ts(IP(2), IP(0), 15, ALU.bitwise_and)
+    ts(IP(3), IP(0), 31, ALU.bitwise_and)
+    cp(V("cf", 5, 8), V("ip", 1, 4))
+    for k, (a, s) in enumerate(RUNS):
+        affine(V("cw", H * k, H * k + H), V("i128"), s * UNIT, a * UNIT)
+        affine(grun("idn", k), V("i128"), 1.0, float(H * k))
     for d in range(N):
-        const(V("low", d, d + 1), lows[d])
-    runs("d8", H, 8)
-    const(V("pd", 0, 16, 2), -8)
-
-    ts(V("crep"), RI(16), 0.0, ALU.mult, SCOL, ALU.add)
-    ts(SCL, SCL, 1.0 / UP, ALU.max)
-    ts(CF(23), UPPER, float(ALPHA[1] - ALPHA[0]), ALU.mult, float(ALPHA[0]), ALU.add)
-    turned(0, rank, "ss")
+        for j in range(J):
+            cp(on(V("lnb", 8 * j, 8 * j + 8), 32 * RK.index(d), 32), on(V("nbl", 16 * d, 16 * d + 8), 32 * j, 32))
+    affine(V("x0", 0, 4), RI(4), 32.0, LCOL)
+    for a, b in ((0, 12), (12, 24)):
+        move("vs", V("ca", 16 * a, 16 * b), V("cw"), V("lnb", a, b))
+    tr(V("cb", 0, 3 * H), V("ca"))
     for b in range(4):
         for e in (0, 1):
             a, s = RUNS[2 * RK[b] + e]
-            act(on(V("cb", 3 * H + 64 * e, 3 * H + 64 * e + 64, 16), 32 * b, 32), on(V("x0", 0, 4), 32 * b, 32), AF.Identity, scale=s * UNIT, bias=a * UNIT)
+            affine(on(V("cb", 3 * H + 64 * e, 3 * H + 64 * e + 64, 16), 32 * b, 32), on(V("x0", 0, 4), 32 * b, 32), s * UNIT, a * UNIT)
+    move("vs", V("lost", 0, H, 4), V("cb", 0, HM, 16))
+    ts(SCL, SCOL, 15.0, ALU.is_equal, 1.0 - 1.0 / UP, ALU.mult)
+    ts(SCL, SCL, 1.0 / UP, ALU.max)
+    affine(CF(23), UPPER, float(ALPHA[1] - ALPHA[0]), float(ALPHA[0]))
+    affine(GSCL, SCL, 1.0 / UNIT, 0.0)
+    tt(WSCL, GSCL, CF(23), ALU.mult)
+    iota(V("id16"), [[1, 16]], 128, -1)
     ts(V("id16"), V("id16"), 15, ALU.bitwise_and)
-    ts(GSCL, SCL, 1.0 / UNIT, ALU.mult)
-    for d in senders:
-        gathered(d)
-
-    def tables():
-        act(V("d0"), V("d16"), off=V("crep"))
-        act(V("ki"), V("ki"), AF.Identity, bias=SCOL)
-        for k in range(8):
-            act(grun("idn", k), V("i128"), AF.Identity, bias=float(H * k))
-        for h in (0, 1):
-            n0 = M * rank + H * h
-            act(V("sn", 8 * h, 8 * h + 8), V("ki", 0, 8), AF.Identity, scale=float(place(n0 + 1) - place(n0)), bias=float(place(n0)))
-        act(V("want", 0, KC), V("ki", 0, KC), AF.Identity, bias=(1.0 - K) * second)
-        act(V("want", 8, 8 + KC), V("ki", 0, KC), AF.Identity, scale=-float(NM), bias=(K - 1.0) * second * NM)
-        for b in range(4):
-            act(on(V("fq", H, M), 32 * b, 32), on(V("fq", 0, H), 32 * ((b + 1) % 2), 32))
-
-    def own_codes(e):
+    ts(V("d16"), V("id16"), 1.0, ALU.is_equal, UP, ALU.mult)
+    ts(V("d17"), V("id16"), 0.0, ALU.is_gt)
+    tt(V("d16"), V("d16"), V("d17"), ALU.add)
+    ts(V("crep"), RI(16), 0.0, ALU.mult, SCOL, ALU.add)
+    move("vs", V("d0"), V("d16"), V("crep"))
+    fill(V("one"), 1.0)
+    for d, n, k in (("d4", H, 4), ("d32", M, 32), ("d8", H, 8)):
+        select(V(d), V("one", 0, n), [[0, n // k], [1, k]], ALU.is_gt, 0.0, 0, 0)
+    for a in (0, HM):
+        fill(V("xz", a, a + HM), 0.0)
+    affine(V("ki"), RI(16), 16.0, SCOL)
+    for h in (0, 1):
+        n0 = M * rank + H * h
+        affine(V("sn", 8 * h, 8 * h + 8), V("ki", 0, 8), float(place(n0 + 1) - place(n0)), float(place(n0)))
+    for p in (0, 64):
+        iota(on(V("nn", 0, 2), p), [[H, 2]], 0, 1)
+        iota(on(V("nn", 2, 4), p), [[-H, 2]], H + 64, 1)
+    for e, cols in enumerate(((0, 4, 3), (1, 3, 1))):
         a, s = RUNS[2 * rank + e]
-        cols = (0, 4, 3) if e == 0 else (1, 3, 1)
-        ts(V("cv", *cols), V("nn", *cols), s * UNIT, ALU.mult, (a - s * H * e) * UNIT, ALU.add)
-
-    def unpacking(b):
+        affine(V("cv", *cols), V("nn", *cols), s * UNIT, (a - s * H * e) * UNIT)
+    fill(on(V("nr"), 64 - mine), 0.0)
+    for p, firsts in ((0, (0, H + 64)), (64, (64, H))):
+        for i, first in enumerate(firsts):
+            iota(on(V("fq", 64 * i, 64 * i + 64), p), [[M * (2 * i - 1), 2], [0, 32]], -2 * first - 1, -2)
+    for b in range(4):
+        move("vsg", on(V("fq", H, M), 32 * b, 32), on(V("fq", 0, H), 32 * ((b + 1) % 2), 32))
+    for k in (0, 1):
+        affine(CF(24 + k), LCOL, float(HM), float(HM * (k - 1)))
+    for k in range(4):
+        fill(V("ea", (H + 32) * k + H, (H + 32) * (k + 1)), 0.0)
+    for e in (0, 1):
+        select(V("et", 528 * e, 528 * e + 528), V("one"), [[1, 528]], ALU.is_equal, 0.0, -2 - e, -4)
+    unpack = [(V("qe", 128 * b, 128 * b + 128), V("se", 128 * b, 128 * b + 128)) for b in range(4)]
+    for b in range(4):
         a = 528 * (b % 2) + 2 - b // 2 * 2
-        quant(V("qe", 128 * b, 128 * b + 128), V("se", 128 * b, 128 * b + 128), V("et", a, a + 512))
-
-    later = [
-        lambda: ts(V("d16"), V("id16"), 1.0, ALU.is_equal, UP, ALU.mult),
-        lambda: ts(V("d17"), V("id16"), 0.0, ALU.is_gt),
-        lambda: tt(V("d16"), V("d16"), V("d17"), ALU.add),
-        lambda: tt(WSCL, GSCL, CF(23), ALU.mult),
-        lambda: ts(CF(26), LCOL, 16.0, ALU.is_lt, 12.0, ALU.mult),
-        lambda: ts(CF(27), LCOL, 16.0, ALU.is_lt, 4.0, ALU.mult),
-        lambda: fill(V("fs", 2 * GM - 16, 2 * GM), stand[N - 1] - 0.5 + K * (N - 1 not in seconds)),
-        lambda: ts(CF(27), CF(27), 0.5, ALU.add),
-        lambda: ts(V("pd", 1, 16, 2), V("dw", 0, 8), -8.0, ALU.add, CF(26), ALU.add),
-        lambda: ts(CF(22), LCOL, -float(M), ALU.add),
-    ]
-
-    def meanwhile(n=2):
-        for f in later[:n]:
-            f()
-        del later[:n]
+        quant(*unpack[b], V("et", a, a + 512))
+    affine(V("want", 0, KC), V("ki", 0, KC), 1.0, (1.0 - K) * second)
+    affine(V("want", 8, 8 + KC), V("ki", 0, KC), -float(NM), (K - 1.0) * second * NM)
+    fill(V("dd", 0, SEG * KC, SEG), 0.0)
+    fill(V("di", 0, SEG * KC), 1.0)
+    fill(V("di", 0, SEG * KC, SEG), 2.0 * M)
+    fill(V("di", 32, SEG * KC, SEG), H - 31.0)
+    iota(V("di", SEG - 1, SEG * KC, SEG), [[0, KC]], H - 31, -1)
+    affine(CF(22), LCOL, 1.0, -float(M))
+    fill(V("kr"), K - 1.0)
+    fill(V("km", 32, 160), 0.0)
+    for d in range(N):
+        fill(V("low", d, d + 1), float(lows[d]))
+    fill(V("dw"), -8.0)
+    fill(V("pd", 0, 16, 2), -8.0)
+    ts(CF(26), LCOL, 16.0, ALU.is_lt, 12.0, ALU.mult)
+    affine(V("pd", 1, 16, 2), V("dw", 0, 8), 1.0, CF(26))
+    affine(CF(28), CF(26), 1.0 / 3, 0.5)
 
     ACC = lambda k: V("acc", k, k + 1)
     for t in range(R):
-        qc, sp = "qc%d" % t, "scp%d" % t
+        qc, sp, nq, ns = "qc%d" % t, "scp%d" % t, "qc%d" % (t + 1), "scp%d" % (t + 1)
         final = t + 1 == R
-        if final:
-            quant(V("qw"), V("sw"), V("wt"))
-        turned(t, senders[0], "vs" if t else "ss", meanwhile)
-        turned(t, senders[1], "ss")
-        turned(t, senders[2], "ss")
         for d in range(N):
-            themselves(t, d)
+            turned(t, d)
         if not t:
-            act(V("ca"), V("cw"), off=V("lnb"))
-        meanwhile()
-        act(V("ra", H, 2 * H + 32), V("fh"), off=V("lnb", 8, 18))
-        cp(V("ra", 0, H), V("fh"), V("lnb", 0, 8))
-        act(V("ra", 2 * H + 32, 3 * H), V("fh"), off=V("lnb", 18, 24))
-        if not t:
-            tables()
-            tr(V("cb", 0, 3 * H), V("ca"))
-            dmas("dw", [("y", A(V("wt")), T.w[:], [V("wt")], [V("fh")])])
-        tr(V("rb", 0, H), V("ra", 0, H))
-        tr(V("rb", H, 2 * H + 32), V("ra", H, 2 * H + 32))
-        tr(V("rb", 2 * H + 32, 3 * H), V("ra", 2 * H + 32, 3 * H))
+            dmas("dw", [("y", A(V("wt")), T.w[:], [V("wt")], [V("fh", 0, 16)])])
+            quant(V("qw"), V("sw"), V("wt"))
+        for by, a, b in (("v", 0, 8), ("s", 8, 18), ("s", 18, 24)):
+            move(by, V("ra", 16 * a, 16 * b), V("fh"), V("lnb", a, b))
+            tr(V("rb", 16 * a, 16 * b), V("ra", 16 * a, 16 * b))
         four = lambda a, b: V("rb", H * a, H * b, 16)
         for r, a, b in ((1, 3, 4), (3, 0, 1), (1, 0, 3), (2, 0, 2), (2, 2, 4), (3, 1, 4)):
             tt(V("lost", 32 * a + r, 32 * b, 4), four((a + r) % 4, (b - 1 + r) % 4 + 1), four(a, b), ALU.is_gt)
-        if not t:
-            cp(V("lost", 0, H, 4), V("cb", 0, HM, 16))
-        meanwhile(3)
         scan(V("key"), V("d4"), V("lost"), ALU.mult, ALU.add)
-        meanwhile(3)
         tt(V("b2"), V("key", 3, 64, 4), V("key", 67, H, 4), ALU.min)
-        meanwhile(3)
         for e in (0, 1):
             for b in range(4):
                 src = 64 * (b // 2) + 32 * e
                 tt(on(V("xz", M * e, M * e + M, 32), 32 * b, 32), on(V("b2", 0, 8), src, 32), on(V("b2", 8, 16), src, 32), ALU.min)
-        for e in (0, 1):
             repeated(e)
-        for i in (0, 1, 3, 2):
+        for i in range(4):
             tr(piece("fa", i), V("xb", H * i, H * i + H))
-        cross("fa", 0, 0, "s")
-        cross("fa", 0, 1, "g" if t else "v")
-        lift("fa", 1)
-        cross("fa", 1, 0, "s")
-        cross("fa", 1, 1, "v")
-        lift("fa", 0)
-        lift("fa", 3)
-        cross("fa", 3, 1, "s")
-        lift("fa", 2)
-        cross("fa", 3, 0, "v")
-        cross("fa", 2, 0, "v")
-        cross("fa", 2, 1, "s")
-        listed("la", 0, 2)
-        listed("la", 2, 4)
-        for k in range(9):
-            fi, fo, li, lw = ("fa", "fb", "la", "lb") if k % 2 == 0 else ("fb", "fa", "lb", "la")
+        handed("fa", "la")
+        for b in (0, 1):
+            p, a = mine + 32 * b, H * own + 32 * b
+            tt(on(V("nr", 0, 2), p, 32), on(V("xz", a, a + M, H), p, 32), on(V("cv", 0, 2), p, 32), ALU.not_equal)
+            tt(back(on(V("nr", 2, 4), p, 32)), on(V("xz", a + 64, a + 64 + H + 1, H), p, 32), back(on(V("cv", 2, 4), p, 32)), ALU.not_equal)
+        affine(on(V("nr"), mine), on(V("nr"), mine), -2.0 * HM * NM, 0.0)
+
+        def doubling(k):
+            fi, fo, li, lo = ("fa", "fb", "la", "lb") if k % 2 == 0 else ("fb", "fa", "lb", "la")
             for i, by in ((0, "v"), (1, "s"), (3, "v"), (2, "s")):
                 move(by, piece(fo, i), V(fi), V(li, 8 * i, 8 * i + 8))
-            lift(fo, 0)
-            cross(fo, 1, 0, "s")
-            lift(fo, 1)
-            cross(fo, 0, 0, "s")
-            cross(fo, 0, 1, "g" if t else "v")
-            cross(fo, 1, 1, "v")
-            lift(fo, 3)
-            cross(fo, 3, 1, "s")
-            if t:
-                lift(fo, 2)
-                cross(fo, 2, 0, "v")
-                cross(fo, 3, 0, "v")
-                cross(fo, 2, 1, "s")
-                listed(lw, 0, 2)
+            if k < 8:
+                handed(fo, lo)
             else:
-                cross(fo, 2, 0, "v")
-                lift(fo, 2)
-                cross(fo, 2, 1, "s")
-                listed(lw, 0, 2)
-                cross(fo, 3, 0, "v")
-            listed(lw, 2, 4)
-        for by, a, b in (("v", 0, H), ("s", H, M), ("s", M, HM)):
-            move(by, V("fr", a, b), V("fb"), V("lb", a // 16, b // 16))
-        meanwhile(len(later))
-        if not t:
-            own_codes(0)
-            own_codes(1)
-        EE = lambda j, a, b: V("ee", HM * j + a, HM * j + b)
-        same = lambda j, a, b: ts(EE(j, a, b), V("fr", a, b), V("cv", j, j + 1), ALU.is_equal, float(HM), ALU.mult)
-        count = lambda j: scan(V("so", M * j, M * j + M), EE(j, 0, M), EE(j, M, HM), ALU.add, ALU.add)
+                handed(fo, lo, (own, own + 1), (mine // 64,))
+            return fo
+
+        for k in range(EARLY + 1):
+            f = doubling(k)
         for j in range(4):
-            same(j, 0, M)
-        for j in range(3):
-            same(j, M, HM)
-        count(0)
-        same(3, M, HM)
-        for j in (1, 2, 3):
-            count(j)
-        blk = RK.index(rank)
-        mine, at0 = 64 * (blk // 2), M * (blk % 2)
-        scan(on(V("sc", 0, M), mine), on(V("d0", 0, M), mine), on(V("fr", at0, at0 + M), mine), ALU.mult, ALU.add)
-        rho, itself = V("rho", 0, 16), V("rho", 16, 32)
-        for p in (0, 64):
-            act(on(rho, p), on(V("sc", 15, M, 16), mine), AF.Identity, scale=on(GSCL, mine), bias=float(GM))
+            for i in range(4):
+                ts(V("ee", HM * j + H * i, HM * j + H * i + H), piece(f, i), V("cv", j, j + 1), ALU.is_equal, float(HM), ALU.mult)
+            scan(V("so", M * j, M * j + M), V("ee", HM * j, HM * j + M), V("ee", HM * j + M, HM * j + HM), ALU.add, ALU.add, V("nr", j, j + 1))
         ends = V("so", M - 1, 4 * M, M)
         halves(on(V("aa"), 0), ends, ALU.add)
         halves(back(on(V("aa"), 64)), ends, ALU.add)
         for b in range(4):
             halves(on(V("ab"), 32 * b, 32), ends, ALU.add, 32 * ((b + 1) % 2), 32)
         for j in range(8):
-            out, less, size = V("xr", 32 * j, 32 * j + 32), V("fq", 32 * j, 32 * j + 32), V("aa" if j < 4 else "ab", j % 4, j % 4 + 1)
-            if j in (0, 1, 6, 7):
-                ts(out, less, size, ALU.add)
-            else:
-                act(out, less, AF.Identity, bias=size)
-            if j == 1:
-                cp(V("lro"), rho)
-        tt(itself, rho, V("sn"), ALU.is_equal)
-        tr(V("kf", *half[0]), V("xr", *half[0]))
-        tr(V("kf", *half[1]), V("xr", *half[1]))
-        ts(itself, itself, 2.0 * GM - 1, ALU.mult)
+            affine(V("xr", 32 * j, 32 * j + 32), V("fq", 32 * j, 32 * j + 32), 1.0, V("aa" if j < 4 else "ab", j % 4, j % 4 + 1))
+        for h in (0, 1):
+            tr(V("kf", *half[h]), V("xr", *half[h]))
         ms = "ms%d" % t
-        MS = lambda d: V(ms, 4 * d, 4 * d + 4)
+        MS = lambda d, ms=ms: V(ms, 4 * d, 4 * d + 4)
         EA = lambda i, h, n: V("ea", (H + 32) * (2 * i + h), (H + 32) * (2 * i + h) + n)
         for k in (0, 1):
             act(V("sg", M * k, M * k + M), V("kf"), AF.Sign, scale=-1.0, bias=CF(24 + k), accum=ACC(k))
+        affine(V(ms, 4 * N + 1, 4 * N + 4, 2), V("acc", 0, 2), -0.5, (M - 1) / 2)
         for h in (0, 1):
             for i in (0, 1):
                 ts(EA(i, h, H), V("kf", *half[h]), V("xr", 32 * i, 32 * i + 1), ALU.is_gt, 1.0 - 2.0 * second, ALU.mult)
-        act(V(ms, 4 * N + 1, 4 * N + 4, 2), V("acc", 0, 2), AF.Identity, scale=-0.5, bias=(M - 1) / 2)
-        tt(itself, itself, rho, ALU.max)
-        if not t:
-            unpacking(0)
         scan(V("pb", 0, H + 32), EA(0, 0, H + 32), EA(0, 1, H + 32), ALU.add, ALU.add)
         scan(back(V("pb", H + 32, 2 * H + 64)), EA(1, 0, H + 32), EA(1, 1, H + 32), ALU.add, ALU.add)
-        cp(V("lrm"), itself)
-        if not t:
-            unpacking(1)
         tr(V("ps"), V("pb", H, H + 64))
         if second:
             ts(V(ms, 4 * N, 4 * N + 4, 2), V("pb", H, H + 64, 32), 0.5 - K, ALU.max, float(stand[rank] + K - 1), ALU.add)
         else:
             ts(V(ms, 4 * N, 4 * N + 4, 2), V("pb", H, H + 64, 32), K - 0.5, ALU.min, float(stand[rank]), ALU.add)
-        spread(MS, "m%d_" % t + "%d", [near, far] + [d for d in pair2 if d != far], MS(N))
-        dmas("dm", [("y", A(MS(rank)), A(MS(N)), [MS(rank)], [MS(N)])])
-        flips = [d for d in range(1, N) if (d in seconds) != (d - 1 in seconds)]
-        for i, d in enumerate(flips):
-            o = V("sgn", 16 * min(i, 1), 16 * min(i, 1) + 16)
-            ts(o, itself, place(M * d) - 0.5, ALU.is_lt, 2.0, ALU.mult)
-            if i:
-                ts(o, o, -1.0, ALU.add)
-                tt(V("sgn", 0, 16), V("sgn", 0, 16), o, ALU.mult)
-            elif len(flips) > 1:
-                ts(o, o, -1.0, ALU.add, SCL, ALU.mult)
+        spread(MS, "m%d_" % t + "%d", nearest, MS(N))
+        dmas("dm%d" % t, [("y", A(MS(rank)), A(MS(N)), [MS(rank)], [MS(N)])])
         for k in range(KC):
-            out = V("dd", SEG * k + 1, SEG * k + SEG)
-            if k < 3:
-                ts(out, V("ps"), V("want", k, k + 1), ALU.not_equal, float(NM), ALU.mult)
-            else:
-                act(out, V("ps"), AF.Abs, scale=float(NM), bias=V("want", 8 + k, 9 + k))
-        act(V("rtf"), V("idn"), off=V("lro"))
-        row = V("rtf", 0, M, 1, 0, 1)
-        dmas("drt", [("y", T.rt[0:1, M * t:M * t + M], A(row), [], [row])])
-        if len(flips) == 1:
-            ts(V("sgn", 0, 16), V("sgn", 0, 16), -1.0, ALU.add, SCL, ALU.mult)
-        if not t:
-            unpacking(2)
+            ts(V("dd", SEG * k + 1, SEG * k + SEG), V("ps"), V("want", k, k + 1), ALU.not_equal, float(NM), ALU.mult,
+               (AF.Abs, float(NM), V("want", 8 + k, 9 + k)))
         scan(V("de", 0, SEG * KC), V("dd", 0, SEG * KC), V("di", 0, SEG * KC), ALU.min, ALU.add)
-        if not final:
-            a = H * (t + 1)
-            pick(V("qr", a, a + H), V("sr", a, a + H), V("qu"), V("su"), V("cu", a // 16, a // 16 + 8))
-            height(7, t + 1, qc, sp, 0, M)
         for p in (0, 64):
             halves(on(V("e1", 0, KC), p), V("de", SEG - 1, SEG * KC, SEG), ALU.min)
-        if not t:
-            unpacking(3)
         for b in range(4):
             tt(on(V("e2", 0, KC), 32 * b, 32), on(V("e1", 0, KC), 32 * b, 32), on(V("e1", 0, KC), 32 * (b ^ 1), 32), ALU.min)
-        for d in range(1, N):
-            ts(V("iv", d, H, 8), itself, place(M * d) - 0.5, ALU.is_gt, float(beyond[d - 1] - beyond[d]), ALU.mult)
         ts(V("j1", 0, KC), V("e2", 0, KC), CF(22), ALU.add, -1.0, ALU.mult)
-        spaced = lambda by, s, b: move(by, on(V("xz", 32 * s, NM, H), 32 * b, 32), on(V(ms, 0, 4 * N, 2), 32 * s, 32))
-        col = lambda d, c: V(ms, 4 * (N if d == rank else d) + c, 4 * (N if d == rank else d) + c + 1)
-        ge, gt = V(ms, 1, 4 * N, 4), V(ms, 3, 4 * N, 4)
-        allows = lambda: ts(V("km", 0, 32), V("kr", 0, 32), col(pair[1], 3), ALU.subtract, col(pair[0], 1), ALU.min)
-        if not final:
-            tr(V("ho", 0, H), bank(7, H))
-        if OPT["early"]:
-            allows()
-        qz, sz, qb, sb = [n + str(t) for n in ("qz", "sz", "qb", "sb")]
+        qz, sz, qb, sb, qp, pp = [n + str(t) for n in ("qz", "sz", "qb", "sb", "qp", "sp")]
         a = K * second
         pick(V(qz, a, a + K), V(sz, a, a + K), V(qc, 0, M), V(sp, 0, M), V("j1", 0, KC))
         swap(qz, sz, a, K - a, near, "ac%d" % t, "as%d" % t)
-        todo = [(s, b) for b in range(4) for s in range(4)]
-        for s, b in todo[OPT["nv"]:]:
-            spaced("s", s, b)
-        todo = todo[:OPT["nv"]]
-
-        def some(n):
-            for s, b in todo[:n]:
-                spaced("v", s, b)
-            del todo[:n]
-
-        if not OPT["early"]:
-            allows()
-        else:
-            tr(V("kt", 0, 32), V("km", 0, 32))
-        if not final:
-            tr(V("ho", H, M), V("bl", 512 * 7 + H, 512 * 7 + M))
-        unpack = [(V("qe", 128 * b, 128 * b + 128), V("se", 128 * b, 128 * b + 128)) for b in range(4)]
-        for h in (0, 1):
-            for b in range(4):
-                mm(bank(4 * h + b, H), *unpack[b], V(qc, *half[h]), V(sp, *half[h]), True, False)
-        if not OPT["early"]:
-            tr(V("kt", 0, 32), V("km", 0, 32))
-            some(2)
+        col = lambda d, c: V(ms, 4 * (N if d == rank else d) + c, 4 * (N if d == rank else d) + c + 1)
+        ts(V("km", 0, 32), V("kr"), col(pair[1], 3), ALU.subtract, col(pair[0], 1), ALU.min)
+        tr(V("kt", 0, 32), V("km", 0, 32))
         red(V("kk", 4, 5), V("kt", 0, 32), ALU.max)
-        some(2)
         ts(V("fl", 0, KC), V("ki", 0, KC), V("kk", 4, 5), ALU.is_gt, float(K), ALU.mult)
-        some(2)
-        red(V("kk", 5, 6), gt, ALU.add, True)
         tt(V("fl", 8, 8 + KC), V("fl", 0, KC), V("ki", 0, KC), ALU.add)
-        scan(V("kw", 0, N), gt, ge, ALU.add, ALU.subtract, V("kk", 5, 6))
-        some(16)
         cp(V("j2", 0, KC), V("fl", 8, 8 + KC))
-        ts(V("kw", 0, N), V("kw", 0, N), K - 0.5 * N, ALU.add, 0.0, ALU.min)
-        for e in range(OPT["nr"]):
-            repeated(e)
         a = stand[rank]
         pick(V(qb, a, a + K), V(sb, a, a + K), V(qz), V(sz), V("j2", 0, KC))
         swap(qb, sb, a, stand[far], far, "bc%d" % t, "bs%d" % t)
-        for e in range(OPT["nr"], 4):
+        for s in range(4):
+            for b in range(4):
+                move("vsg", on(V("xz", 32 * s, NM, H), 32 * b, 32), on(V(ms, 0, 4 * N, 2), 32 * s, 32))
+        for e in range(4):
             repeated(e)
-        tt(V("km", 32, 160, 32), V("kw", 0, N), ge, ALU.add)
-        for k in range(8):
-            tr(grun("fs", k), V("xb", H * k, H * k + H))
+            for k in (2 * e, 2 * e + 1):
+                tr(grun("fs", k), V("xb", H * k, H * k + H))
+        ge, gt = V(ms, 1, 4 * N, 4), V(ms, 3, 4 * N, 4)
+        red(V("kk", 5, 6), gt, ALU.add, True)
+        scan(V("kw"), gt, ge, ALU.add, ALU.subtract, V("kk", 5, 6))
+        ts(V("kw"), V("kw"), K - 0.5 * N, ALU.add, 0.0, ALU.min)
+        tt(V("km", 32, 160, 32), V("kw"), ge, ALU.add)
         scan(V("kt", 32, 160), V("d32", 0, H), V("km", 32, 160), ALU.mult, ALU.add)
-        act(V("rs", H, M), V("fs"), off=V("lrm", 8, 16))
-        cp(V("rs", 0, H), V("fs"), V("lrm", 0, 8))
         tr(V("ku"), V("kt", 32, 160))
-        at, us, me = V("sc", 15, M, 16), V("um", 0, 16), V("rho", 16, 32)
-        qp, pp = "qp%d" % t, "sp%d" % t
-        scan(V("sc", 0, M), V("d0", 0, M), V("rs"), ALU.mult, ALU.add)
-        scan(V("kt", 32, 160), V("d32", 0, H), V("ku"), ALU.mult, ALU.max)
+        scan(V("kv"), V("d32", 0, H), V("ku"), ALU.mult, ALU.max)
+        tt(V("kk", 0, N), V("kv", 31, H, 32), V("low"), ALU.add)
+        if not final:
+            height(7, t + 1, qc, sp, 0, M)
+            for h in (0, 1):
+                tr(V("ho", *half[h]), bank(7, H, H * h))
+        for h in (0, 1):
+            for b in range(4):
+                mm(bank(4 * h + b, H), *unpack[b], V(qc, *half[h]), V(sp, *half[h]), True, False)
+        for k in range(EARLY + 1, 9):
+            doubling(k)
+        rho, us, me = V("rho"), V("us"), V("me")
+        for h in (0, 1):
+            move("vs"[h], V("fr", *half[h]), V("fb"), V("lb", 8 * (own + h), 8 * (own + h) + 8))
+            scan(on(V("s2", *half[h]), mine), on(V("d0", 0, H), mine), on(V("fr", *half[h]), mine), ALU.mult, ALU.add)
+        for p in (0, 64):
+            ts(on(V("lro"), p), on(V("s2", 15, M, 16), mine), on(GSCL, mine), ALU.mult, float(GM), ALU.add)
+            affine(on(rho, p), on(V("s2", 15, M, 16), mine), on(GSCL, mine), float(GM))
+        for h in (0, 1):
+            move("vs"[h], V("rs", *half[h]), V("fs"), V("lro", 8 * h, 8 * h + 8))
+            scan(V("s3", *half[h]), V("d0", 0, H), V("rs", *half[h]), ALU.mult, ALU.add)
+        at = V("s3", 15, M, 16)
         ts(V("pl"), at, SCL, ALU.mult, float(PAD + 2 * K - 1), ALU.min)
-        tt(us, at, V("sgn", 0, 16), ALU.mult)
-        tt(V("kk", 0, N), V("kt", 63, 160, 32), V("low"), ALU.add)
+        move("vs", V("rtf"), V("idn"), V("lro"))
+        row = V("rtf", 0, M, 1, 0, 1)
+        dmas("drt%d" % t, [("y", T.rt[0:1, M * t:M * t + M], A(row), [], [row])])
         for h in (0, 1):
             pick(V(qp, *half[h]), V(pp, *half[h]), V(qb), V(sb), V("pl", 8 * h, 8 * h + 8))
         for h in (0, 1):
             for b in range(4):
                 mm(bank(4 * h + b, H), *unpack[b], V(qp, *half[h]), V(pp, *half[h]), False, True)
-        for d in range(N):
-            ts(V("iv", 4 + d, H, 8), us, V("kk", d, d + 1), ALU.is_lt)
-        member = V("iw", 7, H, 8)
-
-        def cast(b, by):
-            src, out = bank(b, H), V("hb", 4 * H * (b // 4) + b % 4, 4 * H * (b // 4) + 4 * H, 4)
-            if by == "v":
-                ts(out, src, 0.5, ALU.mult)
-            else:
-                act(out, src, scale=0.5)
-
-        def anew(h):
+                ts(V("hb", 4 * H * h + b, 4 * H * h + 4 * H, 4), bank(4 * h + b, H), 0.5, ALU.mult, also=(AF.Identity, 0.5, 0.0))
+        for h in (0, 1):
             quant(V(qc, M + H * h, M + H * h + H), V(sp, M + H * h, M + H * h + H), V("hb", 4 * H * h, 4 * H * h + 4 * H))
-            if not final:
-                height(h, t + 1, qc, sp, M + H * h, H)
-
-        for b in (0, 2, 4, 6):
-            cast(b, "s")
-        cast(1, "v")
+        flips = [d for d in range(1, N) if (d in seconds) != (d - 1 in seconds)]
+        for i, d in enumerate(flips):
+            o = V("sgn", 16 * min(i, 1), 16 * min(i, 1) + 16)
+            ts(o, rho, place(M * d) - 0.5, ALU.is_lt, 2.0, ALU.mult)
+            if i:
+                ts(o, o, -1.0, ALU.add)
+                tt(V("sgn", 0, 16), V("sgn", 0, 16), o, ALU.mult)
+            else:
+                ts(o, o, -1.0, ALU.add, SCL, ALU.mult)
+        tt(us, at, V("sgn", 0, 16), ALU.mult)
+        tt(V("self"), rho, V("sn"), ALU.is_equal)
+        affine(V("iv", 0, H, 8), V("self"), -1.0, -float(beyond[0]))
+        for d in range(N):
+            if d:
+                ts(V("iv", d, H, 8), rho, place(M * d) - 0.5, ALU.is_gt, float(beyond[d - 1] - beyond[d]), ALU.mult)
+            ts(V("iv", 4 + d, H, 8), us, V("kk", d, d + 1), ALU.is_lt)
         scan(V("iw"), V("d8"), V("iv"), ALU.mult, ALU.add)
-        cast(3, "v")
-        if final:
-            ts(me, member, 0.5, ALU.is_gt, float(M), ALU.mult)
-        cast(5, "v")
-        if final:
-            tt(me, me, V("ki"), ALU.add)
-        else:
-            scan(V("px"), V("pd"), member, ALU.add, ALU.max)
-        cast(7, "v")
-        anew(0)
-        if final:
-            cp(V("kl"), me)
-        else:
-            ts(V("mx1"), V("px", 1, 16, 2), CF(27), ALU.is_lt)
-        anew(1)
-        nq, ns = "qc%d" % (t + 1), "scp%d" % (t + 1)
+        member = V("iw", 7, H, 8)
+        ts(me, member, 0.5, ALU.is_gt, float(M), ALU.mult)
+        tt(me, me, V("ki"), ALU.add)
+        cp(V("kl"), me)
         if not final:
+            scan(V("px"), V("pd"), member, ALU.add, ALU.max)
+            ts(V("mx1"), V("px", 1, 16, 2), CF(28), ALU.is_lt)
+            ts(V("mx"), V("px", 1, 16, 2), CF(28), ALU.is_gt)
             tt(V("xo"), V("ho", 0, M, 32), V("mx1"), ALU.mult)
-            ts(V("mx"), V("px", 1, 16, 2), CF(27), ALU.is_gt)
             for h in (0, 1):
+                height(h, t + 1, qc, sp, M + H * h, H)
                 tr(V("ht", *half[h]), bank(h, H))
-                if h:
-                    tt(me, me, V("ki"), ALU.add)
-                else:
-                    ts(me, member, 0.5, ALU.is_gt, float(M), ALU.mult)
                 for c in range(4 * h, 4 * h + 4):
-                    out, new = V("xh%d" % (t + 1), 8 * rank + c, 8 * rank + c + 1), V("ht", 32 * c, 32 * c + 1)
-                    if c > 5:
-                        ts(out, new, V("mx", c, c + 1), ALU.mult, V("xo", c, c + 1), ALU.add)
-                    else:
-                        act(out, new, AF.Identity, scale=V("mx", c, c + 1), bias=V("xo", c, c + 1))
+                    affine(V("xh%d" % (t + 1), 8 * rank + c, 8 * rank + c + 1), V("ht", 32 * c, 32 * c + 1), V("mx", c, c + 1), V("xo", c, c + 1))
             share(t + 1)
-            cp(V("kl"), me)
-            turned(t + 1, rank, "ss", lambda: pick(V(nq, 0, M), V(ns, 0, M), V(qc), V(sp), V("kl")))
+            pick(V(nq, 0, M), V(ns, 0, M), V(qc), V(sp), V("kl"))
 
-    outs = []
     for h in (0, 1):
         pick(V(nq, *half[h]), V(ns, *half[h]), V(qc, 0, M + H * h + H), V(sp, 0, M + H * h + H), V("kl", 8 * h, 8 * h + 8))
         mm(bank(h, H), V("qw"), V("sw"), V(nq, *half[h]), V(ns, *half[h]), True, True)
-        outs.append(("y", T.oc[:, 4 * H * h:4 * H * h + 4 * H], A(V(nq, *half[h])).bitcast(dt.uint8), [], [V(nq, *half[h])]))
+        move("vs", V("ys", *half[h]), bank(h, H))
+        dmas("dout", [("y", T.oc[:, 4 * H * h:4 * H * h + 4 * H], A(V(nq, *half[h])).bitcast(dt.uint8), [], [V(nq, *half[h])])])
+        dmas("dout", [("ys"[h], T.y[:, H * h:H * h + H], A(V("ys", *half[h])), [], [V("ys", *half[h])])])
     for k in range(4):
         o = V(ns, 0, M, 1, 32 * k, 32 * k + 4)
-        outs.append(("s", T.osc[4 * k:4 * k + 4, 0:M], A(o), [], [o]))
-    for h in (0, 1):
-        cp(V("ys", *half[h]), bank(h, H))
-        outs.append(("ys"[h], T.y[:, H * h:H * h + H], A(V("ys", *half[h])), [], [V("ys", *half[h])]))
-    dmas("dout", outs)
+        dmas("dout", [("ys"[k % 2], T.osc[4 * k:4 * k + 4, 0:M], A(o), [], [o])])
+
+    for i, qn in ordered(calls):
+        calls[i][1][0](qn)
     for sem in sorted(cnt):
         if max(known[q].get(sem, 0) for q in known) < cnt[sem]:
             queue["y" if sem == "dout" else "g"].wait_ge(T.sem[sem], cnt[sem])

import numpy as np
from concourse.bass import DstId, RemoteDMATransfer
from concourse.mybir import dt, AluOpType, AxisListType, ActivationFunctionType

ALU = AluOpType
AF = ActivationFunctionType
N, M, K, J, R = 4, 256, 80, 3, 3
NM = N * M
HM = NM // 2
H = M // 2
KC = K // 16
PAD = 16
SEG = 65
EARLY = 3
RUNS = ((-2048, 8), (-1024, 4), (-512, 2), (-256, 1), (128, 1), (256, 2), (512, 4), (1024, 8))
UNIT = 1.0 / 4096
OWN = ((2, 3, 4, 5), (0, 1, 6, 7))
ALPHA = (4, 1)
RK = (1, 2, 0, 3)
GM, WM = 2048, 8192
UP = float(2 ** 30)
C8, U8, F32, B16, I32, U16 = "float8_e4m3fn_x4", "uint8", "float32", "bfloat16", "int32", "uint16"
PLAN = {"wake": 300, "gather": 1.3, "call": 360, "way": 1000, "row": 20, "load": 1300, "v": 60, "g": 150}

WIDTHS = {
    B16: {"xt": 4 * M, "ut": 512, "wt": 512, "one": 528, "et": 2 * 528, "d0": M, "dw": 16,
          "xb": NM, "xz": NM, "d32": M, "cw": NM, "ca": 384, "cb": HM,
          "fs": 2 * GM, "fa": 2 * WM, "fb": 2 * WM, "sc": HM, "s2": M, "s3": M, "rs": M, "hb": 4 * M,
          "fr": M, "ee": 4 * HM, "so": 4 * M, "cv": 16, "ea": 4 * (H + 32), "pb": 2 * H + 64, "ps": 64, "dd": 336, "di": 336, "de": 336,
          "sg": 2 * M, "kr": 32, "km": 160, "kt": 160, "ku": H, "kv": H, "iv": H, "iw": H, "d8": H, "d4": H, "lost": H, "key": H},
    C8: {"qu": 128, "qw": 128, "qr": 384, "qe": 512},
    U8: {"su": 128, "sw": 128, "sr": 384, "se": 512},
    F32: {"i128": H, "idn": 2 * GM, "rtf": M, "xe": NM, "fh": NM, "ra": 384, "rb": HM,
          "ht": M, "ho": M, "acc": 16, "ys": M, "fq": M, "xr": M, "kf": M},
    U16: {"la": 32, "lb": 32, "nbl": 64, "lnb": 24},
    I32: {"iu": 24, "id16": 16, "nbe": 16},
}
SCRATCH = {"bl": ("psum", [128, 4096], F32)}
for _d, _parts in WIDTHS.items():
    for _n, _w in _parts.items():
        SCRATCH[_n] = ("sbuf", [128, _w], _d)
SMALL = {
    "zf": (F32, {"d16": 16, "d17": 16, "cf": 32, "sn": 16, "ki": 16, "x0": 16, "b2": 16, "nn": 4, "nr": 4, "aa": 4, "ab": 4, "kw": 4,
                 "low": 4, "want": 16, "e1": 8, "e2": 8, "kk": 8, "fl": 16, "us": 16, "sgn": 32, "px": 16, "pd": 16,
                 "rho": 16, "self": 16, "me": 16, "mx": 8, "mx1": 8, "xo": 8}),
    "zi": (I32, {"ip": 16}),
    "zu": (U16, {"crep": 16, "cu": 24, "lro": 16, "j1": 6, "j2": 6, "pl": 16, "kl": 16}),
}
AT = {}
for _b, (_d, _parts) in SMALL.items():
    _o = 0
    for _n, _w in _parts.items():
        AT[_n] = (_b, _o, _w)
        _o += -(-_w // 16) * 16
    SCRATCH[_b] = ("sbuf", [128, _o], _d)
for _t in range(R):
    SCRATCH["xh%d" % _t] = ("sbuf", [128, 32], F32)
    SCRATCH["ms%d" % _t] = ("sbuf", [128, 32], B16)
    for _n, _w in (("z", 2 * K), ("b", PAD + 2 * K), ("p", M)):
        SCRATCH["q%s%d" % (_n, _t)] = ("sbuf", [128, _w], C8)
        SCRATCH["s%s%d" % (_n, _t)] = ("sbuf", [128, _w], U8)
for _t in range(R + 1):
    SCRATCH["qc%d" % _t] = ("sbuf", [128, 2 * M if _t < R else M], C8)
    SCRATCH["scp%d" % _t] = ("sbuf", [128, 2 * M if _t < R else M], U8)

SEMAPHORES = (["ev", "es", "et", "eg", "loc"] + ["nb%d" % d for d in range(N)] + ["%s%d_%d" % (k, t, d) for k in "hm" for t in range(R) for d in range(N)]
              + ["%s%d" % (k, t) for t in range(R) for k in ("ac", "as", "bc", "bs", "dm", "drt")]
              + ["dx0", "dx1", "du", "dw", "dnb", "dout"])
BYTES = {C8: 4, U8: 1, F32: 4, B16: 2, I32: 4, U16: 2}


def place(n):
    return GM + RUNS[n // H][0] + RUNS[n // H][1] * (n % H)


def meets(a, b):
    if a[1] >= b[2] or b[1] >= a[2] or a[4] >= b[5] or b[4] >= a[5]:
        return False
    return not (a[3] == b[3] and a[3] > 1 and (a[1] - b[1]) % a[3])


def split(reads, writes):
    ps = [r for r in list(reads) + list(writes) if SCRATCH[r[0]][0] == "psum"]
    return ([r for r in reads if SCRATCH[r[0]][0] != "psum"],
            [r for r in writes if SCRATCH[r[0]][0] != "psum"] + [(r[0], r[1] // 512 * 512, -(-r[2] // 512) * 512, 1, 0, 128) for r in ps])


def noted(hist, reads, writes, tag):
    for r in writes:
        hist[r[0]] = [h for h in hist.get(r[0], [])
                      if not ((r[3] == 1 or h[0] == r) and r[1] <= h[0][1] and h[0][2] <= r[2] and r[4] <= h[0][4] and h[0][5] <= r[5])]
    for r, w in [(r, False) for r in reads] + [(r, True) for r in writes]:
        hist.setdefault(r[0], []).append((r, w, tag))


def behind(hist, reads, writes):
    return [tag for r, w in [(r, False) for r in reads] + [(r, True) for r in writes]
            for e, ew, tag in hist.get(r[0], []) if (w or ew) and meets(r, e)]


def ordered(calls):
    wake, n = PLAN["wake"], len(calls)
    hist, before, after = {}, [], [[] for _ in calls]
    for i, (cost, run, reads, writes, follows, kind) in enumerate(calls):
        reads, writes = split(reads, writes)
        before.append([(j, wake) for j in set(behind(hist, reads, writes))] if follows is None else [(follows, 0)])
        for j, w in before[i]:
            after[j].append((i, w))
        noted(hist, reads, writes, i)
    chain = [0.0] * n
    for i in range(n - 1, -1, -1):
        chain[i] = min(calls[i][0].values()) + max([w + chain[j] for j, w in after[i]], default=0)
    left = [len(b) for b in before]
    ready = {i: 0.0 for i in range(n) if not left[i]}
    free, crossed, out, due = {}, -wake, [], [0.0] * n

    def start(i, q):
        t = max(ready[i], free.get(q, 0.0))
        if q == "g" and calls[i][5] != "remote":
            t = max(t, free.get("gc", -wake) + wake)
        if q == "v" and calls[i][5] == "port":
            t = max(t, crossed + wake)
        return t

    while ready:
        best = {}
        for i in ready:
            cost = calls[i][0]
            q = min(cost, key=lambda q: start(i, q) + cost[q] + (PLAN.get(q, 0) if len(cost) > 1 else 0))
            best[i] = (q, start(i, q), cost[q])
        first = min(best, key=lambda i: (best[i][1] + best[i][2], i))
        q, end = best[first][0], best[first][1] + best[first][2]
        i = first if q is None else max([j for j in best if best[j][0] == q and (best[j][1] < end or j == first)], key=lambda j: (chain[j] - best[j][1], -j))
        q, t, c = best[i]
        out.append((t, len(out), i, q))
        if q is not None:
            free[q] = t + c
        if q == "g" and calls[i][5] != "remote":
            free["gc"] = t + c
        if q == "v" and calls[i][5] == "cross":
            crossed = t + c
        del ready[i]
        for j, w in after[i]:
            left[j] -= 1
            due[j] = max(due[j], t + c + w)
            if not left[j]:
                ready[j] = due[j]
    return [(i, q) for t, k, i, q in sorted(out)]


def rank_program(g, core, T, topo):
    rank = T.rank_of(core)
    if rank is None:
        return
    queue = {"v": g.vector, "s": g.scalar, "t": g.tensor, "g": g, "y": g.sync}
    esem = {"v": "ev", "s": "es", "t": "et", "g": "eg"}
    cnt, known, clock, hist, calls, crossed = {}, {k: {} for k in queue}, {}, {}, [], [0]

    def V(name, a=0, b=None, step=1, p0=0, p1=128):
        buf, off, w = AT[name] if name in AT else (name, 0, SCRATCH[name][1][1])
        return (buf, off + a, off + (w if b is None else b), step, p0, p1)

    def on(r, p0, n=64):
        return r[:4] + (p0, p0 + n)

    def back(r):
        return r[:6] + (True,)

    def A(r):
        if len(r) > 6:
            return T[r[0]][r[4]:r[5], r[2] - 1:r[1] - 1:-1]
        return T[r[0]][r[4]:r[5], r[1]:r[2]] if r[3] == 1 else T[r[0]][r[4]:r[5], r[1]:r[2]:r[3]]

    size = lambda r: len(range(*r[1:4]))
    kind = lambda r: SCRATCH[r[0]][2]

    def use(qn, reads, writes):
        reads, writes = split(reads, writes)
        need = {}
        for sem, val in behind(hist, reads, writes):
            if known[qn].get(sem, 0) < val:
                need[sem] = max(need.get(sem, 0), val)
        for sem in sorted(need):
            if any(o != sem and clock[(o, need[o])].get(sem, 0) >= need[sem] for o in need):
                continue
            queue[qn].wait_ge(T.sem[sem], need[sem])
        for sem in need:
            for s2, v2 in clock[(sem, need[sem])].items():
                known[qn][s2] = max(known[qn].get(s2, 0), v2)
            known[qn][sem] = max(known[qn].get(sem, 0), need[sem])

    def counted(sem, n, reads, writes, before):
        cnt[sem] = cnt.get(sem, 0) + n
        clock[(sem, cnt[sem])] = dict(before)
        noted(hist, *split(reads, writes), (sem, cnt[sem]))

    def upto(qn, sem, val):
        if known[qn].get(sem, 0) < val:
            queue[qn].wait_ge(T.sem[sem], val)
            known[qn][sem] = val

    def put(ways, outs, ins, how=None):
        def run(qn):
            use(qn, ins, outs)
            if qn == "g":
                upto("g", "eg", cnt.get("eg", 0))
            if qn == "v" and how == "port":
                upto("v", "ev", crossed[0])
            ways[qn][1]().then_inc(T.sem[esem[qn]], 1)
            counted(esem[qn], 1, ins, outs, known[qn])
            if how == "cross":
                crossed[0] = cnt["ev"]
        calls.append(({q: w[0] for q, w in ways.items()}, [run], ins, outs, None, how))

    def lands(cycles, outs):
        calls.append(({None: cycles}, [lambda qn: None], [], outs, len([c for c in calls]) - 1 - lands_behind[0], None))
        lands_behind[0] += 1

    lands_behind = [0]

    def dmas(sem, items, cycles=PLAN["load"]):
        def run(qn):
            merged = {}
            for q, out, in_, outs, ins in items:
                use(q, ins, outs)
                queue[q].dma_start(out, in_).then_inc(T.sem[sem], 16)
                for s, v in known[q].items():
                    merged[s] = max(merged.get(s, 0), v)
            counted(sem, 16 * len(items), [r for i in items for r in i[4]], [r for i in items for r in i[3]], merged)
        calls.append(({items[0][0]: 60.0 * len(items)}, [run], [r for i in items for r in i[4]], [r for i in items for r in i[3]], None, None))
        lands_behind[0] = 0
        lands(cycles, [r for i in items for r in i[3]])

    def cycles(n, *sides):
        return max(64.0, n * (0.5 if all(BYTES[kind(r)] == 2 for r in sides) else 1.0))

    gather = lambda off, fixed: fixed + PLAN["gather"] * 16 * size(off)
    ind = lambda win, off: A(win).indirect(A(off))

    def move(by, out, in_, off=None):
        ways = {}
        if "v" in by:
            ways["v"] = (gather(off, 60) if off else cycles(size(out), out, in_),
                         lambda: g.vector.tensor_copy(A(out), A(in_) if off is None else ind(in_, off)))
        if "s" in by:
            ways["s"] = (gather(off, 80) if off else max(64.0, size(out)),
                         lambda: g.scalar.activation(A(out), A(in_) if off is None else ind(in_, off), AF.Copy))
        if "g" in by:
            ways["g"] = (200.0 + 2 * size(out), lambda: g.affine_select(A(out), A(in_), [[0, size(out)]], ALU.is_gt, 0.0, 1, 0))
        put(ways, [out], [in_] + ([off] if off else []), "port" if off or kind(out) == kind(in_) else None)

    def cp(out, in_, off=None):
        move("v", out, in_, off)

    val = lambda s: A(s) if isinstance(s, tuple) else s

    def ts(out, in0, s1, op0, s2=None, op1=None, also=None):
        if op1 is None:
            fn = lambda: g.vector.tensor_scalar(A(out), A(in0), val(s1), None, op0)
        else:
            fn = lambda: g.vector.tensor_scalar(A(out), A(in0), val(s1), val(s2), op0, op1)
        ways = {"v": (cycles(size(out), out, in0), fn)}
        if also:
            ways["s"] = (max(64.0, size(out)), lambda: g.scalar.activation(A(out), A(in0), also[0], scale=val(also[1]), bias=val(also[2])))
        cols = [s for s in (s1, s2) + tuple(also or ()) if isinstance(s, tuple)]
        put(ways, [out], [in0] + cols, "port" if kind(in0) == B16 else None)

    def affine(out, in_, scale, bias):
        ts(out, in_, scale, ALU.mult, bias, ALU.add, (AF.Identity, scale, bias))

    def tt(out, a, b, op):
        put({"v": (max(64.0, 2.0 * size(out)), lambda: g.vector.tensor_tensor(A(out), A(a), A(b), op))}, [out], [a, b], "cross" if a[4] != b[4] else None)

    def red(out, in_, op, negate=False):
        put({"v": (max(64.0, size(in_)), lambda: g.vector.tensor_reduce(A(out), A(in_), AxisListType.X, op, negate=negate))}, [out], [in_])

    def scan(out, d0, d1, op0, op1, first=0.0):
        put({"v": (cycles(size(out), out, d0, d1), lambda: g.vector.tensor_tensor_scan(A(out), A(d0), A(d1), val(first), op0, op1))},
            [out], [d0, d1] + ([first] if isinstance(first, tuple) else []))

    def tr(out, in_):
        put({"v": (cycles(size(out), out, in_), lambda: g.vector.transpose(A(out), A(in_)))}, [out], [in_], "port" if in_[0] != "bl" else None)

    def act(out, in_, func, accum=None, **kw):
        def fn():
            k2 = {k: val(v) for k, v in kw.items()}
            if accum is not None:
                k2["accum_out"] = A(accum)
            return g.scalar.activation(A(out), A(in_), func, **k2)
        put({"s": (max(64.0, size(out)) + (24 if accum else 0), fn)}, [out] + ([accum] if accum else []), [in_] + [v for v in kw.values() if isinstance(v, tuple)])

    def counting(out, pattern, base, cm):
        if kind(out) == I32:
            return lambda: g.iota(A(out), pattern, base, cm)
        return lambda: g.iota(A(out), pattern, base, cm, allow_small_or_imprecise_dtypes=True)

    def iota(out, pattern, base, cm):
        put({"g": (160.0 + 2 * size(out), counting(out, pattern, base, cm))}, [out], [])

    def fill(out, c, by="vg"):
        ways = {"v": (cycles(size(out), out), lambda: g.vector.memset(A(out), c))}
        if "g" in by:
            ways["g"] = (160.0 + 2 * size(out), counting(out, [[0, size(out)]], int(c), 0))
        put(ways, [out], [])

    def select(out, in_, pattern, cmp, fillv, base, cm):
        put({"g": (200.0 + 2 * size(out), lambda: g.affine_select(A(out), A(in_), pattern, cmp, fillv, base, cm))}, [out], [in_])

    def quant(q, s, in_):
        put({"v": (15 + 0.27 * size(in_), lambda: g.vector.quantize_mx(A(q), A(s), A(in_)))}, [q, s], [in_])

    def mm(out, lq, ls, rq, rs, start, stop):
        put({"t": (0.75 * (size(out) + 16), lambda: g.tensor.matmul_mx(A(out), A(lq), A(ls), A(rq), A(rs), start, stop))}, [out], [lq, ls, rq, rs])

    def pick(qo, so, qi, si, off):
        put({"v": (gather(off, 60), lambda: g.vector.tensor_copy(A(qo).bitcast(dt.uint32), A(qi).bitcast(dt.uint32).indirect(A(off))))}, [qo], [qi, off], "port")
        move("s", so, si, off)

    def halves(out, r, op, p=0, n=64):
        tt(out, on(r, p, n), on(r, 64 + p, n), op)

    beside = lambda a, b: topo.same_plane(topo.chip(T.cores[a]), topo.chip(T.cores[b]))
    farthest = lambda r: sorted([(r + k) % N for k in range(1, N)], key=lambda d: beside(r, d))
    pair_of = lambda r: sorted([r] + [d for d in range(N) if d != r and beside(r, d)])
    far_of = lambda r: [d for d in range(N) if d not in pair_of(r)][pair_of(r).index(r)]
    nearest = lambda r: sorted([d for d in range(N) if d != r], key=lambda d: (not beside(r, d), d != far_of(r)))
    others = farthest(rank)
    mask3 = 0xFFFF
    for d in others:
        mask3 &= topo.mask(core, T.cores[d])
    groups = bin(mask3).count("1")

    def remote(src, call, n, landings):
        def run(qn):
            use("g", [src], [])
            call()
            cnt["loc"] = cnt.get("loc", 0) + n
            for sem, r in landings:
                counted(sem, n, [], [r], {})
        calls.append(({"g": float(PLAN["call"])}, [run], [src], [], None, "remote"))
        lands_behind[0] = 0
        for i, (sem, r) in enumerate(landings):
            lands(PLAN["way"] + (i + 1) * 128 // n * (PLAN["row"] + size(r) * BYTES[kind(r)] // 20), [r])

    def spread(piece, sem, turn=farthest, src=None):
        src = src or piece(rank)
        ids = [DstId(rid=topo.addr(T.cores[d])[0], pnc=topo.addr(T.cores[d])[1]) for d in turn(rank)]
        call = lambda: g.remote_dma_fused([RemoteDMATransfer(dst_ids=ids, dma_engine_mask=mask3, remote_sem=T.sem[sem % rank], srcs=[A(src)],
                                                             dsts=[A(piece(rank)) for d in others])], local_sem=T.sem.loc)
        remote(src, call, groups, [(sem % d, piece(d)) for d in sorted(others, key=lambda d: turn(d).index(rank))])

    pair, far = pair_of(rank), far_of(rank)
    near, second = sum(pair) - rank, pair.index(rank)
    seconds = (pair[1], pair_of(far)[1])
    stand = [PAD + K * (0 not in pair_of(d)) for d in range(N)]
    lows = [1 - stand[d] - K if d in seconds else stand[d] for d in range(N)]
    beyond = [sum(low > lows[d] for low in lows) for d in range(N)]

    def swap(q, s, a, there, d, semc, sems):
        dst = T.cores[d]
        rid, pid = topo.addr(dst)[:2]
        mask, n = topo.mask(core, dst), len(topo.engines(core, dst))
        qa, sa = V(q, a, a + K), V(s, a, a + K)
        remote(qa, lambda: g.remote_dma(A(qa).bitcast(dt.uint8), A(qa).bitcast(dt.uint8), T.sem[semc], T.sem.loc, pid, rid, mask), n, [(semc, V(q, there, there + K))])
        remote(sa, lambda: g.remote_dma(A(sa), A(sa), T.sem[sems], T.sem.loc, pid, rid, mask), n, [(sems, V(s, there, there + K))])

    def turned(t, d):
        h = V("xh%d" % t, 8 * d, 8 * d + 8)
        for e in (0, 1):
            move("vs", V("xe", M * d + 16 * e, M * d + M, 32), h)
        tr(V("fh", M * d, M * d + M), V("xe", M * d, M * d + M))
        b = 32 * RK.index(d)
        move("vs", on(V("rb", 3 * H, 4 * H, 16), b, 32), on(h, b, 32))

    def repeated(e):
        scan(V("xb", M * e, M * e + M), V("d32"), V("xz", M * e, M * e + M), ALU.mult, ALU.add)

    def grun(f, k):
        a, s = RUNS[k]
        return V(f, GM + a, GM + a + s * H, s)

    def wrun(f, h, k):
        a, s = RUNS[k]
        return V(f, WM + ALPHA[h] * a, WM + ALPHA[h] * (a + s * H), ALPHA[h] * s)

    piece = lambda f, i: wrun(f, 0, OWN[0][i])
    CF = lambda k: V("cf", k, k + 1)
    SCL, UPPER, SCOL, LCOL, GSCL, WSCL = [CF(k) for k in (0, 5, 6, 7, 16, 17)]

    def handed(f, l, pieces=range(4), to=(0, 1)):
        for i in pieces:
            scan(V("sc", H * i, H * i + H), V("d0", 0, H), piece(f, i), ALU.mult, ALU.add)
        for i in range(4):
            for h in to:
                move("vsg", on(wrun(f, h, OWN[1 - h][i]), 64 * h), on(piece(f, i), 64 - 64 * h))
        for i in list(pieces)[::2]:
            ts(V(l, 8 * i, 8 * i + 16), V("sc", H * i + 15, H * i + M, 16), WSCL, ALU.mult, float(WM), ALU.add)

    bank = lambda k, w, a=0: V("bl", 512 * k + a, 512 * k + a + w)
    half = [(H * h, H * h + H) for h in (0, 1)]
    blk = RK.index(rank)
    mine, own = 64 * (blk // 2), 2 * (blk % 2)

    for q in (0, 1):
        loads = []
        for k in range(q, 2 * J, 2):
            o = V("nbe", 0, 16 - 2 * q, 1, 16 * k, 16 * k + 16)
            loads.append(("ys"[q], A(o), T.nb[:, 16 * (k // 2) + 2 * q:16 * (k // 2) + 16], [o], []))
        dmas(("dnb", "du")[q], loads + [("s", A(V("ut", 0, 16)), T.u[:, 0:16], [V("ut", 0, 16)], [])] * q)
    for h in (0, 1):
        o = V("xt", 4 * H * h, 4 * H * h + 4 * H)
        dmas("dx%d" % h, [("ys"[h], A(o), T.x[:, 4 * H * h:4 * H * h + 4 * H], [o], [])], PLAN["load"] * (1.4 + 0.3 * h))
    IP = lambda k: V("ip", k, k + 1)
    RI = lambda n: V("i128", 0, n)
    iota(V("iu"), [[1, 3], [0, 8]], 0, 0)
    iota(IP(0), [[0, 1]], 0, 1)
    iota(V("i128"), [[1, H]], 0, 0)
    o = 16 * rank
    fill(V("ut", 16, 512), 0.0, "v")
    fill(on(V("nbl", o, o + 8), 96, 32), 0, "v")
    for e in (0, 1):
        cp(on(V("nbl", o + e, o + 8, 2), 0, 96), on(V("nbe", e, 16, 4), 0, 96))
    spread(lambda d: V("nbl", 16 * d, 16 * d + 8), "nb%d")
    cp(V("cu"), V("iu"))
    quant(V("qu"), V("su"), V("ut"))

    def height(k, t, q, s, a, n):
        mm(bank(k, n), V("qr", 128 * t, 128 * t + 128), V("sr", 128 * t, 128 * t + 128), V(q, a, a + n), V(s, a, a + n), True, True)

    def share(t):
        spread(lambda d: V("xh%d" % t, 8 * d, 8 * d + 8), "h%d_" % t + "%d")

    for t in range(R):
        pick(V("qr", H * t, H * t + H), V("sr", H * t, H * t + H), V("qu"), V("su"), V("cu", 8 * t, 8 * t + 8))
    for h in (0, 1):
        quant(V("qc0", *half[h]), V("scp0", *half[h]), V("xt", 4 * H * h, 4 * H * h + 4 * H))
        height(h, 0, "qc0", "scp0", H * h, H)
        tr(V("ht", *half[h]), bank(h, H))
    move("vs", V("xh0", 8 * rank, 8 * rank + 8), V("ht", 0, M, 32))
    share(0)

    fill(V("xe", 0, M), 0.0, "v")
    for d in range(1, N):
        move("vs", V("xe", M * d, M * d + M), V("xe", 0, M))
    ts(IP(1), IP(0), 6, ALU.logical_shift_right)
    ts(IP(2), IP(0), 15, ALU.bitwise_and)
    ts(IP(3), IP(0), 31, ALU.bitwise_and)
    cp(V("cf", 5, 8), V("ip", 1, 4))
    for k, (a, s) in enumerate(RUNS):
        affine(V("cw", H * k, H * k + H), V("i128"), s * UNIT, a * UNIT)
        affine(grun("idn", k), V("i128"), 1.0, float(H * k))
    for d in range(N):
        for j in range(J):
            cp(on(V("lnb", 8 * j, 8 * j + 8), 32 * RK.index(d), 32), on(V("nbl", 16 * d, 16 * d + 8), 32 * j, 32))
    affine(V("x0", 0, 4), RI(4), 32.0, LCOL)
    for a, b in ((0, 12), (12, 24)):
        move("vs", V("ca", 16 * a, 16 * b), V("cw"), V("lnb", a, b))
    tr(V("cb", 0, 3 * H), V("ca"))
    for b in range(4):
        for e in (0, 1):
            a, s = RUNS[2 * RK[b] + e]
            affine(on(V("cb", 3 * H + 64 * e, 3 * H + 64 * e + 64, 16), 32 * b, 32), on(V("x0", 0, 4), 32 * b, 32), s * UNIT, a * UNIT)
    move("vs", V("lost", 0, H, 4), V("cb", 0, HM, 16))
    ts(SCL, SCOL, 15.0, ALU.is_equal, 1.0 - 1.0 / UP, ALU.mult)
    ts(SCL, SCL, 1.0 / UP, ALU.max)
    affine(CF(23), UPPER, float(ALPHA[1] - ALPHA[0]), float(ALPHA[0]))
    affine(GSCL, SCL, 1.0 / UNIT, 0.0)
    tt(WSCL, GSCL, CF(23), ALU.mult)
    iota(V("id16"), [[1, 16]], 128, -1)
    ts(V("id16"), V("id16"), 15, ALU.bitwise_and)
    ts(V("d16"), V("id16"), 1.0, ALU.is_equal, UP, ALU.mult)
    ts(V("d17"), V("id16"), 0.0, ALU.is_gt)
    tt(V("d16"), V("d16"), V("d17"), ALU.add)
    ts(V("crep"), RI(16), 0.0, ALU.mult, SCOL, ALU.add)
    move("vs", V("d0"), V("d16"), V("crep"))
    fill(V("one"), 1.0)
    for d, n, k in (("d4", H, 4), ("d32", M, 32), ("d8", H, 8)):
        select(V(d), V("one", 0, n), [[0, n // k], [1, k]], ALU.is_gt, 0.0, 0, 0)
    for a in (0, HM):
        fill(V("xz", a, a + HM), 0.0)
    affine(V("ki"), RI(16), 16.0, SCOL)
    for h in (0, 1):
        n0 = M * rank + H * h
        affine(V("sn", 8 * h, 8 * h + 8), V("ki", 0, 8), float(place(n0 + 1) - place(n0)), float(place(n0)))
    for p in (0, 64):
        iota(on(V("nn", 0, 2), p), [[H, 2]], 0, 1)
        iota(on(V("nn", 2, 4), p), [[-H, 2]], H + 64, 1)
    for e, cols in enumerate(((0, 4, 3), (1, 3, 1))):
        a, s = RUNS[2 * rank + e]
        affine(V("cv", *cols), V("nn", *cols), s * UNIT, (a - s * H * e) * UNIT)
    fill(on(V("nr"), 64 - mine), 0.0)
    for p, firsts in ((0, (0, H + 64)), (64, (64, H))):
        for i, first in enumerate(firsts):
            iota(on(V("fq", 64 * i, 64 * i + 64), p), [[M * (2 * i - 1), 2], [0, 32]], -2 * first - 1, -2)
    for b in range(4):
        move("vsg", on(V("fq", H, M), 32 * b, 32), on(V("fq", 0, H), 32 * ((b + 1) % 2), 32))
    for k in (0, 1):
        affine(CF(24 + k), LCOL, float(HM), float(HM * (k - 1)))
    for k in range(4):
        fill(V("ea", (H + 32) * k + H, (H + 32) * (k + 1)), 0.0)
    for e in (0, 1):
        select(V("et", 528 * e, 528 * e + 528), V("one"), [[1, 528]], ALU.is_equal, 0.0, -2 - e, -4)
    unpack = [(V("qe", 128 * b, 128 * b + 128), V("se", 128 * b, 128 * b + 128)) for b in range(4)]
    for b in range(4):
        a = 528 * (b % 2) + 2 - b // 2 * 2
        quant(*unpack[b], V("et", a, a + 512))
    affine(V("want", 0, KC), V("ki", 0, KC), 1.0, (1.0 - K) * second)
    affine(V("want", 8, 8 + KC), V("ki", 0, KC), -float(NM), (K - 1.0) * second * NM)
    fill(V("dd", 0, SEG * KC, SEG), 0.0)
    fill(V("di", 0, SEG * KC), 1.0)
    fill(V("di", 0, SEG * KC, SEG), 2.0 * M)
    fill(V("di", 32, SEG * KC, SEG), H - 31.0)
    iota(V("di", SEG - 1, SEG * KC, SEG), [[0, KC]], H - 31, -1)
    affine(CF(22), LCOL, 1.0, -float(M))
    fill(V("kr"), K - 1.0)
    fill(V("km", 32, 160), 0.0)
    for d in range(N):
        fill(V("low", d, d + 1), float(lows[d]))
    fill(V("dw"), -8.0)
    fill(V("pd", 0, 16, 2), -8.0)
    ts(CF(26), LCOL, 16.0, ALU.is_lt, 12.0, ALU.mult)
    affine(V("pd", 1, 16, 2), V("dw", 0, 8), 1.0, CF(26))
    affine(CF(28), CF(26), 1.0 / 3, 0.5)

    ACC = lambda k: V("acc", k, k + 1)
    for t in range(R):
        qc, sp, nq, ns = "qc%d" % t, "scp%d" % t, "qc%d" % (t + 1), "scp%d" % (t + 1)
        final = t + 1 == R
        for d in range(N):
            turned(t, d)
        if not t:
            dmas("dw", [("y", A(V("wt")), T.w[:], [V("wt")], [V("fh", 0, 16)])])
            quant(V("qw"), V("sw"), V("wt"))
        for by, a, b in (("v", 0, 8), ("s", 8, 18), ("s", 18, 24)):
            move(by, V("ra", 16 * a, 16 * b), V("fh"), V("lnb", a, b))
            tr(V("rb", 16 * a, 16 * b), V("ra", 16 * a, 16 * b))
        four = lambda a, b: V("rb", H * a, H * b, 16)
        for r, a, b in ((1, 3, 4), (3, 0, 1), (1, 0, 3), (2, 0, 2), (2, 2, 4), (3, 1, 4)):
            tt(V("lost", 32 * a + r, 32 * b, 4), four((a + r) % 4, (b - 1 + r) % 4 + 1), four(a, b), ALU.is_gt)
        scan(V("key"), V("d4"), V("lost"), ALU.mult, ALU.add)
        tt(V("b2"), V("key", 3, 64, 4), V("key", 67, H, 4), ALU.min)
        for e in (0, 1):
            for b in range(4):
                src = 64 * (b // 2) + 32 * e
                tt(on(V("xz", M * e, M * e + M, 32), 32 * b, 32), on(V("b2", 0, 8), src, 32), on(V("b2", 8, 16), src, 32), ALU.min)
            repeated(e)
        for i in range(4):
            tr(piece("fa", i), V("xb", H * i, H * i + H))
        handed("fa", "la")
        for b in (0, 1):
            p, a = mine + 32 * b, H * own + 32 * b
            tt(on(V("nr", 0, 2), p, 32), on(V("xz", a, a + M, H), p, 32), on(V("cv", 0, 2), p, 32), ALU.not_equal)
            tt(back(on(V("nr", 2, 4), p, 32)), on(V("xz", a + 64, a + 64 + H + 1, H), p, 32), back(on(V("cv", 2, 4), p, 32)), ALU.not_equal)
        affine(on(V("nr"), mine), on(V("nr"), mine), -2.0 * HM * NM, 0.0)

        def doubling(k):
            fi, fo, li, lo = ("fa", "fb", "la", "lb") if k % 2 == 0 else ("fb", "fa", "lb", "la")
            for i, by in ((0, "v"), (1, "s"), (3, "v"), (2, "s")):
                move(by, piece(fo, i), V(fi), V(li, 8 * i, 8 * i + 8))
            if k < 8:
                handed(fo, lo)
            else:
                handed(fo, lo, (own, own + 1), (mine // 64,))
            return fo

        for k in range(EARLY + 1):
            f = doubling(k)
        for j in range(4):
            for i in range(4):
                ts(V("ee", HM * j + H * i, HM * j + H * i + H), piece(f, i), V("cv", j, j + 1), ALU.is_equal, float(HM), ALU.mult)
            scan(V("so", M * j, M * j + M), V("ee", HM * j, HM * j + M), V("ee", HM * j + M, HM * j + HM), ALU.add, ALU.add, V("nr", j, j + 1))
        ends = V("so", M - 1, 4 * M, M)
        halves(on(V("aa"), 0), ends, ALU.add)
        halves(back(on(V("aa"), 64)), ends, ALU.add)
        for b in range(4):
            halves(on(V("ab"), 32 * b, 32), ends, ALU.add, 32 * ((b + 1) % 2), 32)
        for j in range(8):
            affine(V("xr", 32 * j, 32 * j + 32), V("fq", 32 * j, 32 * j + 32), 1.0, V("aa" if j < 4 else "ab", j % 4, j % 4 + 1))
        for h in (0, 1):
            tr(V("kf", *half[h]), V("xr", *half[h]))
        ms = "ms%d" % t
        MS = lambda d, ms=ms: V(ms, 4 * d, 4 * d + 4)
        EA = lambda i, h, n: V("ea", (H + 32) * (2 * i + h), (H + 32) * (2 * i + h) + n)
        for k in (0, 1):
            act(V("sg", M * k, M * k + M), V("kf"), AF.Sign, scale=-1.0, bias=CF(24 + k), accum=ACC(k))
        affine(V(ms, 4 * N + 1, 4 * N + 4, 2), V("acc", 0, 2), -0.5, (M - 1) / 2)
        for h in (0, 1):
            for i in (0, 1):
                ts(EA(i, h, H), V("kf", *half[h]), V("xr", 32 * i, 32 * i + 1), ALU.is_gt, 1.0 - 2.0 * second, ALU.mult)
        scan(V("pb", 0, H + 32), EA(0, 0, H + 32), EA(0, 1, H + 32), ALU.add, ALU.add)
        scan(back(V("pb", H + 32, 2 * H + 64)), EA(1, 0, H + 32), EA(1, 1, H + 32), ALU.add, ALU.add)
        tr(V("ps"), V("pb", H, H + 64))
        if second:
            ts(V(ms, 4 * N, 4 * N + 4, 2), V("pb", H, H + 64, 32), 0.5 - K, ALU.max, float(stand[rank] + K - 1), ALU.add)
        else:
            ts(V(ms, 4 * N, 4 * N + 4, 2), V("pb", H, H + 64, 32), K - 0.5, ALU.min, float(stand[rank]), ALU.add)
        spread(MS, "m%d_" % t + "%d", nearest, MS(N))
        dmas("dm%d" % t, [("y", A(MS(rank)), A(MS(N)), [MS(rank)], [MS(N)])])
        for k in range(KC):
            ts(V("dd", SEG * k + 1, SEG * k + SEG), V("ps"), V("want", k, k + 1), ALU.not_equal, float(NM), ALU.mult,
               (AF.Abs, float(NM), V("want", 8 + k, 9 + k)))
        scan(V("de", 0, SEG * KC), V("dd", 0, SEG * KC), V("di", 0, SEG * KC), ALU.min, ALU.add)
        for p in (0, 64):
            halves(on(V("e1", 0, KC), p), V("de", SEG - 1, SEG * KC, SEG), ALU.min)
        for b in range(4):
            tt(on(V("e2", 0, KC), 32 * b, 32), on(V("e1", 0, KC), 32 * b, 32), on(V("e1", 0, KC), 32 * (b ^ 1), 32), ALU.min)
        ts(V("j1", 0, KC), V("e2", 0, KC), CF(22), ALU.add, -1.0, ALU.mult)
        qz, sz, qb, sb, qp, pp = [n + str(t) for n in ("qz", "sz", "qb", "sb", "qp", "sp")]
        a = K * second
        pick(V(qz, a, a + K), V(sz, a, a + K), V(qc, 0, M), V(sp, 0, M), V("j1", 0, KC))
        swap(qz, sz, a, K - a, near, "ac%d" % t, "as%d" % t)
        col = lambda d, c: V(ms, 4 * (N if d == rank else d) + c, 4 * (N if d == rank else d) + c + 1)
        ts(V("km", 0, 32), V("kr"), col(pair[1], 3), ALU.subtract, col(pair[0], 1), ALU.min)
        tr(V("kt", 0, 32), V("km", 0, 32))
        red(V("kk", 4, 5), V("kt", 0, 32), ALU.max)
        ts(V("fl", 0, KC), V("ki", 0, KC), V("kk", 4, 5), ALU.is_gt, float(K), ALU.mult)
        tt(V("fl", 8, 8 + KC), V("fl", 0, KC), V("ki", 0, KC), ALU.add)
        cp(V("j2", 0, KC), V("fl", 8, 8 + KC))
        a = stand[rank]
        pick(V(qb, a, a + K), V(sb, a, a + K), V(qz), V(sz), V("j2", 0, KC))
        swap(qb, sb, a, stand[far], far, "bc%d" % t, "bs%d" % t)
        for s in range(4):
            for b in range(4):
                move("vsg", on(V("xz", 32 * s, NM, H), 32 * b, 32), on(V(ms, 0, 4 * N, 2), 32 * s, 32))
        for e in range(4):
            repeated(e)
            for k in (2 * e, 2 * e + 1):
                tr(grun("fs", k), V("xb", H * k, H * k + H))
        ge, gt = V(ms, 1, 4 * N, 4), V(ms, 3, 4 * N, 4)
        red(V("kk", 5, 6), gt, ALU.add, True)
        scan(V("kw"), gt, ge, ALU.add, ALU.subtract, V("kk", 5, 6))
        ts(V("kw"), V("kw"), K - 0.5 * N, ALU.add, 0.0, ALU.min)
        tt(V("km", 32, 160, 32), V("kw"), ge, ALU.add)
        scan(V("kt", 32, 160), V("d32", 0, H), V("km", 32, 160), ALU.mult, ALU.add)
        tr(V("ku"), V("kt", 32, 160))
        scan(V("kv"), V("d32", 0, H), V("ku"), ALU.mult, ALU.max)
        tt(V("kk", 0, N), V("kv", 31, H, 32), V("low"), ALU.add)
        if not final:
            height(7, t + 1, qc, sp, 0, M)
            for h in (0, 1):
                tr(V("ho", *half[h]), bank(7, H, H * h))
        for h in (0, 1):
            for b in range(4):
                mm(bank(4 * h + b, H), *unpack[b], V(qc, *half[h]), V(sp, *half[h]), True, False)
        for k in range(EARLY + 1, 9):
            doubling(k)
        rho, us, me = V("rho"), V("us"), V("me")
        for h in (0, 1):
            move("vs"[h], V("fr", *half[h]), V("fb"), V("lb", 8 * (own + h), 8 * (own + h) + 8))
            scan(on(V("s2", *half[h]), mine), on(V("d0", 0, H), mine), on(V("fr", *half[h]), mine), ALU.mult, ALU.add)
        for p in (0, 64):
            ts(on(V("lro"), p), on(V("s2", 15, M, 16), mine), on(GSCL, mine), ALU.mult, float(GM), ALU.add)
            affine(on(rho, p), on(V("s2", 15, M, 16), mine), on(GSCL, mine), float(GM))
        for h in (0, 1):
            move("vs"[h], V("rs", *half[h]), V("fs"), V("lro", 8 * h, 8 * h + 8))
            scan(V("s3", *half[h]), V("d0", 0, H), V("rs", *half[h]), ALU.mult, ALU.add)
        at = V("s3", 15, M, 16)
        ts(V("pl"), at, SCL, ALU.mult, float(PAD + 2 * K - 1), ALU.min)
        move("vs", V("rtf"), V("idn"), V("lro"))
        row = V("rtf", 0, M, 1, 0, 1)
        dmas("drt%d" % t, [("y", T.rt[0:1, M * t:M * t + M], A(row), [], [row])])
        for h in (0, 1):
            pick(V(qp, *half[h]), V(pp, *half[h]), V(qb), V(sb), V("pl", 8 * h, 8 * h + 8))
        for h in (0, 1):
            for b in range(4):
                mm(bank(4 * h + b, H), *unpack[b], V(qp, *half[h]), V(pp, *half[h]), False, True)
                ts(V("hb", 4 * H * h + b, 4 * H * h + 4 * H, 4), bank(4 * h + b, H), 0.5, ALU.mult, also=(AF.Identity, 0.5, 0.0))
        for h in (0, 1):
            quant(V(qc, M + H * h, M + H * h + H), V(sp, M + H * h, M + H * h + H), V("hb", 4 * H * h, 4 * H * h + 4 * H))
        flips = [d for d in range(1, N) if (d in seconds) != (d - 1 in seconds)]
        for i, d in enumerate(flips):
            o = V("sgn", 16 * min(i, 1), 16 * min(i, 1) + 16)
            ts(o, rho, place(M * d) - 0.5, ALU.is_lt, 2.0, ALU.mult)
            if i:
                ts(o, o, -1.0, ALU.add)
                tt(V("sgn", 0, 16), V("sgn", 0, 16), o, ALU.mult)
            else:
                ts(o, o, -1.0, ALU.add, SCL, ALU.mult)
        tt(us, at, V("sgn", 0, 16), ALU.mult)
        tt(V("self"), rho, V("sn"), ALU.is_equal)
        affine(V("iv", 0, H, 8), V("self"), -1.0, -float(beyond[0]))
        for d in range(N):
            if d:
                ts(V("iv", d, H, 8), rho, place(M * d) - 0.5, ALU.is_gt, float(beyond[d - 1] - beyond[d]), ALU.mult)
            ts(V("iv", 4 + d, H, 8), us, V("kk", d, d + 1), ALU.is_lt)
        scan(V("iw"), V("d8"), V("iv"), ALU.mult, ALU.add)
        member = V("iw", 7, H, 8)
        ts(me, member, 0.5, ALU.is_gt, float(M), ALU.mult)
        tt(me, me, V("ki"), ALU.add)
        cp(V("kl"), me)
        if not final:
            scan(V("px"), V("pd"), member, ALU.add, ALU.max)
            ts(V("mx1"), V("px", 1, 16, 2), CF(28), ALU.is_lt)
            ts(V("mx"), V("px", 1, 16, 2), CF(28), ALU.is_gt)
            tt(V("xo"), V("ho", 0, M, 32), V("mx1"), ALU.mult)
            for h in (0, 1):
                height(h, t + 1, qc, sp, M + H * h, H)
                tr(V("ht", *half[h]), bank(h, H))
                for c in range(4 * h, 4 * h + 4):
                    affine(V("xh%d" % (t + 1), 8 * rank + c, 8 * rank + c + 1), V("ht", 32 * c, 32 * c + 1), V("mx", c, c + 1), V("xo", c, c + 1))
            share(t + 1)
            pick(V(nq, 0, M), V(ns, 0, M), V(qc), V(sp), V("kl"))

    for h in (0, 1):
        pick(V(nq, *half[h]), V(ns, *half[h]), V(qc, 0, M + H * h + H), V(sp, 0, M + H * h + H), V("kl", 8 * h, 8 * h + 8))
        mm(bank(h, H), V("qw"), V("sw"), V(nq, *half[h]), V(ns, *half[h]), True, True)
        move("vs", V("ys", *half[h]), bank(h, H))
        dmas("dout", [("y", T.oc[:, 4 * H * h:4 * H * h + 4 * H], A(V(nq, *half[h])).bitcast(dt.uint8), [], [V(nq, *half[h])])])
        dmas("dout", [("ys"[h], T.y[:, H * h:H * h + H], A(V("ys", *half[h])), [], [V("ys", *half[h])])])
    for k in range(4):
        o = V(ns, 0, M, 1, 32 * k, 32 * k + 4)
        dmas("dout", [("ys"[k % 2], T.osc[4 * k:4 * k + 4, 0:M], A(o), [], [o])])

    for i, qn in ordered(calls):
        calls[i][1][0](qn)
    for sem in sorted(cnt):
        if max(known[q].get(sem, 0) for q in known) < cnt[sem]:
            queue["y" if sem == "dout" else "g"].wait_ge(T.sem[sem], cnt[sem])
